import numpy as np, ml_dtypes
CORES = [6,15,38,47]
N = 4
BF = ml_dtypes.bfloat16
W, H0, L, RO, Q = 4096, 1024, 256, 3, 3
def base(rng):
    price = rng.integers(0, 101, (N, 8, 1, W)) + rng.integers(0, 28, (N, 8, 16, W))
    packs = rng.integers(0, W, (N, 8, 16, H0)); prev = rng.integers(0, H0, (N, 8, H0)); lots = rng.integers(0, W, (N, 8, 16, L))
    lots[:, :, 0, ::4] = lots[:1, :, 0, ::4]
    o = np.stack([rng.permutation(np.array([5, 20, 35, 50, 60, 70, 80, 90])) for q in range(N)])
    slack = o[:, :, None, None] + rng.integers(0, 9, (N, 8, 16, RO))
    return price, packs, prev, lots, rng.integers(1, 8, (N, 8, 16)), rng.integers(0, 16, (N, 8, 16)), slack
def pack(price, packs, prev, lots, inc, wt, slack):
    c = lambda a, n: np.ascontiguousarray(np.reshape(a, (N, 128, n))).astype(np.int32)
    return {"price": np.ascontiguousarray(price.reshape(N, 128, W)).astype(np.float32).astype(BF), "packs": c(packs, H0), "prev": np.ascontiguousarray(prev).astype(np.int32),
            "lots": c(lots, L), "inc": c(inc, 1), "wt": c(wt, 1), "slack": c(slack, RO)}
def edge(rng, hi, *s):
    return np.where(rng.random(s) < 0.2, rng.integers(0, hi + 1, s), hi * rng.integers(0, 2, s))
def setup_inputs(rng):
    return pack(*base(rng))
def setup_inputs_spread(rng):
    price, packs, prev, lots, inc, wt, slack = base(rng)
    price = np.minimum((np.exp2(7.65 * rng.random((N, 8, 1, W))) * rng.random((N, 8, 16, W))).astype(np.int64), 200)
    packs = np.minimum((W * rng.random((N, 8, 16, H0)) ** 3).astype(np.int64), W - 1)
    lots = W - 1 - np.minimum((W * rng.random((N, 8, 16, L)) ** 2).astype(np.int64), W - 1)
    prev = np.minimum((H0 * rng.random((N, 8, H0)) ** 2).astype(np.int64), H0 - 1)
    slack = np.minimum(np.exp2(8 * rng.random((N, 8, 1, 1)) * rng.random((N, 8, 16, RO))).astype(np.int64) - 1, 255)
    return pack(price, packs, prev, lots, inc, wt, slack)
def setup_inputs_ends(rng):
    hi = np.where(np.arange(8) == 6, 127, 200)[None, :, None, None]
    k = rng.integers(0, 3, (N, 8, 1, W)); price = hi * np.where(k == 2, rng.integers(0, 2, (N, 8, 16, W)), k)
    price[..., 0] = 0; price[..., W - 1] = hi[..., 0]
    price[:, 2:4, :, 0] = 200; price[:, 2:4, :, W - 1] = 0; price[:, 5, 9:, W - 1] = 0
    packs = edge(rng, W - 1, N, 8, 16, H0); prev = edge(rng, H0 - 1, N, 8, H0); lots = edge(rng, W - 1, N, 8, 16, L)
    inc = 1 + 6 * rng.integers(0, 2, (N, 8, 16)); inc[:, 7] = 7; inc[:, 6, 0] = 1
    o = np.argsort(rng.random((N, 8, 16)), axis=2)
    slack = np.repeat((255 * (o >= np.array([16, 9, 16, 9, 12, 16, 8, 8])[None, :, None]))[..., None], RO, axis=3)
    wt = 15 * rng.integers(0, 2, (N, 8, 16)); wt[:, 7] = 0
    full = np.array([15] * 8 + [9] + [0] * 7); wt[:, 6] = full[o[:, 6]]; wt[:, 0] = full[o[:, 0]]
    c = np.array([0, 3, L - 1]); lots[:, 6, 0, c] = W - 1; lots[:, 6, 15, c] = W - 1
    v = np.arange(W)
    back = lambda t, to: int(np.argmax(((v + (v >> 5) + 77 * (t + 1)) & (W - 1)) == to))
    lots[:, 7, 0, c] = W - 1; lots[:, 7, 1, c] = back(0, W - 1); lots[:, 7, 2, c] = back(0, back(1, W - 1))
    return pack(price, packs, prev, lots, inc, wt, slack)
def setup_inputs_corners(rng):
    price, packs, prev, lots, inc, wt, slack = base(rng); a = np.arange(H0)
    kinds = [a, np.maximum(a - 1, 0), 0 * a, 0 * a + H0 - 1, (a + 1) % H0, a ^ 1, H0 - L + a % L]
    for q in range(N):
        for g, k in enumerate(rng.permutation(8)):
            if k < 7: prev[q, g] = kinds[int(k)]
            wt[q, g] = (0, 15, 1, 7)[int(rng.integers(0, 4))] if k < 4 else wt[q, g]
            inc[q, g] = 1 if k % 3 == 0 else 7 if k % 3 == 1 else inc[q, g]
    s = [int(g) for g in rng.permutation(8)]
    for g in s[:4]: slack[:, g] = 255
    lots[:, s[0], :RO] = W - 1; wt[:, s[0]] = 0; price[:, s[0], :, W - 1] = 127; inc[:, s[0]] = 7
    lots[:, s[1], 0] = 0; price[:, s[1], :, 0] = 127 * rng.integers(0, 2, (N, 16))
    m = rng.permutation(W); lots[:, s[2], 0] = m[(np.arange(N * L) % (W - 1) + 1).reshape(N, L)]; lots[int(rng.integers(0, N)), s[2], 0, L - 1] = m[0]
    for q in range(N): lots[q, s[3], 0] = rng.permutation(W)[:L]
    packs[:, s[4], :, H0 - L:] = lots[:, s[4]]
    slack[:, s[4]] = 0; slack[:, s[5]] = 0; h = W // 2
    price[:, s[5], :, :h] = rng.integers(0, 3, (N, 16, h)); price[:, s[5], :, h:] = 127; lots[:, s[5]] = rng.integers(h, W, (N, 16, L)); packs[:, s[5]] = rng.integers(0, h, (N, 16, H0))
    nxt = lambda z, u, t: (((z * (2 * u + 1)) >> 5) + z + 77 * (t + 1)) & (W - 1)
    g = s[6]; b = int(rng.integers(0, N)); k = L // 2
    wt[:, g] = 0; inc[:, g] = 7; inc[b, g] = 1 + rng.permutation(16) % 5
    slack[:, g] = 255; slack[:, g, :, RO - 1] = 254 - rng.integers(0, 55, (N, 16)) * (np.arange(N) % 2)[:, None]
    e = rng.integers(0, W, L); own = nxt(e, 0, 0); own[k:] = nxt(own[k:], 0, 1)
    lots[:, g, 0] = own; lots[:, g, 1, :k] = e[:k]; lots[:, g, 2, k:] = e[k:]
    dear = np.zeros(W, bool); dear[own] = True; low = rng.random(W) < 0.5
    v = 200 - (rng.random((N, 16, W)) * np.where(low, 32, 8)).astype(np.int64)
    v[b] = np.where(low, rng.integers(0, 4, (16, W)), v[b])
    price[:, g] = np.where(dear, v, rng.integers(0, 3, W))
    g = s[7]; wt[:, g] = 15; inc[:, g] = 7; slack[:, g] = 255; price[:, g] = 200
    e = rng.integers(0, W, L); lots[:, g, 1] = e; lots[:, g, 0] = nxt(e, (16 * 15 * 200) & 1023, 0)
    return pack(price, packs, prev, lots, inc, wt, slack)
def setup_inputs_ties(rng):
    price, packs, prev, lots, inc, wt, slack = base(rng)
    s0 = rng.integers(0, 21, (N, 8, 16)); b = rng.integers(0, 106, (N, 8, 16)); slack = np.repeat(s0[..., None], RO, axis=3)
    n = rng.choice(np.array([0, 7, 8, 9, 10, 16]), (N, 8, 1, W)); low = rng.random((N, 8, 1, W)) < 0.5
    o = np.argsort(rng.random((N, 8, W, 16)), axis=3).transpose(0, 1, 3, 2)
    price = b[..., None] + np.where(low, 0, s0[..., None] + (o < n))
    return pack(price, packs, prev, lots, inc, wt, slack)
def check_inputs(d):
    bad = []
    for k, lo, hi in (("price", 0, 200), ("packs", 0, W - 1), ("prev", 0, H0 - 1), ("lots", 0, W - 1), ("inc", 1, 7), ("wt", 0, 15), ("slack", 0, 255)):
        v = np.asarray(d[k]).astype(np.float64)
        if not (np.min(v) >= lo and np.max(v) <= hi): bad.append("range of " + k)
        elif np.any(v != np.floor(v)): bad.append("whole numbers in " + k)
    return bad
def pick(p, t):
    return np.take_along_axis(p, t.reshape(N, 8, 1, 16 * L), 3).reshape(N, 8, 16, 16, L)
def reference(price, packs, prev, lots, inc, wt, slack):
    p = price.astype(np.float32).astype(np.int64).reshape(N, 8, 16, W)
    h = np.zeros((N, 8, 16, H0 + RO * L), np.int64); h[..., :H0] = packs.reshape(N, 8, 16, H0)
    v = np.zeros((N, 8, H0 + RO * L), np.int64); v[..., :H0] = prev
    t = lots.astype(np.int64).reshape(N, 8, 16, L)
    up = inc.astype(np.int64).reshape(N, 8, 16, 1); wr = wt.astype(np.int64).reshape(N, 8, 16, 1); sl = slack.astype(np.int64).reshape(N, 8, 16, RO)
    a = np.zeros((N, 8, L), np.int64) + (H0 - L + np.arange(L))
    for rnd in range(RO):
        x = pick(p, t); bind = np.zeros((N, 8, L), np.int64) - 1
        for e in range(Q):
            anc = np.take_along_axis(h, a[:, :, None, :], 3); y = pick(p, anc)
            rows = np.add.reduce((x - y > sl[:, :, :, rnd][:, :, :, None, None]).astype(np.int64), axis=2)
            rev = rows >= 9
            t = np.where(rev, anc, t); x = np.where(rev[:, :, None], y, x)
            bind = np.where(np.any(rev, axis=2), a, bind); last = a
            a = np.take_along_axis(v, a, 2)
        lo = H0 + L * rnd
        h[..., lo:lo + L] = t; v[..., lo:lo + L] = np.where(bind >= 0, bind, last)
        flag = np.zeros((N, 8, W), np.int64); np.put_along_axis(flag, t[:, :, rnd], 1, 2)
        offer = p * flag[:, :, None]; s = np.add.reduce(offer, axis=0)[None] - offer
        if rnd + 1 < RO:
            u = np.add.reduce(wr * np.max(x, axis=3), axis=2) & 1023
            t = (((t * (2 * u + 1)[:, :, None]) >> 5) + t + 77 * (rnd + 1)) & (W - 1)
            a = np.zeros((N, 8, L), np.int64) + (lo + np.arange(L))
        p = np.minimum(p + ((up * s) >> 6), 255)
    return {"yp": p.reshape(N, 128, W).astype(np.float32).astype(BF), "yh": np.ascontiguousarray(h[..., H0:]).reshape(N, 128, RO * L).astype(np.float32), "yv": np.ascontiguousarray(v[..., H0:]).astype(np.float32)}

@@ -1,0 +1,699 @@
+import numpy as np
+from concourse.bass import DstId, RemoteDMATransfer
+from concourse.mybir import dt, AluOpType, AxisListType, ActivationFunctionType
+
+A = AluOpType
+AF = ActivationFunctionType
+LW = 272
+CH = [(0, 16), (16, 104), (104, 192), (192, 272)]
+NH = len(CH)
+RT = ["svvvvvssvvvv", "vvvvvvssvvvv", "vvvvvvssvvvv"]
+YR = ["sssssssvssss", "ssssvssvssss", "ssssvssssvsv"]
+MR = ["vss", "sss"]
+TG = [[1], [2, 3]]
+NE = 2176
+BIG = 32768.0
+SDUP = (0, 1, 2, 3, 4, 5, 6, 7)
+
+SCRATCH = {
+    "p0": ("sbuf", [128, 4096], "bfloat16"),
+    "F1": ("sbuf", [128, 4352], "float32"),
+    "F2": ("sbuf", [128, 4352], "float32"),
+    "F3": ("sbuf", [128, 4352], "float32"),
+    "pkI": ("sbuf", [128, 768], "int32"),
+    "pkJ": ("sbuf", [128, LW], "int32"),
+    "PK": ("sbuf", [128, 1792], "float32"),
+    "VT": ("sbuf", [128, 1024], "int32"),
+    "small": ("sbuf", [128, 8], "int32"),
+    "slI": ("sbuf", [128, 4], "int32"),
+    "sm": ("sbuf", [128, 32], "float32"),
+    "pI": ("sbuf", [128, 4], "int32"),
+    "row8": ("sbuf", [128, 8], "float32"),
+    "B8": ("sbuf", [128, 8], "float32"),
+    "one16": ("sbuf", [128, 16], "float32"),
+    "SELK": ("sbuf", [128, 2048], "bfloat16"),
+    "SELH": ("sbuf", [128, 2048], "float16"),
+    "ones": ("sbuf", [128, 128], "bfloat16"),
+    "cB": ("sbuf", [128, 384], "bfloat16"),
+    "IDN": ("sbuf", [128, 128], "float32"),
+    "onesF": ("sbuf", [128, 128], "float32"),
+    "IDB": ("sbuf", [128, 256], "bfloat16"),
+    "BD": ("sbuf", [128, 128], "bfloat16"),
+    "BE": ("sbuf", [128, 128], "bfloat16"),
+    "WT": ("sbuf", [128, 128], "bfloat16"),
+    "TT0": ("sbuf", [128, LW], "uint16"),
+    "TT1": ("sbuf", [128, LW], "uint16"),
+    "A16": ("sbuf", [128, 3 * LW], "uint16"),
+    "AE": ("sbuf", [128, 3 * LW], "float32"),
+    "Wt": ("sbuf", [128, LW], "int32"),
+    "WF": ("sbuf", [128, LW], "float32"),
+    "TI": ("sbuf", [128, LW], "int32"),
+    "TJ": ("sbuf", [128, LW], "int32"),
+    "Y": ("sbuf", [128, 48 * LW], "bfloat16"),
+    "C": ("sbuf", [128, 16 * LW], "bfloat16"),
+    "XS": ("sbuf", [128, 16 * LW], "bfloat16"),
+    "XM": ("sbuf", [128, 4096], "bfloat16"),
+    "SM": ("sbuf", [128, 4096], "bfloat16"),
+    "MK": ("sbuf", [128, 4096], "bfloat16"),
+    "SG": ("sbuf", [128, 768], "bfloat16"),
+    "uI": ("sbuf", [128, 256], "int32"),
+    "uJ": ("sbuf", [128, 256], "int32"),
+    "qF": ("sbuf", [128, 256], "float32"),
+    "qI": ("sbuf", [128, 256], "int32"),
+    "KY": ("sbuf", [128, 3, 32], "float32"),
+    "KB": ("sbuf", [128, 32], "float32"),
+    "KM": ("sbuf", [128, 3, 32], "float32"),
+    "k1": ("sbuf", [128, 32], "float32"),
+    "k2": ("sbuf", [128, 32], "float32"),
+    "kI": ("sbuf", [128, 32], "int32"),
+    "kJ": ("sbuf", [128, 32], "int32"),
+    "kF": ("sbuf", [128, 32], "float32"),
+    "LU": ("sbuf", [128, 64], "uint16"),
+    "i16": ("sbuf", [128, 16], "float32"),
+    "L1c": ("sbuf", [128, 16], "float32"),
+    "VH": ("sbuf", [128, 256], "float16"),
+    "PV": ("sbuf", [128, 48], "float32"),
+    "yvb": ("sbuf", [128, 384], "float32"),
+    "CF": ("sbuf", [128, 16], "float32"),
+    "IDW": ("sbuf", [128, 4096], "float32"),
+    "RB": ("sbuf", [128, 256], "float32"),
+    "IX": ("sbuf", [128, 256], "float32"),
+    "QM": ("sbuf", [128, 256], "bfloat16"),
+    "EQ": ("sbuf", [128, NE], "bfloat16"),
+    "EM": ("sbuf", [128, NE], "bfloat16"),
+    "SC": ("sbuf", [128, NE], "bfloat16"),
+    "E16": ("sbuf", [128, 2], "uint16"),
+    "DJ": ("sbuf", [128, 16], "float32"),
+    "DJt": ("sbuf", [128, 16], "float32"),
+    "dE": ("sbuf", [128, 16], "float32"),
+    "dF": ("sbuf", [128, 16], "float32"),
+    "dG": ("sbuf", [128, 16], "float32"),
+    "SV": ("sbuf", [128, 768], "bfloat16"),
+    "SL": ("sbuf", [128, 48], "uint16"),
+    "LV": ("sbuf", [128, 3 * 768], "bfloat16"),
+    "LL": ("sbuf", [128, 3 * 64], "uint16"),
+    "sv": ("sbuf", [128, 768], "float32"),
+    "g1": ("sbuf", [128, 512], "float32"),
+    "t1": ("sbuf", [128, 256], "float32"),
+    "i1": ("sbuf", [128, 768], "int32"),
+    "Z0": ("psum", [128, 512], "float32"),
+    "Z1": ("psum", [128, 512], "float32"),
+    "Z2": ("psum", [128, 512], "float32"),
+    "Z3": ("psum", [128, 512], "float32"),
+    "ZT": ("psum", [128, 512], "float32"),
+    "ZX": ("psum", [128, 512], "float32"),
+    "ZB": ("psum", [128, 3, 16], "float32"),
+    "ZM": ("psum", [128, 512], "float32"),
+}
+NDMA = 90
+SEMAPHORES = ["cv", "cs", "cp", "cg", "lsem", "arr0", "arr1", "arr2"] + ["d%d" % i for i in range(NDMA)]
+
+MODELS = [
+    (0.050, 0.92e-3, 1.35e-3, 2.8e-3, 0.70e-3, 0.08, 1.0, 4.5),
+    (0.045, 0.84e-3, 0.95e-3, 1.6e-3, 0.60e-3, 0.05, 0.8, 3.5),
+    (0.055, 1.20e-3, 2.40e-3, 5.5e-3, 0.95e-3, 0.10, 1.3, 7.0),
+    (0.050, 1.10e-3, 1.40e-3, 5.5e-3, 0.60e-3, 0.18, 0.8, 5.0),
+    (0.060, 1.00e-3, 1.90e-3, 2.0e-3, 0.80e-3, 0.05, 1.0, 4.0),
+    (0.065, 1.10e-3, 1.20e-3, 3.0e-3, 0.90e-3, 0.12, 1.0, 6.0),
+]
+TRIES = 1500
+
+
+def cv(n, per=1.0):
+    return (1.0, max(64, n * per), 0, 0, 0, 0)
+
+
+def cgat(n):
+    return (1.0, 0, n, 0, 0, 0)
+
+
+def csca(n):
+    return (1.0, 0, 0, n, 0, 0)
+
+
+def cmm(n, k=1):
+    return (0.2 * k, 0, 0, 0, k * max(64, n), 0)
+
+
+def cfix(x):
+    return (0, 0, 0, 0, 0, x)
+
+
+def price_ops(ops, md):
+    cost, lat = [], []
+    for o in ops:
+        c = o["cost"]
+        cost.append(c[0] * md[0] + c[1] * md[1] + c[2] * md[2] + c[3] * md[3] + c[4] * md[4] + c[5])
+        lat.append(o["lat"] * (md[6] if o["kind"] == "d" else 1.0) if o["kind"] != "n" else md[7])
+    return cost, lat
+
+
+def run_order(ops, order, cost, lat, wake):
+    free, fin = {}, [0.0] * len(ops)
+    end = 0.0
+    for i in order:
+        o = ops[i]
+        e = o["e"]
+        s = free.get(e, 0.0) if e != "n" else 0.0
+        for p in o["full"]:
+            if fin[p] + wake > s:
+                s = fin[p] + wake
+        f = s + cost[i]
+        free[e] = f
+        fin[i] = f + lat[i]
+        if fin[i] > end:
+            end = fin[i]
+    return end
+
+
+def schedule(ops, succ, prio, cost, lat, wake, window):
+    m = len(ops)
+    left = [len(o["full"]) + len(o["order"]) for o in ops]
+    ready = [0.0] * m
+    free, pend = {}, {}
+    for i, o in enumerate(ops):
+        free[o["e"]] = 0.0
+        pend.setdefault(o["e"], [])
+        if not left[i]:
+            pend[o["e"]].append(i)
+    names = sorted(pend)
+    start = [0.0] * m
+    for _ in range(m):
+        t0, e = 1e30, None
+        for x in names:
+            if pend[x]:
+                t = max(free[x], min(ready[i] for i in pend[x]))
+                if t < t0:
+                    t0, e = t, x
+        i = max((i for i in pend[e] if ready[i] <= t0 + window), key=lambda i: (prio[i], -i))
+        s = max(t0, ready[i])
+        start[i] = s
+        pend[e].remove(i)
+        free[e] = s + cost[i] if e != "n" else 0.0
+        for j, f in succ[i]:
+            ready[j] = max(ready[j], s + cost[i] + (lat[i] + wake if f else 0.0))
+            left[j] -= 1
+            if not left[j]:
+                pend[ops[j]["e"]].append(j)
+    return sorted(range(m), key=lambda i: (start[i], i))
+
+
+PLAN = {}
+
+
+def plan(ops):
+    if "order" in PLAN:
+        return PLAN["order"]
+    m = len(ops)
+    succ = [[] for _ in ops]
+    for i, o in enumerate(ops):
+        for p in o["full"]:
+            succ[p].append((i, True))
+        for p in o["order"]:
+            succ[p].append((i, False))
+    priced = [price_ops(ops, md) for md in MODELS]
+    cost, lat = priced[0]
+    base = [0.0] * m
+    for i in range(m - 1, -1, -1):
+        b = 0.0
+        for j, f in succ[i]:
+            b = max(b, base[j] + (lat[i] + MODELS[0][5] if f else 0.0))
+        base[i] = b + cost[i] + ops[i]["up"]
+    rng = np.random.default_rng(2)
+    ref, best, bestn = None, None, np.zeros(m)
+    for k in range(TRIES):
+        if k < 4:
+            noise, window = np.zeros(m), (0.05, 0.15, 0.3, 0.02)[k]
+        else:
+            noise = bestn + rng.normal(0.0, (40.0, 8.0)[k % 2], m) * (rng.random(m) < (0.1, 0.03, 0.01)[k % 3])
+            window = best[2] if k % 5 else float(rng.choice([0.02, 0.05, 0.1, 0.2]))
+        order = schedule(ops, succ, [base[i] + float(noise[i]) for i in range(m)], cost, lat, MODELS[0][5], window)
+        ts = [run_order(ops, order, c, l, md[5]) for (c, l), md in zip(priced, MODELS)]
+        if ref is None:
+            ref = ts
+        sc = sum(a / b for a, b in zip(ts, ref))
+        if best is None or sc < best[0]:
+            best, bestn = (sc, order, window, ts), noise
+    PLAN["order"] = best[1]
+    PLAN["ts"] = (ref, best[3])
+    return best[1]
+
+
+def rank_program(g, core, T, topo):
+    rank = T.rank_of(core)
+    if rank is None:
+        return
+    n = len(T.cores)
+    Q = {"v": g.vector, "s": g.scalar, "p": g.tensor, "g": g, "y": g.sync}
+    CSEM = {"v": "cv", "s": "cs", "p": "cp", "g": "cg"}
+    ops = []
+    lastw, readers = {}, {}
+
+    def add(e, kind, body, r, w, cost, lat=0.0, up=0.0, after=()):
+        i = len(ops)
+        full, order = set(), set()
+        comp = kind == "c"
+        for k in list(r) + list(after):
+            if k in lastw:
+                full.add(lastw[k])
+        for k in w:
+            if k in lastw:
+                full.add(lastw[k])
+            for x in readers.get(k, []):
+                if comp and ops[x]["e"] == e and ops[x]["kind"] == "c":
+                    order.add(x)
+                else:
+                    full.add(x)
+        full.discard(i)
+        ops.append({"e": e, "kind": kind, "body": body, "full": sorted(full), "order": sorted(order - full),
+                    "cost": cost, "lat": lat, "up": up})
+        for k in r:
+            readers.setdefault(k, []).append(i)
+        for k in w:
+            lastw[k] = i
+            readers[k] = []
+
+    def V(f, r=(), w=(), c=cv(1)):
+        add("v", "c", [f], r, w, c)
+
+    def S(f, r=(), w=(), c=cv(1)):
+        add("s", "c", [f], r, w, c)
+
+    def PE(fs, r=(), w=(), c=None):
+        fs = fs if isinstance(fs, list) else [fs]
+        add("p", "c", fs, r, w, c if c else cmm(16, len(fs)))
+
+    def G(f, r=(), w=(), c=cfix(0.2), after=()):
+        add("g", "c", [f], r, w, c, after=after)
+
+    def dma(e, pairs, r=(), w=(), lat=2.3, up=0.0, after=()):
+        add(e, "d", pairs, r, w, cfix(0.06 * len(pairs)), lat, up, after)
+
+    RF, GF, RQ, INC, WTF, SLF, SB, HF, C14, C15 = 0, 1, 2, 3, 4, 8, 12, 16, 17, 18
+    sm = T.sm
+    col = lambda c: sm[:, c:c + 1]
+    HA = range(NH)
+    HS = range(1, NH)
+    ALL = ["c"] + list(HS)
+    part = lambda h: ["c"] if h == 0 else [h]
+    TT = lambda t: T["TT%d" % (t % 2)]
+    tk = lambda t, hs: ["TT%d_%s" % (t % 2, h) for h in hs]
+    TIB = lambda t: T.TI if t % 2 == 0 else T.TJ
+    ik = lambda t, hs: [("TI_%s" if t % 2 == 0 else "TJ_%s") % h for h in hs]
+    ek = lambda e, hs: ["AE%d_%s" % (e, h) for h in hs]
+    win = lambda t: T.p0[:, 0:4096] if t == 0 else T["F%d" % t][:, 0:4096]
+    wkey = lambda t: ["win%d" % t]
+
+    def alist(t, e, a, b):
+        return TT(t - 1)[:, a:b] if e == 1 and t > 0 else T.A16[:, LW * (e - 1) + a:LW * (e - 1) + b]
+
+    def ak(t, e, hs):
+        return tk(t - 1, hs) if e == 1 and t > 0 else ["A16_%d_%s" % (e, h) for h in hs]
+
+    dma("y", [(T.pkJ[:, 16:LW], T.packs[:, 768:1024]), (T.pkJ[:, 0:16], T.packs[0:128:16, 768:1024])], w=["pkJ"], lat=3, up=2000)
+    dma("y", [(T.slI[:, 0:3], T.slack[:])], w=["slI"], lat=3, up=1800)
+    dma("y", [(T.p0[:], T.price[:])], w=["win0"], lat=5, up=1600)
+    dma("y", [(T.TI[:, 16:LW], T.lots[:]), (T.TI[:, 0:16], T.lots[0:128:16, :])], w=ik(0, ALL), lat=4, up=1500)
+    dma("s", [(T.VT[r:128:16, :], T.prev[:]) for r in range(8)], w=["VTa"], lat=7)
+    dma("y", [(T.VT[r:128:16, :], T.prev[:]) for r in range(8, 16)], w=["VTb"], lat=7)
+    dma("y", [(T.pkI[:], T.packs[:, 0:768])], w=["pkI"], lat=9)
+    dma("y", [(T.small[:, 0:1], T.inc[:]), (T.small[:, 4:5], T.wt[:])], w=["smallI"], lat=9)
+    VTR = ["VTa", "VTb"]
+
+    G(lambda q: q.iota(T.pI[:, 0:1], [[1, 1]], 0, 1), w=["pI"])
+    G(lambda q: q.iota(T.row8[:], [[1, 8]], 0, 0, allow_small_or_imprecise_dtypes=True), w=["row8"])
+    G(lambda q: q.iota(T.i16[:], [[16, 16]], 0, 0, allow_small_or_imprecise_dtypes=True), w=["i16"])
+
+    V(lambda q: q.memset(T.SELK[:], 0.0), w=["SELK"], c=cv(1024))
+    V(lambda q: q.memset(T.one16[:], 1.0), w=["one16"])
+    V(lambda q: q.memset(T.ones[:], 1.0), w=["ones"])
+    for i, x in enumerate((-8.5, -1.0, 15.0)):
+        V(lambda q, i=i, x=x: q.memset(T.cB[:, 128 * i:128 * i + 128], x * BIG), w=["cB%d" % i])
+    V(lambda q: q.tensor_scalar(T.pI[:, 1:2], T.pI[:, 0:1], 15, None, A.bitwise_and), r=["pI"], w=["pI1"])
+    V(lambda q: q.tensor_scalar(T.pI[:, 2:3], T.pI[:, 0:1], 4, None, A.logical_shift_right), r=["pI"], w=["pI2"])
+    V(lambda q: q.tensor_copy(col(RF), T.pI[:, 1:2]), r=["pI1"], w=["RF"])
+    V(lambda q: q.tensor_copy(col(GF), T.pI[:, 2:3]), r=["pI2"], w=["GF"])
+    V(lambda q: q.tensor_scalar(T.B8[:], T.row8[:], col(GF), None, A.is_equal), r=["row8", "GF"], w=["B8"])
+    V(lambda q: q.tensor_scalar(T.L1c[:], T.i16[:], col(RF), None, A.add), r=["i16", "RF"], w=["L1c"])
+    for gg in range(8):
+        V(lambda q, gg=gg: q.tensor_scalar(T.SELK[:, 16 * gg:16 * gg + 129 * 15 + 1:129], T.one16[:],
+                                           T.B8[:, gg:gg + 1], BIG, A.mult, A.mult),
+          r=["one16", "B8", "SELK"], w=["SELK%d" % gg])
+    SELK = ["SELK"] + ["SELK%d" % gg for gg in range(8)]
+    V(lambda q: q.tensor_copy(T.A16[:, 0:LW], T.pkJ[:]), r=["pkJ"], w=ak(0, 1, ALL), c=cv(LW))
+    V(lambda q: q.tensor_copy(sm[:, SLF:SLF + 3], T.slI[:, 0:3]), r=["slI"], w=["SLF"])
+    V(lambda q: q.tensor_copy(T.TT0[:], T.TI[:]), r=ik(0, ALL), w=tk(0, ALL), c=cv(LW))
+    V(lambda q: q.tensor_scalar(T.AE[:, 0:LW], T.pkJ[:], 4096.0, None, A.add), r=["pkJ"], w=ek(1, ALL), c=cv(LW))
+    V(lambda q: q.tensor_copy(T.VH[:], T.VT[:, 768:1024]), r=VTR, w=["VH"], c=cv(256))
+    V(lambda q: q.tensor_scalar(T.SELH[:], T.SELK[:], 1.0 / BIG, None, A.mult), r=SELK, w=["SELH"], c=cv(1024))
+    for e in range(3):
+        V(lambda q, e=e: q.memset(col(SB + e), 0.5 - 4096.0 * (e + 1)), w=["SB%d" % e])
+    V(lambda q: q.memset(col(HF), -0.5), w=["HF"])
+    V(lambda q: q.memset(T.onesF[:], 1.0), w=["onesF"], c=cv(128))
+    G(lambda q: q.affine_select(T.IDB[:, 0:128], T.ones[:], [[-1, 128]], A.is_equal, 0.0, 0, 1), r=["ones"], w=["IDB"], c=cfix(0.45))
+    V(lambda q: q.tensor_scalar(T.IDB[:, 128:256], T.IDB[:, 0:128], -1.0, None, A.mult), r=["IDB"], w=["IDM"])
+    G(lambda q: q.iota(T.IDW[:], [[1, 4096]], -2048, 0, allow_small_or_imprecise_dtypes=True), w=["IDW"], c=cfix(8.5))
+    G(lambda q: q.iota(T.IX[:], [[1, 256]], 0, 0, allow_small_or_imprecise_dtypes=True), w=["IX"], c=cfix(0.7))
+    G(lambda q: q.affine_select(T.IDN[:], T.onesF[:], [[-1, 128]], A.is_equal, 0.0, 0, 1), r=["onesF"], w=["IDN"], c=cfix(0.45))
+    V(lambda q: q.tensor_copy(T.PK[:, 768:1024], T.pkJ[:, 16:LW]), r=["pkJ"], w=["PKb"], c=cv(256))
+    V(lambda q: q.tensor_copy(T.PK[:, 0:768], T.pkI[:]), r=["pkI"], w=["PKa"], c=cv(768))
+    V(lambda q: q.memset(T.F1[:, 4096:4352], 0.0), w=["win1d"], c=cv(256))
+    V(lambda q: q.tensor_scalar(col(RQ), col(RF), 1.0, None, A.add), r=["RF"], w=["RQ"])
+    V(lambda q: q.tensor_scalar(T.QM[:], T.IX[:], col(RQ), 1.0e9, A.is_equal, A.mult), r=["IX", "RQ"], w=["QM"], c=cv(256))
+    seg = [256 * c - 8 * c * (c - 1) for c in range(17)]
+    dma("y", [(T.EM[:, seg[c]:seg[c + 1]], T.QM[:, 0:256 - 16 * c]) for c in range(16)], r=["QM"], w=["EM"])
+    V(lambda q: q.tensor_scalar(col(C14), col(RF), -8.0, 248.0, A.mult, A.add), r=["RF"], w=["c14"])
+    V(lambda q: q.tensor_tensor(col(C15), col(C14), col(RF), A.mult), r=["c14", "RF"], w=["c15"])
+    V(lambda q: q.tensor_scalar(T.E16[:, 0:1], col(C15), 255.0, None, A.add), r=["c15"], w=["E16"])
+    V(lambda q: q.tensor_scalar(T.DJt[:], T.L1c[:], 4096.0, None, A.add), r=["L1c"], w=["DJt"])
+    V(lambda q: q.tensor_scalar(T.dF[:], T.DJt[:], 4350.5, None, A.is_lt), r=["DJt"], w=["dF"])
+    V(lambda q: q.tensor_tensor(T.DJ[:], T.dF[:], T.DJt[:], A.mult), r=["dF", "DJt"], w=["DJ"])
+    V(lambda q: q.tensor_scalar(col(INC), T.small[:, 0:1], 1.0 / 64, None, A.mult), r=["smallI"], w=["INC"])
+    V(lambda q: q.tensor_copy(col(WTF), T.small[:, 4:5]), r=["smallI"], w=["WTF"])
+    G(lambda q: q.affine_select(T.BD[:], T.ones[:], [[-16, 8], [0, 16]], A.is_ge, 0.0, 0, 1), r=["ones"], w=["BD"], c=cfix(0.45))
+    G(lambda q: q.affine_select(T.BE[:], T.BD[:], [[16, 8], [0, 16]], A.is_ge, 0.0, 15, -1), r=["BD"], w=["BE"], c=cfix(0.45))
+    V(lambda q: q.tensor_scalar(T.WT[:], T.BE[:], col(WTF), None, A.mult), r=["BE", "WTF"], w=["WT"])
+
+    KY, KB = T.KY, T.KB
+    K2 = [(KY[:, 0, 16:32], "KY01", 4096.0), (KY[:, 1, 0:16], "KY10", 8192.0)]
+    K3 = [(KY[:, 1, 16:32], "KY11", 8192.0), (KY[:, 2, 0:16], "KY20", 12288.0), (KB[:, 0:16], "KB0", 0.0)]
+    K4 = [(KY[:, 2, 16:32], "KY21", 12288.0), (KB[:, 16:32], "KB1", 0.0)]
+
+    def conv(dst, keys):
+        PE([lambda q, k=k: q.matmul(T.ZM[:, 256:272], T.SELH[:, 128 * k:128 * k + 128], T.VH[:, k:256:16], k == 0, k == 15)
+            for k in range(16)], r=["VH", "SELH"], w=["bM"])
+        if dst < 48:
+            V(lambda q: q.tensor_scalar(T.LU[:, dst:dst + 16], T.ZM[:, 256:272], 1.0 / 16, None, A.mult), r=["bM"], w=["LU%d" % dst])
+        V(lambda q: q.tensor_scalar(T.kF[:, 0:16], T.ZM[:, 256:272], 1.0 / 16, None, A.mult), r=["bM"], w=["kF"])
+        for ap, nm, off in keys:
+            S(lambda q, ap=ap, off=off: q.activation(ap, T.kF[:, 0:16], AF.Copy, bias=off), r=["kF"], w=[nm])
+
+    def parents(src):
+        V(lambda q: q.tensor_copy(T.VH[:], T.VT[:, 0:1024].indirect(T.LU[:, src:src + 16])), r=VTR + ["LU%d" % src], w=["VH"], c=cgat(256))
+
+    def newest(t):
+        base = 768.0 + 256 * t
+        S(lambda q: q.activation(KY[:, 0, 0:16], T.L1c[:], AF.Copy, bias=base + 4096.0), r=["L1c"], w=["KY00"])
+
+    def package(t, e):
+        c, b = LW * (e - 1) + 16, 16 * (e - 1)
+        S(lambda q: q.activation(T.AE[:, c:c + 256], T.PK[:, 0:1024 + 256 * t].indirect(T.LU[:, b:b + 16]), AF.Copy, bias=4096.0 * e),
+          r=["PKa", "PKb"] + ["PK%d_%d" % (i, h) for i in range(t) for h in HS] + ["LU%d" % b], w=ek(e, HS), c=cgat(256))
+        V(lambda q: q.tensor_scalar(T.A16[:, c:c + 256], T.AE[:, c:c + 256], -4096.0 * e, None, A.add),
+          r=ek(e, HS), w=ak(t, e, HS), c=cv(256))
+
+    def clist(t, e):
+        if e == 0:
+            dma("y", [(TT(t)[:, 0:16], TT(t)[t:128:16, 16:LW])], r=tk(t, HS), w=tk(t, ["c"]))
+            dma("y", [(TIB(t)[:, 0:16], TIB(t)[t:128:16, 16:LW])], r=ik(t, HS), w=ik(t, ["c"]))
+        else:
+            o = LW * (e - 1)
+            dma("y", [(alist(t, e, 0, 16), alist(t, e, 16, LW)[t:128:16, :])], r=ak(t, e, HS), w=ak(t, e, ["c"]))
+            dma("y", [(T.AE[:, o:o + 16], T.AE[t:128:16, o + 16:o + LW])], r=ek(e, HS), w=ek(e, ["c"]))
+
+    blocks = lambda m: [(x, min(x + 512, 16 * m)) for x in range(0, 16 * m, 512)]
+
+    def gy(t, e, h):
+        a, b = CH[h]
+        o = 16 * (LW * (e - 1) + a)
+        out, lst = T.Y[:, o:o + 16 * (b - a)], win(t).indirect(alist(t, e, a, b))
+        r, w, c = wkey(t) + ak(t, e, part(h)) + ["SLF"], ["Y%d_%d" % (e, h)], cgat(16 * (b - a))
+        if YR[t][NH * (e - 1) + h] == "v":
+            V(lambda q: q.tensor_scalar(out, lst, col(SLF + t), None, A.add), r=r, w=w, c=c)
+        else:
+            S(lambda q: q.activation(out, lst, AF.Identity, bias=col(SLF + t)), r=r, w=w, c=c)
+
+    def gx(t, e, h):
+        a, b = CH[h]
+        o = 16 * LW * (e - 1)
+        c0, c1 = 16 * a, 16 * b
+        m = b - a
+        z = T["Z%d" % h]
+        lst = win(t).indirect(TT(t)[:, a:b])
+        r = wkey(t) + tk(t, part(h))
+        ck = ["C%d_%d" % (h, x) for x, y in blocks(m)]
+        if RT[t][NH * (e - 1) + h] == "v":
+            V(lambda q: q.tensor_tensor(T.C[:, c0:c1], lst, T.Y[:, o + c0:o + c1], A.is_gt), r=r + ["Y%d_%d" % (e, h)], w=ck, c=cgat(16 * m))
+            sh = 0
+        else:
+            S(lambda q: q.activation(T.XS[:, c0:c1], lst, AF.Copy), r=r, w=["XS%d" % h], c=cgat(16 * m))
+            for x, y in blocks(m):
+                PE([lambda q, x=x, y=y: q.matmul(T.ZX[:, 0:y - x], T.IDB[:, 0:128], T.XS[:, c0 + x:c0 + y], True, False),
+                    lambda q, x=x, y=y: q.matmul(T.ZX[:, 0:y - x], T.IDB[:, 128:256], T.Y[:, o + c0 + x:o + c0 + y], False, True)],
+                   r=["XS%d" % h, "IDB", "IDM", "Y%d_%d" % (e, h)], w=["bX"], c=cmm(y - x, 2))
+                S(lambda q, x=x, y=y: q.activation(T.C[:, c0 + x:c0 + y], T.ZX[:, 0:y - x], AF.Sign, bias=col(HF)),
+                  r=["bX", "HF"], w=["C%d_%d" % (h, x)], c=cv(y - x))
+            sh = 1
+        PE([lambda q: q.matmul(z[:, 0:m], T.cB[0:1, 128 * sh:128 * sh + 128], T.ones[0:1, 0:m], True, False)] +
+           [lambda q, k=k: q.matmul(z[:, 0:m], T.SELK[:, 128 * k:128 * k + 128], T.C[:, c0 + k:c1:16], False, k == 15)
+            for k in range(16)], r=ck + ["cB%d" % sh, "ones"] + SELK, w=["bZ%d" % h], c=cmm(m, 17))
+
+    def tops(t, e, h):
+        a, b = CH[h]
+        m = b - a
+        z, ti = T["Z%d" % h], TIB(t)
+        o = LW * (e - 1)
+        V(lambda q: q.tensor_tensor(T.ZT[:, a:b], z[:, 0:m], T.AE[:, o + a:o + b], A.min), r=["bZ%d" % h] + ek(e, part(h)), w=["bT%d" % h], c=cv(m))
+        cur, ck = (ti, ik(t, part(h))) if e == 1 else (T.Wt, ["W%d" % h])
+        if e < 3 or h == 0:
+            V(lambda q: q.tensor_tensor(T.Wt[:, a:b], T.ZT[:, a:b], cur[:, a:b], A.max), r=["bT%d" % h] + ck, w=["W%d" % h], c=cv(m))
+        else:
+            V(lambda q: q.tensor_tensor(T.WF[:, a:b], T.ZT[:, a:b], cur[:, a:b], A.max), r=["bT%d" % h] + ck, w=["WF%d" % h], c=cv(m))
+            V(lambda q: q.tensor_copy(T.Wt[:, a:b], T.WF[:, a:b]), r=["WF%d" % h], w=["W%d" % h], c=cv(m))
+        V(lambda q: q.tensor_scalar(ti[:, a:b], T.Wt[:, a:b], 4095, None, A.bitwise_and), r=["W%d" % h], w=ik(t, part(h)), c=cv(m))
+        V(lambda q: q.tensor_copy(TT(t)[:, a:b], ti[:, a:b]), r=ik(t, part(h)), w=tk(t, part(h)), c=cv(m))
+
+    def fin(t, h):
+        a, b = CH[h]
+        p = 1024 + 256 * t - 16
+        V(lambda q: q.tensor_copy(T.PK[:, p + a:p + b], TIB(t)[:, a:b]), r=ik(t, [h]), w=["PK%d_%d" % (t, h)], c=cv(b - a))
+        if t < 2:
+            S(lambda q: q.activation(T.AE[:, a:b], T.PK[:, p + a:p + b], AF.Copy, bias=4096.0), r=["PK%d_%d" % (t, h)], w=ek(1, [h]), c=cv(b - a))
+        for e in range(3):
+            S(lambda q, e=e: q.activation(T.SG[:, 256 * e + a - 16:256 * e + b - 16], T.WF[:, a:b], AF.Sign, bias=col(SB + e)),
+              r=["WF%d" % h, "SB%d" % e], w=["SG%d_%d" % (e, h)], c=cv(b - a))
+
+    def gm(t, h):
+        a, b = CH[h]
+        x, y = 16 * (a - 16), 16 * (b - 16)
+        lst = win(t).indirect(TT(t)[:, a:b])
+        r, w, c = wkey(t) + tk(t, [h]), ["XM%d" % h], cgat(y - x)
+        if MR[t][h - 1] == "v":
+            V(lambda q: q.tensor_copy(T.XM[:, x:y], lst), r=r, w=w, c=c)
+        else:
+            S(lambda q: q.activation(T.XM[:, x:y], lst, AF.Copy), r=r, w=w, c=c)
+        V(lambda q: q.tensor_tensor_scan(T.SM[:, x:y], T.MK[:, x:y], T.XM[:, x:y], 0.0, A.min, A.max),
+          r=["MK", "XM%d" % h], w=["SM%d" % h], c=cv((y - x) // 2))
+
+    def tnew(t, hs):
+        a, b = CH[hs[0]][0], CH[hs[-1]][1]
+        x, y = a - 16, b - 16
+        m = b - a
+        nm = str(hs[0])
+        uk = ["bT%d" % h for h in hs]
+        PE(lambda q: q.matmul(T.ZM[:, x:y], T.WT[:], T.SM[:, 16 * x + 15:16 * y:16], True, True), r=["WT"] + ["SM%d" % h for h in hs], w=["bM"], c=cmm(m))
+        V(lambda q: q.tensor_copy(T.uI[:, x:y], T.ZM[:, x:y]), r=["bM"], w=["uI" + nm], c=cv(m))
+        V(lambda q: q.tensor_scalar(T.uJ[:, x:y], T.uI[:, x:y], 1023, None, A.bitwise_and), r=["uI" + nm], w=["uJ" + nm], c=cv(m))
+        V(lambda q: q.tensor_scalar(T.ZT[:, a:b], T.uJ[:, x:y], 2.0, 33.0, A.mult, A.add), r=["uJ" + nm], w=uk, c=cv(m))
+        V(lambda q: q.tensor_tensor(T.qF[:, x:y], T.ZT[:, a:b], TIB(t)[:, a:b], A.mult), r=uk + ik(t, hs), w=["qF" + nm], c=cv(m))
+        V(lambda q: q.tensor_scalar(T.qI[:, x:y], T.qF[:, x:y], 2464.0 * (t + 1), None, A.add), r=["qF" + nm], w=["qI" + nm], c=cv(m))
+        V(lambda q: q.tensor_scalar(TIB(t + 1)[:, a:b], T.qI[:, x:y], 5, 4095, A.logical_shift_right, A.bitwise_and),
+          r=["qI" + nm], w=ik(t + 1, hs), c=cv(m))
+        V(lambda q: q.tensor_copy(TT(t + 1)[:, a:b], TIB(t + 1)[:, a:b]), r=ik(t + 1, hs), w=tk(t + 1, hs), c=cv(m))
+
+    def bind(t):
+        PE([lambda q: q.matmul(T.ZB[:], T.cB[0:1, 256:384], T.ones[0:1, 0:48], True, False)] +
+           [lambda q, k=k: q.matmul(T.ZB[:], T.SELK[:, 128 * k:128 * k + 128], T.SG[:, k:768:16], False, k == 15) for k in range(16)],
+           r=["SG%d_%d" % (e, h) for e in range(3) for h in HS] + SELK + ["cB2", "ones"], w=["bB"])
+        c = 16 if t == 2 else 32
+        ds = range(c // 16)
+        for d in ds:
+            V(lambda q, d=d: q.tensor_tensor(T.KM[:, :, 16 * d:16 * d + 16], T.ZB[:], KY[:, :, 16 * d:16 * d + 16], A.min),
+              r=["bB"] + ["KY%d%d" % (e, d) for e in range(3)], w=["KM%d" % d])
+        V(lambda q: q.tensor_tensor(T.k1[:, 0:c], T.KM[:, 0, 0:c], T.KM[:, 1, 0:c], A.max), r=["KM%d" % d for d in ds], w=["k1"])
+        V(lambda q: q.tensor_tensor(T.k2[:, 0:c], T.k1[:, 0:c], T.KM[:, 2, 0:c], A.max), r=["k1"] + ["KM%d" % d for d in ds], w=["k2"])
+        V(lambda q: q.tensor_tensor(T.kI[:, 0:c], T.k2[:, 0:c], KB[:, 0:c], A.max), r=["k2"] + ["KB%d" % d for d in ds], w=["kI"])
+        V(lambda q: q.tensor_scalar(T.kJ[:, 0:c], T.kI[:, 0:c], 4095, None, A.bitwise_and), r=["kI"], w=["kJ"])
+        if t < 2:
+            V(lambda q: q.tensor_copy(T.LU[:, 16:48], T.kJ[:]), r=["kJ"], w=["LU16", "LU32"])
+            V(lambda q: q.tensor_copy(T.kF[:], T.kJ[:]), r=["kJ"], w=["kF"])
+            S(lambda q: q.activation(T.PV[:, 16 * t:16 * t + 16], T.kF[:, 0:16], AF.Copy), r=["kF"], w=["PV%d" % t])
+            S(lambda q: q.activation(KY[:, 0, 16:32], T.kF[:, 0:16], AF.Copy, bias=4096.0), r=["kF"], w=["KY01"])
+            S(lambda q: q.activation(KY[:, 1, :], T.kF[:], AF.Copy, bias=8192.0), r=["kF"], w=["KY10", "KY11"])
+            S(lambda q: q.activation(KY[:, 2, 0:16], T.kF[:, 16:32], AF.Copy, bias=12288.0), r=["kF"], w=["KY20"])
+            S(lambda q: q.activation(KB[:, 0:16], T.kF[:, 16:32], AF.Copy), r=["kF"], w=["KB0"])
+            newest(t + 1)
+        else:
+            V(lambda q: q.tensor_copy(T.PV[:, 32:48], T.kJ[:, 0:16]), r=["kJ"], w=["PV2"])
+
+    def outv(t):
+        PE(lambda q: q.matmul(T.ZM[0:16, 384:512], T.PV[:, 16 * t:16 * t + 16], T.IDN[:], True, True), r=["PV%d" % t, "IDN"], w=["bM"], c=cmm(128, 4))
+        V(lambda q: q.tensor_copy(T.yvb[0:16, 128 * t:128 * t + 128], T.ZM[0:16, 384:512]), r=["bM"], w=["yvb%d" % t], c=cv(128))
+        for i, e in enumerate(("y", "s") if t == 2 else ("y",)):
+            gs = range(8)[i::2] if t == 2 else range(8)
+            dma(e, [(T.yv[gg:gg + 1, 256 * t:256 * t + 256], T.yvb[0:16, 128 * t + 16 * gg:128 * t + 16 * gg + 16]) for gg in gs],
+                r=["yvb%d" % t], w=["yv%d_%d" % (t, i)])
+
+    def outh(t, hs):
+        a, b = CH[hs[0]][0] - 16, CH[hs[-1]][1] - 16
+        p = 1024 + 256 * t
+        dma("y", [(T.yh[:, 256 * t + a:256 * t + b], T.PK[:, p + a:p + b])], r=["PK%d_%d" % (t, h) for h in hs], w=["yh%d_%d" % (t, a)])
+
+    def dedupe(t):
+        cl, ci, ck, cik = TT(t)[:, 0:16], TIB(t)[:, 0:16], tk(t, ["c"]), ik(t, ["c"])
+        S(lambda q: q.activation(T.SV[:, 256 * t:256 * t + 256], win(t).indirect(cl), AF.Copy), r=wkey(t) + ck, w=["SV%d" % t], c=cgat(256))
+        S(lambda q: q.activation(T.RB[:], T.IDW[:].indirect(cl), AF.Copy), r=["IDW"] + ck, w=["RB"], c=cgat(256))
+        V(lambda q: q.tensor_scalar(T.CF[:], ci, -1.0, 2048.0, A.mult, A.add), r=cik, w=["CF"])
+        for c in range(16):
+            if c in SDUP:
+                S(lambda q, c=c: q.activation(T.EQ[:, seg[c]:seg[c + 1]], T.RB[:, 16 * c:256], AF.Square, bias=T.CF[:, c:c + 1]),
+                  r=["RB", "CF"], w=["EQ%d" % c], c=cv(256 - 16 * c))
+            else:
+                V(lambda q, c=c: q.tensor_scalar(T.EQ[:, seg[c]:seg[c + 1]], T.RB[:, 16 * c:256], T.CF[:, c:c + 1], 0.0, A.add, A.not_equal),
+                  r=["RB", "CF"], w=["EQ%d" % c], c=cv(256 - 16 * c))
+        V(lambda q: q.tensor_tensor_scan(T.SC[:], T.EM[:], T.EQ[:], 1.0e9, A.max, A.min), r=["EM"] + ["EQ%d" % c for c in range(16)], w=["SC"], c=cv(NE, .5))
+        V(lambda q: q.tensor_scalar(T.dE[:], T.SC[:].indirect(T.E16[:, 0:1]), 0.5, None, A.is_lt), r=["SC", "E16"], w=["dE"])
+        V(lambda q: q.tensor_tensor(T.dF[:], T.dE[:], T.DJ[:], A.mult), r=["dE", "DJ"], w=["dF"])
+        V(lambda q: q.tensor_tensor(T.dG[:], T.dF[:], ci, A.max), r=["dF"] + cik, w=["dG"])
+        V(lambda q: q.tensor_copy(T.SL[:, 16 * t:16 * t + 16], T.dG[:]), r=["dG"], w=["SL%d" % t])
+
+    others = [d for d in range(n) if d != rank]
+    common = [e for e in topo.engines(core, T.cores[others[0]]) if all(e in topo.engines(core, T.cores[d]) for d in others)]
+    mask = sum(1 << e for e in common)
+
+    def send(t):
+        for key, buf, land, w, st in (("SV%d" % t, T.SV, T.LV, 256, 768), ("SL%d" % t, T.SL, T.LL, 16, 64)):
+            ids, dsts = [], []
+            for d in others:
+                rid, pid = topo.addr(T.cores[d])[0:2]
+                slot = (rank - d - 1) % n
+                ids.append(DstId(rid=rid, pnc=pid))
+                dsts.append(land[:, st * t + w * slot:st * t + w * slot + w])
+            tr = RemoteDMATransfer(dst_ids=ids, dma_engine_mask=mask, remote_sem=T.sem["arr%d" % t],
+                                   srcs=[buf[:, w * t:w * t + w]], dsts=dsts, alu_op=0)
+            add("g", "r", tr, [key], ["sent" + key], cfix(1.0))
+        add("n", "n", ("arr%d" % t, 2 * len(common) * len(others)), ["sentSV%d" % t, "sentSL%d" % t], ["LV%d" % t], cfix(0.0), 1.0)
+
+    def update(t):
+        F = T["F%d" % (t + 1)]
+        fk = "win%d" % (t + 1)
+        L = lambda a, b: T.LL[:, 64 * t + 16 * a:64 * t + 16 * b]
+        lk = "LV%d" % t
+        cols = lambda i: slice(256 * i, 256 * i + 256)
+        S(lambda q: q.activation(T.sv[:], T.LV[:, 768 * t:768 * t + 768], AF.Copy, scale=col(INC)), r=[lk, "INC"], w=["sv"], c=cv(768))
+        fr = [fk, "win1d", lk] if t == 0 else [fk, lk]
+        for i in range(2):
+            S(lambda q, i=i: q.activation(T.g1[:, cols(i)], F[:].indirect(L(i, i + 1)), AF.Copy), r=fr, w=["g1_%d" % i], c=cgat(256))
+            V(lambda q, i=i: q.tensor_tensor(F[:].indirect(L(i, i + 1)), T.g1[:, cols(i)], T.sv[:, cols(i)], A.add), r=["g1_%d" % i, "sv", lk], w=[fk], c=csca(256))
+        V(lambda q: q.tensor_tensor(T.t1[:], F[:].indirect(L(2, 3)), T.sv[:, 512:768], A.add), r=fr + ["sv"], w=["t1"], c=cgat(256))
+        V(lambda q: q.tensor_scalar(T.i1[:, 512:768], T.t1[:], -0.4921875, 255.0, A.add, A.min), r=["t1"], w=["i1b"], c=cv(256))
+        V(lambda q: q.tensor_copy(F[:].indirect(L(2, 3)), T.i1[:, 512:768]), r=["i1b", lk], w=[fk], c=csca(256))
+        V(lambda q: q.tensor_scalar(T.i1[:, 0:512], F[:].indirect(L(0, 2)), -0.4921875, 255.0, A.add, A.min), r=[fk, lk], w=["i1a"], c=cgat(512))
+        for i in range(2):
+            V(lambda q, i=i: q.tensor_copy(F[:].indirect(L(i, i + 1)), T.i1[:, cols(i)]), r=["i1a", lk], w=[fk], c=csca(256))
+
+    newest(0)
+    conv(16, K2)
+    parents(16)
+    conv(32, K3)
+    package(0, 2)
+    package(0, 3)
+    clist(0, 2)
+    clist(0, 3)
+    for t in range(3):
+        late = tk(t, ["c"]) + ik(t, ["c"]) + [k for e in (1, 2, 3) for k in ak(t, e, ["c"]) + ek(e, ["c"])]
+        if t == 0:
+            G(lambda q: q.iota(T.MK[:], [[0, 256], [256, 16]], 0, 0, allow_small_or_imprecise_dtypes=True), w=["MK"], c=cfix(8.5), after=late)
+            dma("g", [(T.F1[:, 0:4096], T.price[:])], r=["win0"], w=["win1"], lat=6, after=late)
+        else:
+            dma("y", [(T["F%d" % (t + 1)][:], T["F%d" % t][:])], r=["win%d" % t] + (["win1d"] if t == 1 else []), w=["win%d" % (t + 1)], lat=5, after=late)
+        for e in (1, 2, 3):
+            for h in HA:
+                gy(t, e, h)
+            for h in HA:
+                gx(t, e, h)
+            for h in HA:
+                tops(t, e, h)
+        dedupe(t)
+        send(t)
+        if t < 2:
+            parents(32)
+            conv(48, K4)
+        update(t)
+        if t == 2:
+            dma("g", [(T.yp[:], T.F3[:, 0:4096])], r=["win3"], w=["yp"], lat=6)
+        for h in HS:
+            fin(t, h)
+        if t < 2:
+            for h in HS:
+                gm(t, h)
+            for hs in TG:
+                tnew(t, hs)
+            clist(t + 1, 1)
+            clist(t + 1, 0)
+            outh(t, list(HS))
+        else:
+            for h in HS:
+                outh(t, [h])
+        bind(t)
+        outv(t)
+        if t < 2:
+            package(t + 1, 2)
+            package(t + 1, 3)
+            clist(t + 1, 2)
+            clist(t + 1, 3)
+
+    order = plan(ops)
+    total, snap, tok = {}, {}, {}
+    seen = {e: {} for e in Q}
+    nd = [0]
+
+    def merge(d, s, v):
+        if d.get(s, 0) < v:
+            d[s] = v
+
+    def sync(e, toks):
+        best = {}
+        for s, v in toks:
+            if seen[e].get(s, 0) < v:
+                merge(best, s, v)
+        for s in sorted(best):
+            if any(o != s and best[o] and snap.get((o, best[o]), {}).get(s, 0) >= best[s] for o in best):
+                best[s] = 0
+        for s in sorted(best):
+            v = best[s]
+            if v:
+                Q[e].wait_ge(T.sem[s], v)
+                merge(seen[e], s, v)
+                for o, w in snap.get((s, v), {}).items():
+                    merge(seen[e], o, w)
+
+    for i in order:
+        o = ops[i]
+        e, kind, body = o["e"], o["kind"], o["body"]
+        if kind == "n":
+            total[body[0]] = body[1]
+            tok[i] = body
+            continue
+        sync(e, [tok[p] for p in o["full"] if p in tok])
+        if kind == "c":
+            s = CSEM[e]
+            for f in body:
+                f(Q[e]).then_inc(T.sem[s], 1)
+                total[s] = total.get(s, 0) + 1
+                snap[(s, total[s])] = dict(seen[e])
+            tok[i] = (s, total[s])
+        elif kind == "d":
+            s = "d%d" % nd[0]
+            nd[0] += 1
+            for out, in_ in body:
+                Q[e].dma_start(out, in_).then_inc(T.sem[s], 16)
+            total[s] = 16 * len(body)
+            tok[i] = (s, total[s])
+            snap[tok[i]] = dict(seen[e])
+        else:
+            g.remote_dma_fused([body], local_sem=T.sem.lsem)
+            total["lsem"] = total.get("lsem", 0) + len(common)
+    for s in sorted(total):
+        if seen["g"].get(s, 0) < total[s]:
+            g.wait_ge(T.sem[s], total[s])

@@ -5,15 +5,23 @@ from concourse.mybir import dt, AluOpType, AxisListType, ActivationFunctionType
 A = AluOpType
 AF = ActivationFunctionType
 LW = 272
-CH = [(0, 16), (16, 104), (104, 192), (192, 272)]
-NH = len(CH)
-RT = ["svvvvvssvvvv", "vvvvvvssvvvv", "vvvvvvssvvvv"]
-YR = ["sssssssvssss", "ssssvssvssss", "ssssvssssvsv"]
-MR = ["vss", "sss"]
-TG = [[1], [2, 3]]
+CH = [(0, 128), (128, 192), (192, 256), (256, 272)]
+PCS = [(256, 272), (0, 64), (64, 128), (128, 192), (192, 256)]
+RT = ["vvvvv" * 3] * 3
+YR = ["svsss" + "sssss" * 2] + ["sssss" * 3] * 2
+MR = ["ssss", "ssss"]
+TG = [[0], [1, 2, 3]]
 NE = 2176
 BIG = 32768.0
-SDUP = (0, 1, 2, 3, 4, 5, 6, 7)
+SQ = 8192.0
+SDUP = tuple(range(12))
+LATE = (True, True, True)
+HOT = 0.0
+XB = 2.0
+NF = 8
+FLS = ("ssv", "ssv", "vsv")
+MCV = "s"
+MAGIC = 1.5 * 2 ** 23
 
 SCRATCH = {
     "p0": ("sbuf", [128, 4096], "bfloat16"),
@@ -33,47 +41,45 @@ SCRATCH = {
     "one16": ("sbuf", [128, 16], "float32"),
     "SELK": ("sbuf", [128, 2048], "bfloat16"),
     "SELH": ("sbuf", [128, 2048], "float16"),
-    "ones": ("sbuf", [128, 128], "bfloat16"),
-    "cB": ("sbuf", [128, 384], "bfloat16"),
-    "IDN": ("sbuf", [128, 128], "float32"),
-    "onesF": ("sbuf", [128, 128], "float32"),
-    "IDB": ("sbuf", [128, 256], "bfloat16"),
-    "BD": ("sbuf", [128, 128], "bfloat16"),
-    "BE": ("sbuf", [128, 128], "bfloat16"),
+    "SELW": ("sbuf", [128, 2048], "bfloat16"),
+    "ones": ("sbuf", [128, LW], "bfloat16"),
+    "cB": ("sbuf", [128, 256], "bfloat16"),
+    "IDN": ("sbuf", [128, 256], "float32"),
+    "IDH": ("sbuf", [128, 256], "float16"),
+    "IDB": ("sbuf", [128, 384], "bfloat16"),
+    "IXG": ("sbuf", [128, 128], "float32"),
     "WT": ("sbuf", [128, 128], "bfloat16"),
     "TT0": ("sbuf", [128, LW], "uint16"),
     "TT1": ("sbuf", [128, LW], "uint16"),
-    "A16": ("sbuf", [128, 3 * LW], "uint16"),
-    "AE": ("sbuf", [128, 3 * LW], "float32"),
-    "Wt": ("sbuf", [128, LW], "int32"),
-    "WF": ("sbuf", [128, LW], "float32"),
+    "TH0": ("sbuf", [128, LW], "float16"),
+    "TH1": ("sbuf", [128, LW], "float16"),
     "TI": ("sbuf", [128, LW], "int32"),
-    "TJ": ("sbuf", [128, LW], "int32"),
+    "A16": ("sbuf", [128, 3 * LW], "uint16"),
+    "AE": ("sbuf", [128, 2 * LW], "float32"),
     "Y": ("sbuf", [128, 48 * LW], "bfloat16"),
     "C": ("sbuf", [128, 16 * LW], "bfloat16"),
-    "XS": ("sbuf", [128, 16 * LW], "bfloat16"),
+    "XS": ("sbuf", [128, 1024], "bfloat16"),
     "XM": ("sbuf", [128, 4096], "bfloat16"),
     "SM": ("sbuf", [128, 4096], "bfloat16"),
-    "MK": ("sbuf", [128, 4096], "bfloat16"),
+    "MI": ("sbuf", [128, 1024], "bfloat16"),
+    "MK": ("sbuf", [128, 1024], "bfloat16"),
     "SG": ("sbuf", [128, 768], "bfloat16"),
-    "uI": ("sbuf", [128, 256], "int32"),
-    "uJ": ("sbuf", [128, 256], "int32"),
-    "qF": ("sbuf", [128, 256], "float32"),
-    "qI": ("sbuf", [128, 256], "int32"),
+    "MC": ("sbuf", [128, 16], "bfloat16"),
+    "kf": ("sbuf", [128, LW], "bfloat16"),
+    "qF": ("sbuf", [128, LW], "float32"),
+    "qI": ("sbuf", [128, LW], "int32"),
+    "KS": ("sbuf", [128, 64], "float32"),
     "KY": ("sbuf", [128, 3, 32], "float32"),
-    "KB": ("sbuf", [128, 32], "float32"),
-    "KM": ("sbuf", [128, 3, 32], "float32"),
-    "k1": ("sbuf", [128, 32], "float32"),
-    "k2": ("sbuf", [128, 32], "float32"),
+    "KM": ("sbuf", [128, 4, 32], "float32"),
+    "k1": ("sbuf", [128, 2, 32], "float32"),
     "kI": ("sbuf", [128, 32], "int32"),
     "kJ": ("sbuf", [128, 32], "int32"),
-    "kF": ("sbuf", [128, 32], "float32"),
-    "LU": ("sbuf", [128, 64], "uint16"),
+    "LU": ("sbuf", [128, 48], "uint16"),
     "i16": ("sbuf", [128, 16], "float32"),
     "L1c": ("sbuf", [128, 16], "float32"),
     "VH": ("sbuf", [128, 256], "float16"),
-    "PV": ("sbuf", [128, 48], "float32"),
-    "yvb": ("sbuf", [128, 384], "float32"),
+    "VG": ("sbuf", [128, 256], "float16"),
+    "YV": ("sbuf", [128, 768], "float32"),
     "CF": ("sbuf", [128, 16], "float32"),
     "IDW": ("sbuf", [128, 4096], "float32"),
     "RB": ("sbuf", [128, 256], "float32"),
@@ -87,7 +93,6 @@ SCRATCH = {
     "DJt": ("sbuf", [128, 16], "float32"),
     "dE": ("sbuf", [128, 16], "float32"),
     "dF": ("sbuf", [128, 16], "float32"),
-    "dG": ("sbuf", [128, 16], "float32"),
     "SV": ("sbuf", [128, 768], "bfloat16"),
     "SL": ("sbuf", [128, 48], "uint16"),
     "LV": ("sbuf", [128, 3 * 768], "bfloat16"),
@@ -96,27 +101,28 @@ SCRATCH = {
     "g1": ("sbuf", [128, 512], "float32"),
     "t1": ("sbuf", [128, 256], "float32"),
     "i1": ("sbuf", [128, 768], "int32"),
+    "r1": ("sbuf", [128, 768], "float32"),
+    "r2": ("sbuf", [128, 768], "float32"),
     "Z0": ("psum", [128, 512], "float32"),
     "Z1": ("psum", [128, 512], "float32"),
     "Z2": ("psum", [128, 512], "float32"),
     "Z3": ("psum", [128, 512], "float32"),
-    "ZT": ("psum", [128, 512], "float32"),
     "ZX": ("psum", [128, 512], "float32"),
     "ZB": ("psum", [128, 3, 16], "float32"),
     "ZM": ("psum", [128, 512], "float32"),
+    "ZR": ("psum", [128, 512], "float32"),
 }
-NDMA = 90
-SEMAPHORES = ["cv", "cs", "cp", "cg", "lsem", "arr0", "arr1", "arr2"] + ["d%d" % i for i in range(NDMA)]
+NDMA = 70
+SEMAPHORES = ["cv", "cs", "cp", "cg", "lsem"] + ["arrS%s%d" % (x, t) for x in "VL" for t in range(3)] + ["d%d" % i for i in range(NDMA)]
 
 MODELS = [
-    (0.050, 0.92e-3, 1.35e-3, 2.8e-3, 0.70e-3, 0.08, 1.0, 4.5),
-    (0.045, 0.84e-3, 0.95e-3, 1.6e-3, 0.60e-3, 0.05, 0.8, 3.5),
-    (0.055, 1.20e-3, 2.40e-3, 5.5e-3, 0.95e-3, 0.10, 1.3, 7.0),
-    (0.050, 1.10e-3, 1.40e-3, 5.5e-3, 0.60e-3, 0.18, 0.8, 5.0),
-    (0.060, 1.00e-3, 1.90e-3, 2.0e-3, 0.80e-3, 0.05, 1.0, 4.0),
-    (0.065, 1.10e-3, 1.20e-3, 3.0e-3, 0.90e-3, 0.12, 1.0, 6.0),
+    (0.02, 0.88e-3, 1.20e-3, 2.8e-3, 0.80e-3, 0.10, 2.0, 5.0, 0.04, 0.07e-3),
+    (0.01, 0.85e-3, 0.98e-3, 1.9e-3, 0.85e-3, 0.06, 1.8, 6.0, 0.03, 0.05e-3),
+    (0.02, 1.20e-3, 1.95e-3, 4.8e-3, 1.20e-3, 0.10, 2.2, 4.5, 0.04, 0.08e-3),
+    (0.04, 0.92e-3, 1.75e-3, 1.9e-3, 0.60e-3, 0.15, 2.5, 3.5, 0.06, 0.04e-3),
+    (0.01, 0.95e-3, 1.10e-3, 4.0e-3, 0.90e-3, 0.15, 2.0, 7.0, 0.03, 0.09e-3),
 ]
-TRIES = 1500
+TRIES, MOVES, HEAT = 1500, 14000, 0.012
 
 
 def cv(n, per=1.0):
@@ -124,15 +130,15 @@ def cv(n, per=1.0):
 
 
 def cgat(n):
-    return (1.0, 0, n, 0, 0, 0)
+    return (0.0, 65, n, 0, 0, 0)
 
 
 def csca(n):
-    return (1.0, 0, 0, n, 0, 0)
+    return (0.0, 60, 0, n, 0, 0)
 
 
 def cmm(n, k=1):
-    return (0.2 * k, 0, 0, 0, k * max(64, n), 0)
+    return (0.3 * k, 0, 0, 0, k * max(64, n), 0)
 
 
 def cfix(x):
@@ -140,44 +146,70 @@ def cfix(x):
 
 
 def price_ops(ops, md):
-    cost, lat = [], []
+    cost, dur, lat = [], [], []
     for o in ops:
         c = o["cost"]
-        cost.append(c[0] * md[0] + c[1] * md[1] + c[2] * md[2] + c[3] * md[3] + c[4] * md[4] + c[5])
-        lat.append(o["lat"] * (md[6] if o["kind"] == "d" else 1.0) if o["kind"] != "n" else md[7])
-    return cost, lat
+        cost.append(c[0] * md[0] * (1.3 if o["e"] == "s" else 1.0) + c[1] * md[1] + c[2] * md[2] + c[3] * md[3] + c[4] * md[4] + c[5])
+        dur.append(o["rows"] * md[8] + o["bytes"] * md[9])
+        lat.append({"d": md[6], "n": md[7]}.get(o["kind"], 0.0))
+    return cost, dur, lat
 
 
-def run_order(ops, order, cost, lat, wake):
-    free, fin = {}, [0.0] * len(ops)
-    end = 0.0
+def run_order(ops, order, pr, wake, why=None):
+    cost, dur, lat = pr
+    free, last, fin = {}, {}, [0.0] * len(ops)
+    end = dfree = 0.0
+    dlast = tail = -1
     for i in order:
         o = ops[i]
         e = o["e"]
         s = free.get(e, 0.0) if e != "n" else 0.0
+        w, own = last.get(e, -1), True
         for p in o["full"]:
             if fin[p] + wake > s:
-                s = fin[p] + wake
+                s, w, own = fin[p] + wake, p, False
         f = s + cost[i]
-        free[e] = f
+        free[e], last[e] = f, i
+        if dur[i]:
+            if dfree > f:
+                f, w, own = dfree, dlast, True
+            f = dfree = f + dur[i]
+            dlast = i
         fin[i] = f + lat[i]
+        if why is not None:
+            why[i] = (w, own)
         if fin[i] > end:
-            end = fin[i]
-    return end
+            end, tail = fin[i], i
+    return end, tail
 
 
-def schedule(ops, succ, prio, cost, lat, wake, window):
+def moved(order, i, j, link, ahead):
+    a, b = order.index(j), order.index(i)
+    span = order[a:b + 1] if ahead else order[a:b + 1][::-1]
+    take = {span[-1]}
+    for x in span[::-1]:
+        if x in take:
+            take.update(p for p, f in link[x])
+    if span[0] in take:
+        return None
+    span = [x for x in span if x in take] + [x for x in span if x not in take]
+    return order[:a] + (span if ahead else span[::-1]) + order[b + 1:]
+
+
+def schedule(ops, pred, succ, prio, pr, wake, slope, back=False):
+    cost, dur, lat = pr
     m = len(ops)
-    left = [len(o["full"]) + len(o["order"]) for o in ops]
+    left = [len(p) for p in pred]
     ready = [0.0] * m
     free, pend = {}, {}
     for i, o in enumerate(ops):
         free[o["e"]] = 0.0
         pend.setdefault(o["e"], [])
         if not left[i]:
+            ready[i] = dur[i] + lat[i] if back else 0.0
             pend[o["e"]].append(i)
     names = sorted(pend)
-    start = [0.0] * m
+    order, dfree, fin = [], 0.0, [0.0] * m
     for _ in range(m):
         t0, e = 1e30, None
         for x in names:
@@ -185,17 +217,25 @@ def schedule(ops, succ, prio, cost, lat, wake, window):
                 t = max(free[x], min(ready[i] for i in pend[x]))
                 if t < t0:
                     t0, e = t, x
-        i = max((i for i in pend[e] if ready[i] <= t0 + window), key=lambda i: (prio[i], -i))
+        i = max(pend[e], key=lambda i: (prio[i] - slope * max(0.0, ready[i] - t0), -i))
+        fill = [k for k in pend[e] if k != i and max(t0, ready[k]) + cost[k] <= ready[i]]
+        if fill:
+            i = max(fill, key=lambda i: (prio[i], -i))
         s = max(t0, ready[i])
-        start[i] = s
+        order.append(i)
         pend[e].remove(i)
-        free[e] = s + cost[i] if e != "n" else 0.0
-        for j, f in succ[i]:
-            ready[j] = max(ready[j], s + cost[i] + (lat[i] + wake if f else 0.0))
+        f = fin[i] = s + cost[i]
+        free[e] = f if e != "n" else 0.0
+        done = f
+        if dur[i] and not back:
+            done = dfree = max(f, dfree) + dur[i]
+        for j, full in succ[i]:
+            delay = (dur[j] + lat[j] if back else lat[i]) + wake
+            ready[j] = max(ready[j], done + delay if full else f)
             left[j] -= 1
             if not left[j]:
                 pend[ops[j]["e"]].append(j)
-    return sorted(range(m), key=lambda i: (start[i], i))
+    return order, fin
 
 
 PLAN = {}
@@ -205,38 +245,66 @@ def plan(ops):
     if "order" in PLAN:
         return PLAN["order"]
     m = len(ops)
+    pred = [[(p, True) for p in o["full"]] + [(p, False) for p in o["order"]] for o in ops]
     succ = [[] for _ in ops]
-    for i, o in enumerate(ops):
-        for p in o["full"]:
-            succ[p].append((i, True))
-        for p in o["order"]:
-            succ[p].append((i, False))
+    for i in range(m):
+        for p, f in pred[i]:
+            succ[p].append((i, f))
     priced = [price_ops(ops, md) for md in MODELS]
-    cost, lat = priced[0]
+    cost, dur, lat = priced[0]
+    wake = MODELS[0][5]
+    up = np.array([o["up"] for o in ops])
     base = [0.0] * m
     for i in range(m - 1, -1, -1):
         b = 0.0
         for j, f in succ[i]:
-            b = max(b, base[j] + (lat[i] + MODELS[0][5] if f else 0.0))
-        base[i] = b + cost[i] + ops[i]["up"]
+            b = max(b, base[j] + (dur[i] + lat[i] + wake if f else 0.0))
+        base[i] = b + cost[i] + (0.0 if succ[i] else dur[i] + lat[i])
     rng = np.random.default_rng(2)
-    ref, best, bestn = None, None, np.zeros(m)
+    ref, best = None, None
     for k in range(TRIES):
-        if k < 4:
-            noise, window = np.zeros(m), (0.05, 0.15, 0.3, 0.02)[k]
+        slope = float(rng.choice([1.0, 2.0, 3.0, 5.0, 8.0, 12.0, 20.0]))
+        if k == 0:
+            prio = np.array(base)
+        elif k % 10 == 1:
+            prio = np.array(schedule(ops, succ, pred, list(best[4]), priced[0], wake, slope, True)[1])
         else:
-            noise = bestn + rng.normal(0.0, (40.0, 8.0)[k % 2], m) * (rng.random(m) < (0.1, 0.03, 0.01)[k % 3])
-            window = best[2] if k % 5 else float(rng.choice([0.02, 0.05, 0.1, 0.2]))
-        order = schedule(ops, succ, [base[i] + float(noise[i]) for i in range(m)], cost, lat, MODELS[0][5], window)
-        ts = [run_order(ops, order, c, l, md[5]) for (c, l), md in zip(priced, MODELS)]
+            prio = best[2] + rng.normal(0.0, (8.0, 2.0, 0.5)[k % 3], m) * (rng.random(m) < (0.1, 0.03, 0.01, 0.005)[k % 4])
+            slope = best[3] if k % 5 else slope
+        order, fin = schedule(ops, pred, succ, [float(x) for x in prio + up], priced[0], wake, slope)
+        ts = [run_order(ops, order, pr, md[5])[0] for pr, md in zip(priced, MODELS)]
         if ref is None:
             ref = ts
         sc = sum(a / b for a, b in zip(ts, ref))
-        if best is None or sc < best[0]:
-            best, bestn = (sc, order, window, ts), noise
-    PLAN["order"] = best[1]
-    PLAN["ts"] = (ref, best[3])
-    return best[1]
+        if best is None or sc <= best[0]:
+            best = (sc, order, prio, slope, fin, ts)
+    order, sc, ts = best[1], best[0], best[5]
+    why = [None] * m
+    for k in range(MOVES):
+        md = k % len(MODELS)
+        i = run_order(ops, order, priced[md], MODELS[md][5], why)[1]
+        arcs = []
+        while i >= 0:
+            j, own = why[i]
+            if own and j >= 0:
+                arcs.append((i, j))
+            i = j
+        i, j = arcs[int(rng.integers(len(arcs)))]
+        for _ in range(int(rng.integers(4))):
+            if why[j][1] and why[j][0] >= 0:
+                j = why[j][0]
+        ahead = bool(rng.integers(2))
+        new = moved(order, i, j, pred if ahead else succ, ahead)
+        if new is None:
+            continue
+        t2 = [run_order(ops, new, pr, x[5])[0] for pr, x in zip(priced, MODELS)]
+        s2 = sum(a / b for a, b in zip(t2, ref))
+        if s2 <= sc + HEAT * (1 - k / MOVES) * rng.random():
+            order, sc, ts = new, s2, t2
+    PLAN["order"] = order
+    PLAN["ts"] = (best[5], ts)
+    PLAN["ops"] = ops
+    return order
 
 
 def rank_program(g, core, T, topo):
@@ -247,315 +315,337 @@ def rank_program(g, core, T, topo):
     Q = {"v": g.vector, "s": g.scalar, "p": g.tensor, "g": g, "y": g.sync}
     CSEM = {"v": "cv", "s": "cs", "p": "cp", "g": "cg"}
     ops = []
-    lastw, readers = {}, {}
+    lastw, readers, lastb = {}, {}, {}
+    hot = [0.0]
 
-    def add(e, kind, body, r, w, cost, lat=0.0, up=0.0, after=()):
+    def add(e, kind, body, r, w, cost, up=0.0, after=(), bk=(), rows=0, nbytes=0):
         i = len(ops)
         full, order = set(), set()
-        comp = kind == "c"
         for k in list(r) + list(after):
             if k in lastw:
                 full.add(lastw[k])
         for k in w:
             if k in lastw:
                 full.add(lastw[k])
-            for x in readers.get(k, []):
-                if comp and ops[x]["e"] == e and ops[x]["kind"] == "c":
-                    order.add(x)
-                else:
-                    full.add(x)
+            full.update(readers.get(k, []))
+        for k in bk:
+            if k in lastb:
+                (order if ops[lastb[k]]["e"] == e else full).add(lastb[k])
+            lastb[k] = i
         full.discard(i)
         ops.append({"e": e, "kind": kind, "body": body, "full": sorted(full), "order": sorted(order - full),
-                    "cost": cost, "lat": lat, "up": up})
+                    "cost": cost, "up": up + hot[0], "name": (list(w) + [""])[0], "rows": rows, "bytes": nbytes})
         for k in r:
             readers.setdefault(k, []).append(i)
         for k in w:
             lastw[k] = i
             readers[k] = []
 
-    def V(f, r=(), w=(), c=cv(1)):
-        add("v", "c", [f], r, w, c)
+    def V(f, r=(), w=(), c=cv(1), bk=()):
+        add("v", "c", [f], r, w, c, bk=bk)
 
-    def S(f, r=(), w=(), c=cv(1)):
-        add("s", "c", [f], r, w, c)
+    def S(f, r=(), w=(), c=cv(1), bk=()):
+        add("s", "c", [f], r, w, c, bk=bk)
 
-    def PE(fs, r=(), w=(), c=None):
-        fs = fs if isinstance(fs, list) else [fs]
-        add("p", "c", fs, r, w, c if c else cmm(16, len(fs)))
+    def PE(fs, r, w, c, bk):
+        add("p", "c", fs, r, w, c, bk=bk)
 
-    def G(f, r=(), w=(), c=cfix(0.2), after=()):
-        add("g", "c", [f], r, w, c, after=after)
+    def G(f, r=(), w=(), c=cfix(0.2), up=0.0):
+        add("g", "c", [f], r, w, c, up)
 
-    def dma(e, pairs, r=(), w=(), lat=2.3, up=0.0, after=()):
-        add(e, "d", pairs, r, w, cfix(0.06 * len(pairs)), lat, up, after)
+    def dma(e, pairs, r, w, rows, rb, up=0.0, issued=()):
+        before = [lastw[k] for k in issued]
+        add(e, "d", pairs, r, w, cfix((0.6 if e == "g" else 0.06) * len(pairs)), up, rows=rows / 16, nbytes=rows * rb / 16)
+        ops[-1]["order"] += before
 
-    RF, GF, RQ, INC, WTF, SLF, SB, HF, C14, C15 = 0, 1, 2, 3, 4, 8, 12, 16, 17, 18
+    PF, RF, GF, RQ, INC, W2, W3, SLF, HR, HX, C14, C15, TOP, R0 = 0, 1, 2, 3, 4, 5, 6, 8, 12, 13, 14, 15, 16, 17
     sm = T.sm
     col = lambda c: sm[:, c:c + 1]
+    NH = len(CH)
     HA = range(NH)
-    HS = range(1, NH)
-    ALL = ["c"] + list(HS)
-    part = lambda h: ["c"] if h == 0 else [h]
+    HS = range(NH - 1)
+    HC = NH - 1
+    chunk = lambda a: [h for h in HA if CH[h][0] <= a < CH[h][1]][0]
     TT = lambda t: T["TT%d" % (t % 2)]
-    tk = lambda t, hs: ["TT%d_%s" % (t % 2, h) for h in hs]
-    TIB = lambda t: T.TI if t % 2 == 0 else T.TJ
-    ik = lambda t, hs: [("TI_%s" if t % 2 == 0 else "TJ_%s") % h for h in hs]
-    ek = lambda e, hs: ["AE%d_%s" % (e, h) for h in hs]
+    tk = lambda t, hs: ["TT%d_%d" % (t % 2, h) for h in hs]
+    TH = lambda t: T["TH%d" % (t % 2)]
+    fk = lambda t, hs: ["TH%d_%d" % (t % 2, h) for h in hs]
     win = lambda t: T.p0[:, 0:4096] if t == 0 else T["F%d" % t][:, 0:4096]
-    wkey = lambda t: ["win%d" % t]
+    wkey = lambda t: ["win%d" % t] + ([] if t else ["win0a"])
 
     def alist(t, e, a, b):
         return TT(t - 1)[:, a:b] if e == 1 and t > 0 else T.A16[:, LW * (e - 1) + a:LW * (e - 1) + b]
 
     def ak(t, e, hs):
-        return tk(t - 1, hs) if e == 1 and t > 0 else ["A16_%d_%s" % (e, h) for h in hs]
+        return tk(t - 1, hs) if e == 1 and t > 0 else ["A16_%d_%d" % (e, h) for h in hs]
 
-    dma("y", [(T.pkJ[:, 16:LW], T.packs[:, 768:1024]), (T.pkJ[:, 0:16], T.packs[0:128:16, 768:1024])], w=["pkJ"], lat=3, up=2000)
-    dma("y", [(T.slI[:, 0:3], T.slack[:])], w=["slI"], lat=3, up=1800)
-    dma("y", [(T.p0[:], T.price[:])], w=["win0"], lat=5, up=1600)
-    dma("y", [(T.TI[:, 16:LW], T.lots[:]), (T.TI[:, 0:16], T.lots[0:128:16, :])], w=ik(0, ALL), lat=4, up=1500)
-    dma("s", [(T.VT[r:128:16, :], T.prev[:]) for r in range(8)], w=["VTa"], lat=7)
-    dma("y", [(T.VT[r:128:16, :], T.prev[:]) for r in range(8, 16)], w=["VTb"], lat=7)
-    dma("y", [(T.pkI[:], T.packs[:, 0:768])], w=["pkI"], lat=9)
-    dma("y", [(T.small[:, 0:1], T.inc[:]), (T.small[:, 4:5], T.wt[:])], w=["smallI"], lat=9)
-    VTR = ["VTa", "VTb"]
+    def alots(t, e, a, b):
+        return T.PK[:, 768 + 256 * t + a:768 + 256 * t + b] if e == 1 else T.AE[:, LW * (e - 2) + a:LW * (e - 2) + b]
 
-    G(lambda q: q.iota(T.pI[:, 0:1], [[1, 1]], 0, 1), w=["pI"])
-    G(lambda q: q.iota(T.row8[:], [[1, 8]], 0, 0, allow_small_or_imprecise_dtypes=True), w=["row8"])
-    G(lambda q: q.iota(T.i16[:], [[16, 16]], 0, 0, allow_small_or_imprecise_dtypes=True), w=["i16"])
+    def ek(t, e, hs):
+        return ["AE%d_%d" % (e, h) if e > 1 else "AC%d" % t if h == HC else "PK%d_%d" % (t - 1, h) for h in hs]
 
-    V(lambda q: q.memset(T.SELK[:], 0.0), w=["SELK"], c=cv(1024))
+    dma("y", [(T.pkJ[:, 0:256], T.packs[:, 768:1024]), (T.pkJ[:, 256:LW], T.packs[0:128:16, 768:1024])], [], ["pkJ"], 256, 544, up=2000)
+    dma("y", [(T.p0[:, 0:2048], T.price[:, 0:2048])], [], ["win0a"], 128, 4096, up=1700, issued=["pkJ"])
+    add("v", "c", [lambda q: q.memset(T.VT[:], 0)], [], ["VT"], cv(1024), up=1650)
+    clear = len(ops) - 1
+    dma("y", [(T.VT[0:128:16, :], T.prev[:]), (T.VT[1:128:16, :], T.packs[0:128:16, :])], [], ["VT"], 128, 512, up=1600, issued=["win0a"])
+    dma("y", [(T.TI[:, 0:256], T.lots[:]), (T.TI[:, 256:LW], T.lots[0:128:16, :]), (T.slI[:, 0:3], T.slack[:])], [], ["TI", "slI"], 384, 370, up=1580, issued=["VT"])
+    dma("y", [(T.p0[:, 2048:4096], T.price[:, 2048:4096])], [], ["win0"], 128, 4096, up=1550, issued=["TI"])
+    dma("y", [(T.pkI[:], T.packs[:, 0:768])], [], ["pkI"], 128, 3072, up=1300, issued=["win0"])
+    dma("y", [(T.small[:, 4:5], T.wt[:])], [], ["wtI"], 128, 4, up=1200, issued=["pkI"])
+    add("g", "d", [(T.small[:, 0:1], T.inc[:])], [], ["incI"], cfix(1.6), up=80, rows=8)
+
+    fl = dict(allow_small_or_imprecise_dtypes=True)
+    G(lambda q: q.iota(T.pI[:, 0:1], [[1, 1]], 0, 1), w=["pI"], up=100)
+    G(lambda q: q.iota(T.row8[:], [[1, 8]], 0, 0, **fl), w=["row8"], up=100)
+    G(lambda q: q.iota(T.IX[:], [[1, 256]], 0, 0, **fl), w=["IX"], c=cfix(0.7), up=100)
+    G(lambda q: q.iota(T.i16[:], [[16, 16]], 0, 0, **fl), w=["i16"], up=100)
+    G(lambda q: q.iota(T.IXG[:], [[1, 8], [0, 16]], 0, 0, **fl), w=["IXG"], c=cfix(0.4), up=100)
+    G(lambda q: q.iota(T.MI[:], [[0, 64], [1, 16]], 0, 0, **fl), w=["MI"], c=cfix(2.1), up=90)
+    G(lambda q: q.iota(T.IDW[:], [[1, 4096]], 0, 0, **fl), w=["IDW"], c=cfix(8.0))
+
+    add("v", "c", [lambda q: q.memset(T.SELK[:], 0.0)], [], ["SELK"], cv(1024))
+    ops[-1]["order"].append(clear)
     V(lambda q: q.memset(T.one16[:], 1.0), w=["one16"])
-    V(lambda q: q.memset(T.ones[:], 1.0), w=["ones"])
-    for i, x in enumerate((-8.5, -1.0, 15.0)):
-        V(lambda q, i=i, x=x: q.memset(T.cB[:, 128 * i:128 * i + 128], x * BIG), w=["cB%d" % i])
+    V(lambda q: q.memset(T.ones[:], 1.0), w=["ones"], c=cv(LW // 2))
+    V(lambda q: q.memset(T.cB[:], 0.0), w=["cB"], c=cv(128))
+    V(lambda q: q.memset(T.cB[0:1, 0:128], -0.5 * BIG), w=["cB"])
+    V(lambda q: q.memset(T.cB[0:1, 128:256], 33.0), w=["cB"])
+    V(lambda q: q.memset(T.cB[32:33, 128:256], 192.0 * 2048), w=["cB"])
+    V(lambda q: q.tensor_copy(col(PF), T.pI[:, 0:1]), r=["pI"], w=["PF"])
     V(lambda q: q.tensor_scalar(T.pI[:, 1:2], T.pI[:, 0:1], 15, None, A.bitwise_and), r=["pI"], w=["pI1"])
     V(lambda q: q.tensor_scalar(T.pI[:, 2:3], T.pI[:, 0:1], 4, None, A.logical_shift_right), r=["pI"], w=["pI2"])
-    V(lambda q: q.tensor_copy(col(RF), T.pI[:, 1:2]), r=["pI1"], w=["RF"])
-    V(lambda q: q.tensor_copy(col(GF), T.pI[:, 2:3]), r=["pI2"], w=["GF"])
-    V(lambda q: q.tensor_scalar(T.B8[:], T.row8[:], col(GF), None, A.is_equal), r=["row8", "GF"], w=["B8"])
+    V(lambda q: q.tensor_copy(sm[:, RF:GF + 1], T.pI[:, 1:3]), r=["pI1", "pI2"], w=["RF"])
+    V(lambda q: q.tensor_scalar(T.B8[:], T.row8[:], col(GF), None, A.is_equal), r=["row8", "RF"], w=["B8"])
     V(lambda q: q.tensor_scalar(T.L1c[:], T.i16[:], col(RF), None, A.add), r=["i16", "RF"], w=["L1c"])
     for gg in range(8):
         V(lambda q, gg=gg: q.tensor_scalar(T.SELK[:, 16 * gg:16 * gg + 129 * 15 + 1:129], T.one16[:],
                                            T.B8[:, gg:gg + 1], BIG, A.mult, A.mult),
           r=["one16", "B8", "SELK"], w=["SELK%d" % gg])
     SELK = ["SELK"] + ["SELK%d" % gg for gg in range(8)]
-    V(lambda q: q.tensor_copy(T.A16[:, 0:LW], T.pkJ[:]), r=["pkJ"], w=ak(0, 1, ALL), c=cv(LW))
+    V(lambda q: q.tensor_copy(T.A16[:, 0:LW], T.pkJ[:]), r=["pkJ"], w=ak(0, 1, HA), c=cv(LW))
     V(lambda q: q.tensor_copy(sm[:, SLF:SLF + 3], T.slI[:, 0:3]), r=["slI"], w=["SLF"])
-    V(lambda q: q.tensor_copy(T.TT0[:], T.TI[:]), r=ik(0, ALL), w=tk(0, ALL), c=cv(LW))
-    V(lambda q: q.tensor_scalar(T.AE[:, 0:LW], T.pkJ[:], 4096.0, None, A.add), r=["pkJ"], w=ek(1, ALL), c=cv(LW))
-    V(lambda q: q.tensor_copy(T.VH[:], T.VT[:, 768:1024]), r=VTR, w=["VH"], c=cv(256))
-    V(lambda q: q.tensor_scalar(T.SELH[:], T.SELK[:], 1.0 / BIG, None, A.mult), r=SELK, w=["SELH"], c=cv(1024))
-    for e in range(3):
-        V(lambda q, e=e: q.memset(col(SB + e), 0.5 - 4096.0 * (e + 1)), w=["SB%d" % e])
-    V(lambda q: q.memset(col(HF), -0.5), w=["HF"])
-    V(lambda q: q.memset(T.onesF[:], 1.0), w=["onesF"], c=cv(128))
-    G(lambda q: q.affine_select(T.IDB[:, 0:128], T.ones[:], [[-1, 128]], A.is_equal, 0.0, 0, 1), r=["ones"], w=["IDB"], c=cfix(0.45))
-    V(lambda q: q.tensor_scalar(T.IDB[:, 128:256], T.IDB[:, 0:128], -1.0, None, A.mult), r=["IDB"], w=["IDM"])
-    G(lambda q: q.iota(T.IDW[:], [[1, 4096]], -2048, 0, allow_small_or_imprecise_dtypes=True), w=["IDW"], c=cfix(8.5))
-    G(lambda q: q.iota(T.IX[:], [[1, 256]], 0, 0, allow_small_or_imprecise_dtypes=True), w=["IX"], c=cfix(0.7))
-    G(lambda q: q.affine_select(T.IDN[:], T.onesF[:], [[-1, 128]], A.is_equal, 0.0, 0, 1), r=["onesF"], w=["IDN"], c=cfix(0.45))
-    V(lambda q: q.tensor_copy(T.PK[:, 768:1024], T.pkJ[:, 16:LW]), r=["pkJ"], w=["PKb"], c=cv(256))
+    V(lambda q: q.tensor_copy(T.TT0[:], T.TI[:]), r=["TI"], w=tk(0, HA), c=cv(LW))
+    V(lambda q: q.tensor_scalar(T.TH0[:], T.TI[:], -2048.0, None, A.add), r=["TI"], w=fk(0, HA), c=cv(LW))
+    V(lambda q: q.tensor_scalar(T.TH1[:], T.pkJ[:], -2048.0, None, A.add), r=["pkJ"], w=fk(1, HA), c=cv(LW))
+    V(lambda q: q.tensor_copy(T.PK[:, 768:768 + LW], T.pkJ[:]), r=["pkJ"], w=ek(0, 1, HA), c=cv(LW))
     V(lambda q: q.tensor_copy(T.PK[:, 0:768], T.pkI[:]), r=["pkI"], w=["PKa"], c=cv(768))
-    V(lambda q: q.memset(T.F1[:, 4096:4352], 0.0), w=["win1d"], c=cv(256))
+    V(lambda q: q.tensor_scalar(sm[:, R0:R0 + 2], T.row8[:, 0:2], col(RF), None, A.is_equal), r=["row8", "RF"], w=["R0"])
+    V(lambda q: q.tensor_scalar(T.VH[:], T.VT[:, 768:1024], col(R0), None, A.mult), r=["VT", "R0"], w=["VH"], c=cv(256))
+    V(lambda q: q.tensor_scalar(T.SELH[:], T.SELK[:], 1.0 / BIG, None, A.mult), r=SELK, w=["SELH"], c=cv(1024))
+    V(lambda q: q.memset(col(HR), -8.5 * 512), w=["HR"])
+    V(lambda q: q.memset(col(HX), -0.5 * 512), w=["HX"])
+    V(lambda q: q.memset(col(TOP), 255.4921875), w=["TOP"])
+    V(lambda q: q.tensor_scalar(T.IDN[:, 0:128], T.IX[:, 0:128], col(PF), None, A.is_equal), r=["IX", "PF"], w=["IDN"], c=cv(128))
+    S(lambda q: q.activation(T.IDN[:, 128:256], T.IDN[:, 0:128], AF.Copy, scale=-1.0), r=["IDN"], w=["IDM"], c=cv(128))
+    V(lambda q: q.tensor_copy(T.IDH[:], T.IDN[:]), r=["IDN", "IDM"], w=["IDH"], c=cv(256))
+    S(lambda q: q.activation(T.IDB[:, 0:256], T.IDN[:], AF.Copy), r=["IDN", "IDM"], w=["IDB"], c=cv(256))
+    S(lambda q: q.activation(T.IDB[:, 256:384], T.IDN[:, 0:128], AF.Copy, scale=-2048.0), r=["IDN"], w=["ID2"], c=cv(128))
+    for t in range(3):
+        G(lambda q, t=t: q.iota(T["F%d" % (t + 1)][:, 4096:4352], [[0, 256]], 0, 0, **fl), w=["dump%d" % t], c=cfix(0.6))
+    add("s", "c", [lambda q: q.activation(T.MK[:], T.MI[:], AF.Sigmoid, bias=col(HX), scale=512.0)], ["MI", "HX"], ["MK"], (1, 1024, 0, 0, 0, 1.3), up=90)
     V(lambda q: q.tensor_scalar(col(RQ), col(RF), 1.0, None, A.add), r=["RF"], w=["RQ"])
-    V(lambda q: q.tensor_scalar(T.QM[:], T.IX[:], col(RQ), 1.0e9, A.is_equal, A.mult), r=["IX", "RQ"], w=["QM"], c=cv(256))
+    V(lambda q: q.tensor_scalar(T.QM[:], T.IX[:], col(RQ), 1.0e16, A.is_equal, A.mult), r=["IX", "RQ"], w=["QM"], c=cv(256))
     seg = [256 * c - 8 * c * (c - 1) for c in range(17)]
-    dma("y", [(T.EM[:, seg[c]:seg[c + 1]], T.QM[:, 0:256 - 16 * c]) for c in range(16)], r=["QM"], w=["EM"])
+    for c in range(16):
+        S(lambda q, c=c: q.activation(T.EM[:, seg[c]:seg[c + 1]], T.QM[:, 0:256 - 16 * c], AF.Copy), r=["QM"], w=["EM%d" % c], c=cv(256 - 16 * c))
     V(lambda q: q.tensor_scalar(col(C14), col(RF), -8.0, 248.0, A.mult, A.add), r=["RF"], w=["c14"])
     V(lambda q: q.tensor_tensor(col(C15), col(C14), col(RF), A.mult), r=["c14", "RF"], w=["c15"])
     V(lambda q: q.tensor_scalar(T.E16[:, 0:1], col(C15), 255.0, None, A.add), r=["c15"], w=["E16"])
-    V(lambda q: q.tensor_scalar(T.DJt[:], T.L1c[:], 4096.0, None, A.add), r=["L1c"], w=["DJt"])
-    V(lambda q: q.tensor_scalar(T.dF[:], T.DJt[:], 4350.5, None, A.is_lt), r=["DJt"], w=["dF"])
+    V(lambda q: q.tensor_scalar(T.DJt[:], T.L1c[:], 4096.0, SQ, A.add, A.mult), r=["L1c"], w=["DJt"])
+    V(lambda q: q.tensor_scalar(T.dF[:], T.L1c[:], 254.5, None, A.is_lt), r=["L1c"], w=["dF"])
     V(lambda q: q.tensor_tensor(T.DJ[:], T.dF[:], T.DJt[:], A.mult), r=["dF", "DJt"], w=["DJ"])
-    V(lambda q: q.tensor_scalar(col(INC), T.small[:, 0:1], 1.0 / 64, None, A.mult), r=["smallI"], w=["INC"])
-    V(lambda q: q.tensor_copy(col(WTF), T.small[:, 4:5]), r=["smallI"], w=["WTF"])
-    G(lambda q: q.affine_select(T.BD[:], T.ones[:], [[-16, 8], [0, 16]], A.is_ge, 0.0, 0, 1), r=["ones"], w=["BD"], c=cfix(0.45))
-    G(lambda q: q.affine_select(T.BE[:], T.BD[:], [[16, 8], [0, 16]], A.is_ge, 0.0, 15, -1), r=["BD"], w=["BE"], c=cfix(0.45))
-    V(lambda q: q.tensor_scalar(T.WT[:], T.BE[:], col(WTF), None, A.mult), r=["BE", "WTF"], w=["WT"])
+    V(lambda q: q.tensor_scalar(col(INC), T.small[:, 0:1], 1.0 / 64, None, A.mult), r=["incI"], w=["INC"])
+    V(lambda q: q.tensor_scalar(col(W2), T.small[:, 4:5], 2.0, None, A.mult), r=["wtI"], w=["W2"])
+    V(lambda q: q.tensor_scalar(col(W3), T.small[:, 4:5], 2.0 / BIG, None, A.mult), r=["wtI"], w=["W3"])
+    V(lambda q: q.tensor_scalar(T.WT[:], T.IXG[:], col(GF), col(W2), A.is_equal, A.mult), r=["IXG", "RF", "W2"], w=["WT"], c=cv(128))
+    for i in range(2):
+        S(lambda q, i=i: q.activation(T.SELW[:, 1024 * i:1024 * i + 1024], T.SELK[:, 1024 * i:1024 * i + 1024], AF.Copy, scale=col(W3)),
+          r=SELK + ["W3"], w=["SELW%d" % i], c=cv(1024))
 
-    KY, KB = T.KY, T.KB
-    K2 = [(KY[:, 0, 16:32], "KY01", 4096.0), (KY[:, 1, 0:16], "KY10", 8192.0)]
-    K3 = [(KY[:, 1, 16:32], "KY11", 8192.0), (KY[:, 2, 0:16], "KY20", 12288.0), (KB[:, 0:16], "KB0", 0.0)]
-    K4 = [(KY[:, 2, 16:32], "KY21", 12288.0), (KB[:, 16:32], "KB1", 0.0)]
+    KS, KY, KM = T.KS, T.KY, T.KM
 
-    def conv(dst, keys):
-        PE([lambda q, k=k: q.matmul(T.ZM[:, 256:272], T.SELH[:, 128 * k:128 * k + 128], T.VH[:, k:256:16], k == 0, k == 15)
-            for k in range(16)], r=["VH", "SELH"], w=["bM"])
-        if dst < 48:
-            V(lambda q: q.tensor_scalar(T.LU[:, dst:dst + 16], T.ZM[:, 256:272], 1.0 / 16, None, A.mult), r=["bM"], w=["LU%d" % dst])
-        V(lambda q: q.tensor_scalar(T.kF[:, 0:16], T.ZM[:, 256:272], 1.0 / 16, None, A.mult), r=["bM"], w=["kF"])
-        for ap, nm, off in keys:
-            S(lambda q, ap=ap, off=off: q.activation(ap, T.kF[:, 0:16], AF.Copy, bias=off), r=["kF"], w=[nm])
+    def conv(d):
+        PE([lambda q, k=k: q.matmul(T.ZM[:, 384:400], T.SELH[:, 128 * k:128 * k + 128], T.VH[:, k:256:16], k == 0, k == 15)
+            for k in range(16)], ["VH", "SELH"], ["zc"], cmm(16, 16), ["bM"])
+        if d < 3:
+            V(lambda q: q.tensor_copy(T.LU[:, 16 * d:16 * d + 16], T.ZM[:, 384:400]), r=["zc"], w=["LU%d" % d], bk=["bM"])
+        S(lambda q: q.activation(KS[:, 16 * d:16 * d + 16], T.ZM[:, 384:400], AF.Copy), r=["zc"], w=["KS%d" % d], bk=["bM"])
 
-    def parents(src):
-        V(lambda q: q.tensor_copy(T.VH[:], T.VT[:, 0:1024].indirect(T.LU[:, src:src + 16])), r=VTR + ["LU%d" % src], w=["VH"], c=cgat(256))
+    def parents(d):
+        V(lambda q: q.tensor_scalar(T.VH[:], T.VT[:].indirect(T.LU[:, 16 * d:16 * d + 16]), col(R0), None, A.mult),
+          r=["VT", "R0", "LU%d" % d], w=["VH"], c=cgat(256))
 
-    def newest(t):
-        base = 768.0 + 256 * t
-        S(lambda q: q.activation(KY[:, 0, 0:16], T.L1c[:], AF.Copy, bias=base + 4096.0), r=["L1c"], w=["KY00"])
+    def first(e):
+        V(lambda q: q.tensor_scalar(T.VG[:], T.VT[:].indirect(T.LU[:, 16 * e - 16:16 * e]), -2048.0, col(R0 + 1), A.add, A.mult),
+          r=["VT", "R0", "LU%d" % (e - 1)], w=["VG"], c=cgat(256))
+        PE([lambda q, k=k: q.matmul(T.ZR[:, 384:400], T.SELH[:, 128 * k:128 * k + 128], T.VG[:, 16 * k:16 * k + 16], k == 0, k == 15)
+            for k in range(16)], ["VG", "SELH"], ["zf"], cmm(16, 16), ["bR"])
+        V(lambda q: q.tensor_scalar(alist(0, e, 256, LW), T.ZR[:, 384:400], 2048.0, None, A.add), r=["zf"], w=ak(0, e, [HC]), bk=["bR"])
+        S(lambda q: q.activation(alots(0, e, 256, LW), T.ZR[:, 384:400], AF.Copy), r=["zf"], w=ek(0, e, [HC]), bk=["bR"])
+
+    def keys(t):
+        c = 16 if t == 2 else 32
+        S(lambda q: q.activation(KS[:, 0:16], T.L1c[:], AF.Copy, bias=768.0 + 256 * t), r=["L1c"], w=["KS0"])
+        for e in range(3):
+            S(lambda q, e=e: q.activation(KY[:, e, 0:c], KS[:, 16 * e:16 * e + c], AF.Copy, bias=4096.0 * (e + 1)),
+              r=["KS%d" % d for d in range(e, e + c // 16)], w=["KY%d" % e])
+        S(lambda q: q.activation(KM[:, 3, 0:c], KS[:, 32:32 + c], AF.Copy), r=["KS%d" % d for d in range(2, 2 + c // 16)], w=["KM3"])
 
     def package(t, e):
-        c, b = LW * (e - 1) + 16, 16 * (e - 1)
-        S(lambda q: q.activation(T.AE[:, c:c + 256], T.PK[:, 0:1024 + 256 * t].indirect(T.LU[:, b:b + 16]), AF.Copy, bias=4096.0 * e),
-          r=["PKa", "PKb"] + ["PK%d_%d" % (i, h) for i in range(t) for h in HS] + ["LU%d" % b], w=ek(e, HS), c=cgat(256))
-        V(lambda q: q.tensor_scalar(T.A16[:, c:c + 256], T.AE[:, c:c + 256], -4096.0 * e, None, A.add),
-          r=ek(e, HS), w=ak(t, e, HS), c=cv(256))
+        S(lambda q: q.activation(alots(t, e, 0, 256), T.PK[:, 0:1024 + 256 * t].indirect(T.LU[:, 16 * e - 16:16 * e]), AF.Copy, bias=-2048.0),
+          r=["PKa"] + ["PK%d_%d" % (i, h) for i in range(-1, t) for h in HS] + ["LU%d" % (e - 1)], w=ek(t, e, HS), c=cgat(256))
+        V(lambda q: q.tensor_scalar(alist(t, e, 0, 256), alots(t, e, 0, 256), 2048.0, None, A.add), r=ek(t, e, HS), w=ak(t, e, HS), c=cv(256))
 
     def clist(t, e):
-        if e == 0:
-            dma("y", [(TT(t)[:, 0:16], TT(t)[t:128:16, 16:LW])], r=tk(t, HS), w=tk(t, ["c"]))
-            dma("y", [(TIB(t)[:, 0:16], TIB(t)[t:128:16, 16:LW])], r=ik(t, HS), w=ik(t, ["c"]))
-        else:
-            o = LW * (e - 1)
-            dma("y", [(alist(t, e, 0, 16), alist(t, e, 16, LW)[t:128:16, :])], r=ak(t, e, HS), w=ak(t, e, ["c"]))
-            dma("y", [(T.AE[:, o:o + 16], T.AE[t:128:16, o + 16:o + LW])], r=ek(e, HS), w=ek(e, ["c"]))
+        dma("y", [(alist(t, e, 256, LW), alist(t, e, 0, 256)[t:128:16, :])], ak(t, e, HS), ak(t, e, [HC]), 128, 32)
+        dma("y", [(alots(t, e, 256, LW), alots(t, e, 0, 256)[t:128:16, :])], ek(t, e, HS), ek(t, e, [HC]), 128, 64)
+        if e == 1:
+            dma("y", [(TH(t - 1)[:, 256:LW], TH(t - 1)[t:128:16, 0:256])], fk(t - 1, HS), fk(t - 1, [HC]), 128, 32)
 
-    blocks = lambda m: [(x, min(x + 512, 16 * m)) for x in range(0, 16 * m, 512)]
+    NP = len(PCS)
 
-    def gy(t, e, h):
-        a, b = CH[h]
+    def gy(t, e, i):
+        a, b = PCS[i]
         o = 16 * (LW * (e - 1) + a)
         out, lst = T.Y[:, o:o + 16 * (b - a)], win(t).indirect(alist(t, e, a, b))
-        r, w, c = wkey(t) + ak(t, e, part(h)) + ["SLF"], ["Y%d_%d" % (e, h)], cgat(16 * (b - a))
-        if YR[t][NH * (e - 1) + h] == "v":
+        r, w, c = wkey(t) + ak(t, e, [chunk(a)]) + ["SLF"], ["Y%d_%d" % (e, i)], cgat(16 * (b - a))
+        if YR[t][NP * (e - 1) + i] == "v":
             V(lambda q: q.tensor_scalar(out, lst, col(SLF + t), None, A.add), r=r, w=w, c=c)
         else:
             S(lambda q: q.activation(out, lst, AF.Identity, bias=col(SLF + t)), r=r, w=w, c=c)
 
-    def gx(t, e, h):
+    def diff(t, e, h):
         a, b = CH[h]
+        z = T["Z%d" % h][:, 256:256 + b - a]
+        one, lots, lk = (T.IDH, TH(t - 1)[:, a:b], fk(t - 1, [h])) if e == 1 else (T.IDN, alots(t, e, a, b), ek(t, e, [h]))
+        PE([lambda q: q.matmul(z, one[:, 0:128], lots, True, False),
+            lambda q: q.matmul(z, T.IDH[:, 128:256], TH(t)[:, a:b], False, True)],
+           ["IDN", "IDH"] + lk + fk(t, [h]), ["zD%d" % h], cmm(b - a, 2 if e == 1 else 5), ["bZ%d" % h])
+
+    def gx(t, e, i):
+        a, b = PCS[i]
+        h = chunk(a)
         o = 16 * LW * (e - 1)
         c0, c1 = 16 * a, 16 * b
         m = b - a
-        z = T["Z%d" % h]
+        z = T["Z%d" % h][:, a - CH[h][0]:b - CH[h][0]]
         lst = win(t).indirect(TT(t)[:, a:b])
-        r = wkey(t) + tk(t, part(h))
-        ck = ["C%d_%d" % (h, x) for x, y in blocks(m)]
-        if RT[t][NH * (e - 1) + h] == "v":
-            V(lambda q: q.tensor_tensor(T.C[:, c0:c1], lst, T.Y[:, o + c0:o + c1], A.is_gt), r=r + ["Y%d_%d" % (e, h)], w=ck, c=cgat(16 * m))
-            sh = 0
+        r = wkey(t) + tk(t, [h])
+        blocks = [(x, min(x + 512, 16 * m)) for x in range(0, 16 * m, 512)]
+        ck = ["C%d_%d" % (i, x) for x, y in blocks]
+        if RT[t][NP * (e - 1) + i] == "v":
+            V(lambda q: q.tensor_tensor(T.C[:, c0:c1], lst, T.Y[:, o + c0:o + c1], A.is_gt), r=r + ["Y%d_%d" % (e, i)], w=ck, c=cgat(16 * m))
         else:
-            S(lambda q: q.activation(T.XS[:, c0:c1], lst, AF.Copy), r=r, w=["XS%d" % h], c=cgat(16 * m))
-            for x, y in blocks(m):
-                PE([lambda q, x=x, y=y: q.matmul(T.ZX[:, 0:y - x], T.IDB[:, 0:128], T.XS[:, c0 + x:c0 + y], True, False),
+            S(lambda q: q.activation(T.XS[:, 0:16 * m], lst, AF.Copy), r=r, w=["XS"], c=cgat(16 * m))
+            for x, y in blocks:
+                PE([lambda q, x=x, y=y: q.matmul(T.ZX[:, 0:y - x], T.IDB[:, 0:128], T.XS[:, x:y], True, False),
                     lambda q, x=x, y=y: q.matmul(T.ZX[:, 0:y - x], T.IDB[:, 128:256], T.Y[:, o + c0 + x:o + c0 + y], False, True)],
-                   r=["XS%d" % h, "IDB", "IDM", "Y%d_%d" % (e, h)], w=["bX"], c=cmm(y - x, 2))
-                S(lambda q, x=x, y=y: q.activation(T.C[:, c0 + x:c0 + y], T.ZX[:, 0:y - x], AF.Sign, bias=col(HF)),
-                  r=["bX", "HF"], w=["C%d_%d" % (h, x)], c=cv(y - x))
-            sh = 1
-        PE([lambda q: q.matmul(z[:, 0:m], T.cB[0:1, 128 * sh:128 * sh + 128], T.ones[0:1, 0:m], True, False)] +
-           [lambda q, k=k: q.matmul(z[:, 0:m], T.SELK[:, 128 * k:128 * k + 128], T.C[:, c0 + k:c1:16], False, k == 15)
-            for k in range(16)], r=ck + ["cB%d" % sh, "ones"] + SELK, w=["bZ%d" % h], c=cmm(m, 17))
+                   ["XS", "IDB", "Y%d_%d" % (e, i)], ["zX"], cmm(y - x, 2), ["bX"])
+                S(lambda q, x=x, y=y: q.activation(T.C[:, c0 + x:c0 + y], T.ZX[:, 0:y - x], AF.Sigmoid, bias=col(HX), scale=512.0),
+                  r=["zX", "HX"], w=["C%d_%d" % (i, x)], c=cv(y - x), bk=["bX"])
+        PE([lambda q, k=k: q.matmul(z, T.SELK[:, 128 * k:128 * k + 128], T.C[:, c0 + k:c1:16], k == 0, k == 15) for k in range(16)],
+           ck + SELK, ["zC%d" % i], cmm(m, 16), ["bZ%d" % h])
 
     def tops(t, e, h):
         a, b = CH[h]
         m = b - a
-        z, ti = T["Z%d" % h], TIB(t)
-        o = LW * (e - 1)
-        V(lambda q: q.tensor_tensor(T.ZT[:, a:b], z[:, 0:m], T.AE[:, o + a:o + b], A.min), r=["bZ%d" % h] + ek(e, part(h)), w=["bT%d" % h], c=cv(m))
-        cur, ck = (ti, ik(t, part(h))) if e == 1 else (T.Wt, ["W%d" % h])
-        if e < 3 or h == 0:
-            V(lambda q: q.tensor_tensor(T.Wt[:, a:b], T.ZT[:, a:b], cur[:, a:b], A.max), r=["bT%d" % h] + ck, w=["W%d" % h], c=cv(m))
+        z, bk = T["Z%d" % h], ["bZ%d" % h]
+        d = z[:, 256:256 + m]
+        mask, mk = (T.MC[:], "MC") if h == HC else (T.SG[:, 256 * (e - 1) + a:256 * (e - 1) + b], "SG%d_%d" % (e, h))
+        zk = ["zC%d" % i for i in range(NP) if chunk(PCS[i][0]) == h]
+        if h == HC and MCV == "v":
+            V(lambda q: q.tensor_scalar(mask, z[:, 0:m], 8.5 * BIG, None, A.is_gt), r=zk, w=[mk], c=cv(m), bk=bk)
         else:
-            V(lambda q: q.tensor_tensor(T.WF[:, a:b], T.ZT[:, a:b], cur[:, a:b], A.max), r=["bT%d" % h] + ck, w=["WF%d" % h], c=cv(m))
-            V(lambda q: q.tensor_copy(T.Wt[:, a:b], T.WF[:, a:b]), r=["WF%d" % h], w=["W%d" % h], c=cv(m))
-        V(lambda q: q.tensor_scalar(ti[:, a:b], T.Wt[:, a:b], 4095, None, A.bitwise_and), r=["W%d" % h], w=ik(t, part(h)), c=cv(m))
-        V(lambda q: q.tensor_copy(TT(t)[:, a:b], ti[:, a:b]), r=ik(t, part(h)), w=tk(t, part(h)), c=cv(m))
+            S(lambda q: q.activation(mask, z[:, 0:m], AF.Sigmoid, bias=col(HR), scale=512.0 / BIG), r=zk + ["HR"], w=[mk], c=cv(m), bk=bk)
+        V(lambda q: q.tensor_tensor(d, d, mask, A.mult), r=[mk], w=["zD%d" % h], c=cv(m), bk=bk)
+        V(lambda q: q.tensor_tensor(TH(t)[:, a:b], d, TH(t)[:, a:b], A.add), r=["zD%d" % h], w=fk(t, [h]), c=cv(m), bk=bk)
+        if (t, e) != (2, 3) or h == HC:
+            V(lambda q: q.tensor_scalar(TT(t)[:, a:b], TH(t)[:, a:b], 2048.0, None, A.add), r=fk(t, [h]), w=tk(t, [h]), c=cv(m, .5))
+        if e == 3 and h != HC:
+            V(lambda q: q.tensor_scalar(alots(t + 1, 1, a, b), TH(t)[:, a:b], 2048.0, None, A.add), r=fk(t, [h]),
+              w=ek(t + 1, 1, [h]) + (["AC%d" % t] if a == 0 else []), c=cv(m))
 
-    def fin(t, h):
-        a, b = CH[h]
-        p = 1024 + 256 * t - 16
-        V(lambda q: q.tensor_copy(T.PK[:, p + a:p + b], TIB(t)[:, a:b]), r=ik(t, [h]), w=["PK%d_%d" % (t, h)], c=cv(b - a))
-        if t < 2:
-            S(lambda q: q.activation(T.AE[:, a:b], T.PK[:, p + a:p + b], AF.Copy, bias=4096.0), r=["PK%d_%d" % (t, h)], w=ek(1, [h]), c=cv(b - a))
-        for e in range(3):
-            S(lambda q, e=e: q.activation(T.SG[:, 256 * e + a - 16:256 * e + b - 16], T.WF[:, a:b], AF.Sign, bias=col(SB + e)),
-              r=["WF%d" % h, "SB%d" % e], w=["SG%d_%d" % (e, h)], c=cv(b - a))
-
-    def gm(t, h):
-        a, b = CH[h]
-        x, y = 16 * (a - 16), 16 * (b - 16)
+    def gm(t, i):
+        a, b = PCS[i]
+        x, y = 16 * a, 16 * b
         lst = win(t).indirect(TT(t)[:, a:b])
-        r, w, c = wkey(t) + tk(t, [h]), ["XM%d" % h], cgat(y - x)
-        if MR[t][h - 1] == "v":
+        r, w, c = wkey(t) + tk(t, [chunk(a)]), ["XM%d" % i], cgat(y - x)
+        if MR[t][i - 1] == "v":
             V(lambda q: q.tensor_copy(T.XM[:, x:y], lst), r=r, w=w, c=c)
         else:
             S(lambda q: q.activation(T.XM[:, x:y], lst, AF.Copy), r=r, w=w, c=c)
-        V(lambda q: q.tensor_tensor_scan(T.SM[:, x:y], T.MK[:, x:y], T.XM[:, x:y], 0.0, A.min, A.max),
-          r=["MK", "XM%d" % h], w=["SM%d" % h], c=cv((y - x) // 2))
+        V(lambda q: q.tensor_tensor_scan(T.SM[:, x:y], T.MK[:, 0:y - x], T.XM[:, x:y], 0.0, A.mult, A.max),
+          r=["MK", "XM%d" % i], w=["SM%d" % i], c=cv((y - x) // 2))
 
     def tnew(t, hs):
         a, b = CH[hs[0]][0], CH[hs[-1]][1]
-        x, y = a - 16, b - 16
+        l = min(b, 256)
         m = b - a
         nm = str(hs[0])
-        uk = ["bT%d" % h for h in hs]
-        PE(lambda q: q.matmul(T.ZM[:, x:y], T.WT[:], T.SM[:, 16 * x + 15:16 * y:16], True, True), r=["WT"] + ["SM%d" % h for h in hs], w=["bM"], c=cmm(m))
-        V(lambda q: q.tensor_copy(T.uI[:, x:y], T.ZM[:, x:y]), r=["bM"], w=["uI" + nm], c=cv(m))
-        V(lambda q: q.tensor_scalar(T.uJ[:, x:y], T.uI[:, x:y], 1023, None, A.bitwise_and), r=["uI" + nm], w=["uJ" + nm], c=cv(m))
-        V(lambda q: q.tensor_scalar(T.ZT[:, a:b], T.uJ[:, x:y], 2.0, 33.0, A.mult, A.add), r=["uJ" + nm], w=uk, c=cv(m))
-        V(lambda q: q.tensor_tensor(T.qF[:, x:y], T.ZT[:, a:b], TIB(t)[:, a:b], A.mult), r=uk + ik(t, hs), w=["qF" + nm], c=cv(m))
-        V(lambda q: q.tensor_scalar(T.qI[:, x:y], T.qF[:, x:y], 2464.0 * (t + 1), None, A.add), r=["qF" + nm], w=["qI" + nm], c=cv(m))
-        V(lambda q: q.tensor_scalar(TIB(t + 1)[:, a:b], T.qI[:, x:y], 5, 4095, A.logical_shift_right, A.bitwise_and),
-          r=["qI" + nm], w=ik(t + 1, hs), c=cv(m))
-        V(lambda q: q.tensor_copy(TT(t + 1)[:, a:b], TIB(t + 1)[:, a:b]), r=ik(t + 1, hs), w=tk(t + 1, hs), c=cv(m))
+        sk = ["SM%d" % i for i in range(1, NP) if HC in hs or chunk(PCS[i][0]) in hs] + ["WT", "SELW0", "SELW1"]
+
+        def sums(z, first):
+            fs = [lambda q: q.matmul(z[:, a:l], T.WT[:], T.SM[:, 16 * a + 15:16 * l:16], first, first)] if l > a else []
+            if HC in hs:
+                fs += [lambda q, k=k: q.matmul(z[:, 256:LW], T.SELW[:, 128 * k:128 * k + 128], T.SM[:, 256 * k + 15:256 * k + 256:16],
+                                               first and k == 0, first and k == 15) for k in range(16)]
+            return fs
+        pc = cmm(m, 1) if HC not in hs else cmm(64, 16 + m // 64)
+        PE(sums(T.ZM, True), sk, ["zU"], pc, ["bM"])
+        PE([lambda q: q.matmul(T.ZR[:, a:b], T.cB[0:33, 128:256], T.ones[0:33, 0:m], True, False)] + sums(T.ZR, False),
+           sk + ["cB", "ones"], ["zR"], pc, ["bR"])
+        S(lambda q: q.activation(T.kf[:, a:b], T.ZM[:, a:b], AF.Copy, bias=191.5 + 1.0 / 2048, scale=1.0 / 2048), r=["zU"], w=["kf" + nm], c=cv(m), bk=["bM"])
+        PE([lambda q: q.matmul(T.ZR[:, a:b], T.IDB[:, 256:384], T.kf[:, a:b], False, True)], ["ID2", "kf" + nm], ["zR"], cmm(m), ["bR"])
+        V(lambda q: q.tensor_tensor(T.qF[:, a:b], T.ZR[:, a:b], alots(t + 1, 1, a, b), A.mult), r=["zR"] + ek(t + 1, 1, hs), w=["qF" + nm], c=cv(m), bk=["bR"])
+        V(lambda q: q.tensor_scalar(T.qI[:, a:b], T.qF[:, a:b], 2464.0 * (t + 1), None, A.add), r=["qF" + nm], w=["qI" + nm], c=cv(m))
+        V(lambda q: q.tensor_scalar(T.TI[:, a:b], T.qI[:, a:b], 5, 4095, A.logical_shift_right, A.bitwise_and),
+          r=["qI" + nm, "TI"], w=["TI" + nm], c=cv(m))
+        V(lambda q: q.tensor_copy(TT(t + 1)[:, a:b], T.TI[:, a:b]), r=["TI" + nm], w=tk(t + 1, hs), c=cv(m))
+        V(lambda q: q.tensor_scalar(TH(t + 1)[:, a:b], TT(t + 1)[:, a:b], -2048.0, None, A.add), r=tk(t + 1, hs), w=fk(t + 1, hs), c=cv(m, .5))
 
     def bind(t):
-        PE([lambda q: q.matmul(T.ZB[:], T.cB[0:1, 256:384], T.ones[0:1, 0:48], True, False)] +
+        PE([lambda q: q.matmul(T.ZB[:], T.cB[0:1, 0:128], T.ones[0:1, 0:48], True, False)] +
            [lambda q, k=k: q.matmul(T.ZB[:], T.SELK[:, 128 * k:128 * k + 128], T.SG[:, k:768:16], False, k == 15) for k in range(16)],
-           r=["SG%d_%d" % (e, h) for e in range(3) for h in HS] + SELK + ["cB2", "ones"], w=["bB"])
+           ["SG%d_%d" % (e, h) for e in (1, 2, 3) for h in HS] + SELK + ["cB", "ones"], ["zB"], cmm(48, 17), ["bB"])
         c = 16 if t == 2 else 32
         ds = range(c // 16)
         for d in ds:
-            V(lambda q, d=d: q.tensor_tensor(T.KM[:, :, 16 * d:16 * d + 16], T.ZB[:], KY[:, :, 16 * d:16 * d + 16], A.min),
-              r=["bB"] + ["KY%d%d" % (e, d) for e in range(3)], w=["KM%d" % d])
-        V(lambda q: q.tensor_tensor(T.k1[:, 0:c], T.KM[:, 0, 0:c], T.KM[:, 1, 0:c], A.max), r=["KM%d" % d for d in ds], w=["k1"])
-        V(lambda q: q.tensor_tensor(T.k2[:, 0:c], T.k1[:, 0:c], T.KM[:, 2, 0:c], A.max), r=["k1"] + ["KM%d" % d for d in ds], w=["k2"])
-        V(lambda q: q.tensor_tensor(T.kI[:, 0:c], T.k2[:, 0:c], KB[:, 0:c], A.max), r=["k2"] + ["KB%d" % d for d in ds], w=["kI"])
+            V(lambda q, d=d: q.tensor_tensor(KM[:, 0:3, 16 * d:16 * d + 16], T.ZB[:], KY[:, :, 16 * d:16 * d + 16], A.min),
+              r=["zB"] + ["KY%d" % e for e in range(3)], w=["KM_%d" % d], bk=["bB"])
+        V(lambda q: q.tensor_tensor(T.k1[:, :, 0:c], KM[:, 0:2, 0:c], KM[:, 2:4, 0:c], A.max), r=["KM3"] + ["KM_%d" % d for d in ds], w=["k1"], c=cv(4 * c))
+        V(lambda q: q.tensor_tensor(T.kI[:, 0:c], T.k1[:, 0, 0:c], T.k1[:, 1, 0:c], A.max), r=["k1"], w=["kI"])
         V(lambda q: q.tensor_scalar(T.kJ[:, 0:c], T.kI[:, 0:c], 4095, None, A.bitwise_and), r=["kI"], w=["kJ"])
+        V(lambda q: q.tensor_copy(T.LU[:, 16:16 + c], T.kJ[:, 0:c]), r=["kJ"], w=["LU1", "LU2"])
         if t < 2:
-            V(lambda q: q.tensor_copy(T.LU[:, 16:48], T.kJ[:]), r=["kJ"], w=["LU16", "LU32"])
-            V(lambda q: q.tensor_copy(T.kF[:], T.kJ[:]), r=["kJ"], w=["kF"])
-            S(lambda q: q.activation(T.PV[:, 16 * t:16 * t + 16], T.kF[:, 0:16], AF.Copy), r=["kF"], w=["PV%d" % t])
-            S(lambda q: q.activation(KY[:, 0, 16:32], T.kF[:, 0:16], AF.Copy, bias=4096.0), r=["kF"], w=["KY01"])
-            S(lambda q: q.activation(KY[:, 1, :], T.kF[:], AF.Copy, bias=8192.0), r=["kF"], w=["KY10", "KY11"])
-            S(lambda q: q.activation(KY[:, 2, 0:16], T.kF[:, 16:32], AF.Copy, bias=12288.0), r=["kF"], w=["KY20"])
-            S(lambda q: q.activation(KB[:, 0:16], T.kF[:, 16:32], AF.Copy), r=["kF"], w=["KB0"])
-            newest(t + 1)
-        else:
-            V(lambda q: q.tensor_copy(T.PV[:, 32:48], T.kJ[:, 0:16]), r=["kJ"], w=["PV2"])
+            V(lambda q: q.tensor_copy(KS[:, 16:48], T.kJ[:]), r=["kJ"], w=["KS1", "KS2"])
 
     def outv(t):
-        PE(lambda q: q.matmul(T.ZM[0:16, 384:512], T.PV[:, 16 * t:16 * t + 16], T.IDN[:], True, True), r=["PV%d" % t, "IDN"], w=["bM"], c=cmm(128, 4))
-        V(lambda q: q.tensor_copy(T.yvb[0:16, 128 * t:128 * t + 128], T.ZM[0:16, 384:512]), r=["bM"], w=["yvb%d" % t], c=cv(128))
-        for i, e in enumerate(("y", "s") if t == 2 else ("y",)):
-            gs = range(8)[i::2] if t == 2 else range(8)
-            dma(e, [(T.yv[gg:gg + 1, 256 * t:256 * t + 256], T.yvb[0:16, 128 * t + 16 * gg:128 * t + 16 * gg + 16]) for gg in gs],
-                r=["yvb%d" % t], w=["yv%d_%d" % (t, i)])
+        S(lambda q: q.activation(T.YV[:, 256 * t:256 * t + 256], T.IDW[:].indirect(T.LU[:, 16:32]), AF.Copy), r=["IDW", "LU1"], w=["YV%d" % t], c=cgat(256))
+        dma("y", [(T.yv[:, 256 * t:256 * t + 256], T.YV[0:128:16, 256 * t:256 * t + 256])], ["YV%d" % t], ["yv%d" % t], 16, 512)
 
     def outh(t, hs):
-        a, b = CH[hs[0]][0] - 16, CH[hs[-1]][1] - 16
-        p = 1024 + 256 * t
-        dma("y", [(T.yh[:, 256 * t + a:256 * t + b], T.PK[:, p + a:p + b])], r=["PK%d_%d" % (t, h) for h in hs], w=["yh%d_%d" % (t, a)])
+        a, b = CH[hs[0]][0], CH[hs[-1]][1]
+        dma("y", [(T.yh[:, 256 * t + a:256 * t + b], alots(t + 1, 1, a, b))], ek(t + 1, 1, hs), ["yh%d_%d" % (t, a)], 128, 4 * (b - a))
 
     def dedupe(t):
-        cl, ci, ck, cik = TT(t)[:, 0:16], TIB(t)[:, 0:16], tk(t, ["c"]), ik(t, ["c"])
+        cl, ck = TT(t)[:, 256:LW], tk(t, [HC])
+        S(lambda q: q.activation(T.RB[:], T.IDW[:].indirect(cl), AF.Copy, scale=-SQ), r=["IDW"] + ck, w=["RB"], c=cgat(256))
         S(lambda q: q.activation(T.SV[:, 256 * t:256 * t + 256], win(t).indirect(cl), AF.Copy), r=wkey(t) + ck, w=["SV%d" % t], c=cgat(256))
-        S(lambda q: q.activation(T.RB[:], T.IDW[:].indirect(cl), AF.Copy), r=["IDW"] + ck, w=["RB"], c=cgat(256))
-        V(lambda q: q.tensor_scalar(T.CF[:], ci, -1.0, 2048.0, A.mult, A.add), r=cik, w=["CF"])
+        V(lambda q: q.tensor_scalar(T.CF[:], TH(t)[:, 256:LW], 2048.0, -SQ, A.add, A.mult), r=fk(t, [HC]), w=["CF"])
         for c in range(16):
             if c in SDUP:
-                S(lambda q, c=c: q.activation(T.EQ[:, seg[c]:seg[c + 1]], T.RB[:, 16 * c:256], AF.Square, bias=T.CF[:, c:c + 1]),
+                S(lambda q, c=c: q.activation(T.EQ[:, seg[c]:seg[c + 1]], T.RB[:, 16 * c:256], AF.Square, bias=T.CF[:, c:c + 1], scale=-1.0),
                   r=["RB", "CF"], w=["EQ%d" % c], c=cv(256 - 16 * c))
             else:
-                V(lambda q, c=c: q.tensor_scalar(T.EQ[:, seg[c]:seg[c + 1]], T.RB[:, 16 * c:256], T.CF[:, c:c + 1], 0.0, A.add, A.not_equal),
+                V(lambda q, c=c: q.tensor_scalar(T.EQ[:, seg[c]:seg[c + 1]], T.RB[:, 16 * c:256], T.CF[:, c:c + 1], SQ * SQ, A.not_equal, A.mult),
                   r=["RB", "CF"], w=["EQ%d" % c], c=cv(256 - 16 * c))
-        V(lambda q: q.tensor_tensor_scan(T.SC[:], T.EM[:], T.EQ[:], 1.0e9, A.max, A.min), r=["EM"] + ["EQ%d" % c for c in range(16)], w=["SC"], c=cv(NE, .5))
-        V(lambda q: q.tensor_scalar(T.dE[:], T.SC[:].indirect(T.E16[:, 0:1]), 0.5, None, A.is_lt), r=["SC", "E16"], w=["dE"])
-        V(lambda q: q.tensor_tensor(T.dF[:], T.dE[:], T.DJ[:], A.mult), r=["dE", "DJ"], w=["dF"])
-        V(lambda q: q.tensor_tensor(T.dG[:], T.dF[:], ci, A.max), r=["dF"] + cik, w=["dG"])
-        V(lambda q: q.tensor_copy(T.SL[:, 16 * t:16 * t + 16], T.dG[:]), r=["dG"], w=["SL%d" % t])
+        V(lambda q: q.tensor_tensor_scan(T.SC[:], T.EM[:], T.EQ[:], 1.0e16, A.max, A.min),
+          r=["EM%d" % c for c in range(16)] + ["EQ%d" % c for c in range(16)], w=["SC"], c=cv(NE, .5))
+        V(lambda q: q.tensor_tensor(T.dE[:], T.SC[:].indirect(T.E16[:, 0:1]), T.DJ[:], A.subtract), r=["SC", "E16", "DJ"], w=["dE"], c=cgat(16))
+        V(lambda q: q.tensor_tensor(T.dF[:], T.dE[:], T.CF[:], A.min), r=["dE", "CF"], w=["dF"])
+        V(lambda q: q.tensor_scalar(T.SL[:, 16 * t:16 * t + 16], T.dF[:], -1.0 / SQ, None, A.mult), r=["dF"], w=["SL%d" % t])
 
     others = [d for d in range(n) if d != rank]
     common = [e for e in topo.engines(core, T.cores[others[0]]) if all(e in topo.engines(core, T.cores[d]) for d in others)]
@@ -569,68 +659,75 @@ def rank_program(g, core, T, topo):
                 slot = (rank - d - 1) % n
                 ids.append(DstId(rid=rid, pnc=pid))
                 dsts.append(land[:, st * t + w * slot:st * t + w * slot + w])
-            tr = RemoteDMATransfer(dst_ids=ids, dma_engine_mask=mask, remote_sem=T.sem["arr%d" % t],
+            tr = RemoteDMATransfer(dst_ids=ids, dma_engine_mask=mask, remote_sem=T.sem["arr" + key],
                                    srcs=[buf[:, w * t:w * t + w]], dsts=dsts, alu_op=0)
-            add("g", "r", tr, [key], ["sent" + key], cfix(1.0))
-        add("n", "n", ("arr%d" % t, 2 * len(common) * len(others)), ["sentSV%d" % t, "sentSL%d" % t], ["LV%d" % t], cfix(0.0), 1.0)
+            add("g", "r", tr, [key], ["sent" + key], cfix(3.0 if t == 0 and w == 256 else 0.8), rows=48, nbytes=48 * 2 * w * XB)
+            add("n", "n", ("arr" + key, len(common) * len(others)), ["sent" + key], ["got" + key], cfix(0.0))
 
     def update(t):
         F = T["F%d" % (t + 1)]
-        fk = "win%d" % (t + 1)
+        wk = "win%d" % (t + 1)
         L = lambda a, b: T.LL[:, 64 * t + 16 * a:64 * t + 16 * b]
-        lk = "LV%d" % t
+        lk = "gotSL%d" % t
         cols = lambda i: slice(256 * i, 256 * i + 256)
-        S(lambda q: q.activation(T.sv[:], T.LV[:, 768 * t:768 * t + 768], AF.Copy, scale=col(INC)), r=[lk, "INC"], w=["sv"], c=cv(768))
-        fr = [fk, "win1d", lk] if t == 0 else [fk, lk]
+        for i in range(3):
+            S(lambda q, i=i: q.activation(T.sv[:, cols(i)], T.LV[:, 768 * t + 256 * i:768 * t + 256 * i + 256], AF.Copy, scale=col(INC)),
+              r=["gotSV%d" % t, "INC"], w=["sv%d" % i], c=cv(256))
+        fr = [wk, "dump%d" % t, lk] + ["cp%d_%d" % (t, i) for i in range(NF)]
         for i in range(2):
             S(lambda q, i=i: q.activation(T.g1[:, cols(i)], F[:].indirect(L(i, i + 1)), AF.Copy), r=fr, w=["g1_%d" % i], c=cgat(256))
-            V(lambda q, i=i: q.tensor_tensor(F[:].indirect(L(i, i + 1)), T.g1[:, cols(i)], T.sv[:, cols(i)], A.add), r=["g1_%d" % i, "sv", lk], w=[fk], c=csca(256))
-        V(lambda q: q.tensor_tensor(T.t1[:], F[:].indirect(L(2, 3)), T.sv[:, 512:768], A.add), r=fr + ["sv"], w=["t1"], c=cgat(256))
-        V(lambda q: q.tensor_scalar(T.i1[:, 512:768], T.t1[:], -0.4921875, 255.0, A.add, A.min), r=["t1"], w=["i1b"], c=cv(256))
-        V(lambda q: q.tensor_copy(F[:].indirect(L(2, 3)), T.i1[:, 512:768]), r=["i1b", lk], w=[fk], c=csca(256))
-        V(lambda q: q.tensor_scalar(T.i1[:, 0:512], F[:].indirect(L(0, 2)), -0.4921875, 255.0, A.add, A.min), r=[fk, lk], w=["i1a"], c=cgat(512))
-        for i in range(2):
-            V(lambda q, i=i: q.tensor_copy(F[:].indirect(L(i, i + 1)), T.i1[:, cols(i)]), r=["i1a", lk], w=[fk], c=csca(256))
+            V(lambda q, i=i: q.tensor_tensor(F[:].indirect(L(i, i + 1)), T.g1[:, cols(i)], T.sv[:, cols(i)], A.add), r=["g1_%d" % i, "sv%d" % i, lk], w=[wk], c=csca(256))
+        V(lambda q: q.tensor_tensor(T.t1[:], F[:].indirect(L(2, 3)), T.sv[:, 512:768], A.add), r=fr + ["sv2"], w=["t1"], c=cgat(256))
 
-    newest(0)
-    conv(16, K2)
-    parents(16)
-    conv(32, K3)
+        for i in range(3):
+            src, r, c = (T.t1[:], ["t1"], cv(256)) if i == 2 else (F[:].indirect(L(i, i + 1)), [wk, lk], cgat(256))
+            if FLS[t][i] == "v":
+                V(lambda q, i=i, src=src: q.tensor_scalar(T.i1[:, cols(i)], src, -0.4921875, 255.0, A.add, A.min), r=r, w=["i1%d" % i], c=c)
+            else:
+                S(lambda q, i=i, src=src: q.activation(T.r1[:, cols(i)], src, AF.Relu, bias=col(TOP), scale=-1.0), r=r + ["TOP"], w=["r1%d" % i], c=c)
+                S(lambda q, i=i: q.activation(T.r2[:, cols(i)], T.r1[:, cols(i)], AF.Copy, bias=MAGIC + 255, scale=-1.0), r=["r1%d" % i], w=["i1%d" % i], c=cv(256))
+        for i in range(3):
+            if FLS[t][i] == "v":
+                V(lambda q, i=i: q.tensor_copy(F[:].indirect(L(i, i + 1)), T.i1[:, cols(i)]), r=["i1%d" % i, lk], w=[wk], c=csca(256))
+            else:
+                V(lambda q, i=i: q.tensor_scalar(F[:].indirect(L(i, i + 1)), T.r2[:, cols(i)], 1.0, -MAGIC, A.mult, A.add), r=["i1%d" % i, lk], w=[wk], c=csca(256))
+
+    hot[0] = HOT
+    conv(1)
+    parents(1)
+    first(2)
+    conv(2)
+    first(3)
+    hot[0] = 0.0
     package(0, 2)
     package(0, 3)
-    clist(0, 2)
-    clist(0, 3)
     for t in range(3):
-        late = tk(t, ["c"]) + ik(t, ["c"]) + [k for e in (1, 2, 3) for k in ak(t, e, ["c"]) + ek(e, ["c"])]
-        if t == 0:
-            G(lambda q: q.iota(T.MK[:], [[0, 256], [256, 16]], 0, 0, allow_small_or_imprecise_dtypes=True), w=["MK"], c=cfix(8.5), after=late)
-            dma("g", [(T.F1[:, 0:4096], T.price[:])], r=["win0"], w=["win1"], lat=6, after=late)
-        else:
-            dma("y", [(T["F%d" % (t + 1)][:], T["F%d" % t][:])], r=["win%d" % t] + (["win1d"] if t == 1 else []), w=["win%d" % (t + 1)], lat=5, after=late)
+        for i in range(NF):
+            w = 4096 // NF
+            G(lambda q, t=t, i=i, w=w: q.affine_select(T["F%d" % (t + 1)][:, w * i:w * i + w], win(t)[:, w * i:w * i + w], [[0, w]], A.is_equal, 0.0, 0, 0),
+              r=wkey(t), w=["cp%d_%d" % (t, i)], c=(0, 2 * w, 0, 0, 0, 0.17))
+        if t < 2:
+            parents(2)
+            conv(3)
+        keys(t)
         for e in (1, 2, 3):
-            for h in HA:
-                gy(t, e, h)
-            for h in HA:
-                gx(t, e, h)
-            for h in HA:
-                tops(t, e, h)
+            for f, xs in ((gy, range(NP)), (diff, HA), (gx, range(NP)), (tops, HA)):
+                for x in xs:
+                    hot[0] = HOT if x == (0 if f in (gy, gx) else HC) else 0.0
+                    f(t, e, x)
+        hot[0] = HOT
         dedupe(t)
         send(t)
-        if t < 2:
-            parents(32)
-            conv(48, K4)
         update(t)
+        hot[0] = 0.0
         if t == 2:
-            dma("g", [(T.yp[:], T.F3[:, 0:4096])], r=["win3"], w=["yp"], lat=6)
-        for h in HS:
-            fin(t, h)
+            dma("g", [(T.yp[:], T.F3[:, 0:4096])], ["win3"], ["yp"], 128, 8192)
         if t < 2:
-            for h in HS:
-                gm(t, h)
+            clist(t + 1, 1)
+            for i in range(1, NP):
+                gm(t, i)
             for hs in TG:
                 tnew(t, hs)
-            clist(t + 1, 1)
-            clist(t + 1, 0)
             outh(t, list(HS))
         else:
             for h in HS:

@@ -5,26 +5,42 @@ from concourse.mybir import dt, AluOpType, AxisListType, ActivationFunctionType
 A = AluOpType
 AF = ActivationFunctionType
 LW = 272
-CH = [(0, 128), (128, 192), (192, 256), (256, 272)]
-PCS = [(256, 272), (0, 64), (64, 128), (128, 192), (192, 256)]
-RT = ["vvvvv" * 3] * 3
-YR = ["svsss" + "sssss" * 2] + ["sssss" * 3] * 2
-MR = ["ssss", "ssss"]
-TG = [[0], [1, 2, 3]]
+RT = ["v" * 18] * 2 + ["v" * 17 + "s"]
+FREE = False
+CH = [(0, 96), (96, 192), (192, 256), (256, 272)]
+PCS = [(256, 272), (0, 48), (48, 96), (96, 144), (144, 192), (192, 256)]
+YR = ["sv" + "s" * 16] + ["s" * 18] * 2
+MR = ["sssss"] * 2
+TG = [[0], [1], [2, 3]]
 NE = 2176
 BIG = 32768.0
 SQ = 8192.0
-SDUP = tuple(range(12))
+SDUP = 16
 LATE = (True, True, True)
-HOT = 0.0
-XB = 2.0
+HOT = (0.0, 0.0, 0.0)
+XB = 1.2
+UF = ("ggt", "ggt", "ttt")
+EMD = 8
+WIDE = True
+PCALL = 0.010
+REACH = 0.35
+LOADS = ["VT", "pkJ", "win0", "TI", "pkI"]
+LEAN = 1.0
+QC = False
+PKS = False
+SLOPES = [1.0, 2.0, 3.0, 5.0, 8.0, 12.0, 20.0]
+LAST = True
+SP = (0, 3, 7, 16)
+SEED = 3
+PA = 2048
+PG = 16
 NF = 8
-FLS = ("ssv", "ssv", "vsv")
-MCV = "s"
+FLS = ("sss", "sss", "ssv")
+MCV = ("ssss",) * 3
 MAGIC = 1.5 * 2 ** 23
 
 SCRATCH = {
-    "p0": ("sbuf", [128, 4096], "bfloat16"),
+    "p0": ("sbuf", [128, 4352], "bfloat16"),
     "F1": ("sbuf", [128, 4352], "float32"),
     "F2": ("sbuf", [128, 4352], "float32"),
     "F3": ("sbuf", [128, 4352], "float32"),
@@ -40,15 +56,18 @@ SCRATCH = {
     "B8": ("sbuf", [128, 8], "float32"),
     "one16": ("sbuf", [128, 16], "float32"),
     "SELK": ("sbuf", [128, 2048], "bfloat16"),
-    "SELH": ("sbuf", [128, 2048], "float16"),
     "SELW": ("sbuf", [128, 2048], "bfloat16"),
     "ones": ("sbuf", [128, LW], "bfloat16"),
     "cB": ("sbuf", [128, 256], "bfloat16"),
     "IDN": ("sbuf", [128, 256], "float32"),
-    "IDH": ("sbuf", [128, 256], "float16"),
-    "IDB": ("sbuf", [128, 384], "bfloat16"),
+    "IDH": ("sbuf", [128, 256], "bfloat16"),
+    "IDB": ("sbuf", [128, 256], "bfloat16"),
     "IXG": ("sbuf", [128, 128], "float32"),
     "WT": ("sbuf", [128, 128], "bfloat16"),
+    "IDI": ("sbuf", [128, 128], "bfloat16"),
+    "BE": ("sbuf", [128, 128], "bfloat16"),
+    "KF": ("sbuf", [128, 192], "float32"),
+    "KG": ("sbuf", [128, 256], "float32"),
     "TT0": ("sbuf", [128, LW], "uint16"),
     "TT1": ("sbuf", [128, LW], "uint16"),
     "TH0": ("sbuf", [128, LW], "float16"),
@@ -107,8 +126,8 @@ SCRATCH = {
     "Z1": ("psum", [128, 512], "float32"),
     "Z2": ("psum", [128, 512], "float32"),
     "Z3": ("psum", [128, 512], "float32"),
+    "Z4": ("psum", [128, 512], "float32"),
     "ZX": ("psum", [128, 512], "float32"),
-    "ZB": ("psum", [128, 3, 16], "float32"),
     "ZM": ("psum", [128, 512], "float32"),
     "ZR": ("psum", [128, 512], "float32"),
 }
@@ -116,13 +135,13 @@ NDMA = 70
 SEMAPHORES = ["cv", "cs", "cp", "cg", "lsem"] + ["arrS%s%d" % (x, t) for x in "VL" for t in range(3)] + ["d%d" % i for i in range(NDMA)]
 
 MODELS = [
-    (0.02, 0.88e-3, 1.20e-3, 2.8e-3, 0.80e-3, 0.10, 2.0, 5.0, 0.04, 0.07e-3),
-    (0.01, 0.85e-3, 0.98e-3, 1.9e-3, 0.85e-3, 0.06, 1.8, 6.0, 0.03, 0.05e-3),
-    (0.02, 1.20e-3, 1.95e-3, 4.8e-3, 1.20e-3, 0.10, 2.2, 4.5, 0.04, 0.08e-3),
-    (0.04, 0.92e-3, 1.75e-3, 1.9e-3, 0.60e-3, 0.15, 2.5, 3.5, 0.06, 0.04e-3),
-    (0.01, 0.95e-3, 1.10e-3, 4.0e-3, 0.90e-3, 0.15, 2.0, 7.0, 0.03, 0.09e-3),
+    (0.02, 0.83e-3, 1.25e-3, 3.0e-3, 0.83e-3, 0.14, 2.0, 3.0, 0.035, 0.06e-3),
+    (0.03, 0.87e-3, 1.02e-3, 1.9e-3, 0.87e-3, 0.16, 2.0, 3.0, 0.03, 0.05e-3),
+    (0.03, 1.10e-3, 1.70e-3, 4.2e-3, 1.10e-3, 0.15, 2.2, 3.5, 0.04, 0.08e-3),
+    (0.02, 0.92e-3, 1.60e-3, 1.9e-3, 0.92e-3, 0.20, 2.4, 2.5, 0.05, 0.04e-3),
+    (0.03, 1.20e-3, 1.90e-3, 5.0e-3, 1.20e-3, 0.18, 2.2, 4.0, 0.04, 0.07e-3),
 ]
-TRIES, MOVES, HEAT = 1500, 14000, 0.012
+TRIES, MOVES, HEAT = 300, 60000, 0.004
 
 
 def cv(n, per=1.0):
@@ -138,7 +157,7 @@ def csca(n):
 
 
 def cmm(n, k=1):
-    return (0.3 * k, 0, 0, 0, k * max(64, n), 0)
+    return (0, 0, 0, 0, k * max(64, n), PCALL * k)
 
 
 def cfix(x):
@@ -155,41 +174,51 @@ def price_ops(ops, md):
     return cost, dur, lat
 
 
-def run_order(ops, order, pr, wake, why=None):
+def run_order(ops, order, pr, wake, why=None, old=None, at=0):
     cost, dur, lat = pr
-    free, last, fin = {}, {}, [0.0] * len(ops)
-    end = dfree = 0.0
-    dlast = tail = -1
-    for i in order:
-        o = ops[i]
-        e = o["e"]
-        s = free.get(e, 0.0) if e != "n" else 0.0
-        w, own = last.get(e, -1), True
-        for p in o["full"]:
-            if fin[p] + wake > s:
-                s, w, own = fin[p] + wake, p, False
+    free, last = dict.fromkeys("vspgyn", 0.0), dict.fromkeys("vspgyn", -1)
+    dfree, dlast = 0.0, -1
+    seen, gone = (old[1][:], old[2][:]) if old else ([0.0] * len(ops), [0.0] * len(ops))
+    for i in order[:at]:
+        free[ops[i]["e"]] = gone[i]
+        if dur[i]:
+            dfree = seen[i] - lat[i] - wake
+    for i in order[at:]:
+        e, full = ops[i]["wait"]
+        s, w = free[e], -1
+        for p in full:
+            if seen[p] > s:
+                s, w = seen[p], p
         f = s + cost[i]
-        free[e], last[e] = f, i
+        if why is not None:
+            why[i] = (w, False, last[e]) if w >= 0 else (last[e], True, last[e])
+            last[e] = i
+        if e != "n":
+            free[e] = gone[i] = f
         if dur[i]:
             if dfree > f:
-                f, w, own = dfree, dlast, True
+                f = dfree
+                if why is not None:
+                    why[i] = (dlast, True, dlast)
             f = dfree = f + dur[i]
             dlast = i
-        fin[i] = f + lat[i]
-        if why is not None:
-            why[i] = (w, own)
-        if fin[i] > end:
-            end, tail = fin[i], i
-    return end, tail
+        seen[i] = f + lat[i] + wake
+    return max(seen), seen, gone
 
 
-def moved(order, i, j, link, ahead):
+def moved(ops, order, i, j, link, ahead):
     a, b = order.index(j), order.index(i)
+    if a > b:
+        return None
     span = order[a:b + 1] if ahead else order[a:b + 1][::-1]
-    take = {span[-1]}
+    take, held = {span[-1]}, set()
     for x in span[::-1]:
-        if x in take:
+        e = ops[x]["e"]
+        if x in take or e in held:
+            take.add(x)
             take.update(p for p, f in link[x])
+            if e != ops[span[-1]]["e"] and e != "n":
+                held.add(e)
     if span[0] in take:
         return None
     span = [x for x in span if x in take] + [x for x in span if x not in take]
@@ -245,6 +274,14 @@ def plan(ops):
     if "order" in PLAN:
         return PLAN["order"]
     m = len(ops)
+    above = []
+    for o in ops:
+        far = near = 0
+        for p in o["full"]:
+            far |= above[p]
+            near |= 1 << p
+        above.append(far | near)
+        o["wait"] = (o["e"], [p for p in o["full"] if not far >> p & 1])
     pred = [[(p, True) for p in o["full"]] + [(p, False) for p in o["order"]] for o in ops]
     succ = [[] for _ in ops]
     for i in range(m):
@@ -260,10 +297,10 @@ def plan(ops):
         for j, f in succ[i]:
             b = max(b, base[j] + (dur[i] + lat[i] + wake if f else 0.0))
         base[i] = b + cost[i] + (0.0 if succ[i] else dur[i] + lat[i])
-    rng = np.random.default_rng(2)
+    rng = np.random.default_rng(SEED)
     ref, best = None, None
     for k in range(TRIES):
-        slope = float(rng.choice([1.0, 2.0, 3.0, 5.0, 8.0, 12.0, 20.0]))
+        slope = float(rng.choice(SLOPES))
         if k == 0:
             prio = np.array(base)
         elif k % 10 == 1:
@@ -278,31 +315,55 @@ def plan(ops):
         sc = sum(a / b for a, b in zip(ts, ref))
         if best is None or sc <= best[0]:
             best = (sc, order, prio, slope, fin, ts)
-    order, sc, ts = best[1], best[0], best[5]
-    why = [None] * m
+    order = best[1]
+    why, arcs = [None] * m, None
+    either = [i for i in range(m) if ops[i]["both"]]
+
+    def turn(o):
+        o["e"] = "s" if o["e"] == "v" else "v"
+        o["wait"] = (o["e"], o["wait"][1])
     for k in range(MOVES):
-        md = k % len(MODELS)
-        i = run_order(ops, order, priced[md], MODELS[md][5], why)[1]
-        arcs = []
-        while i >= 0:
-            j, own = why[i]
-            if own and j >= 0:
-                arcs.append((i, j))
-            i = j
+        md = k // 16 % len(MODELS)
+        if k % 512 == 0:
+            seen, gone = run_order(ops, order, priced[0], wake)[1:]
+            place = {x: n for n, x in enumerate(order)}
+            order = sorted(order, key=lambda x: ((gone[x] - cost[x] if ops[x]["e"] != "n" else seen[x] - lat[x] - wake) + 1e-9 * place[x]))
+            runs = [run_order(ops, order, pr, x[5]) for pr, x in zip(priced, MODELS)]
+            sc = sum(a[0] / b for a, b in zip(runs, ref))
+        if k % 16 == 0 or not arcs:
+            end, seen = run_order(ops, order, priced[md], MODELS[md][5], why)[0:2]
+            i = seen.index(end)
+            arcs = []
+            while i >= 0:
+                j, own = why[i][0:2]
+                if own and j >= 0:
+                    arcs.append((i, j))
+                i = j
         i, j = arcs[int(rng.integers(len(arcs)))]
-        for _ in range(int(rng.integers(4))):
-            if why[j][1] and why[j][0] >= 0:
-                j = why[j][0]
+        for _ in range(int(rng.geometric(REACH)) - 1):
+            if why[j][2] >= 0:
+                j = why[j][2]
         ahead = bool(rng.integers(2))
-        new = moved(order, i, j, pred if ahead else succ, ahead)
-        if new is None:
-            continue
-        t2 = [run_order(ops, new, pr, x[5])[0] for pr, x in zip(priced, MODELS)]
-        s2 = sum(a / b for a, b in zip(t2, ref))
-        if s2 <= sc + HEAT * (1 - k / MOVES) * rng.random():
-            order, sc, ts = new, s2, t2
+        flip = [x for x in (i, j, int(rng.choice(either))) if ops[x]["both"]][:1] if k % 4 == 3 else []
+        for x in flip:
+            turn(ops[x])
+        new = order if flip else moved(ops, order, i, j, pred if ahead else succ, ahead)
+        room = HEAT * (1 - k / MOVES) * rng.random()
+        for x in flip:
+            room += LEAN * cost[x] / ref[0] * (1 if ops[x]["e"] == "s" else -1)
+        if new is not None:
+            at = order.index(flip[0]) if flip else min(order.index(i), order.index(j))
+            one = run_order(ops, new, priced[md], MODELS[md][5], None, runs[md], at)
+            if one[0] <= runs[md][0] + room * ref[md]:
+                r2 = [one if x == md else run_order(ops, new, priced[x], MODELS[x][5], None, runs[x], at) for x in range(len(MODELS))]
+                s2 = sum(a[0] / b for a, b in zip(r2, ref))
+                if s2 <= sc + room:
+                    order, sc, runs, flip = new, s2, r2, []
+        for x in flip:
+            turn(ops[x])
+    PLAN["queues"] = [o["e"] for o in ops]
     PLAN["order"] = order
-    PLAN["ts"] = (best[5], ts)
+    PLAN["ts"] = (best[5], [a[0] for a in runs])
     PLAN["ops"] = ops
     return order
 
@@ -318,7 +379,7 @@ def rank_program(g, core, T, topo):
     lastw, readers, lastb = {}, {}, {}
     hot = [0.0]
 
-    def add(e, kind, body, r, w, cost, up=0.0, after=(), bk=(), rows=0, nbytes=0):
+    def add(e, kind, body, r, w, cost, up=0.0, after=(), bk=(), rows=0, nbytes=0, both=None):
         i = len(ops)
         full, order = set(), set()
         for k in list(r) + list(after):
@@ -330,11 +391,11 @@ def rank_program(g, core, T, topo):
             full.update(readers.get(k, []))
         for k in bk:
             if k in lastb:
-                (order if ops[lastb[k]]["e"] == e else full).add(lastb[k])
+                (order if ops[lastb[k]]["e"] == e and not both and not ops[lastb[k]]["both"] else full).add(lastb[k])
             lastb[k] = i
         full.discard(i)
         ops.append({"e": e, "kind": kind, "body": body, "full": sorted(full), "order": sorted(order - full),
-                    "cost": cost, "up": up + hot[0], "name": (list(w) + [""])[0], "rows": rows, "bytes": nbytes})
+                    "cost": cost, "up": up + hot[0], "name": (list(w) + [""])[0], "rows": rows, "bytes": nbytes, "both": both})
         for k in r:
             readers.setdefault(k, []).append(i)
         for k in w:
@@ -346,6 +407,16 @@ def rank_program(g, core, T, topo):
 
     def S(f, r=(), w=(), c=cv(1), bk=()):
         add("s", "c", [f], r, w, c, bk=bk)
+
+    def VS(e, fv, fs, r, w, c, bk=()):
+        add(e, "c", None, r, w, c, bk=bk, both={"v": [fv], "s": [fs]})
+
+    def move(e, out, in_, r, w, c, scale=None, bias=None, bk=()):
+        sc, op = ([scale, bias], [A.mult, A.add]) if scale is not None and bias is not None else \
+            ([scale, None], [A.mult]) if scale is not None else ([bias or 0.0, None], [A.add])
+        kw = {k: x for k, x in (("scale", scale), ("bias", bias)) if x is not None}
+        func = AF.Copy if bias is None or isinstance(bias, float) else AF.Identity
+        VS(e, lambda q: q.tensor_scalar(out, in_, *sc, *op), lambda q: q.activation(out, in_, func, **kw), r, w, c, bk)
 
     def PE(fs, r, w, c, bk):
         add("p", "c", fs, r, w, c, bk=bk)
@@ -382,19 +453,28 @@ def rank_program(g, core, T, topo):
     def alots(t, e, a, b):
         return T.PK[:, 768 + 256 * t + a:768 + 256 * t + b] if e == 1 else T.AE[:, LW * (e - 2) + a:LW * (e - 2) + b]
 
+    def aless(t, e, h):
+        a, b = CH[h]
+        return (TH(t - 1)[:, a:b], fk(t - 1, [h])) if e == 1 else (alots(t, e, a, b), ek(t, e, [h]))
+
     def ek(t, e, hs):
         return ["AE%d_%d" % (e, h) if e > 1 else "AC%d" % t if h == HC else "PK%d_%d" % (t - 1, h) for h in hs]
 
-    dma("y", [(T.pkJ[:, 0:256], T.packs[:, 768:1024]), (T.pkJ[:, 256:LW], T.packs[0:128:16, 768:1024])], [], ["pkJ"], 256, 544, up=2000)
-    dma("y", [(T.p0[:, 0:2048], T.price[:, 0:2048])], [], ["win0a"], 128, 4096, up=1700, issued=["pkJ"])
+    dma("y", [(T.p0[:, 0:PA], T.price[:, 0:PA])], [], ["win0a"], 128, 2 * PA, up=1700)
     add("v", "c", [lambda q: q.memset(T.VT[:], 0)], [], ["VT"], cv(1024), up=1650)
     clear = len(ops) - 1
-    dma("y", [(T.VT[0:128:16, :], T.prev[:]), (T.VT[1:128:16, :], T.packs[0:128:16, :])], [], ["VT"], 128, 512, up=1600, issued=["win0a"])
-    dma("y", [(T.TI[:, 0:256], T.lots[:]), (T.TI[:, 256:LW], T.lots[0:128:16, :]), (T.slI[:, 0:3], T.slack[:])], [], ["TI", "slI"], 384, 370, up=1580, issued=["VT"])
-    dma("y", [(T.p0[:, 2048:4096], T.price[:, 2048:4096])], [], ["win0"], 128, 4096, up=1550, issued=["TI"])
-    dma("y", [(T.pkI[:], T.packs[:, 0:768])], [], ["pkI"], 128, 3072, up=1300, issued=["win0"])
-    dma("y", [(T.small[:, 4:5], T.wt[:])], [], ["wtI"], 128, 4, up=1200, issued=["pkI"])
-    add("g", "d", [(T.small[:, 0:1], T.inc[:])], [], ["incI"], cfix(1.6), up=80, rows=8)
+    loads = {
+        "VT": ([(T.VT[0:128:16, :], T.prev[:]), (T.VT[1:128:16, :], T.packs[0:128:16, :])], ["VT"], 128, 512),
+        "pkJ": ([(T.pkJ[:, 0:256], T.packs[:, 768:1024]), (T.pkJ[:, 256:LW], T.packs[0:128:16, 768:1024]), (T.slI[:, 0:3], T.slack[:])],
+                ["pkJ", "slI"], 384, 370),
+        "win0": ([(T.p0[:, PA:4096], T.price[:, PA:4096])], ["win0"], 128, 8192 - 2 * PA),
+        "TI": ([(T.TI[:, 0:256], T.lots[:]), (T.TI[:, 256:LW], T.lots[0:128:16, :])], ["TI"], 256, 544),
+        "pkI": ([(T.pkI[:], T.packs[:, 0:768])], ["pkI"], 128, 3072),
+    }
+    for x, y in zip(["win0a"] + LOADS, LOADS):
+        dma("y", loads[y][0], [], *loads[y][1:], up=1500, issued=[x])
+    dma("s", [(T.small[:, 4:5], T.wt[:])], [], ["wtI"], 128, 4, up=1900)
+    dma("y", [(T.small[:, 0:1], T.inc[:])], [], ["incI"], 128, 4, up=1200, issued=["pkI"])
 
     fl = dict(allow_small_or_imprecise_dtypes=True)
     G(lambda q: q.iota(T.pI[:, 0:1], [[1, 1]], 0, 1), w=["pI"], up=100)
@@ -408,17 +488,17 @@ def rank_program(g, core, T, topo):
     add("v", "c", [lambda q: q.memset(T.SELK[:], 0.0)], [], ["SELK"], cv(1024))
     ops[-1]["order"].append(clear)
     V(lambda q: q.memset(T.one16[:], 1.0), w=["one16"])
-    V(lambda q: q.memset(T.ones[:], 1.0), w=["ones"], c=cv(LW // 2))
-    V(lambda q: q.memset(T.cB[:], 0.0), w=["cB"], c=cv(128))
-    V(lambda q: q.memset(T.cB[0:1, 0:128], -0.5 * BIG), w=["cB"])
-    V(lambda q: q.memset(T.cB[0:1, 128:256], 33.0), w=["cB"])
-    V(lambda q: q.memset(T.cB[32:33, 128:256], 192.0 * 2048), w=["cB"])
+    G(lambda q: q.iota(T.ones[:], [[0, LW]], 1, 0, **fl), w=["ones"], c=cfix(0.6))
+    G(lambda q: q.iota(T.cB[:], [[0, 256]], 0, 0, **fl), w=["cB"], c=cfix(0.6))
+    for ap, x in ((T.cB[0:1, 0:128], -15.5 * BIG), (T.cB[0:1, 128:256], 33.0), (T.cB[32:33, 128:256], 192.0 * 2048)):
+        V(lambda q, ap=ap, x=x: q.memset(ap, x), w=["cB"])
+    G(lambda q: q.iota(sm[:, HR:HX + 1], [[-9 * 512, 2]], 17 * 256, 0, **fl), w=["HR", "HX"], up=100)
     V(lambda q: q.tensor_copy(col(PF), T.pI[:, 0:1]), r=["pI"], w=["PF"])
     V(lambda q: q.tensor_scalar(T.pI[:, 1:2], T.pI[:, 0:1], 15, None, A.bitwise_and), r=["pI"], w=["pI1"])
     V(lambda q: q.tensor_scalar(T.pI[:, 2:3], T.pI[:, 0:1], 4, None, A.logical_shift_right), r=["pI"], w=["pI2"])
     V(lambda q: q.tensor_copy(sm[:, RF:GF + 1], T.pI[:, 1:3]), r=["pI1", "pI2"], w=["RF"])
     V(lambda q: q.tensor_scalar(T.B8[:], T.row8[:], col(GF), None, A.is_equal), r=["row8", "RF"], w=["B8"])
-    V(lambda q: q.tensor_scalar(T.L1c[:], T.i16[:], col(RF), None, A.add), r=["i16", "RF"], w=["L1c"])
+    move("s", T.L1c[:], T.i16[:], ["i16", "RF"], ["L1c"], cv(1), bias=col(RF))
     for gg in range(8):
         V(lambda q, gg=gg: q.tensor_scalar(T.SELK[:, 16 * gg:16 * gg + 129 * 15 + 1:129], T.one16[:],
                                            T.B8[:, gg:gg + 1], BIG, A.mult, A.mult),
@@ -427,39 +507,41 @@ def rank_program(g, core, T, topo):
     V(lambda q: q.tensor_copy(T.A16[:, 0:LW], T.pkJ[:]), r=["pkJ"], w=ak(0, 1, HA), c=cv(LW))
     V(lambda q: q.tensor_copy(sm[:, SLF:SLF + 3], T.slI[:, 0:3]), r=["slI"], w=["SLF"])
     V(lambda q: q.tensor_copy(T.TT0[:], T.TI[:]), r=["TI"], w=tk(0, HA), c=cv(LW))
-    V(lambda q: q.tensor_scalar(T.TH0[:], T.TI[:], -2048.0, None, A.add), r=["TI"], w=fk(0, HA), c=cv(LW))
-    V(lambda q: q.tensor_scalar(T.TH1[:], T.pkJ[:], -2048.0, None, A.add), r=["pkJ"], w=fk(1, HA), c=cv(LW))
+    V(lambda q: q.tensor_scalar(T.TH0[:], T.TT0[:], -2048.0, None, A.add), r=tk(0, HA), w=fk(0, HA), c=cv(LW, .5))
+    V(lambda q: q.tensor_scalar(T.TH1[:], T.A16[:, 0:LW], -2048.0, None, A.add), r=ak(0, 1, HA), w=fk(1, HA), c=cv(LW, .5))
     V(lambda q: q.tensor_copy(T.PK[:, 768:768 + LW], T.pkJ[:]), r=["pkJ"], w=ek(0, 1, HA), c=cv(LW))
     V(lambda q: q.tensor_copy(T.PK[:, 0:768], T.pkI[:]), r=["pkI"], w=["PKa"], c=cv(768))
     V(lambda q: q.tensor_scalar(sm[:, R0:R0 + 2], T.row8[:, 0:2], col(RF), None, A.is_equal), r=["row8", "RF"], w=["R0"])
     V(lambda q: q.tensor_scalar(T.VH[:], T.VT[:, 768:1024], col(R0), None, A.mult), r=["VT", "R0"], w=["VH"], c=cv(256))
-    V(lambda q: q.tensor_scalar(T.SELH[:], T.SELK[:], 1.0 / BIG, None, A.mult), r=SELK, w=["SELH"], c=cv(1024))
-    V(lambda q: q.memset(col(HR), -8.5 * 512), w=["HR"])
-    V(lambda q: q.memset(col(HX), -0.5 * 512), w=["HX"])
     V(lambda q: q.memset(col(TOP), 255.4921875), w=["TOP"])
     V(lambda q: q.tensor_scalar(T.IDN[:, 0:128], T.IX[:, 0:128], col(PF), None, A.is_equal), r=["IX", "PF"], w=["IDN"], c=cv(128))
     S(lambda q: q.activation(T.IDN[:, 128:256], T.IDN[:, 0:128], AF.Copy, scale=-1.0), r=["IDN"], w=["IDM"], c=cv(128))
-    V(lambda q: q.tensor_copy(T.IDH[:], T.IDN[:]), r=["IDN", "IDM"], w=["IDH"], c=cv(256))
-    S(lambda q: q.activation(T.IDB[:, 0:256], T.IDN[:], AF.Copy), r=["IDN", "IDM"], w=["IDB"], c=cv(256))
-    S(lambda q: q.activation(T.IDB[:, 256:384], T.IDN[:, 0:128], AF.Copy, scale=-2048.0), r=["IDN"], w=["ID2"], c=cv(128))
+    S(lambda q: q.activation(T.IDH[:], T.IDN[:], AF.Copy), r=["IDN", "IDM"], w=["IDH"], c=cv(256))
+    S(lambda q: q.activation(T.IDB[:, 0:128], T.IDN[:, 0:128], AF.Copy, scale=-2048.0), r=["IDN"], w=["ID2"], c=cv(128))
+    S(lambda q: q.activation(T.IDB[:, 128:256], T.IDN[:, 0:128], AF.Copy, scale=2048.0), r=["IDN"], w=["ID3"], c=cv(128))
     for t in range(3):
         G(lambda q, t=t: q.iota(T["F%d" % (t + 1)][:, 4096:4352], [[0, 256]], 0, 0, **fl), w=["dump%d" % t], c=cfix(0.6))
+    G(lambda q: q.iota(T.p0[:, 4096:4352], [[0, 256]], 0, 0, **fl), w=["dump3"], c=cfix(0.6))
     add("s", "c", [lambda q: q.activation(T.MK[:], T.MI[:], AF.Sigmoid, bias=col(HX), scale=512.0)], ["MI", "HX"], ["MK"], (1, 1024, 0, 0, 0, 1.3), up=90)
-    V(lambda q: q.tensor_scalar(col(RQ), col(RF), 1.0, None, A.add), r=["RF"], w=["RQ"])
+    move("s", col(RQ), col(RF), ["RF"], ["RQ"], cv(1), bias=1.0)
     V(lambda q: q.tensor_scalar(T.QM[:], T.IX[:], col(RQ), 1.0e16, A.is_equal, A.mult), r=["IX", "RQ"], w=["QM"], c=cv(256))
     seg = [256 * c - 8 * c * (c - 1) for c in range(17)]
     for c in range(16):
-        S(lambda q, c=c: q.activation(T.EM[:, seg[c]:seg[c + 1]], T.QM[:, 0:256 - 16 * c], AF.Copy), r=["QM"], w=["EM%d" % c], c=cv(256 - 16 * c))
-    V(lambda q: q.tensor_scalar(col(C14), col(RF), -8.0, 248.0, A.mult, A.add), r=["RF"], w=["c14"])
-    V(lambda q: q.tensor_tensor(col(C15), col(C14), col(RF), A.mult), r=["c14", "RF"], w=["c15"])
-    V(lambda q: q.tensor_scalar(T.E16[:, 0:1], col(C15), 255.0, None, A.add), r=["c15"], w=["E16"])
-    V(lambda q: q.tensor_scalar(T.DJt[:], T.L1c[:], 4096.0, SQ, A.add, A.mult), r=["L1c"], w=["DJt"])
+        if c < EMD:
+            dma("y", [(T.EM[:, seg[c]:seg[c + 1]], T.QM[:, 0:256 - 16 * c])], ["QM"], ["EM%d" % c], 128, 512 - 32 * c, issued=["pkI"])
+        else:
+            S(lambda q, c=c: q.activation(T.EM[:, seg[c]:seg[c + 1]], T.QM[:, 0:256 - 16 * c], AF.Copy), r=["QM"], w=["EM%d" % c], c=cv(256 - 16 * c))
+    move("s", col(C14), col(RF), ["RF"], ["c14"], cv(1), -8.0, 248.0)
+    V(lambda q: q.tensor_scalar(T.E16[:, 0:1], col(C14), col(RF), 255.0, A.mult, A.add), r=["c14", "RF"], w=["E16"])
+    move("s", T.DJt[:], T.L1c[:], ["L1c"], ["DJt"], cv(1), SQ, 4096.0 * SQ)
     V(lambda q: q.tensor_scalar(T.dF[:], T.L1c[:], 254.5, None, A.is_lt), r=["L1c"], w=["dF"])
     V(lambda q: q.tensor_tensor(T.DJ[:], T.dF[:], T.DJt[:], A.mult), r=["dF", "DJt"], w=["DJ"])
     V(lambda q: q.tensor_scalar(col(INC), T.small[:, 0:1], 1.0 / 64, None, A.mult), r=["incI"], w=["INC"])
     V(lambda q: q.tensor_scalar(col(W2), T.small[:, 4:5], 2.0, None, A.mult), r=["wtI"], w=["W2"])
     V(lambda q: q.tensor_scalar(col(W3), T.small[:, 4:5], 2.0 / BIG, None, A.mult), r=["wtI"], w=["W3"])
     V(lambda q: q.tensor_scalar(T.WT[:], T.IXG[:], col(GF), col(W2), A.is_equal, A.mult), r=["IXG", "RF", "W2"], w=["WT"], c=cv(128))
+    if FREE:
+        V(lambda q: q.tensor_scalar(T.BE[:], T.IXG[:], col(GF), BIG, A.is_equal, A.mult), r=["IXG", "RF"], w=["BE"], c=cv(128))
     for i in range(2):
         S(lambda q, i=i: q.activation(T.SELW[:, 1024 * i:1024 * i + 1024], T.SELK[:, 1024 * i:1024 * i + 1024], AF.Copy, scale=col(W3)),
           r=SELK + ["W3"], w=["SELW%d" % i], c=cv(1024))
@@ -467,11 +549,11 @@ def rank_program(g, core, T, topo):
     KS, KY, KM = T.KS, T.KY, T.KM
 
     def conv(d):
-        PE([lambda q, k=k: q.matmul(T.ZM[:, 384:400], T.SELH[:, 128 * k:128 * k + 128], T.VH[:, k:256:16], k == 0, k == 15)
-            for k in range(16)], ["VH", "SELH"], ["zc"], cmm(16, 16), ["bM"])
+        PE([lambda q, k=k: q.matmul(T.ZM[:, 384:400], T.SELK[:, 128 * k:128 * k + 128], T.VH[:, k:256:16], k == 0, k == 15)
+            for k in range(16)], ["VH"] + SELK, ["zc"], cmm(16, 16), ["bM"])
         if d < 3:
-            V(lambda q: q.tensor_copy(T.LU[:, 16 * d:16 * d + 16], T.ZM[:, 384:400]), r=["zc"], w=["LU%d" % d], bk=["bM"])
-        S(lambda q: q.activation(KS[:, 16 * d:16 * d + 16], T.ZM[:, 384:400], AF.Copy), r=["zc"], w=["KS%d" % d], bk=["bM"])
+            V(lambda q: q.tensor_scalar(T.LU[:, 16 * d:16 * d + 16], T.ZM[:, 384:400], 1.0 / BIG, None, A.mult), r=["zc"], w=["LU%d" % d], bk=["bM"])
+        S(lambda q: q.activation(KS[:, 16 * d:16 * d + 16], T.ZM[:, 384:400], AF.Copy, scale=1.0 / BIG), r=["zc"], w=["KS%d" % d], bk=["bM"])
 
     def parents(d):
         V(lambda q: q.tensor_scalar(T.VH[:], T.VT[:].indirect(T.LU[:, 16 * d:16 * d + 16]), col(R0), None, A.mult),
@@ -480,22 +562,22 @@ def rank_program(g, core, T, topo):
     def first(e):
         V(lambda q: q.tensor_scalar(T.VG[:], T.VT[:].indirect(T.LU[:, 16 * e - 16:16 * e]), -2048.0, col(R0 + 1), A.add, A.mult),
           r=["VT", "R0", "LU%d" % (e - 1)], w=["VG"], c=cgat(256))
-        PE([lambda q, k=k: q.matmul(T.ZR[:, 384:400], T.SELH[:, 128 * k:128 * k + 128], T.VG[:, 16 * k:16 * k + 16], k == 0, k == 15)
-            for k in range(16)], ["VG", "SELH"], ["zf"], cmm(16, 16), ["bR"])
-        V(lambda q: q.tensor_scalar(alist(0, e, 256, LW), T.ZR[:, 384:400], 2048.0, None, A.add), r=["zf"], w=ak(0, e, [HC]), bk=["bR"])
-        S(lambda q: q.activation(alots(0, e, 256, LW), T.ZR[:, 384:400], AF.Copy), r=["zf"], w=ek(0, e, [HC]), bk=["bR"])
+        PE([lambda q, k=k: q.matmul(T.ZM[:, 448:464], T.SELK[:, 128 * k:128 * k + 128], T.VG[:, 16 * k:16 * k + 16], k == 0, k == 15)
+            for k in range(16)], ["VG"] + SELK, ["zf"], cmm(16, 16), ["bM"])
+        V(lambda q: q.tensor_scalar(alist(0, e, 256, LW), T.ZM[:, 448:464], 1.0 / BIG, 2048.0, A.mult, A.add), r=["zf"], w=ak(0, e, [HC]), bk=["bM"])
+        S(lambda q: q.activation(alots(0, e, 256, LW), T.ZM[:, 448:464], AF.Copy, scale=1.0 / BIG), r=["zf"], w=ek(0, e, [HC]), bk=["bM"])
 
     def keys(t):
         c = 16 if t == 2 else 32
         S(lambda q: q.activation(KS[:, 0:16], T.L1c[:], AF.Copy, bias=768.0 + 256 * t), r=["L1c"], w=["KS0"])
         for e in range(3):
-            S(lambda q, e=e: q.activation(KY[:, e, 0:c], KS[:, 16 * e:16 * e + c], AF.Copy, bias=4096.0 * (e + 1)),
+            S(lambda q, e=e: q.activation(KY[:, e, 0:c], KS[:, 16 * e:16 * e + c], AF.Copy, bias=-4096.0 * (e + 1) - 1, scale=-1.0),
               r=["KS%d" % d for d in range(e, e + c // 16)], w=["KY%d" % e])
-        S(lambda q: q.activation(KM[:, 3, 0:c], KS[:, 32:32 + c], AF.Copy), r=["KS%d" % d for d in range(2, 2 + c // 16)], w=["KM3"])
+        S(lambda q: q.activation(KM[:, 3, 0:c], KS[:, 32:32 + c], AF.Copy, bias=-1.0, scale=-1.0), r=["KS%d" % d for d in range(2, 2 + c // 16)], w=["KM3"])
 
     def package(t, e):
-        S(lambda q: q.activation(alots(t, e, 0, 256), T.PK[:, 0:1024 + 256 * t].indirect(T.LU[:, 16 * e - 16:16 * e]), AF.Copy, bias=-2048.0),
-          r=["PKa"] + ["PK%d_%d" % (i, h) for i in range(-1, t) for h in HS] + ["LU%d" % (e - 1)], w=ek(t, e, HS), c=cgat(256))
+        move("s", alots(t, e, 0, 256), T.PK[:, 0:1024 + 256 * t].indirect(T.LU[:, 16 * e - 16:16 * e]),
+             ["PKa"] + ["PK%d_%d" % (i, h) for i in range(-1, t) for h in HS] + ["LU%d" % (e - 1)], ek(t, e, HS), cgat(256), bias=-2048.0)
         V(lambda q: q.tensor_scalar(alist(t, e, 0, 256), alots(t, e, 0, 256), 2048.0, None, A.add), r=ek(t, e, HS), w=ak(t, e, HS), c=cv(256))
 
     def clist(t, e):
@@ -507,22 +589,27 @@ def rank_program(g, core, T, topo):
     NP = len(PCS)
 
     def gy(t, e, i):
-        a, b = PCS[i]
+        who = YR[t][NP * (e - 1):NP * e] + "."
+        if who[i] == "+":
+            return
+        j = i + 1
+        while who[j] == "+":
+            j += 1
+        a, b = PCS[i][0], PCS[j - 1][1]
         o = 16 * (LW * (e - 1) + a)
         out, lst = T.Y[:, o:o + 16 * (b - a)], win(t).indirect(alist(t, e, a, b))
-        r, w, c = wkey(t) + ak(t, e, [chunk(a)]) + ["SLF"], ["Y%d_%d" % (e, i)], cgat(16 * (b - a))
-        if YR[t][NP * (e - 1) + i] == "v":
-            V(lambda q: q.tensor_scalar(out, lst, col(SLF + t), None, A.add), r=r, w=w, c=c)
-        else:
-            S(lambda q: q.activation(out, lst, AF.Identity, bias=col(SLF + t)), r=r, w=w, c=c)
+        r, w, c = wkey(t) + ak(t, e, [chunk(PCS[x][0]) for x in range(i, j)]) + ["SLF"], ["Y%d_%d" % (e, x) for x in range(i, j)], cgat(16 * (b - a))
+        move(who[i], out, lst, r, w, c, bias=col(SLF + t))
 
     def diff(t, e, h):
         a, b = CH[h]
         z = T["Z%d" % h][:, 256:256 + b - a]
-        one, lots, lk = (T.IDH, TH(t - 1)[:, a:b], fk(t - 1, [h])) if e == 1 else (T.IDN, alots(t, e, a, b), ek(t, e, [h]))
-        PE([lambda q: q.matmul(z, one[:, 0:128], lots, True, False),
-            lambda q: q.matmul(z, T.IDH[:, 128:256], TH(t)[:, a:b], False, True)],
-           ["IDN", "IDH"] + lk + fk(t, [h]), ["zD%d" % h], cmm(b - a, 2 if e == 1 else 5), ["bZ%d" % h])
+        lots, lk = aless(t, e, h)
+        PE([lambda q: q.matmul(z, (T.IDH if e == 1 else T.IDN)[:, 128:256], lots, True, False),
+            lambda q: q.matmul(z, T.IDH[:, 0:128], TH(t)[:, a:b], False, True)],
+           ["IDM", "IDH"] + lk + fk(t, [h]), ["zD%d" % h], cmm(b - a, 2 if e == 1 else 5), ["bZ%d" % h])
+
+    held = []
 
     def gx(t, e, i):
         a, b = PCS[i]
@@ -540,44 +627,74 @@ def rank_program(g, core, T, topo):
         else:
             S(lambda q: q.activation(T.XS[:, 0:16 * m], lst, AF.Copy), r=r, w=["XS"], c=cgat(16 * m))
             for x, y in blocks:
-                PE([lambda q, x=x, y=y: q.matmul(T.ZX[:, 0:y - x], T.IDB[:, 0:128], T.XS[:, x:y], True, False),
-                    lambda q, x=x, y=y: q.matmul(T.ZX[:, 0:y - x], T.IDB[:, 128:256], T.Y[:, o + c0 + x:o + c0 + y], False, True)],
-                   ["XS", "IDB", "Y%d_%d" % (e, i)], ["zX"], cmm(y - x, 2), ["bX"])
-                S(lambda q, x=x, y=y: q.activation(T.C[:, c0 + x:c0 + y], T.ZX[:, 0:y - x], AF.Sigmoid, bias=col(HX), scale=512.0),
+                PE([lambda q, x=x, y=y: q.matmul(T.ZX[:, 0:y - x], T.IDB[:, 128:256], T.XS[:, x:y], True, False),
+                    lambda q, x=x, y=y: q.matmul(T.ZX[:, 0:y - x], T.IDB[:, 0:128], T.Y[:, o + c0 + x:o + c0 + y], False, True)],
+                   ["XS", "ID2", "ID3", "Y%d_%d" % (e, i)], ["zX"], cmm(y - x, 2), ["bX"])
+                S(lambda q, x=x, y=y: q.activation(T.C[:, c0 + x:c0 + y], T.ZX[:, 0:y - x], AF.Sigmoid, bias=col(HX), scale=0.25),
                   r=["zX", "HX"], w=["C%d_%d" % (i, x)], c=cv(y - x), bk=["bX"])
-        PE([lambda q, k=k: q.matmul(z, T.SELK[:, 128 * k:128 * k + 128], T.C[:, c0 + k:c1:16], k == 0, k == 15) for k in range(16)],
-           ck + SELK, ["zC%d" % i], cmm(m, 16), ["bZ%d" % h])
+        w0 = c0
+        if WIDE:
+            held.extend(ck)
+            if b < CH[h][1]:
+                return
+            ck, m, w0 = held[:], b - CH[h][0], 16 * CH[h][0]
+            z = T["Z%d" % h][:, 0:m]
+            held.clear()
+        for x in range(0, 16, PG):
+            PE([lambda q, k=k: q.matmul(z, T.SELK[:, 128 * k:128 * k + 128], T.C[:, w0 + k:c1:16], k == 0, k == 15) for k in range(x, x + PG)],
+               ck + SELK, ["zC%d" % i] if x in (0, 16 - PG) else [], cmm(m, PG), ["bZ%d" % h])
+            if x:
+                ops[-1]["full"] = [p for p in ops[-1]["full"] if p != len(ops) - 1 - x // PG]
+                ops[-1]["order"] = [len(ops) - 2]
 
     def tops(t, e, h):
         a, b = CH[h]
         m = b - a
-        z, bk = T["Z%d" % h], ["bZ%d" % h]
-        d = z[:, 256:256 + m]
+        z, d, dk, bk = T["Z%d" % h][:, 0:m], T["Z%d" % h][:, 256:256 + m], ["zD%d" % h], ["bZ%d" % h]
+        lots, lk = aless(t, e, h)
         mask, mk = (T.MC[:], "MC") if h == HC else (T.SG[:, 256 * (e - 1) + a:256 * (e - 1) + b], "SG%d_%d" % (e, h))
         zk = ["zC%d" % i for i in range(NP) if chunk(PCS[i][0]) == h]
-        if h == HC and MCV == "v":
-            V(lambda q: q.tensor_scalar(mask, z[:, 0:m], 8.5 * BIG, None, A.is_gt), r=zk, w=[mk], c=cv(m), bk=bk)
-        else:
-            S(lambda q: q.activation(mask, z[:, 0:m], AF.Sigmoid, bias=col(HR), scale=512.0 / BIG), r=zk + ["HR"], w=[mk], c=cv(m), bk=bk)
-        V(lambda q: q.tensor_tensor(d, d, mask, A.mult), r=[mk], w=["zD%d" % h], c=cv(m), bk=bk)
-        V(lambda q: q.tensor_tensor(TH(t)[:, a:b], d, TH(t)[:, a:b], A.add), r=["zD%d" % h], w=fk(t, [h]), c=cv(m), bk=bk)
+        VS(MCV[e - 1][h], lambda q: q.tensor_scalar(mask, z, 8.5 * BIG, None, A.is_lt),
+           lambda q: q.activation(mask, z, AF.Sigmoid, bias=col(HR), scale=-512.0 / BIG), zk + ["HR"], [mk], cv(m), bk)
+        V(lambda q: q.tensor_tensor(d, d, mask, A.mult), r=[mk], w=dk, c=cv(m), bk=bk)
+        V(lambda q: q.tensor_tensor(TH(t)[:, a:b], d, lots, A.add), r=dk + lk, w=fk(t, [h]), c=cv(m), bk=bk)
         if (t, e) != (2, 3) or h == HC:
             V(lambda q: q.tensor_scalar(TT(t)[:, a:b], TH(t)[:, a:b], 2048.0, None, A.add), r=fk(t, [h]), w=tk(t, [h]), c=cv(m, .5))
-        if e == 3 and h != HC:
+        if e == 3 and h != HC and PKS:
+            y = T["Z%d" % h][:, 384:384 + m]
+            PE([lambda q: q.matmul(y, T.IDH[:, 0:128], TH(t)[:, a:b], True, True)], ["IDH"] + fk(t, [h]), ["zP%d" % h], cmm(m), bk)
+            move("s", alots(t + 1, 1, a, b), y, ["zP%d" % h], ek(t + 1, 1, [h]) + (["AC%d" % t] if a == 0 else []), cv(m), bias=2048.0, bk=bk)
+        elif e == 3 and h != HC:
             V(lambda q: q.tensor_scalar(alots(t + 1, 1, a, b), TH(t)[:, a:b], 2048.0, None, A.add), r=fk(t, [h]),
               w=ek(t + 1, 1, [h]) + (["AC%d" % t] if a == 0 else []), c=cv(m))
+        elif e == 3:
+            V(lambda q: q.tensor_scalar(T.CF[:], TH(t)[:, a:b], 2048.0, -SQ, A.add, A.mult), r=fk(t, [h]), w=["CF"])
+
+    zq = T["Z%d" % HC][:, 384:400]
 
     def gm(t, i):
         a, b = PCS[i]
         x, y = 16 * a, 16 * b
         lst = win(t).indirect(TT(t)[:, a:b])
         r, w, c = wkey(t) + tk(t, [chunk(a)]), ["XM%d" % i], cgat(y - x)
-        if MR[t][i - 1] == "v":
-            V(lambda q: q.tensor_copy(T.XM[:, x:y], lst), r=r, w=w, c=c)
-        else:
-            S(lambda q: q.activation(T.XM[:, x:y], lst, AF.Copy), r=r, w=w, c=c)
+        move(MR[t][i - 1], T.XM[:, x:y], lst, r, w, c)
         V(lambda q: q.tensor_tensor_scan(T.SM[:, x:y], T.MK[:, 0:y - x], T.XM[:, x:y], 0.0, A.mult, A.max),
           r=["MK", "XM%d" % i], w=["SM%d" % i], c=cv((y - x) // 2))
+        if QC:
+            ks = range(a // 16, b // 16)
+            PE([lambda q, k=k: q.matmul(zq, T.SELW[:, 128 * k:128 * k + 128], T.SM[:, 256 * k + 15:256 * k + 256:16], k == 0, k == 15) for k in ks],
+               ["SM%d" % i, "SELW0", "SELW1"], ["zQ%d" % i], cmm(16, len(ks)), ["bZ%d" % HC])
+
+    def tclaim(t):
+        x, lots, lk = slice(256, LW), alots(t + 1, 1, 256, LW), ek(t + 1, 1, [HC])
+        move("s", T.dE[:], lots, lk, ["dE"], cv(1), 33.0, 2464.0 * (t + 1))
+        V(lambda q: q.tensor_copy(T.kI[:, 0:16], zq), r=["zQ%d" % i for i in range(1, NP)], w=["kI"], bk=["bZ%d" % HC])
+        V(lambda q: q.tensor_scalar(T.qI[:, x], T.kI[:, 0:16], 2047, None, A.bitwise_and), r=["kI"], w=["qIc"])
+        V(lambda q: q.tensor_tensor(T.qF[:, x], T.qI[:, x], lots, A.mult), r=["qIc"] + lk, w=["qFc"])
+        V(lambda q: q.tensor_tensor(T.qI[:, x], T.qF[:, x], T.dE[:], A.add), r=["qFc", "dE"], w=["qIc"])
+        V(lambda q: q.tensor_scalar(T.TI[:, x], T.qI[:, x], 5, 4095, A.logical_shift_right, A.bitwise_and), r=["qIc", "TI"], w=["TIc"])
+        V(lambda q: q.tensor_copy(TT(t + 1)[:, x], T.TI[:, x]), r=["TIc"], w=tk(t + 1, [HC]))
+        V(lambda q: q.tensor_scalar(TH(t + 1)[:, x], T.TI[:, x], -2048.0, None, A.add), r=["TIc"], w=fk(t + 1, [HC]))
 
     def tnew(t, hs):
         a, b = CH[hs[0]][0], CH[hs[-1]][1]
@@ -596,8 +713,8 @@ def rank_program(g, core, T, topo):
         PE(sums(T.ZM, True), sk, ["zU"], pc, ["bM"])
         PE([lambda q: q.matmul(T.ZR[:, a:b], T.cB[0:33, 128:256], T.ones[0:33, 0:m], True, False)] + sums(T.ZR, False),
            sk + ["cB", "ones"], ["zR"], pc, ["bR"])
-        S(lambda q: q.activation(T.kf[:, a:b], T.ZM[:, a:b], AF.Copy, bias=191.5 + 1.0 / 2048, scale=1.0 / 2048), r=["zU"], w=["kf" + nm], c=cv(m), bk=["bM"])
-        PE([lambda q: q.matmul(T.ZR[:, a:b], T.IDB[:, 256:384], T.kf[:, a:b], False, True)], ["ID2", "kf" + nm], ["zR"], cmm(m), ["bR"])
+        move("s", T.kf[:, a:b], T.ZM[:, a:b], ["zU"], ["kf" + nm], cv(m), 1.0 / 2048, 191.5 + 1.0 / 2048, ["bM"])
+        PE([lambda q: q.matmul(T.ZR[:, a:b], T.IDB[:, 0:128], T.kf[:, a:b], False, True)], ["ID2", "kf" + nm], ["zR"], cmm(m), ["bR"])
         V(lambda q: q.tensor_tensor(T.qF[:, a:b], T.ZR[:, a:b], alots(t + 1, 1, a, b), A.mult), r=["zR"] + ek(t + 1, 1, hs), w=["qF" + nm], c=cv(m), bk=["bR"])
         V(lambda q: q.tensor_scalar(T.qI[:, a:b], T.qF[:, a:b], 2464.0 * (t + 1), None, A.add), r=["qF" + nm], w=["qI" + nm], c=cv(m))
         V(lambda q: q.tensor_scalar(T.TI[:, a:b], T.qI[:, a:b], 5, 4095, A.logical_shift_right, A.bitwise_and),
@@ -606,24 +723,57 @@ def rank_program(g, core, T, topo):
         V(lambda q: q.tensor_scalar(TH(t + 1)[:, a:b], TT(t + 1)[:, a:b], -2048.0, None, A.add), r=tk(t + 1, hs), w=fk(t + 1, hs), c=cv(m, .5))
 
     def bind(t):
-        PE([lambda q: q.matmul(T.ZB[:], T.cB[0:1, 0:128], T.ones[0:1, 0:48], True, False)] +
-           [lambda q, k=k: q.matmul(T.ZB[:], T.SELK[:, 128 * k:128 * k + 128], T.SG[:, k:768:16], False, k == 15) for k in range(16)],
-           ["SG%d_%d" % (e, h) for e in (1, 2, 3) for h in HS] + SELK + ["cB", "ones"], ["zB"], cmm(48, 17), ["bB"])
+        zb, BB = (T.ZM[:, 400:448], "bM") if t == 2 and FREE else (T.ZX[:, 0:48], "bX")
+        shift = [lambda q: q.matmul(zb, T.cB[0:1, 0:128], T.ones[0:1, 0:48], True, False)]
+        if t == 2 and FREE:
+            a = CH[HC - 1][0]
+            for e in range(3):
+                PE(shift[e:] + [lambda q, k=k, e=e: q.matmul(zb[:, 16 * e:16 * e + a // 16], T.SELK[:, 128 * k:128 * k + 128],
+                                                             T.SG[:, 256 * e + k:256 * e + a:16], False, k == 15 and e == 2) for k in range(16)],
+                   ["SG%d_%d" % (e + 1, h) for h in HS[:-1]] + SELK + ["cB", "ones"], ["zB"], cmm(16, 17), [BB])
+        else:
+            PE(shift + [lambda q, k=k: q.matmul(zb, T.SELK[:, 128 * k:128 * k + 128], T.SG[:, k:768:16], False, k == 15) for k in range(16)],
+               ["SG%d_%d" % (e, h) for e in (1, 2, 3) for h in HS] + SELK + ["cB", "ones"], ["zB"], cmm(48, 17), [BB])
         c = 16 if t == 2 else 32
         ds = range(c // 16)
         for d in ds:
-            V(lambda q, d=d: q.tensor_tensor(KM[:, 0:3, 16 * d:16 * d + 16], T.ZB[:], KY[:, :, 16 * d:16 * d + 16], A.min),
-              r=["zB"] + ["KY%d" % e for e in range(3)], w=["KM_%d" % d], bk=["bB"])
-        V(lambda q: q.tensor_tensor(T.k1[:, :, 0:c], KM[:, 0:2, 0:c], KM[:, 2:4, 0:c], A.max), r=["KM3"] + ["KM_%d" % d for d in ds], w=["k1"], c=cv(4 * c))
-        V(lambda q: q.tensor_tensor(T.kI[:, 0:c], T.k1[:, 0, 0:c], T.k1[:, 1, 0:c], A.max), r=["k1"], w=["kI"])
+            V(lambda q, d=d: q.tensor_tensor(KM[:, 0:3, 16 * d:16 * d + 16], zb, KY[:, :, 16 * d:16 * d + 16], A.max),
+              r=["zB"] + ["KY%d" % e for e in range(3)], w=["KM_%d" % d], bk=[BB])
+        V(lambda q: q.tensor_tensor(T.k1[:, :, 0:c], KM[:, 0:2, 0:c], KM[:, 2:4, 0:c], A.min), r=["KM3"] + ["KM_%d" % d for d in ds], w=["k1"], c=cv(4 * c))
+        V(lambda q: q.tensor_tensor(T.kI[:, 0:c], T.k1[:, 0, 0:c], T.k1[:, 1, 0:c], A.min), r=["k1"], w=["kI"])
         V(lambda q: q.tensor_scalar(T.kJ[:, 0:c], T.kI[:, 0:c], 4095, None, A.bitwise_and), r=["kI"], w=["kJ"])
-        V(lambda q: q.tensor_copy(T.LU[:, 16:16 + c], T.kJ[:, 0:c]), r=["kJ"], w=["LU1", "LU2"])
+        V(lambda q: q.tensor_scalar(T.LU[:, 16:16 + c], T.kJ[:, 0:c], -1.0, 4095.0, A.mult, A.add), r=["kJ"], w=["LU1", "LU2"])
         if t < 2:
-            V(lambda q: q.tensor_copy(KS[:, 16:48], T.kJ[:]), r=["kJ"], w=["KS1", "KS2"])
+            V(lambda q: q.tensor_scalar(KS[:, 16:48], T.kJ[:], -1.0, 4095.0, A.mult, A.add), r=["kJ"], w=["KS1", "KS2"])
 
     def outv(t):
-        S(lambda q: q.activation(T.YV[:, 256 * t:256 * t + 256], T.IDW[:].indirect(T.LU[:, 16:32]), AF.Copy), r=["IDW", "LU1"], w=["YV%d" % t], c=cgat(256))
-        dma("y", [(T.yv[:, 256 * t:256 * t + 256], T.YV[0:128:16, 256 * t:256 * t + 256])], ["YV%d" % t], ["yv%d" % t], 16, 512)
+        x = slice(256 * t, 256 * t + (CH[HC - 1][0] if t == 2 and FREE else 256))
+        n = (x.stop - x.start) // 16
+        move("s", T.YV[:, x], T.IDW[:].indirect(T.LU[:, 16:16 + n]), ["IDW", "LU1"], ["YV%d" % t], cgat(16 * n))
+        dma("y", [(T.yv[:, x], T.YV[0:128:16, x])], ["YV%d" % t], ["yv%d" % t], 16, 512)
+
+    def keys_free():
+        a, b = CH[HC - 1]
+        m = b - a
+        move("s", T.KF[:, 0:m], T.IX[:, a:b], ["IX"], ["KF0"], cv(m), -1.0, -4096.0 - 1281)
+        for e, d, x in ((1, 1, -8193.0), (2, 2, -12289.0), (3, 2, -1.0)):
+            move("s", (T.KG if e == 3 else T.KF)[:, m * e:m * e + m], T.IDW[:].indirect(T.LU[:, 16 * d + a // 16:16 * d + b // 16]),
+                 ["IDW", "LU%d" % d], ["KF%d" % e], cgat(m), -1.0, x)
+
+    def bind_free():
+        h = HC - 1
+        a, b = CH[h]
+        m = b - a
+        z = T.ZR[:, 0:3 * m]
+        PE([lambda q: q.matmul(z, T.cB[0:1, 0:128], T.ones[0:1, 0:3 * m], True, False)] +
+           [lambda q, e=e: q.matmul(z[:, m * e:m * e + m], T.BE[:], T.SG[:, 256 * e + a:256 * e + b], False, e == 2) for e in range(3)],
+           ["SG%d_%d" % (e, h) for e in (1, 2, 3)] + ["BE", "cB", "ones"], ["zR"], cmm(m, 6), ["bR"])
+        V(lambda q: q.tensor_tensor(T.KG[:, 0:3 * m], z, T.KF[:, 0:3 * m], A.max), r=["zR", "KF0", "KF1", "KF2"], w=["KG"], c=cv(3 * m), bk=["bR"])
+        V(lambda q: q.tensor_tensor(T.KF[:, 0:2 * m], T.KG[:, 0:2 * m], T.KG[:, 2 * m:4 * m], A.min), r=["KG", "KF3"], w=["KF0", "KF1"], c=cv(4 * m))
+        V(lambda q: q.tensor_tensor(T.qI[:, 0:m], T.KF[:, 0:m], T.KF[:, m:2 * m], A.min), r=["KF0", "KF1"], w=["qIf"] + ["qI%d" % x for x in HA], c=cv(2 * m))
+        V(lambda q: q.tensor_scalar(T.TI[:, 0:m], T.qI[:, 0:m], 4095, None, A.bitwise_and), r=["qIf"], w=["TIf"] + ["TI%d" % x for x in HA], c=cv(m))
+        V(lambda q: q.tensor_scalar(T.YV[:, 512 + a:512 + b], T.TI[:, 0:m], -1.0, 4095.0, A.mult, A.add), r=["TIf"], w=["YVf"], c=cv(m))
+        dma("y", [(T.yv[:, 512 + a:512 + b], T.YV[0:128:16, 512 + a:512 + b])], ["YVf"], ["yvf"], 8, 4 * m)
 
     def outh(t, hs):
         a, b = CH[hs[0]][0], CH[hs[-1]][1]
@@ -631,19 +781,17 @@ def rank_program(g, core, T, topo):
 
     def dedupe(t):
         cl, ck = TT(t)[:, 256:LW], tk(t, [HC])
-        S(lambda q: q.activation(T.RB[:], T.IDW[:].indirect(cl), AF.Copy, scale=-SQ), r=["IDW"] + ck, w=["RB"], c=cgat(256))
-        S(lambda q: q.activation(T.SV[:, 256 * t:256 * t + 256], win(t).indirect(cl), AF.Copy), r=wkey(t) + ck, w=["SV%d" % t], c=cgat(256))
-        V(lambda q: q.tensor_scalar(T.CF[:], TH(t)[:, 256:LW], 2048.0, -SQ, A.add, A.mult), r=fk(t, [HC]), w=["CF"])
+        move("s", T.RB[:], T.IDW[:].indirect(cl), ["IDW"] + ck, ["RB"], cgat(256), scale=-SQ)
+        move("s", T.SV[:, 256 * t:256 * t + 256], win(t).indirect(cl), wkey(t) + ck, ["SV%d" % t], cgat(256))
         for c in range(16):
-            if c in SDUP:
-                S(lambda q, c=c: q.activation(T.EQ[:, seg[c]:seg[c + 1]], T.RB[:, 16 * c:256], AF.Square, bias=T.CF[:, c:c + 1], scale=-1.0),
-                  r=["RB", "CF"], w=["EQ%d" % c], c=cv(256 - 16 * c))
-            else:
-                V(lambda q, c=c: q.tensor_scalar(T.EQ[:, seg[c]:seg[c + 1]], T.RB[:, 16 * c:256], T.CF[:, c:c + 1], SQ * SQ, A.not_equal, A.mult),
-                  r=["RB", "CF"], w=["EQ%d" % c], c=cv(256 - 16 * c))
-        V(lambda q: q.tensor_tensor_scan(T.SC[:], T.EM[:], T.EQ[:], 1.0e16, A.max, A.min),
-          r=["EM%d" % c for c in range(16)] + ["EQ%d" % c for c in range(16)], w=["SC"], c=cv(NE, .5))
-        V(lambda q: q.tensor_tensor(T.dE[:], T.SC[:].indirect(T.E16[:, 0:1]), T.DJ[:], A.subtract), r=["SC", "E16", "DJ"], w=["dE"], c=cgat(16))
+            VS("s" if c < SDUP else "v",
+               lambda q, c=c: q.tensor_scalar(T.EQ[:, seg[c]:seg[c + 1]], T.RB[:, 16 * c:256], T.CF[:, c:c + 1], SQ * SQ, A.not_equal, A.mult),
+               lambda q, c=c: q.activation(T.EQ[:, seg[c]:seg[c + 1]], T.RB[:, 16 * c:256], AF.Square, bias=T.CF[:, c:c + 1], scale=-1.0),
+               ["RB", "CF"], ["EQ%d" % c], cv(256 - 16 * c))
+        for x, y in zip(SP, SP[1:]):
+            V(lambda q, x=x, y=y: q.tensor_tensor_scan(T.SC[:, seg[x]:seg[y]], T.EM[:, seg[x]:seg[y]], T.EQ[:, seg[x]:seg[y]], 1.0e16, A.max, A.min),
+              r=["E%s%d" % (k, c) for k in "MQ" for c in range(x, y)], w=["SC%d" % x], c=cv(seg[y] - seg[x], .5))
+        V(lambda q: q.tensor_tensor(T.dE[:], T.SC[:].indirect(T.E16[:, 0:1]), T.DJ[:], A.subtract), r=["SC%d" % x for x in SP[:-1]] + ["E16", "DJ"], w=["dE"], c=cgat(16))
         V(lambda q: q.tensor_tensor(T.dF[:], T.dE[:], T.CF[:], A.min), r=["dE", "CF"], w=["dF"])
         V(lambda q: q.tensor_scalar(T.SL[:, 16 * t:16 * t + 16], T.dF[:], -1.0 / SQ, None, A.mult), r=["dF"], w=["SL%d" % t])
 
@@ -670,29 +818,46 @@ def rank_program(g, core, T, topo):
         L = lambda a, b: T.LL[:, 64 * t + 16 * a:64 * t + 16 * b]
         lk = "gotSL%d" % t
         cols = lambda i: slice(256 * i, 256 * i + 256)
-        for i in range(3):
-            S(lambda q, i=i: q.activation(T.sv[:, cols(i)], T.LV[:, 768 * t + 256 * i:768 * t + 256 * i + 256], AF.Copy, scale=col(INC)),
-              r=["gotSV%d" % t, "INC"], w=["sv%d" % i], c=cv(256))
+        for i in range(2 if UF[t][2] == "p" else 3):
+            move("s", T.sv[:, cols(i)], T.LV[:, 768 * t + 256 * i:768 * t + 256 * i + 256], ["gotSV%d" % t, "INC"], ["sv%d" % i], cv(256), scale=col(INC))
         fr = [wk, "dump%d" % t, lk] + ["cp%d_%d" % (t, i) for i in range(NF)]
         for i in range(2):
-            S(lambda q, i=i: q.activation(T.g1[:, cols(i)], F[:].indirect(L(i, i + 1)), AF.Copy), r=fr, w=["g1_%d" % i], c=cgat(256))
-            V(lambda q, i=i: q.tensor_tensor(F[:].indirect(L(i, i + 1)), T.g1[:, cols(i)], T.sv[:, cols(i)], A.add), r=["g1_%d" % i, "sv%d" % i, lk], w=[wk], c=csca(256))
-        V(lambda q: q.tensor_tensor(T.t1[:], F[:].indirect(L(2, 3)), T.sv[:, 512:768], A.add), r=fr + ["sv2"], w=["t1"], c=cgat(256))
+            if UF[t][i] == "g":
+                move("s", T.g1[:, cols(i)], F[:].indirect(L(i, i + 1)), fr, ["g1_%d" % i], cgat(256))
+                V(lambda q, i=i: q.tensor_tensor(F[:].indirect(L(i, i + 1)), T.g1[:, cols(i)], T.sv[:, cols(i)], A.add), r=["g1_%d" % i, "sv%d" % i, lk], w=[wk], c=csca(256))
+            else:
+                V(lambda q, i=i: q.tensor_tensor(T.g1[:, cols(i)], F[:].indirect(L(i, i + 1)), T.sv[:, cols(i)], A.add), r=fr + ["sv%d" % i], w=["g1_%d" % i], c=cgat(256))
+                V(lambda q, i=i: q.tensor_copy(F[:].indirect(L(i, i + 1)), T.g1[:, cols(i)]), r=["g1_%d" % i, lk], w=[wk], c=csca(256))
+        zt = T["Z%d" % HC][:, 0:256]
+        if UF[t][2] == "p":
+            move("s", T.t1[:], F[:].indirect(L(2, 3)), fr, ["g1_2"], cgat(256))
+            PE([lambda q: q.matmul(zt, T.IDI[:], T.LV[:, 768 * t + 512:768 * t + 768], True, False),
+                lambda q: q.matmul(zt, T.IDN[:, 0:128], T.t1[:], False, True)], ["IDI", "IDN", "gotSV%d" % t, "g1_2"], ["t1"], cmm(256, 5), ["bZ%d" % HC])
+            S(lambda q: q.activation(T.r1[:, cols(2)], zt, AF.Relu, bias=col(TOP), scale=-1.0), r=["t1", "TOP"], w=["r12"], c=cv(256), bk=["bZ%d" % HC])
+        else:
+            V(lambda q: q.tensor_tensor(T.t1[:], F[:].indirect(L(2, 3)), T.sv[:, 512:768], A.add), r=fr + ["sv2"], w=["t1", "g1_2"], c=cgat(256))
 
         for i in range(3):
-            src, r, c = (T.t1[:], ["t1"], cv(256)) if i == 2 else (F[:].indirect(L(i, i + 1)), [wk, lk], cgat(256))
+            src, r, c = (T.t1[:], ["t1"], cv(256)) if i == 2 else (F[:].indirect(L(i, i + 1)), [wk, lk], cgat(256)) \
+                if UF[t][i] == "g" else (T.g1[:, cols(i)], ["g1_%d" % i], cv(256))
             if FLS[t][i] == "v":
                 V(lambda q, i=i, src=src: q.tensor_scalar(T.i1[:, cols(i)], src, -0.4921875, 255.0, A.add, A.min), r=r, w=["i1%d" % i], c=c)
             else:
-                S(lambda q, i=i, src=src: q.activation(T.r1[:, cols(i)], src, AF.Relu, bias=col(TOP), scale=-1.0), r=r + ["TOP"], w=["r1%d" % i], c=c)
+                if UF[t][i] != "p":
+                    S(lambda q, i=i, src=src: q.activation(T.r1[:, cols(i)], src, AF.Relu, bias=col(TOP), scale=-1.0), r=r + ["TOP"], w=["r1%d" % i], c=c)
                 S(lambda q, i=i: q.activation(T.r2[:, cols(i)], T.r1[:, cols(i)], AF.Copy, bias=MAGIC + 255, scale=-1.0), r=["r1%d" % i], w=["i1%d" % i], c=cv(256))
+                if t == 2 and LAST:
+                    S(lambda q, i=i: q.activation(T.r2[:, cols(i)], T.r2[:, cols(i)], AF.Copy, bias=-MAGIC), w=["i1%d" % i], c=cv(256))
         for i in range(3):
-            if FLS[t][i] == "v":
+            if t == 2 and LAST:
+                V(lambda q, i=i: q.tensor_copy(T.p0[:].indirect(L(i, i + 1)), (T.i1 if FLS[t][i] == "v" else T.r2)[:, cols(i)]),
+                  r=["i1%d" % i, lk, "dump3"] + ["cp3_%d" % x for x in range(NF)], w=["win4"], c=csca(256))
+            elif FLS[t][i] == "v":
                 V(lambda q, i=i: q.tensor_copy(F[:].indirect(L(i, i + 1)), T.i1[:, cols(i)]), r=["i1%d" % i, lk], w=[wk], c=csca(256))
             else:
                 V(lambda q, i=i: q.tensor_scalar(F[:].indirect(L(i, i + 1)), T.r2[:, cols(i)], 1.0, -MAGIC, A.mult, A.add), r=["i1%d" % i, lk], w=[wk], c=csca(256))
 
-    hot[0] = HOT
+    hot[0] = HOT[0]
     conv(1)
     parents(1)
     first(2)
@@ -706,39 +871,59 @@ def rank_program(g, core, T, topo):
             w = 4096 // NF
             G(lambda q, t=t, i=i, w=w: q.affine_select(T["F%d" % (t + 1)][:, w * i:w * i + w], win(t)[:, w * i:w * i + w], [[0, w]], A.is_equal, 0.0, 0, 0),
               r=wkey(t), w=["cp%d_%d" % (t, i)], c=(0, 2 * w, 0, 0, 0, 0.17))
+        for i in range(NF if t == 2 and LAST else 0):
+            add("g", "c", [lambda q, i=i, w=w: q.affine_select(T.p0[:, w * i:w * i + w], T.F2[:, w * i:w * i + w], [[0, w]], A.is_equal, 0.0, 0, 0)],
+                wkey(2), ["cp3_%d" % i] + (wkey(0) if i == 0 else []), (0, 2 * w, 0, 0, 0, 0.17))
+            if i:
+                ops[-1]["order"].append(len(ops) - 2)
         if t < 2:
             parents(2)
             conv(3)
         keys(t)
+        if t == 2 and FREE:
+            keys_free()
         for e in (1, 2, 3):
-            for f, xs in ((gy, range(NP)), (diff, HA), (gx, range(NP)), (tops, HA)):
-                for x in xs:
-                    hot[0] = HOT if x == (0 if f in (gy, gx) else HC) else 0.0
-                    f(t, e, x)
-        hot[0] = HOT
+            for i in range(NP):
+                hot[0] = 0.0 if i else HOT[t]
+                gy(t, e, i)
+            for h in HA:
+                hot[0] = HOT[t] if h == HC else 0.0
+                diff(t, e, h)
+                for i in range(NP):
+                    if chunk(PCS[i][0]) == h:
+                        gx(t, e, i)
+                tops(t, e, h)
         dedupe(t)
         send(t)
         update(t)
         hot[0] = 0.0
-        if t == 2:
+        if t == 2 and LAST:
+            dma("y", [(T.yp[:], T.p0[:, 0:4096])], ["win4"], ["yp"], 128, 8192)
+        elif t == 2:
             dma("g", [(T.yp[:], T.F3[:, 0:4096])], ["win3"], ["yp"], 128, 8192)
         if t < 2:
             clist(t + 1, 1)
             for i in range(1, NP):
                 gm(t, i)
+            if QC:
+                tclaim(t)
             for hs in TG:
-                tnew(t, hs)
+                tnew(t, [h for h in hs if h != HC or not QC])
             outh(t, list(HS))
         else:
             for h in HS:
                 outh(t, [h])
+        hot[0] = HOT[t + 1] if t < 2 else 0.0
         bind(t)
-        outv(t)
+        if t == 2 and FREE:
+            bind_free()
         if t < 2:
             package(t + 1, 2)
             package(t + 1, 3)
             clist(t + 1, 2)
             clist(t + 1, 3)
+        hot[0] = 0.0
+        outv(t)
 
     order = plan(ops)
     total, snap, tok = {}, {}, {}
@@ -767,7 +952,8 @@ def rank_program(g, core, T, topo):
 
     for i in order:
         o = ops[i]
-        e, kind, body = o["e"], o["kind"], o["body"]
+        e, kind = PLAN["queues"][i], o["kind"]
+        body = o["both"][e] if o["both"] else o["body"]
         if kind == "n":
             total[body[0]] = body[1]
             tok[i] = body

@@ -5,39 +5,43 @@ from concourse.mybir import dt, AluOpType, AxisListType, ActivationFunctionType
 A = AluOpType
 AF = ActivationFunctionType
 LW = 272
-RT = ["v" * 18] * 2 + ["v" * 17 + "s"]
-FREE = False
-CH = [(0, 96), (96, 192), (192, 256), (256, 272)]
-PCS = [(256, 272), (0, 48), (48, 96), (96, 144), (144, 192), (192, 256)]
-YR = ["sv" + "s" * 16] + ["s" * 18] * 2
-MR = ["sssss"] * 2
-TG = [[0], [1], [2, 3]]
-NE = 2176
+CH = [[(256, 272), (0, 96), (96, 192), (192, 256)]] * 3
+XW = (64, 64, 48)
+YP = [[(256, 272), (0, 64), (64, 128), (128, 192), (192, 256)]] * 2 + \
+     [[(256, 272), (0, 48), (48, 96), (96, 144), (144, 192), (192, 256)]]
+MP = [(0, 64), (64, 128), (128, 192), (192, 256)]
+TG = [[(0, 96), (96, 192), (192, 272)]] * 2
+SR = [(2, 3, 48), (2, 3, 96)]
+NB = 2
+SP = (0, 3, 8)
+SCAN = True
+A16 = False
+NOWAIT = False
+YT = (0, 1)
+TAIL = True
+PKS = ()
+SEP = (2,)
+UCOPY = True
+FIRST = True
+OH = [(0, 96), (96, 256)]
 BIG = 32768.0
 SQ = 8192.0
-SDUP = 16
-LATE = (True, True, True)
-HOT = (0.0, 0.0, 0.0)
 XB = 1.2
 UF = ("ggt", "ggt", "ttt")
-EMD = 8
-WIDE = True
+FLS = ("sss", "sss", "ssv")
 PCALL = 0.010
 REACH = 0.35
-LOADS = ["VT", "pkJ", "win0", "TI", "pkI"]
-LEAN = 1.0
-QC = False
-PKS = False
-SLOPES = [1.0, 2.0, 3.0, 5.0, 8.0, 12.0, 20.0]
-LAST = True
-SP = (0, 3, 7, 16)
-SEED = 3
+LOADS = ["win0a", "pkA", "wtI", "VT", "win0", "pkC", "pkJ", "TI", "pkI", "incI"]
+LA = 96
+L0 = [(0, LA, ["pkA"]), (LA, 256, ["pkJ"]), (256, LW, ["pkC"])]
+LEAN = 10.0
+SLOPES = [3.0, 8.0, 20.0, 50.0]
+SEED = 4
+DUE = (9.0, 9.5, 100.0, 0.2)
 PA = 2048
-PG = 16
 NF = 8
-FLS = ("sss", "sss", "ssv")
-MCV = ("ssss",) * 3
 MAGIC = 1.5 * 2 ** 23
+SW = 576
 
 SCRATCH = {
     "p0": ("sbuf", [128, 4352], "bfloat16"),
@@ -51,62 +55,62 @@ SCRATCH = {
     "small": ("sbuf", [128, 8], "int32"),
     "slI": ("sbuf", [128, 4], "int32"),
     "sm": ("sbuf", [128, 32], "float32"),
-    "pI": ("sbuf", [128, 4], "int32"),
+    "pI": ("sbuf", [128, 8], "int32"),
     "row8": ("sbuf", [128, 8], "float32"),
     "B8": ("sbuf", [128, 8], "float32"),
     "one16": ("sbuf", [128, 16], "float32"),
     "SELK": ("sbuf", [128, 2048], "bfloat16"),
     "SELW": ("sbuf", [128, 2048], "bfloat16"),
-    "ones": ("sbuf", [128, LW], "bfloat16"),
-    "cB": ("sbuf", [128, 256], "bfloat16"),
+    "ones": ("sbuf", [128, 1024], "bfloat16"),
+    "cB": ("sbuf", [128, 384], "bfloat16"),
+    "IX": ("sbuf", [128, 128], "float32"),
     "IDN": ("sbuf", [128, 256], "float32"),
     "IDH": ("sbuf", [128, 256], "bfloat16"),
     "IDB": ("sbuf", [128, 256], "bfloat16"),
     "IXG": ("sbuf", [128, 128], "float32"),
-    "WT": ("sbuf", [128, 128], "bfloat16"),
     "IDI": ("sbuf", [128, 128], "bfloat16"),
-    "BE": ("sbuf", [128, 128], "bfloat16"),
-    "KF": ("sbuf", [128, 192], "float32"),
-    "KG": ("sbuf", [128, 256], "float32"),
+    "WT": ("sbuf", [128, 128], "bfloat16"),
     "TT0": ("sbuf", [128, LW], "uint16"),
     "TT1": ("sbuf", [128, LW], "uint16"),
-    "TH0": ("sbuf", [128, LW], "float16"),
-    "TH1": ("sbuf", [128, LW], "float16"),
+    "TH0": ("sbuf", [128, 2 * LW], "float16"),
+    "TH1": ("sbuf", [128, 2 * LW], "float16"),
     "TI": ("sbuf", [128, LW], "int32"),
-    "A16": ("sbuf", [128, 3 * LW], "uint16"),
+    "AL": ("sbuf", [128, 3 * LW], "uint16"),
     "AE": ("sbuf", [128, 2 * LW], "float32"),
+    "AH": ("sbuf", [128, 2 * LW], "float16"),
     "Y": ("sbuf", [128, 48 * LW], "bfloat16"),
     "C": ("sbuf", [128, 16 * LW], "bfloat16"),
-    "XS": ("sbuf", [128, 1024], "bfloat16"),
+    "XS": ("sbuf", [128, 1536], "bfloat16"),
     "XM": ("sbuf", [128, 4096], "bfloat16"),
     "SM": ("sbuf", [128, 4096], "bfloat16"),
-    "MI": ("sbuf", [128, 1024], "bfloat16"),
     "MK": ("sbuf", [128, 1024], "bfloat16"),
-    "SG": ("sbuf", [128, 768], "bfloat16"),
-    "MC": ("sbuf", [128, 16], "bfloat16"),
+    "SG": ("sbuf", [128, 3 * SW], "bfloat16"),
     "kf": ("sbuf", [128, LW], "bfloat16"),
+    "uF": ("sbuf", [128, LW], "float32"),
     "qF": ("sbuf", [128, LW], "float32"),
     "qI": ("sbuf", [128, LW], "int32"),
-    "KS": ("sbuf", [128, 64], "float32"),
-    "KY": ("sbuf", [128, 3, 32], "float32"),
-    "KM": ("sbuf", [128, 4, 32], "float32"),
-    "k1": ("sbuf", [128, 2, 32], "float32"),
-    "kI": ("sbuf", [128, 32], "int32"),
-    "kJ": ("sbuf", [128, 32], "int32"),
-    "LU": ("sbuf", [128, 48], "uint16"),
-    "i16": ("sbuf", [128, 16], "float32"),
-    "L1c": ("sbuf", [128, 16], "float32"),
+    "KS": ("sbuf", [128, 72], "float32"),
+    "KO": ("sbuf", [128, 36], "float32"),
+    "KM": ("sbuf", [128, 4, 36], "float32"),
+    "k1": ("sbuf", [128, 2, 36], "float32"),
+    "kI": ("sbuf", [128, 36], "int32"),
+    "kJ": ("sbuf", [128, 36], "int32"),
+    "LU": ("sbuf", [128, 54], "uint16"),
+    "i16": ("sbuf", [128, 32], "float32"),
+    "L1c": ("sbuf", [128, 32], "float32"),
     "VH": ("sbuf", [128, 256], "float16"),
     "VG": ("sbuf", [128, 256], "float16"),
     "YV": ("sbuf", [128, 768], "float32"),
+    "YW": ("sbuf", [128, 96], "float32"),
+    "KF": ("sbuf", [128, 384], "float32"),
+    "BE": ("sbuf", [128, 128], "bfloat16"),
     "CF": ("sbuf", [128, 16], "float32"),
     "IDW": ("sbuf", [128, 4096], "float32"),
     "RB": ("sbuf", [128, 256], "float32"),
-    "IX": ("sbuf", [128, 256], "float32"),
-    "QM": ("sbuf", [128, 256], "bfloat16"),
-    "EQ": ("sbuf", [128, NE], "bfloat16"),
-    "EM": ("sbuf", [128, NE], "bfloat16"),
-    "SC": ("sbuf", [128, NE], "bfloat16"),
+    "EI": ("sbuf", [128, 2176], "bfloat16"),
+    "EQ": ("sbuf", [128, 2176], "bfloat16"),
+    "EM": ("sbuf", [128, 2176], "bfloat16"),
+    "SC": ("sbuf", [128, 2176], "bfloat16"),
     "E16": ("sbuf", [128, 2], "uint16"),
     "DJ": ("sbuf", [128, 16], "float32"),
     "DJt": ("sbuf", [128, 16], "float32"),
@@ -117,8 +121,7 @@ SCRATCH = {
     "LV": ("sbuf", [128, 3 * 768], "bfloat16"),
     "LL": ("sbuf", [128, 3 * 64], "uint16"),
     "sv": ("sbuf", [128, 768], "float32"),
-    "g1": ("sbuf", [128, 512], "float32"),
-    "t1": ("sbuf", [128, 256], "float32"),
+    "g1": ("sbuf", [128, 768], "float32"),
     "i1": ("sbuf", [128, 768], "int32"),
     "r1": ("sbuf", [128, 768], "float32"),
     "r2": ("sbuf", [128, 768], "float32"),
@@ -126,7 +129,7 @@ SCRATCH = {
     "Z1": ("psum", [128, 512], "float32"),
     "Z2": ("psum", [128, 512], "float32"),
     "Z3": ("psum", [128, 512], "float32"),
-    "Z4": ("psum", [128, 512], "float32"),
+    "ZC": ("psum", [128, 512], "float32"),
     "ZX": ("psum", [128, 512], "float32"),
     "ZM": ("psum", [128, 512], "float32"),
     "ZR": ("psum", [128, 512], "float32"),
@@ -137,11 +140,14 @@ SEMAPHORES = ["cv", "cs", "cp", "cg", "lsem"] + ["arrS%s%d" % (x, t) for x in "V
 MODELS = [
     (0.02, 0.83e-3, 1.25e-3, 3.0e-3, 0.83e-3, 0.14, 2.0, 3.0, 0.035, 0.06e-3),
     (0.03, 0.87e-3, 1.02e-3, 1.9e-3, 0.87e-3, 0.16, 2.0, 3.0, 0.03, 0.05e-3),
-    (0.03, 1.10e-3, 1.70e-3, 4.2e-3, 1.10e-3, 0.15, 2.2, 3.5, 0.04, 0.08e-3),
-    (0.02, 0.92e-3, 1.60e-3, 1.9e-3, 0.92e-3, 0.20, 2.4, 2.5, 0.05, 0.04e-3),
-    (0.03, 1.20e-3, 1.90e-3, 5.0e-3, 1.20e-3, 0.18, 2.2, 4.0, 0.04, 0.07e-3),
+    (0.03, 1.10e-3, 1.35e-3, 5.2e-3, 0.90e-3, 0.15, 2.2, 3.5, 0.04, 0.08e-3),
+    (0.02, 1.00e-3, 1.95e-3, 2.2e-3, 0.92e-3, 0.22, 2.4, 2.5, 0.05, 0.04e-3),
+    (0.03, 1.20e-3, 2.10e-3, 5.0e-3, 1.10e-3, 0.20, 2.2, 4.0, 0.04, 0.07e-3),
 ]
-TRIES, MOVES, HEAT = 300, 60000, 0.004
+TRIES, STARTS, TURN, FLIP = 15, 1, True, 9.0
+STEPS = ((1000, 1),)
+BACK, FAR, WIDE, TOP, KEEP, JIT = 1500, 8, 40, 4, 20, 0.002
+ROUNDS, SPAN, SHORT, SHAKE, HEAT, HOME = 900, 60, 120, (8.0, 0.3, 1.0), 0.006, 0.3
 
 
 def cv(n, per=1.0):
@@ -164,6 +170,10 @@ def cfix(x):
     return (0, 0, 0, 0, 0, x)
 
 
+def cgp(n, fix=0.13):
+    return (0, 2 * n, 0, 0, 0, fix)
+
+
 def price_ops(ops, md):
     cost, dur, lat = [], [], []
     for o in ops:
@@ -179,11 +189,34 @@ def run_order(ops, order, pr, wake, why=None, old=None, at=0):
     free, last = dict.fromkeys("vspgyn", 0.0), dict.fromkeys("vspgyn", -1)
     dfree, dlast = 0.0, -1
     seen, gone = (old[1][:], old[2][:]) if old else ([0.0] * len(ops), [0.0] * len(ops))
-    for i in order[:at]:
-        free[ops[i]["e"]] = gone[i]
-        if dur[i]:
-            dfree = seen[i] - lat[i] - wake
-    for i in order[at:]:
+    if old:
+        todo = set("vspgyd")
+        for k in range(at - 1, -1, -1):
+            i = order[k]
+            e = ops[i]["e"]
+            if e in todo:
+                free[e] = gone[i]
+                todo.discard(e)
+            if dur[i] and "d" in todo:
+                dfree = seen[i] - lat[i] - wake
+                todo.discard("d")
+            if not todo:
+                break
+        wait = PLAN["wait"]
+        for i in order[at:]:
+            e, full = wait[i]
+            s = free[e]
+            for p in full:
+                if seen[p] > s:
+                    s = seen[p]
+            s += cost[i]
+            if e != "n":
+                free[e] = gone[i] = s
+                if dur[i]:
+                    s = dfree = (dfree if dfree > s else s) + dur[i]
+            seen[i] = s + lat[i] + wake
+        return max(seen), seen, gone
+    for i in order:
         e, full = ops[i]["wait"]
         s, w = free[e], -1
         for p in full:
@@ -267,6 +300,230 @@ def schedule(ops, pred, succ, prio, pr, wake, slope, back=False):
     return order, fin
 
 
+def refine(ops, order, eng, pred, succ, priced, ref, rng, steps, lo=0, hi=10 ** 6):
+    m, nm = len(ops), len(MODELS)
+    fp = [o["wait"][1] for o in ops]
+    fs = [[j for j, f in succ[i] if f] for i in range(m)]
+    ap = [[p for p, f in pred[i]] for i in range(m)]
+    aq = [[j for j, f in succ[i]] for i in range(m)]
+    eng = eng[:]
+    late = [[x + md[5] for x in pr[2]] for pr, md in zip(priced, MODELS)]
+    st = [[[0.0] * (m + 1) for _ in range(6)] for _ in MODELS]
+    prev, nxt, dprev, dnxt = ([m] * (m + 1) for _ in range(4))
+    isd = [x > 0 for x in priced[0][1]]
+
+    before, behind, past = {}, {}, [0.0] * nm
+
+    def times(order, a, b):
+        last = dict(before)
+        for i in order:
+            e = eng[i]
+            if e != "n":
+                p = prev[i] = last.get(e, m)
+                nxt[p] = last[e] = i
+            if isd[i]:
+                p = dprev[i] = last.get("d", m)
+                dnxt[p] = last["d"] = i
+        for e, i in last.items():
+            (dnxt if e == "d" else nxt)[i] = behind.get(e, m)
+        ahead, back = order[a:], order[b::-1]
+        cur = []
+        for k in range(nm):
+            cost, dur, lt = priced[k][0], priced[k][1], late[k]
+            end, seen, dend, q, after, qd = st[k]
+            for i in ahead:
+                s = end[prev[i]]
+                for p in fp[i]:
+                    if seen[p] > s:
+                        s = seen[p]
+                s = end[i] = s + cost[i]
+                if isd[i]:
+                    d = dend[dprev[i]]
+                    s = dend[i] = (d if d > s else s) + dur[i]
+                seen[i] = s + lt[i]
+            for i in back:
+                s = 0.0
+                for j in fs[i]:
+                    if q[j] > s:
+                        s = q[j]
+                s += lt[i]
+                if isd[i]:
+                    d = qd[dnxt[i]]
+                    s = qd[i] = (d if d > s else s) + dur[i]
+                after[i] = s
+                d = q[nxt[i]]
+                q[i] = (d if d > s else s) + cost[i]
+            cur.append(max(past[k], max([end[i] - cost[i] + q[i] for i in order]), max([dend[i] - dur[i] + qd[i] for i in dmas], default=0.0)))
+        return cur
+
+    def guess(k, seq, a, b, old):
+        cost, lt = priced[k][0], late[k]
+        end, seen, dend, q, after, qd = st[k]
+        t, new, heads = end[a], {}, []
+        for w in seq:
+            for p in fp[w]:
+                x = new.get(p) or seen[p]
+                if x > t:
+                    t = x
+            heads.append(t)
+            t += cost[w]
+            if not isd[w]:
+                new[w] = t + lt[w]
+        t, new, best = q[b], {}, 0.0
+        for w in seq[::-1]:
+            x = after[w]
+            for j in fs[w]:
+                if j in new and new[j] + lt[w] > x:
+                    x = new[j] + lt[w]
+            t = new[w] = (x if x > t else t) + cost[w]
+            x = heads.pop() + t
+            if x > best:
+                best = x
+        if best < cur[k] and max(end[w] - cost[w] + q[w] for w in old) < cur[k] - 1e-6:
+            return cur[k]
+        return best
+
+    def sort(order):
+        cost, end, seen = priced[0][0], st[0][0], st[0][1]
+        place = {x: n for n, x in enumerate(order)}
+        return sorted(order, key=lambda x: (end[x] - cost[x] + 1e-9 * place[x]))
+    dmas = []
+    times(order, 0, m - 1)
+    head, order, tail = order[:lo], order[lo:hi], order[hi:]
+    inside = set(order)
+    for part, ends in ((head, before), (tail[::-1], behind)):
+        for i in part:
+            ends[eng[i]] = i
+            if isd[i]:
+                ends["d"] = i
+        ends.pop("n", 0)
+    later = set(tail)
+    past[:] = [max([x[1][i] + x[3][j] for i in head for j in fs[i] if j in later], default=0.0) for x in st]
+    dmas = [i for i in order if isd[i]]
+    top = len(order) - 1
+    best, tabu, since = (1e30, order, eng[:]), {}, 0
+    for it in range(steps + 1):
+        if it % 100 == 0:
+            if since > BACK:
+                order, since = best[1], 0
+                eng[:] = best[2]
+                times(order, 0, top)
+            order = sort(order)
+            for i in range(m):
+                ops[i]["e"] = eng[i]
+            cur = times(order, 0, top)
+        sc = sum(a / b for a, b in zip(cur, ref))
+        since += 1
+        if sc < best[0] - 1e-9:
+            best, since = (sc, order, eng[:]), 0
+        k = it % nm
+        cost, dur = priced[k][0:2]
+        end, seen, dend, q, after, qd = st[k]
+        x = cur[k] - 1e-7
+        i = next((i for i in order[::-1] if end[i] - cost[i] + q[i] > x or isd[i] and dend[i] - dur[i] + qd[i] > x), m)
+        if i == m:
+            continue
+        rows, row, cand = [], [i], []
+        while True:
+            if isd[i] and dend[dprev[i]] > end[i]:
+                j = dprev[i]
+                while dend[dprev[j]] > end[j]:
+                    j = dprev[j]
+                if j not in inside:
+                    break
+                cand.append(("d", i, dprev[i]))
+                i = j
+                rows.append(row)
+                row = [i]
+                continue
+            s, j = end[prev[i]], prev[i]
+            for p in fp[i]:
+                if seen[p] > s:
+                    s, j = seen[p], p
+            if j not in inside:
+                break
+            if j != prev[i] or s > end[j]:
+                rows.append(row)
+                row = []
+            row.append(j)
+            i = j
+        rows.append(row)
+        for row in rows:
+            n = len(row)
+            for x in range(min(n - 1, FAR)):
+                cand += [("a", row[n - 2 - x], row[-1]), ("b", row[0], row[x + 1]), ("b", row[n - 2 - x], row[-1]), ("a", row[0], row[x + 1])][0:4 if x else 2]
+            if n > 1:
+                cand += [("f", w, w) for w in row if ops[w]["both"] and priced[0][0][w] < FLIP]
+        pick = []
+        for c in (cand if len(cand) <= WIDE else [cand[x] for x in rng.choice(len(cand), WIDE, replace=False)]):
+            kind, v, u = c
+            if kind == "d":
+                pick.append((cur[k], c, None))
+                continue
+            if kind == "f":
+                e = "s" if eng[v] == "v" else "v"
+                x = order.index(v) - 1
+                while x >= 0 and eng[order[x]] != e:
+                    x -= 1
+                a = order[x] if x >= 0 else before.get(e, m)
+                arg = ([v], a, nxt[a] if a < m else next(w for w in order if eng[w] == e), [v])
+            else:
+                old, w = [u], u
+                while w != v:
+                    w = nxt[w]
+                    old.append(w)
+                if kind == "a":
+                    if any(p in old or end[p] - cost[p] >= end[u] for p in ap[v]):
+                        continue
+                    arg = ([v] + old[:-1], prev[u], nxt[v], old)
+                else:
+                    if any(j in old or end[j] <= end[v] - cost[v] for j in aq[u]):
+                        continue
+                    arg = (old[1:] + [u], prev[u], nxt[v], old)
+            pick.append((guess(k, *arg), c, arg))
+        pick.sort(key=lambda x: x[0])
+        good = []
+        for one, c, arg in pick[0:TOP]:
+            s2 = sum((one if x == k else guess(x, *arg) if arg else cur[x]) / ref[x] for x in range(nm)) + JIT * rng.random()
+            kind, v, u = c
+            if kind == "f":
+                made = [(v, v)]
+                s2 += LEAN * priced[0][0][v] / ref[0] * (1 if eng[v] == "s" else -1)
+            else:
+                made = [(v, u)] if kind == "d" else [(v, w) for w in arg[3][:-1]] if kind == "a" else [(w, u) for w in arg[3][1:]]
+            if s2 < best[0] or not any(tabu.get(x, -1) >= it for x in made):
+                good.append((s2, c, made))
+        good.sort(key=lambda x: x[0])
+        for s2, (kind, v, u), made in good:
+            new = order if kind == "f" else moved(ops, order, v, u, succ if kind == "b" else pred, kind != "b")
+            if new is None:
+                continue
+            if kind == "f":
+                eng[v] = ops[v]["e"] = "s" if eng[v] == "v" else "v"
+                a, b = 0, top
+            else:
+                a, b = order.index(u), order.index(v)
+            order = new
+            for x, y in made:
+                tabu[y, x] = it + KEEP + int(rng.integers(KEEP))
+            cur = times(order, a, b)
+            break
+    return best[0], head + best[1] + tail, best[2]
+
+
+def shaken(ops, order, lo, hi, pred, rng):
+    part = order[lo:hi]
+    shift = {x: rng.normal(0.0, SHAKE[0]) * (rng.random() < SHAKE[1]) for x in sorted({ops[i]["tag"] for i in part})}
+    key = {}
+    for n, i in enumerate(part):
+        key[i] = n + shift[ops[i]["tag"]] + rng.normal(0.0, SHAKE[2])
+    for i in sorted(part):
+        for p, f in pred[i]:
+            if p in key and key[p] >= key[i]:
+                key[i] = key[p] + 1e-3
+    return order[:lo] + sorted(part, key=key.get) + order[hi:]
+
+
 PLAN = {}
 
 
@@ -282,7 +539,7 @@ def plan(ops):
             near |= 1 << p
         above.append(far | near)
         o["wait"] = (o["e"], [p for p in o["full"] if not far >> p & 1])
-    pred = [[(p, True) for p in o["full"]] + [(p, False) for p in o["order"]] for o in ops]
+    pred = [[(p, True) for p in o["wait"][1]] + [(p, False) for p in o["order"]] for o in ops]
     succ = [[] for _ in ops]
     for i in range(m):
         for p, f in pred[i]:
@@ -297,13 +554,19 @@ def plan(ops):
         for j, f in succ[i]:
             b = max(b, base[j] + (dur[i] + lat[i] + wake if f else 0.0))
         base[i] = b + cost[i] + (0.0 if succ[i] else dur[i] + lat[i])
+    if DUE:
+        for i in range(m - 1, -1, -1):
+            b = -DUE[2]
+            for j, f in succ[i]:
+                b = max(b, base[j] + (dur[i] + lat[i] + wake + DUE[3] if f else 0.0))
+            base[i] = max(b + cost[i] + (0.0 if succ[i] else dur[i] + lat[i]), -ops[i].get("due", 1e9))
     rng = np.random.default_rng(SEED)
-    ref, best = None, None
-    for k in range(TRIES):
+    ref, best, field, first = None, None, [], [o["e"] for o in ops]
+    for k in range(TRIES * STARTS):
         slope = float(rng.choice(SLOPES))
-        if k == 0:
-            prio = np.array(base)
-        elif k % 10 == 1:
+        if best is None:
+            prio = np.array(base) + rng.normal(0.0, 0.5, m) * (k > 0)
+        elif k % TRIES % 10 == 1 and TURN:
             prio = np.array(schedule(ops, succ, pred, list(best[4]), priced[0], wake, slope, True)[1])
         else:
             prio = best[2] + rng.normal(0.0, (8.0, 2.0, 0.5)[k % 3], m) * (rng.random(m) < (0.1, 0.03, 0.01, 0.005)[k % 4])
@@ -315,57 +578,40 @@ def plan(ops):
         sc = sum(a / b for a, b in zip(ts, ref))
         if best is None or sc <= best[0]:
             best = (sc, order, prio, slope, fin, ts)
-    order = best[1]
-    why, arcs = [None] * m, None
-    either = [i for i in range(m) if ops[i]["both"]]
-
-    def turn(o):
-        o["e"] = "s" if o["e"] == "v" else "v"
-        o["wait"] = (o["e"], o["wait"][1])
-    for k in range(MOVES):
-        md = k // 16 % len(MODELS)
-        if k % 512 == 0:
-            seen, gone = run_order(ops, order, priced[0], wake)[1:]
-            place = {x: n for n, x in enumerate(order)}
-            order = sorted(order, key=lambda x: ((gone[x] - cost[x] if ops[x]["e"] != "n" else seen[x] - lat[x] - wake) + 1e-9 * place[x]))
-            runs = [run_order(ops, order, pr, x[5]) for pr, x in zip(priced, MODELS)]
-            sc = sum(a[0] / b for a, b in zip(runs, ref))
-        if k % 16 == 0 or not arcs:
-            end, seen = run_order(ops, order, priced[md], MODELS[md][5], why)[0:2]
-            i = seen.index(end)
-            arcs = []
-            while i >= 0:
-                j, own = why[i][0:2]
-                if own and j >= 0:
-                    arcs.append((i, j))
-                i = j
-        i, j = arcs[int(rng.integers(len(arcs)))]
-        for _ in range(int(rng.geometric(REACH)) - 1):
-            if why[j][2] >= 0:
-                j = why[j][2]
-        ahead = bool(rng.integers(2))
-        flip = [x for x in (i, j, int(rng.choice(either))) if ops[x]["both"]][:1] if k % 4 == 3 else []
-        for x in flip:
-            turn(ops[x])
-        new = order if flip else moved(ops, order, i, j, pred if ahead else succ, ahead)
-        room = HEAT * (1 - k / MOVES) * rng.random()
-        for x in flip:
-            room += LEAN * cost[x] / ref[0] * (1 if ops[x]["e"] == "s" else -1)
-        if new is not None:
-            at = order.index(flip[0]) if flip else min(order.index(i), order.index(j))
-            one = run_order(ops, new, priced[md], MODELS[md][5], None, runs[md], at)
-            if one[0] <= runs[md][0] + room * ref[md]:
-                r2 = [one if x == md else run_order(ops, new, priced[x], MODELS[x][5], None, runs[x], at) for x in range(len(MODELS))]
-                s2 = sum(a[0] / b for a, b in zip(r2, ref))
-                if s2 <= sc + room:
-                    order, sc, runs, flip = new, s2, r2, []
-        for x in flip:
-            turn(ops[x])
-    PLAN["queues"] = [o["e"] for o in ops]
+        if k % TRIES == TRIES - 1:
+            field.append(best[0:2] + (first,))
+            best = None
+    for steps, keep in STEPS:
+        field = sorted((refine(ops, x[1], x[2], pred, succ, priced, ref, rng, steps) for x in field), key=lambda x: x[0])[0:keep]
+    for k in range(ROUNDS):
+        lo = int(rng.integers(-SPAN // 2, m - SPAN // 2))
+        lo, hi = max(lo, 0), min(lo + SPAN, m)
+        eng = field[0][2][:]
+        for i in field[0][1][lo:hi]:
+            if ops[i]["both"] and rng.random() < HOME:
+                eng[i] = first[i]
+        new = refine(ops, shaken(ops, field[0][1], lo, hi, pred, rng), eng, pred, succ, priced, ref, rng, SHORT, lo, hi)
+        new = refine(ops, new[1], new[2], pred, succ, priced, ref, rng, 0)
+        if new[0] <= field[0][0] + HEAT * (1 - k / ROUNDS):
+            field[0] = new
+    order = field[0][1]
+    for o, e in zip(ops, field[0][2]):
+        o["e"] = e
+        o["wait"] = (e, o["wait"][1])
+    PLAN["queues"] = field[0][2]
     PLAN["order"] = order
-    PLAN["ts"] = (best[5], [a[0] for a in runs])
     PLAN["ops"] = ops
     return order
+
+
+def kb(name, a, b):
+    return ["%s_%d" % (name, i) for i in range(a // 8, (b + 7) // 8)]
+
+
+def split(a, b, w):
+    n = -(-(b - a) // w)
+    cut = [a + 8 * ((b - a) // 8 * i // n) for i in range(n + 1)]
+    return list(zip(cut, cut[1:]))
 
 
 def rank_program(g, core, T, topo):
@@ -377,33 +623,33 @@ def rank_program(g, core, T, topo):
     CSEM = {"v": "cv", "s": "cs", "p": "cp", "g": "cg"}
     ops = []
     lastw, readers, lastb = {}, {}, {}
-    hot = [0.0]
+    tag = ["set-up"]
 
-    def add(e, kind, body, r, w, cost, up=0.0, after=(), bk=(), rows=0, nbytes=0, both=None):
+    def add(e, kind, body, r, w, cost, up=0.0, bk=(), rows=0, nbytes=0, both=None, row=False):
         i = len(ops)
         full, order = set(), set()
-        for k in list(r) + list(after):
+        for k in r:
             if k in lastw:
                 full.add(lastw[k])
         for k in w:
             if k in lastw:
-                full.add(lastw[k])
+                (order if row else full).add(lastw[k])
             full.update(readers.get(k, []))
         for k in bk:
             if k in lastb:
                 (order if ops[lastb[k]]["e"] == e and not both and not ops[lastb[k]]["both"] else full).add(lastb[k])
             lastb[k] = i
         full.discard(i)
-        ops.append({"e": e, "kind": kind, "body": body, "full": sorted(full), "order": sorted(order - full),
-                    "cost": cost, "up": up + hot[0], "name": (list(w) + [""])[0], "rows": rows, "bytes": nbytes, "both": both})
+        ops.append({"tag": tag[0], "e": e, "kind": kind, "body": body, "full": sorted(full), "order": sorted(order - full),
+                    "cost": cost, "up": up, "name": (list(w) + [""])[0], "rows": rows, "bytes": nbytes, "both": both})
         for k in r:
             readers.setdefault(k, []).append(i)
         for k in w:
             lastw[k] = i
             readers[k] = []
 
-    def V(f, r=(), w=(), c=cv(1), bk=()):
-        add("v", "c", [f], r, w, c, bk=bk)
+    def V(f, r=(), w=(), c=cv(1), bk=(), row=False):
+        add("v", "c", [f], r, w, c, bk=bk, row=row)
 
     def S(f, r=(), w=(), c=cv(1), bk=()):
         add("s", "c", [f], r, w, c, bk=bk)
@@ -429,369 +675,350 @@ def rank_program(g, core, T, topo):
         add(e, "d", pairs, r, w, cfix((0.6 if e == "g" else 0.06) * len(pairs)), up, rows=rows / 16, nbytes=rows * rb / 16)
         ops[-1]["order"] += before
 
-    PF, RF, GF, RQ, INC, W2, W3, SLF, HR, HX, C14, C15, TOP, R0 = 0, 1, 2, 3, 4, 5, 6, 8, 12, 13, 14, 15, 16, 17
+    PF, RF, GF, CQ, BQ, RQ, INC, W2, W3, SLF, HR, HX, HD, C14, C15, TOP, R0 = 0, 1, 2, 3, 4, 5, 6, 7, 8, 9, 12, 13, 14, 15, 16, 17, 18
     sm = T.sm
     col = lambda c: sm[:, c:c + 1]
-    NH = len(CH)
-    HA = range(NH)
-    HS = range(NH - 1)
-    HC = NH - 1
-    chunk = lambda a: [h for h in HA if CH[h][0] <= a < CH[h][1]][0]
     TT = lambda t: T["TT%d" % (t % 2)]
-    tk = lambda t, hs: ["TT%d_%d" % (t % 2, h) for h in hs]
-    TH = lambda t: T["TH%d" % (t % 2)]
-    fk = lambda t, hs: ["TH%d_%d" % (t % 2, h) for h in hs]
+    tk = lambda t, a, b: kb("TT%d" % (t % 2), a, b)
+    TH = lambda t, a, b: T["TH%d" % (t % 2)][:, 2 * a + 1:2 * b:2]
+    fk = lambda t, a, b: kb("TH%d" % (t % 2), a, b)
     win = lambda t: T.p0[:, 0:4096] if t == 0 else T["F%d" % t][:, 0:4096]
     wkey = lambda t: ["win%d" % t] + ([] if t else ["win0a"])
+    PKn = lambda t, a, b: T.PK[:, 768 + 256 * t + a:768 + 256 * t + b]
+    pk = lambda t, a, b: kb("PK", 768 + 256 * t + a, 768 + 256 * t + b)
 
     def alist(t, e, a, b):
-        return TT(t - 1)[:, a:b] if e == 1 and t > 0 else T.A16[:, LW * (e - 1) + a:LW * (e - 1) + b]
+        return TT(t - 1)[:, a:b] if e == 1 and t > 0 else T.AL[:, LW * (e - 1) + a:LW * (e - 1) + b]
 
-    def ak(t, e, hs):
-        return tk(t - 1, hs) if e == 1 and t > 0 else ["A16_%d_%d" % (e, h) for h in hs]
+    def ak(t, e, a, b):
+        return tk(t - 1, a, b) if e == 1 and t > 0 else kb("AL%d" % e, a, b)
 
-    def alots(t, e, a, b):
-        return T.PK[:, 768 + 256 * t + a:768 + 256 * t + b] if e == 1 else T.AE[:, LW * (e - 2) + a:LW * (e - 2) + b]
+    def aless(t, e, a, b):
+        if e == 1:
+            return TH(t - 1, a, b), fk(t - 1, a, b)
+        return (T.AH if A16 else T.AE)[:, LW * (e - 2) + a:LW * (e - 2) + b], kb("AE%d" % e, a, b)
 
-    def aless(t, e, h):
-        a, b = CH[h]
-        return (TH(t - 1)[:, a:b], fk(t - 1, [h])) if e == 1 else (alots(t, e, a, b), ek(t, e, [h]))
-
-    def ek(t, e, hs):
-        return ["AE%d_%d" % (e, h) if e > 1 else "AC%d" % t if h == HC else "PK%d_%d" % (t - 1, h) for h in hs]
-
-    dma("y", [(T.p0[:, 0:PA], T.price[:, 0:PA])], [], ["win0a"], 128, 2 * PA, up=1700)
     add("v", "c", [lambda q: q.memset(T.VT[:], 0)], [], ["VT"], cv(1024), up=1650)
     clear = len(ops) - 1
     loads = {
-        "VT": ([(T.VT[0:128:16, :], T.prev[:]), (T.VT[1:128:16, :], T.packs[0:128:16, :])], ["VT"], 128, 512),
-        "pkJ": ([(T.pkJ[:, 0:256], T.packs[:, 768:1024]), (T.pkJ[:, 256:LW], T.packs[0:128:16, 768:1024]), (T.slI[:, 0:3], T.slack[:])],
-                ["pkJ", "slI"], 384, 370),
+        "win0a": ([(T.p0[:, 0:PA], T.price[:, 0:PA])], ["win0a"], 128, 2 * PA),
+        "VT": ([(T.VT[0:128:16, :], T.prev[:])] + [(T.VT[1:128:16, :], T.packs[0:128:16, :])] * FIRST, ["VT"], 64 + 64 * FIRST, 512),
+        "pkA": ([(T.pkJ[:, 0:LA], T.packs[:, 768:768 + LA]), (T.slI[:, 0:3], T.slack[:]), (T.TI[:, 0:LA], T.lots[:, 0:LA])],
+                ["pkA", "slI"] + kb("TI", 0, LA), 384, 8 * LA // 3 + 4),
+        "pkJ": ([(T.pkJ[:, LA:256], T.packs[:, 768 + LA:1024])], ["pkJ"], 128, 1024 - 4 * LA),
+        "pkC": ([(T.pkJ[:, 256:LW], T.packs[0:128:16, 768:1024]), (T.TI[:, 256:LW], T.lots[0:128:16, :])], ["pkC"] + kb("TI", 256, LW), 256, 64),
         "win0": ([(T.p0[:, PA:4096], T.price[:, PA:4096])], ["win0"], 128, 8192 - 2 * PA),
-        "TI": ([(T.TI[:, 0:256], T.lots[:]), (T.TI[:, 256:LW], T.lots[0:128:16, :])], ["TI"], 256, 544),
+        "TI": ([(T.TI[:, LA:256], T.lots[:, LA:256])], ["TI"] + kb("TI", LA, 256), 128, 1024 - 4 * LA),
         "pkI": ([(T.pkI[:], T.packs[:, 0:768])], ["pkI"], 128, 3072),
+        "wtI": ([(T.small[:, 4:5], T.wt[:])], ["wtI"], 128, 4),
+        "incI": ([(T.small[:, 0:1], T.inc[:])], ["incI"], 128, 4),
     }
-    for x, y in zip(["win0a"] + LOADS, LOADS):
-        dma("y", loads[y][0], [], *loads[y][1:], up=1500, issued=[x])
-    dma("s", [(T.small[:, 4:5], T.wt[:])], [], ["wtI"], 128, 4, up=1900)
-    dma("y", [(T.small[:, 0:1], T.inc[:])], [], ["incI"], 128, 4, up=1200, issued=["pkI"])
+    for x, y in zip([None] + LOADS, LOADS):
+        dma("y", loads[y][0], [], *loads[y][1:], up=1500, issued=[x] if x else [])
 
     fl = dict(allow_small_or_imprecise_dtypes=True)
+    WB, CB = 256 // NB, 16 // NB
+    seg = [WB * c - 8 * c * (c - 1) for c in range(CB + 1)]
+    SEG = seg[CB]
     G(lambda q: q.iota(T.pI[:, 0:1], [[1, 1]], 0, 1), w=["pI"], up=100)
     G(lambda q: q.iota(T.row8[:], [[1, 8]], 0, 0, **fl), w=["row8"], up=100)
-    G(lambda q: q.iota(T.IX[:], [[1, 256]], 0, 0, **fl), w=["IX"], c=cfix(0.7), up=100)
-    G(lambda q: q.iota(T.i16[:], [[16, 16]], 0, 0, **fl), w=["i16"], up=100)
-    G(lambda q: q.iota(T.IXG[:], [[1, 8], [0, 16]], 0, 0, **fl), w=["IXG"], c=cfix(0.4), up=100)
-    G(lambda q: q.iota(T.MI[:], [[0, 64], [1, 16]], 0, 0, **fl), w=["MI"], c=cfix(2.1), up=90)
-    G(lambda q: q.iota(T.IDW[:], [[1, 4096]], 0, 0, **fl), w=["IDW"], c=cfix(8.0))
+    G(lambda q: q.iota(T.IX[:], [[1, 128]], 0, 0, **fl), w=["IX"], c=cgp(128), up=100)
+    G(lambda q: q.iota(T.i16[:, 0:16], [[16, 16]], 0, 0, **fl), w=["i16"], up=100)
+    G(lambda q: q.iota(T.i16[:, 16:32], [[0, NB], [16, CB]], 0, 0, **fl), w=["j16"], up=100)
+    G(lambda q: q.iota(T.IXG[:], [[1, 8], [0, 16]], 0, 0, **fl), w=["IXG"], c=cgp(128), up=100)
+    G(lambda q: q.iota(sm[:, HR:HX + 1], [[-9 * 512, 2]], 17 * 256, 0, **fl), w=["HR", "HX"], up=100)
+    G(lambda q: q.iota(col(HD), [[0, 1]], 512 * WB - 768, 0, **fl), w=["HD"], up=100)
+    G(lambda q: q.iota(T.KS[:], [[0, 72]], 0, 0, **fl), w=["KS%d" % d for d in range(4)], c=cgp(72), up=100)
+    G(lambda q: q.iota(T.KO[:], [[-4096, 2], [0, 18]], 0, 0, **fl), w=["KO"])
+    G(lambda q: q.iota(T.ones[:], [[0, 1024]], 1, 0, **fl), w=["ones"], c=cgp(1024))
+    G(lambda q: q.affine_select(T.MK[:], T.ones[:], [[0, 64], [1, 16]], A.not_equal, 0.0, 0, 0), r=["ones"], w=["MK"], c=cgp(1024, 0.17))
+    G(lambda q: q.iota(T.cB[:, 0:256], [[0, 256]], 0, 0, **fl), w=["cB"], c=cgp(256), up=60)
+    for x in range(2):
+        G(lambda q, x=x: q.iota(T.IDW[:, 2048 * x:2048 * x + 2048], [[1, 2048]], 2048 * x, 0, **fl), w=["IDW%d" % x], c=cgp(2048))
+    IDW = ["IDW0", "IDW1"]
+    for t in range(3):
+        G(lambda q, t=t: q.iota(T["F%d" % (t + 1)][:, 4096:4352], [[0, 256]], 0, 0, **fl), w=["dump%d" % t], c=cgp(256))
+    G(lambda q: q.iota(T.p0[:, 4096:4352], [[0, 256]], 0, 0, **fl), w=["dump3"], c=cgp(256))
+    for c in range(CB):
+        G(lambda q, c=c: q.iota(T.EI[:, seg[c]:seg[c + 1]], [[1, WB - 16 * c]], 0, 0, **fl), w=["EI%d" % c], c=cgp(WB - 16 * c), up=60)
 
     add("v", "c", [lambda q: q.memset(T.SELK[:], 0.0)], [], ["SELK"], cv(1024))
     ops[-1]["order"].append(clear)
     V(lambda q: q.memset(T.one16[:], 1.0), w=["one16"])
-    G(lambda q: q.iota(T.ones[:], [[0, LW]], 1, 0, **fl), w=["ones"], c=cfix(0.6))
-    G(lambda q: q.iota(T.cB[:], [[0, 256]], 0, 0, **fl), w=["cB"], c=cfix(0.6))
-    for ap, x in ((T.cB[0:1, 0:128], -15.5 * BIG), (T.cB[0:1, 128:256], 33.0), (T.cB[32:33, 128:256], 192.0 * 2048)):
+    for e in (1, 2, 3):
+        G(lambda q, e=e: q.iota(T.SG[:, SW * e - SW:SW * e], [[0, SW]], 0, 0, **fl), w=kb("SG%d" % e, 0, LW), c=cgp(SW), up=50)
+    for ap, x in ((T.cB[0:1, 0:128], -15.5 * BIG), (T.cB[0:1, 128:256], 33.0), (T.cB[32:33, 128:256], 192.0 * 2048), (T.cB[0:1, 256:384], 16 * BIG)):
         V(lambda q, ap=ap, x=x: q.memset(ap, x), w=["cB"])
-    G(lambda q: q.iota(sm[:, HR:HX + 1], [[-9 * 512, 2]], 17 * 256, 0, **fl), w=["HR", "HX"], up=100)
     V(lambda q: q.tensor_copy(col(PF), T.pI[:, 0:1]), r=["pI"], w=["PF"])
-    V(lambda q: q.tensor_scalar(T.pI[:, 1:2], T.pI[:, 0:1], 15, None, A.bitwise_and), r=["pI"], w=["pI1"])
-    V(lambda q: q.tensor_scalar(T.pI[:, 2:3], T.pI[:, 0:1], 4, None, A.logical_shift_right), r=["pI"], w=["pI2"])
-    V(lambda q: q.tensor_copy(sm[:, RF:GF + 1], T.pI[:, 1:3]), r=["pI1", "pI2"], w=["RF"])
+    for x, (y, op) in enumerate(((15, A.bitwise_and), (4, A.logical_shift_right), (CB - 1, A.bitwise_and))):
+        V(lambda q, x=x, y=y, op=op: q.tensor_scalar(T.pI[:, 1 + x:2 + x], T.pI[:, 0:1], y, None, op), r=["pI"], w=["pI%d" % (1 + x)])
+    V(lambda q: q.tensor_scalar(T.pI[:, 4:5], T.pI[:, 0:1], CB.bit_length() - 1, NB - 1, A.logical_shift_right, A.bitwise_and), r=["pI"], w=["pI4"])
+    V(lambda q: q.tensor_copy(sm[:, RF:BQ + 1], T.pI[:, 1:5]), r=["pI1", "pI2", "pI3", "pI4"], w=["RF"])
     V(lambda q: q.tensor_scalar(T.B8[:], T.row8[:], col(GF), None, A.is_equal), r=["row8", "RF"], w=["B8"])
-    move("s", T.L1c[:], T.i16[:], ["i16", "RF"], ["L1c"], cv(1), bias=col(RF))
+    move("s", T.L1c[:], T.i16[:], ["i16", "j16", "RF"], ["L1c"], cv(1), bias=col(RF))
     for gg in range(8):
         V(lambda q, gg=gg: q.tensor_scalar(T.SELK[:, 16 * gg:16 * gg + 129 * 15 + 1:129], T.one16[:],
                                            T.B8[:, gg:gg + 1], BIG, A.mult, A.mult),
           r=["one16", "B8", "SELK"], w=["SELK%d" % gg])
     SELK = ["SELK"] + ["SELK%d" % gg for gg in range(8)]
-    V(lambda q: q.tensor_copy(T.A16[:, 0:LW], T.pkJ[:]), r=["pkJ"], w=ak(0, 1, HA), c=cv(LW))
     V(lambda q: q.tensor_copy(sm[:, SLF:SLF + 3], T.slI[:, 0:3]), r=["slI"], w=["SLF"])
-    V(lambda q: q.tensor_copy(T.TT0[:], T.TI[:]), r=["TI"], w=tk(0, HA), c=cv(LW))
-    V(lambda q: q.tensor_scalar(T.TH0[:], T.TT0[:], -2048.0, None, A.add), r=tk(0, HA), w=fk(0, HA), c=cv(LW, .5))
-    V(lambda q: q.tensor_scalar(T.TH1[:], T.A16[:, 0:LW], -2048.0, None, A.add), r=ak(0, 1, HA), w=fk(1, HA), c=cv(LW, .5))
-    V(lambda q: q.tensor_copy(T.PK[:, 768:768 + LW], T.pkJ[:]), r=["pkJ"], w=ek(0, 1, HA), c=cv(LW))
-    V(lambda q: q.tensor_copy(T.PK[:, 0:768], T.pkI[:]), r=["pkI"], w=["PKa"], c=cv(768))
+    for a, b, k in L0:
+        V(lambda q, a=a, b=b: q.tensor_copy(T.AL[:, a:b], T.pkJ[:, a:b]), r=k, w=ak(0, 1, a, b), c=cv(b - a))
+        V(lambda q, a=a, b=b: q.tensor_copy(T.TT0[:, a:b], T.TI[:, a:b]), r=kb("TI", a, b), w=tk(0, a, b), c=cv(b - a))
+        V(lambda q, a=a, b=b: q.tensor_scalar(TH(0, a, b), T.TT0[:, a:b], -2048.0, None, A.add), r=tk(0, a, b), w=fk(0, a, b), c=cv(b - a, .5))
+        V(lambda q, a=a, b=b: q.tensor_scalar(TH(1, a, b), T.AL[:, a:b], -2048.0, None, A.add), r=ak(0, 1, a, b), w=fk(1, a, b), c=cv(b - a, .5))
+    V(lambda q: q.tensor_copy(PKn(0, 0, 256), T.pkJ[:, 0:256]), r=["pkA", "pkJ"], w=pk(0, 0, 256), c=cv(256))
+    V(lambda q: q.tensor_copy(T.PK[:, 0:768], T.pkI[:]), r=["pkI"], w=kb("PK", 0, 768), c=cv(768))
     V(lambda q: q.tensor_scalar(sm[:, R0:R0 + 2], T.row8[:, 0:2], col(RF), None, A.is_equal), r=["row8", "RF"], w=["R0"])
     V(lambda q: q.tensor_scalar(T.VH[:], T.VT[:, 768:1024], col(R0), None, A.mult), r=["VT", "R0"], w=["VH"], c=cv(256))
     V(lambda q: q.memset(col(TOP), 255.4921875), w=["TOP"])
-    V(lambda q: q.tensor_scalar(T.IDN[:, 0:128], T.IX[:, 0:128], col(PF), None, A.is_equal), r=["IX", "PF"], w=["IDN"], c=cv(128))
+    V(lambda q: q.tensor_scalar(T.IDN[:, 0:128], T.IX[:], col(PF), None, A.is_equal), r=["IX", "PF"], w=["IDN"], c=cv(128))
     S(lambda q: q.activation(T.IDN[:, 128:256], T.IDN[:, 0:128], AF.Copy, scale=-1.0), r=["IDN"], w=["IDM"], c=cv(128))
     S(lambda q: q.activation(T.IDH[:], T.IDN[:], AF.Copy), r=["IDN", "IDM"], w=["IDH"], c=cv(256))
-    S(lambda q: q.activation(T.IDB[:, 0:128], T.IDN[:, 0:128], AF.Copy, scale=-2048.0), r=["IDN"], w=["ID2"], c=cv(128))
-    S(lambda q: q.activation(T.IDB[:, 128:256], T.IDN[:, 0:128], AF.Copy, scale=2048.0), r=["IDN"], w=["ID3"], c=cv(128))
-    for t in range(3):
-        G(lambda q, t=t: q.iota(T["F%d" % (t + 1)][:, 4096:4352], [[0, 256]], 0, 0, **fl), w=["dump%d" % t], c=cfix(0.6))
-    G(lambda q: q.iota(T.p0[:, 4096:4352], [[0, 256]], 0, 0, **fl), w=["dump3"], c=cfix(0.6))
-    add("s", "c", [lambda q: q.activation(T.MK[:], T.MI[:], AF.Sigmoid, bias=col(HX), scale=512.0)], ["MI", "HX"], ["MK"], (1, 1024, 0, 0, 0, 1.3), up=90)
+    S(lambda q: q.activation(T.IDB[:], T.IDN[:], AF.Copy, scale=-2048.0), r=["IDN", "IDM"], w=["IDB"], c=cv(256))
     move("s", col(RQ), col(RF), ["RF"], ["RQ"], cv(1), bias=1.0)
-    V(lambda q: q.tensor_scalar(T.QM[:], T.IX[:], col(RQ), 1.0e16, A.is_equal, A.mult), r=["IX", "RQ"], w=["QM"], c=cv(256))
-    seg = [256 * c - 8 * c * (c - 1) for c in range(17)]
-    for c in range(16):
-        if c < EMD:
-            dma("y", [(T.EM[:, seg[c]:seg[c + 1]], T.QM[:, 0:256 - 16 * c])], ["QM"], ["EM%d" % c], 128, 512 - 32 * c, issued=["pkI"])
-        else:
-            S(lambda q, c=c: q.activation(T.EM[:, seg[c]:seg[c + 1]], T.QM[:, 0:256 - 16 * c], AF.Copy), r=["QM"], w=["EM%d" % c], c=cv(256 - 16 * c))
-    move("s", col(C14), col(RF), ["RF"], ["c14"], cv(1), -8.0, 248.0)
-    V(lambda q: q.tensor_scalar(T.E16[:, 0:1], col(C14), col(RF), 255.0, A.mult, A.add), r=["c14", "RF"], w=["E16"])
-    move("s", T.DJt[:], T.L1c[:], ["L1c"], ["DJt"], cv(1), SQ, 4096.0 * SQ)
-    V(lambda q: q.tensor_scalar(T.dF[:], T.L1c[:], 254.5, None, A.is_lt), r=["L1c"], w=["dF"])
+    V(lambda q: q.tensor_scalar(T.EM[:, 0:SEG], T.EI[:, 0:SEG], col(RQ), 1.0e16, A.is_equal, A.mult),
+      r=["RQ"] + ["EI%d" % c for c in range(CB)], w=["EM"], c=cv(SEG, .5))
+    move("s", col(C14), col(CQ), ["RF"], ["c14"], cv(1), -8.0, WB - 8.0)
+    move("s", col(C15), col(BQ), ["RF"], ["c15"], cv(1), float(SEG), WB - 1.0)
+    V(lambda q: q.tensor_scalar(T.E16[:, 0:1], col(C14), col(CQ), col(C15), A.mult, A.add), r=["c14", "c15", "RF"], w=["E16"])
+    move("s", T.DJt[:], T.L1c[:, 0:16], ["L1c"], ["DJt"], cv(1), SQ, 4096.0 * SQ)
+    add("s", "c", [lambda q: q.activation(T.dF[:], T.L1c[:, 16:32], AF.Sigmoid, bias=col(HD), scale=-512.0)], ["L1c", "HD"], ["dF"],
+        (1, 64, 0, 0, 0, 1.3), up=90)
     V(lambda q: q.tensor_tensor(T.DJ[:], T.dF[:], T.DJt[:], A.mult), r=["dF", "DJt"], w=["DJ"])
     V(lambda q: q.tensor_scalar(col(INC), T.small[:, 0:1], 1.0 / 64, None, A.mult), r=["incI"], w=["INC"])
+    if any("p" in x for x in UF):
+        move("s", T.IDI[:], T.IDN[:, 0:128], ["IDN", "INC"], ["IDI"], cv(128), scale=col(INC))
     V(lambda q: q.tensor_scalar(col(W2), T.small[:, 4:5], 2.0, None, A.mult), r=["wtI"], w=["W2"])
     V(lambda q: q.tensor_scalar(col(W3), T.small[:, 4:5], 2.0 / BIG, None, A.mult), r=["wtI"], w=["W3"])
     V(lambda q: q.tensor_scalar(T.WT[:], T.IXG[:], col(GF), col(W2), A.is_equal, A.mult), r=["IXG", "RF", "W2"], w=["WT"], c=cv(128))
-    if FREE:
+    if TAIL:
         V(lambda q: q.tensor_scalar(T.BE[:], T.IXG[:], col(GF), BIG, A.is_equal, A.mult), r=["IXG", "RF"], w=["BE"], c=cv(128))
     for i in range(2):
         S(lambda q, i=i: q.activation(T.SELW[:, 1024 * i:1024 * i + 1024], T.SELK[:, 1024 * i:1024 * i + 1024], AF.Copy, scale=col(W3)),
           r=SELK + ["W3"], w=["SELW%d" % i], c=cv(1024))
 
-    KS, KY, KM = T.KS, T.KY, T.KM
+    KS, KM = T.KS, T.KM
+    LU = lambda d: T.LU[:, 18 * d:18 * d + 16]
 
     def conv(d):
-        PE([lambda q, k=k: q.matmul(T.ZM[:, 384:400], T.SELK[:, 128 * k:128 * k + 128], T.VH[:, k:256:16], k == 0, k == 15)
-            for k in range(16)], ["VH"] + SELK, ["zc"], cmm(16, 16), ["bM"])
+        z = T.ZC[:, 0:16]
+        PE([lambda q, k=k: q.matmul(z, T.SELK[:, 128 * k:128 * k + 128], T.VH[:, k:256:16], k == 0, k == 15)
+            for k in range(16)], ["VH"] + SELK, ["zc"], cmm(16, 16), ["bC"])
         if d < 3:
-            V(lambda q: q.tensor_scalar(T.LU[:, 16 * d:16 * d + 16], T.ZM[:, 384:400], 1.0 / BIG, None, A.mult), r=["zc"], w=["LU%d" % d], bk=["bM"])
-        S(lambda q: q.activation(KS[:, 16 * d:16 * d + 16], T.ZM[:, 384:400], AF.Copy, scale=1.0 / BIG), r=["zc"], w=["KS%d" % d], bk=["bM"])
+            V(lambda q: q.tensor_scalar(LU(d), z, 1.0 / BIG, None, A.mult), r=["zc"], w=["LU%d" % d], bk=["bC"])
+        move("s", KS[:, 18 * d:18 * d + 16], z, ["zc"], ["KS%d" % d], cv(1), 1.0 / BIG, 4096.0 * (1 - d), ["bC"])
 
     def parents(d):
-        V(lambda q: q.tensor_scalar(T.VH[:], T.VT[:].indirect(T.LU[:, 16 * d:16 * d + 16]), col(R0), None, A.mult),
-          r=["VT", "R0", "LU%d" % d], w=["VH"], c=cgat(256))
+        V(lambda q: q.tensor_scalar(T.VH[:], T.VT[:].indirect(LU(d)), col(R0), None, A.mult), r=["VT", "R0", "LU%d" % d], w=["VH"], c=cgat(256))
 
     def first(e):
-        V(lambda q: q.tensor_scalar(T.VG[:], T.VT[:].indirect(T.LU[:, 16 * e - 16:16 * e]), -2048.0, col(R0 + 1), A.add, A.mult),
+        z = T.ZX[:, 0:16]
+        lots, lk = aless(0, e, 256, LW)
+        V(lambda q: q.tensor_scalar(T.VG[:], T.VT[:].indirect(LU(e - 1)), -2048.0, col(R0 + 1), A.add, A.mult),
           r=["VT", "R0", "LU%d" % (e - 1)], w=["VG"], c=cgat(256))
-        PE([lambda q, k=k: q.matmul(T.ZM[:, 448:464], T.SELK[:, 128 * k:128 * k + 128], T.VG[:, 16 * k:16 * k + 16], k == 0, k == 15)
-            for k in range(16)], ["VG"] + SELK, ["zf"], cmm(16, 16), ["bM"])
-        V(lambda q: q.tensor_scalar(alist(0, e, 256, LW), T.ZM[:, 448:464], 1.0 / BIG, 2048.0, A.mult, A.add), r=["zf"], w=ak(0, e, [HC]), bk=["bM"])
-        S(lambda q: q.activation(alots(0, e, 256, LW), T.ZM[:, 448:464], AF.Copy, scale=1.0 / BIG), r=["zf"], w=ek(0, e, [HC]), bk=["bM"])
+        PE([lambda q, k=k: q.matmul(z, T.SELK[:, 128 * k:128 * k + 128], T.VG[:, 16 * k:16 * k + 16], k == 0, k == 15)
+            for k in range(16)], ["VG"] + SELK, ["zX"], cmm(16, 16), ["bX"])
+        V(lambda q: q.tensor_scalar(alist(0, e, 256, LW), z, 1.0 / BIG, 2048.0, A.mult, A.add), r=["zX"], w=ak(0, e, 256, LW), bk=["bX"])
+        move("s", lots, z, ["zX"], lk, cv(1), scale=1.0 / BIG, bk=["bX"])
 
     def keys(t):
-        c = 16 if t == 2 else 32
-        S(lambda q: q.activation(KS[:, 0:16], T.L1c[:], AF.Copy, bias=768.0 + 256 * t), r=["L1c"], w=["KS0"])
-        for e in range(3):
-            S(lambda q, e=e: q.activation(KY[:, e, 0:c], KS[:, 16 * e:16 * e + c], AF.Copy, bias=-4096.0 * (e + 1) - 1, scale=-1.0),
-              r=["KS%d" % d for d in range(e, e + c // 16)], w=["KY%d" % e])
-        S(lambda q: q.activation(KM[:, 3, 0:c], KS[:, 32:32 + c], AF.Copy, bias=-1.0, scale=-1.0), r=["KS%d" % d for d in range(2, 2 + c // 16)], w=["KM3"])
+        c = 18 if t == 2 else 36
+        move("s", KS[:, 0:16], T.L1c[:, 0:16], ["L1c"], ["KS0"], cv(1), bias=4096.0 + 768 + 256 * t)
+        move("s", KM[:, 3, 0:c], KS[:, 36:36 + c], ["KS%d" % d for d in range(2, 2 + c // 18)], ["KM3"], cv(1), bias=3 * 4096.0)
 
     def package(t, e):
-        move("s", alots(t, e, 0, 256), T.PK[:, 0:1024 + 256 * t].indirect(T.LU[:, 16 * e - 16:16 * e]),
-             ["PKa"] + ["PK%d_%d" % (i, h) for i in range(-1, t) for h in HS] + ["LU%d" % (e - 1)], ek(t, e, HS), cgat(256), bias=-2048.0)
-        V(lambda q: q.tensor_scalar(alist(t, e, 0, 256), alots(t, e, 0, 256), 2048.0, None, A.add), r=ek(t, e, HS), w=ak(t, e, HS), c=cv(256))
+        src, r = T.PK[:, 0:1024 + 256 * t].indirect(LU(e - 1)), kb("PK", 0, 1024 + 256 * t) + ["LU%d" % (e - 1)]
+        lots, lk = aless(t, e, 0, 256)
+        if A16:
+            if A16 == 2:
+                move("s", T.AE[:, 0:256], src, r, ["AF"], cgat(256))
+                V(lambda q: q.tensor_copy(alist(t, e, 0, 256), T.AE[:, 0:256]), r=["AF"], w=ak(t, e, 0, 256), c=cv(256))
+            else:
+                V(lambda q: q.tensor_copy(alist(t, e, 0, 256), src), r=r, w=ak(t, e, 0, 256), c=cgat(256))
+            V(lambda q: q.tensor_scalar(lots, alist(t, e, 0, 256), -2048.0, None, A.add), r=ak(t, e, 0, 256), w=lk, c=cv(256, .5))
+        else:
+            move("s", lots, src, r, lk, cgat(256), bias=-2048.0)
+            V(lambda q: q.tensor_scalar(alist(t, e, 0, 256), lots, 2048.0, None, A.add), r=lk, w=ak(t, e, 0, 256), c=cv(256))
 
     def clist(t, e):
-        dma("y", [(alist(t, e, 256, LW), alist(t, e, 0, 256)[t:128:16, :])], ak(t, e, HS), ak(t, e, [HC]), 128, 32)
-        dma("y", [(alots(t, e, 256, LW), alots(t, e, 0, 256)[t:128:16, :])], ek(t, e, HS), ek(t, e, [HC]), 128, 64)
+        dma("y", [(alist(t, e, 256, LW), alist(t, e, 0, 256)[t:128:16, :])], ak(t, e, 0, 256), ak(t, e, 256, LW), 128, 32)
         if e == 1:
-            dma("y", [(TH(t - 1)[:, 256:LW], TH(t - 1)[t:128:16, 0:256])], fk(t - 1, HS), fk(t - 1, [HC]), 128, 32)
+            dma("y", [(PKn(t, 256, LW), PKn(t, 0, 256)[t:128:16, :])], pk(t, 0, 256), pk(t, 256, LW), 128, 64)
+            V(lambda q: q.tensor_scalar(TH(t - 1, 256, LW), alist(t, e, 256, LW), -2048.0, None, A.add), r=ak(t, e, 256, LW), w=fk(t - 1, 256, LW))
+        else:
+            (a, ka), (b, kc) = aless(t, e, 0, 256), aless(t, e, 256, LW)
+            dma("y", [(b, a[t:128:16, :])], ka, kc, 128, 32 if A16 else 64)
 
-    NP = len(PCS)
-
-    def gy(t, e, i):
-        who = YR[t][NP * (e - 1):NP * e] + "."
-        if who[i] == "+":
-            return
-        j = i + 1
-        while who[j] == "+":
-            j += 1
-        a, b = PCS[i][0], PCS[j - 1][1]
-        o = 16 * (LW * (e - 1) + a)
-        out, lst = T.Y[:, o:o + 16 * (b - a)], win(t).indirect(alist(t, e, a, b))
-        r, w, c = wkey(t) + ak(t, e, [chunk(PCS[x][0]) for x in range(i, j)]) + ["SLF"], ["Y%d_%d" % (e, x) for x in range(i, j)], cgat(16 * (b - a))
-        move(who[i], out, lst, r, w, c, bias=col(SLF + t))
+    def gy(t, e, a, b):
+        o = 16 * LW * (e - 1)
+        move("s", T.Y[:, o + 16 * a:o + 16 * b], win(t).indirect(alist(t, e, a, b)), wkey(t) + ak(t, e, a, b) + ["SLF"],
+             kb("Y%d" % e, a, b), cgat(16 * (b - a)), bias=col(SLF + t))
 
     def diff(t, e, h):
-        a, b = CH[h]
-        z = T["Z%d" % h][:, 256:256 + b - a]
-        lots, lk = aless(t, e, h)
-        PE([lambda q: q.matmul(z, (T.IDH if e == 1 else T.IDN)[:, 128:256], lots, True, False),
-            lambda q: q.matmul(z, T.IDH[:, 0:128], TH(t)[:, a:b], False, True)],
-           ["IDM", "IDH"] + lk + fk(t, [h]), ["zD%d" % h], cmm(b - a, 2 if e == 1 else 5), ["bZ%d" % h])
+        a, b = CH[t][h]
+        m = b - a
+        lots, lk = aless(t, e, a, b)
+        narrow = e == 1 or A16
+        ID = T.IDH if narrow else T.IDN
+        z = T["Z%d" % h]
+        d = z[:, 192:192 + 2 * m:2] if SCAN else z[:, 192:192 + m]
+        PE([lambda q: q.matmul(d, ID[:, 128:256], lots, True, False),
+            lambda q: q.matmul(d, T.IDH[:, 0:128], TH(t, a, b), False, True)] +
+           [lambda q: q.matmul(z[:, 193:192 + 2 * m:2], ID[:, 0:128], lots, True, True)] * SCAN,
+           ["IDN", "IDM", "IDH"] + lk + fk(t, a, b), ["zD%d" % h], cmm(m, 1 + (1 + SCAN) * (1 if narrow else 4)), ["bZ%d" % h])
 
-    held = []
-
-    def gx(t, e, i):
-        a, b = PCS[i]
-        h = chunk(a)
+    def gx(t, e, a, b):
         o = 16 * LW * (e - 1)
         c0, c1 = 16 * a, 16 * b
-        m = b - a
-        z = T["Z%d" % h][:, a - CH[h][0]:b - CH[h][0]]
         lst = win(t).indirect(TT(t)[:, a:b])
-        r = wkey(t) + tk(t, [h])
-        blocks = [(x, min(x + 512, 16 * m)) for x in range(0, 16 * m, 512)]
-        ck = ["C%d_%d" % (i, x) for x, y in blocks]
-        if RT[t][NP * (e - 1) + i] == "v":
-            V(lambda q: q.tensor_tensor(T.C[:, c0:c1], lst, T.Y[:, o + c0:o + c1], A.is_gt), r=r + ["Y%d_%d" % (e, i)], w=ck, c=cgat(16 * m))
-        else:
-            S(lambda q: q.activation(T.XS[:, 0:16 * m], lst, AF.Copy), r=r, w=["XS"], c=cgat(16 * m))
-            for x, y in blocks:
-                PE([lambda q, x=x, y=y: q.matmul(T.ZX[:, 0:y - x], T.IDB[:, 128:256], T.XS[:, x:y], True, False),
-                    lambda q, x=x, y=y: q.matmul(T.ZX[:, 0:y - x], T.IDB[:, 0:128], T.Y[:, o + c0 + x:o + c0 + y], False, True)],
-                   ["XS", "ID2", "ID3", "Y%d_%d" % (e, i)], ["zX"], cmm(y - x, 2), ["bX"])
-                S(lambda q, x=x, y=y: q.activation(T.C[:, c0 + x:c0 + y], T.ZX[:, 0:y - x], AF.Sigmoid, bias=col(HX), scale=0.25),
-                  r=["zX", "HX"], w=["C%d_%d" % (i, x)], c=cv(y - x), bk=["bX"])
-        w0 = c0
-        if WIDE:
-            held.extend(ck)
-            if b < CH[h][1]:
-                return
-            ck, m, w0 = held[:], b - CH[h][0], 16 * CH[h][0]
-            z = T["Z%d" % h][:, 0:m]
-            held.clear()
-        for x in range(0, 16, PG):
-            PE([lambda q, k=k: q.matmul(z, T.SELK[:, 128 * k:128 * k + 128], T.C[:, w0 + k:c1:16], k == 0, k == 15) for k in range(x, x + PG)],
-               ck + SELK, ["zC%d" % i] if x in (0, 16 - PG) else [], cmm(m, PG), ["bZ%d" % h])
-            if x:
-                ops[-1]["full"] = [p for p in ops[-1]["full"] if p != len(ops) - 1 - x // PG]
-                ops[-1]["order"] = [len(ops) - 2]
+        r = wkey(t) + tk(t, a, b)
+        if (t, e, a) not in SR:
+            V(lambda q: q.tensor_tensor(T.C[:, c0:c1], lst, T.Y[:, o + c0:o + c1], A.is_gt), r=r + kb("Y%d" % e, a, b), w=kb("C", a, b), c=cgat(c1 - c0))
+            if DUE and a < 256:
+                ops[-1]["due"] = DUE[0] + DUE[1] * (3 * t + e - 1 + a / 256)
+            return
+        S(lambda q: q.activation(T.XS[:, 0:c1 - c0], lst, AF.Copy), r=r, w=["XS"], c=cgat(c1 - c0))
+        for x, y in split(a, b, 32):
+            z = T.ZX[:, 0:16 * (y - x)]
+            PE([lambda q, x=x, y=y, z=z: q.matmul(z, T.IDB[:, 128:256], T.XS[:, 16 * x - c0:16 * y - c0], True, False),
+                lambda q, x=x, y=y, z=z: q.matmul(z, T.IDB[:, 0:128], T.Y[:, o + 16 * x:o + 16 * y], False, True)],
+               ["XS", "IDB"] + kb("Y%d" % e, x, y), ["zX"], cmm(16 * (y - x), 2), ["bX"])
+            S(lambda q, x=x, y=y, z=z: q.activation(T.C[:, 16 * x:16 * y], z, AF.Sigmoid, bias=col(HX), scale=0.25),
+              r=["zX", "HX"], w=kb("C", x, y), c=cv(16 * (y - x)), bk=["bX"])
 
     def tops(t, e, h):
-        a, b = CH[h]
-        m = b - a
-        z, d, dk, bk = T["Z%d" % h][:, 0:m], T["Z%d" % h][:, 256:256 + m], ["zD%d" % h], ["bZ%d" % h]
-        lots, lk = aless(t, e, h)
-        mask, mk = (T.MC[:], "MC") if h == HC else (T.SG[:, 256 * (e - 1) + a:256 * (e - 1) + b], "SG%d_%d" % (e, h))
-        zk = ["zC%d" % i for i in range(NP) if chunk(PCS[i][0]) == h]
-        VS(MCV[e - 1][h], lambda q: q.tensor_scalar(mask, z, 8.5 * BIG, None, A.is_lt),
-           lambda q: q.activation(mask, z, AF.Sigmoid, bias=col(HR), scale=-512.0 / BIG), zk + ["HR"], [mk], cv(m), bk)
-        V(lambda q: q.tensor_tensor(d, d, mask, A.mult), r=[mk], w=dk, c=cv(m), bk=bk)
-        V(lambda q: q.tensor_tensor(TH(t)[:, a:b], d, lots, A.add), r=dk + lk, w=fk(t, [h]), c=cv(m), bk=bk)
-        if (t, e) != (2, 3) or h == HC:
-            V(lambda q: q.tensor_scalar(TT(t)[:, a:b], TH(t)[:, a:b], 2048.0, None, A.add), r=fk(t, [h]), w=tk(t, [h]), c=cv(m, .5))
-        if e == 3 and h != HC and PKS:
-            y = T["Z%d" % h][:, 384:384 + m]
-            PE([lambda q: q.matmul(y, T.IDH[:, 0:128], TH(t)[:, a:b], True, True)], ["IDH"] + fk(t, [h]), ["zP%d" % h], cmm(m), bk)
-            move("s", alots(t + 1, 1, a, b), y, ["zP%d" % h], ek(t + 1, 1, [h]) + (["AC%d" % t] if a == 0 else []), cv(m), bias=2048.0, bk=bk)
-        elif e == 3 and h != HC:
-            V(lambda q: q.tensor_scalar(alots(t + 1, 1, a, b), TH(t)[:, a:b], 2048.0, None, A.add), r=fk(t, [h]),
-              w=ek(t + 1, 1, [h]) + (["AC%d" % t] if a == 0 else []), c=cv(m))
-        elif e == 3:
-            V(lambda q: q.tensor_scalar(T.CF[:], TH(t)[:, a:b], 2048.0, -SQ, A.add, A.mult), r=fk(t, [h]), w=["CF"])
+        a, b = CH[t][h]
+        m, l = b - a, min(b, 256)
+        Z, dk, bk = T["Z%d" % h], ["zD%d" % h], ["bZ%d" % h]
+        z = Z[:, 0:m]
+        PE([lambda q, k=k: q.matmul(z, T.SELK[:, 128 * k:128 * k + 128], T.C[:, 16 * a + k:16 * b:16], k == 0, k == 15) for k in range(16)],
+           kb("C", a, b) + SELK, ["zC%d" % h], cmm(m, 16), bk)
+        o = SW * (e - 1)
+        mask, mk = T.SG[:, o + 2 * a + 1:o + 2 * b:2], kb("SG%d" % e, a, b)
+        VS("s", lambda q: q.tensor_scalar(mask, z, 8.5 * BIG, None, A.is_lt),
+           lambda q: q.activation(mask, z, AF.Sigmoid, bias=col(HR), scale=-512.0 / BIG), ["zC%d" % h, "HR"], mk, cv(m), bk)
+        if SCAN:
+            V(lambda q: q.tensor_tensor_scan(T["TH%d" % (t % 2)][:, 2 * a:2 * b], T.SG[:, o + 2 * a:o + 2 * b], Z[:, 192:192 + 2 * m], 0.0, A.mult, A.add),
+              r=dk + mk, w=fk(t, a, b), c=cv(2 * m), bk=bk)
+        else:
+            d = Z[:, 192:192 + m]
+            lots, lk = aless(t, e, a, b)
+            V(lambda q: q.tensor_tensor(d, d, mask, A.mult), r=mk, w=dk, c=cv(m), bk=bk)
+            V(lambda q: q.tensor_tensor(TH(t, a, b), d, lots, A.add), r=dk + lk, w=fk(t, a, b), c=cv(m), bk=bk)
+        x = max(a, 256) if (t, e) == (2, 3) else a
+        if x < b:
+            V(lambda q: q.tensor_scalar(TT(t)[:, x:b], TH(t, x, b), 2048.0, None, A.add), r=fk(t, x, b), w=tk(t, x, b), c=cv(b - x, .5))
+        if e == 3 and a < l and t in PKS:
+            y = Z[:, 384:384 + l - a]
+            PE([lambda q: q.matmul(y, T.IDH[:, 0:128], TH(t, a, l), True, True)], ["IDH"] + fk(t, a, l), ["zP%d" % h], cmm(l - a), bk)
+            move("s", PKn(t + 1, a, l), y, ["zP%d" % h], pk(t + 1, a, l), cv(l - a), bias=2048.0, bk=bk)
+        elif e == 3 and a < l:
+            V(lambda q: q.tensor_scalar(PKn(t + 1, a, l), TH(t, a, l), 2048.0, None, A.add), r=fk(t, a, l), w=pk(t + 1, a, l), c=cv(l - a))
+        if e == 3 and b == LW:
+            V(lambda q: q.tensor_scalar(T.CF[:], TH(t, 256, LW), 2048.0, -SQ, A.add, A.mult), r=fk(t, 256, LW), w=["CF"])
 
-    zq = T["Z%d" % HC][:, 384:400]
-
-    def gm(t, i):
-        a, b = PCS[i]
+    def gm(t, a, b):
         x, y = 16 * a, 16 * b
-        lst = win(t).indirect(TT(t)[:, a:b])
-        r, w, c = wkey(t) + tk(t, [chunk(a)]), ["XM%d" % i], cgat(y - x)
-        move(MR[t][i - 1], T.XM[:, x:y], lst, r, w, c)
+        move("s", T.XM[:, x:y], win(t).indirect(TT(t)[:, a:b]), wkey(t) + tk(t, a, b), kb("XM", a, b), cgat(y - x))
         V(lambda q: q.tensor_tensor_scan(T.SM[:, x:y], T.MK[:, 0:y - x], T.XM[:, x:y], 0.0, A.mult, A.max),
-          r=["MK", "XM%d" % i], w=["SM%d" % i], c=cv((y - x) // 2))
-        if QC:
-            ks = range(a // 16, b // 16)
-            PE([lambda q, k=k: q.matmul(zq, T.SELW[:, 128 * k:128 * k + 128], T.SM[:, 256 * k + 15:256 * k + 256:16], k == 0, k == 15) for k in ks],
-               ["SM%d" % i, "SELW0", "SELW1"], ["zQ%d" % i], cmm(16, len(ks)), ["bZ%d" % HC])
+          r=["MK"] + kb("XM", a, b), w=kb("SM", a, b), c=cv((y - x) // 2))
 
-    def tclaim(t):
-        x, lots, lk = slice(256, LW), alots(t + 1, 1, 256, LW), ek(t + 1, 1, [HC])
-        move("s", T.dE[:], lots, lk, ["dE"], cv(1), 33.0, 2464.0 * (t + 1))
-        V(lambda q: q.tensor_copy(T.kI[:, 0:16], zq), r=["zQ%d" % i for i in range(1, NP)], w=["kI"], bk=["bZ%d" % HC])
-        V(lambda q: q.tensor_scalar(T.qI[:, x], T.kI[:, 0:16], 2047, None, A.bitwise_and), r=["kI"], w=["qIc"])
-        V(lambda q: q.tensor_tensor(T.qF[:, x], T.qI[:, x], lots, A.mult), r=["qIc"] + lk, w=["qFc"])
-        V(lambda q: q.tensor_tensor(T.qI[:, x], T.qF[:, x], T.dE[:], A.add), r=["qFc", "dE"], w=["qIc"])
-        V(lambda q: q.tensor_scalar(T.TI[:, x], T.qI[:, x], 5, 4095, A.logical_shift_right, A.bitwise_and), r=["qIc", "TI"], w=["TIc"])
-        V(lambda q: q.tensor_copy(TT(t + 1)[:, x], T.TI[:, x]), r=["TIc"], w=tk(t + 1, [HC]))
-        V(lambda q: q.tensor_scalar(TH(t + 1)[:, x], T.TI[:, x], -2048.0, None, A.add), r=["TIc"], w=fk(t + 1, [HC]))
-
-    def tnew(t, hs):
-        a, b = CH[hs[0]][0], CH[hs[-1]][1]
+    def tnew(t, a, b):
         l = min(b, 256)
         m = b - a
-        nm = str(hs[0])
-        sk = ["SM%d" % i for i in range(1, NP) if HC in hs or chunk(PCS[i][0]) in hs] + ["WT", "SELW0", "SELW1"]
+        sk = (kb("SM", 0, 256) if b == LW else kb("SM", a, b)) + ["WT", "SELW0", "SELW1"]
 
         def sums(z, first):
             fs = [lambda q: q.matmul(z[:, a:l], T.WT[:], T.SM[:, 16 * a + 15:16 * l:16], first, first)] if l > a else []
-            if HC in hs:
+            if b == LW:
                 fs += [lambda q, k=k: q.matmul(z[:, 256:LW], T.SELW[:, 128 * k:128 * k + 128], T.SM[:, 256 * k + 15:256 * k + 256:16],
                                                first and k == 0, first and k == 15) for k in range(16)]
             return fs
-        pc = cmm(m, 1) if HC not in hs else cmm(64, 16 + m // 64)
+        pc = cmm(m, 1) if b < LW else cmm(64, 16 + m // 64)
         PE(sums(T.ZM, True), sk, ["zU"], pc, ["bM"])
-        PE([lambda q: q.matmul(T.ZR[:, a:b], T.cB[0:33, 128:256], T.ones[0:33, 0:m], True, False)] + sums(T.ZR, False),
-           sk + ["cB", "ones"], ["zR"], pc, ["bR"])
-        move("s", T.kf[:, a:b], T.ZM[:, a:b], ["zU"], ["kf" + nm], cv(m), 1.0 / 2048, 191.5 + 1.0 / 2048, ["bM"])
-        PE([lambda q: q.matmul(T.ZR[:, a:b], T.IDB[:, 0:128], T.kf[:, a:b], False, True)], ["ID2", "kf" + nm], ["zR"], cmm(m), ["bR"])
-        V(lambda q: q.tensor_tensor(T.qF[:, a:b], T.ZR[:, a:b], alots(t + 1, 1, a, b), A.mult), r=["zR"] + ek(t + 1, 1, hs), w=["qF" + nm], c=cv(m), bk=["bR"])
-        V(lambda q: q.tensor_scalar(T.qI[:, a:b], T.qF[:, a:b], 2464.0 * (t + 1), None, A.add), r=["qF" + nm], w=["qI" + nm], c=cv(m))
+        if b == LW and UCOPY:
+            move("s", T.kf[:, a:b], T.ZM[:, a:b], ["zU"], kb("kf", a, b), cv(m), 1.0 / 2048, 191.5 + 1.0 / 2048, ["bM"])
+            move("s", T.uF[:, a:b], T.ZM[:, a:b], ["zU"], ["uF"], cv(m), bias=192.0 * 2048 + 33, bk=["bM"])
+            PE([lambda q: q.matmul(T.ZR[:, a:b], T.IDB[:, 0:128], T.kf[:, a:b], True, False),
+                lambda q: q.matmul(T.ZR[:, a:b], T.IDN[:, 0:128], T.uF[:, a:b], False, True)], ["IDB", "IDN", "uF"] + kb("kf", a, b), ["zR"], cmm(m, 5), ["bR"])
+        else:
+            PE([lambda q: q.matmul(T.ZR[:, a:b], T.cB[0:33, 128:256], T.ones[0:33, 0:m], True, False)] + sums(T.ZR, False),
+               sk + ["cB", "ones"], ["zR"], pc, ["bR"])
+            move("s", T.kf[:, a:b], T.ZM[:, a:b], ["zU"], kb("kf", a, b), cv(m), 1.0 / 2048, 191.5 + 1.0 / 2048, ["bM"])
+            PE([lambda q: q.matmul(T.ZR[:, a:b], T.IDB[:, 0:128], T.kf[:, a:b], False, True)], ["IDB"] + kb("kf", a, b), ["zR"], cmm(m), ["bR"])
+        V(lambda q: q.tensor_tensor(T.qF[:, a:b], T.ZR[:, a:b], PKn(t + 1, a, b), A.mult), r=["zR"] + pk(t + 1, a, b), w=kb("qF", a, b), c=cv(m), bk=["bR"])
+        V(lambda q: q.tensor_scalar(T.qI[:, a:b], T.qF[:, a:b], 2464.0 * (t + 1), None, A.add), r=kb("qF", a, b), w=kb("qI", a, b), c=cv(m))
         V(lambda q: q.tensor_scalar(T.TI[:, a:b], T.qI[:, a:b], 5, 4095, A.logical_shift_right, A.bitwise_and),
-          r=["qI" + nm, "TI"], w=["TI" + nm], c=cv(m))
-        V(lambda q: q.tensor_copy(TT(t + 1)[:, a:b], T.TI[:, a:b]), r=["TI" + nm], w=tk(t + 1, hs), c=cv(m))
-        V(lambda q: q.tensor_scalar(TH(t + 1)[:, a:b], TT(t + 1)[:, a:b], -2048.0, None, A.add), r=tk(t + 1, hs), w=fk(t + 1, hs), c=cv(m, .5))
+          r=kb("qI", a, b), w=kb("TI", a, b), c=cv(m))
+        V(lambda q: q.tensor_copy(TT(t + 1)[:, a:b], T.TI[:, a:b]), r=kb("TI", a, b), w=tk(t + 1, a, b), c=cv(m))
+        V(lambda q: q.tensor_scalar(TH(t + 1, a, b), TT(t + 1)[:, a:b], -2048.0, None, A.add), r=tk(t + 1, a, b), w=fk(t + 1, a, b), c=cv(m, .5))
 
     def bind(t):
-        zb, BB = (T.ZM[:, 400:448], "bM") if t == 2 and FREE else (T.ZX[:, 0:48], "bX")
-        shift = [lambda q: q.matmul(zb, T.cB[0:1, 0:128], T.ones[0:1, 0:48], True, False)]
-        if t == 2 and FREE:
-            a = CH[HC - 1][0]
-            for e in range(3):
-                PE(shift[e:] + [lambda q, k=k, e=e: q.matmul(zb[:, 16 * e:16 * e + a // 16], T.SELK[:, 128 * k:128 * k + 128],
-                                                             T.SG[:, 256 * e + k:256 * e + a:16], False, k == 15 and e == 2) for k in range(16)],
-                   ["SG%d_%d" % (e + 1, h) for h in HS[:-1]] + SELK + ["cB", "ones"], ["zB"], cmm(16, 17), [BB])
-        else:
-            PE(shift + [lambda q, k=k: q.matmul(zb, T.SELK[:, 128 * k:128 * k + 128], T.SG[:, k:768:16], False, k == 15) for k in range(16)],
-               ["SG%d_%d" % (e, h) for e in (1, 2, 3) for h in HS] + SELK + ["cB", "ones"], ["zB"], cmm(48, 17), [BB])
-        c = 16 if t == 2 else 32
-        ds = range(c // 16)
+        zb = T.ZC[:, 64:118]
+        a = CH[t][-1][0] if t == 2 and TAIL else 288
+        x = 36 + a // 16
+        PE([lambda q: q.matmul(zb, T.cB[0:1, 0:128], T.ones[0:1, 0:54], True, False)] +
+           [lambda q: q.matmul(zb[:, x:54], T.cB[0:1, 256:384], T.ones[0:1, x:54], False, False)] * (x < 54) +
+           [lambda q, k=k: q.matmul(zb[:, 0:x], T.SELK[:, 128 * k:128 * k + 128], T.SG[:, 2 * k + 1:2 * SW + 2 * a:32], False, k == 15) for k in range(16)],
+           kb("SG1", 0, LW) + kb("SG2", 0, LW) + kb("SG3", 0, min(a, LW)) + SELK + ["cB", "ones"], ["zB"], cmm(54, 17), ["bC"])
+        c = 18 if t == 2 else 36
+        ds = range(c // 18)
         for d in ds:
-            V(lambda q, d=d: q.tensor_tensor(KM[:, 0:3, 16 * d:16 * d + 16], zb, KY[:, :, 16 * d:16 * d + 16], A.max),
-              r=["zB"] + ["KY%d" % e for e in range(3)], w=["KM_%d" % d], bk=[BB])
+            V(lambda q, d=d: q.tensor_tensor(KM[:, 0:3, 18 * d:18 * d + 18], zb, KS[:, 18 * d:18 * d + 54], A.max),
+              r=["zB"] + ["KS%d" % e for e in range(d, d + 3)], w=["KM_%d" % d], bk=["bC"])
         V(lambda q: q.tensor_tensor(T.k1[:, :, 0:c], KM[:, 0:2, 0:c], KM[:, 2:4, 0:c], A.min), r=["KM3"] + ["KM_%d" % d for d in ds], w=["k1"], c=cv(4 * c))
-        V(lambda q: q.tensor_tensor(T.kI[:, 0:c], T.k1[:, 0, 0:c], T.k1[:, 1, 0:c], A.min), r=["k1"], w=["kI"])
+        V(lambda q: q.tensor_tensor(T.kI[:, 0:c], T.k1[:, 0, 0:c], T.k1[:, 1, 0:c], A.min), r=["k1"], w=["kI"], c=cv(2 * c))
         V(lambda q: q.tensor_scalar(T.kJ[:, 0:c], T.kI[:, 0:c], 4095, None, A.bitwise_and), r=["kI"], w=["kJ"])
-        V(lambda q: q.tensor_scalar(T.LU[:, 16:16 + c], T.kJ[:, 0:c], -1.0, 4095.0, A.mult, A.add), r=["kJ"], w=["LU1", "LU2"])
-        if t < 2:
-            V(lambda q: q.tensor_scalar(KS[:, 16:48], T.kJ[:], -1.0, 4095.0, A.mult, A.add), r=["kJ"], w=["KS1", "KS2"])
+        if t < 2 or t not in YT or TAIL:
+            V(lambda q: q.tensor_copy(T.LU[:, 18:18 + c], T.kJ[:, 0:c]), r=["kJ"], w=["LU%d" % (d + 1) for d in ds])
+        if t < 2 or t in YT:
+            V(lambda q: q.tensor_tensor(KS[:, 18:18 + c], T.kJ[:, 0:c], T.KO[:, 0:c], A.add), r=["kJ", "KO"], w=["KS%d" % (d + 1) for d in ds], c=cv(2 * c))
 
     def outv(t):
-        x = slice(256 * t, 256 * t + (CH[HC - 1][0] if t == 2 and FREE else 256))
-        n = (x.stop - x.start) // 16
-        move("s", T.YV[:, x], T.IDW[:].indirect(T.LU[:, 16:16 + n]), ["IDW", "LU1"], ["YV%d" % t], cgat(16 * n))
-        dma("y", [(T.yv[:, x], T.YV[0:128:16, x])], ["YV%d" % t], ["yv%d" % t], 16, 512)
+        a = CH[t][-1][0] if t == 2 and TAIL else 256
+        x = slice(256 * t, 256 * t + a)
+        if t in YT:
+            V(lambda q: q.transpose(T.YW[:, 32 * t:32 * t + 32], KS[:, 18:50]), r=["KS1", "KS2"], w=["YV%d" % t])
+            dma("y", [(T.yv[gg:gg + 1, x], T.YW[gg // 2 * 32:gg // 2 * 32 + a // 16, 32 * t + gg % 2 * 16:32 * t + gg % 2 * 16 + 16]) for gg in range(8)],
+                ["YV%d" % t], ["yv%d" % t], a // 2, 64)
+        else:
+            move("s", T.YV[:, x], T.IDW[:].indirect(T.LU[:, 18:18 + a // 16]), IDW + ["LU1"], ["YV%d" % t], cgat(a))
+            dma("y", [(T.yv[:, x], T.YV[0:128:16, x])], ["YV%d" % t], ["yv%d" % t], 16, 2 * a)
+        if a < 256:
+            m, z = 256 - a, T.ZR[:, 0:256 - a]
+            for d in (1, 2):
+                move("s", T.KF[:, 128 * d:128 * d + m], T.IDW[:].indirect(T.LU[:, 18 * d + a // 16:18 * d + 16]), IDW + ["LU%d" % d], ["KF%d" % d],
+                     cgat(m), scale=3.0 - 2 * d)
+            PE([lambda q: q.matmul(z, T.cB[0:1, 0:128], T.ones[0:1, 0:m], True, False),
+                lambda q: q.matmul(z, T.BE[:], T.SG[:, 2 * SW + 2 * a + 1:2 * SW + 512:2], False, True)],
+               kb("SG3", a, 256) + ["BE", "cB", "ones"], ["zR"], cmm(m, 2), ["bR"])
+            V(lambda q: q.tensor_tensor(T.KF[:, 0:m], z, T.KF[:, 256:256 + m], A.max), r=["zR", "KF2"], w=["KF0"], c=cv(m), bk=["bR"])
+            V(lambda q: q.tensor_tensor(T.KF[:, 256:256 + m], T.KF[:, 0:m], T.KF[:, 128:128 + m], A.min), r=["KF0", "KF1"], w=["KF2"], c=cv(2 * m))
+            S(lambda q: q.activation(T.YV[:, 512 + a:768], T.KF[:, 256:256 + m], AF.Abs), r=["KF2"], w=["YVf"], c=cv(m))
+            dma("y", [(T.yv[:, 512 + a:768], T.YV[0:128:16, 512 + a:768])], ["YVf"], ["yvf"], 8, 4 * m)
 
-    def keys_free():
-        a, b = CH[HC - 1]
-        m = b - a
-        move("s", T.KF[:, 0:m], T.IX[:, a:b], ["IX"], ["KF0"], cv(m), -1.0, -4096.0 - 1281)
-        for e, d, x in ((1, 1, -8193.0), (2, 2, -12289.0), (3, 2, -1.0)):
-            move("s", (T.KG if e == 3 else T.KF)[:, m * e:m * e + m], T.IDW[:].indirect(T.LU[:, 16 * d + a // 16:16 * d + b // 16]),
-                 ["IDW", "LU%d" % d], ["KF%d" % e], cgat(m), -1.0, x)
-
-    def bind_free():
-        h = HC - 1
-        a, b = CH[h]
-        m = b - a
-        z = T.ZR[:, 0:3 * m]
-        PE([lambda q: q.matmul(z, T.cB[0:1, 0:128], T.ones[0:1, 0:3 * m], True, False)] +
-           [lambda q, e=e: q.matmul(z[:, m * e:m * e + m], T.BE[:], T.SG[:, 256 * e + a:256 * e + b], False, e == 2) for e in range(3)],
-           ["SG%d_%d" % (e, h) for e in (1, 2, 3)] + ["BE", "cB", "ones"], ["zR"], cmm(m, 6), ["bR"])
-        V(lambda q: q.tensor_tensor(T.KG[:, 0:3 * m], z, T.KF[:, 0:3 * m], A.max), r=["zR", "KF0", "KF1", "KF2"], w=["KG"], c=cv(3 * m), bk=["bR"])
-        V(lambda q: q.tensor_tensor(T.KF[:, 0:2 * m], T.KG[:, 0:2 * m], T.KG[:, 2 * m:4 * m], A.min), r=["KG", "KF3"], w=["KF0", "KF1"], c=cv(4 * m))
-        V(lambda q: q.tensor_tensor(T.qI[:, 0:m], T.KF[:, 0:m], T.KF[:, m:2 * m], A.min), r=["KF0", "KF1"], w=["qIf"] + ["qI%d" % x for x in HA], c=cv(2 * m))
-        V(lambda q: q.tensor_scalar(T.TI[:, 0:m], T.qI[:, 0:m], 4095, None, A.bitwise_and), r=["qIf"], w=["TIf"] + ["TI%d" % x for x in HA], c=cv(m))
-        V(lambda q: q.tensor_scalar(T.YV[:, 512 + a:512 + b], T.TI[:, 0:m], -1.0, 4095.0, A.mult, A.add), r=["TIf"], w=["YVf"], c=cv(m))
-        dma("y", [(T.yv[:, 512 + a:512 + b], T.YV[0:128:16, 512 + a:512 + b])], ["YVf"], ["yvf"], 8, 4 * m)
-
-    def outh(t, hs):
-        a, b = CH[hs[0]][0], CH[hs[-1]][1]
-        dma("y", [(T.yh[:, 256 * t + a:256 * t + b], alots(t + 1, 1, a, b))], ek(t + 1, 1, hs), ["yh%d_%d" % (t, a)], 128, 4 * (b - a))
+    def outh(t, a, b):
+        dma("y", [(T.yh[:, 256 * t + a:256 * t + b], PKn(t + 1, a, b))], pk(t + 1, a, b), ["yh%d_%d" % (t, a)], 128, 4 * (b - a))
 
     def dedupe(t):
-        cl, ck = TT(t)[:, 256:LW], tk(t, [HC])
-        move("s", T.RB[:], T.IDW[:].indirect(cl), ["IDW"] + ck, ["RB"], cgat(256), scale=-SQ)
+        cl, ck = TT(t)[:, 256:LW], tk(t, 256, LW)
+        move("s", T.RB[:], T.IDW[:].indirect(cl), IDW + ck, ["RB"], cgat(256), scale=-SQ)
         move("s", T.SV[:, 256 * t:256 * t + 256], win(t).indirect(cl), wkey(t) + ck, ["SV%d" % t], cgat(256))
         for c in range(16):
-            VS("s" if c < SDUP else "v",
-               lambda q, c=c: q.tensor_scalar(T.EQ[:, seg[c]:seg[c + 1]], T.RB[:, 16 * c:256], T.CF[:, c:c + 1], SQ * SQ, A.not_equal, A.mult),
-               lambda q, c=c: q.activation(T.EQ[:, seg[c]:seg[c + 1]], T.RB[:, 16 * c:256], AF.Square, bias=T.CF[:, c:c + 1], scale=-1.0),
-               ["RB", "CF"], ["EQ%d" % c], cv(256 - 16 * c))
-        for x, y in zip(SP, SP[1:]):
-            V(lambda q, x=x, y=y: q.tensor_tensor_scan(T.SC[:, seg[x]:seg[y]], T.EM[:, seg[x]:seg[y]], T.EQ[:, seg[x]:seg[y]], 1.0e16, A.max, A.min),
-              r=["E%s%d" % (k, c) for k in "MQ" for c in range(x, y)], w=["SC%d" % x], c=cv(seg[y] - seg[x], .5))
-        V(lambda q: q.tensor_tensor(T.dE[:], T.SC[:].indirect(T.E16[:, 0:1]), T.DJ[:], A.subtract), r=["SC%d" % x for x in SP[:-1]] + ["E16", "DJ"], w=["dE"], c=cgat(16))
+            o = SEG * (c // CB)
+            eq, rb = T.EQ[:, o + seg[c % CB]:o + seg[c % CB + 1]], T.RB[:, 16 * c:WB * (c // CB + 1)]
+            VS("s", lambda q, c=c, eq=eq, rb=rb: q.tensor_scalar(eq, rb, T.CF[:, c:c + 1], SQ * SQ, A.not_equal, A.mult),
+               lambda q, c=c, eq=eq, rb=rb: q.activation(eq, rb, AF.Square, bias=T.CF[:, c:c + 1], scale=-1.0),
+               ["RB", "CF"], ["EQ%d" % c], cv(WB - 16 * (c % CB)))
+        sk = []
+        for b in range(NB):
+            for x, y in zip(SP, SP[1:]):
+                o = slice(SEG * b + seg[x], SEG * b + seg[y])
+                sk.append("SC%d" % (CB * b + x))
+                V(lambda q, o=o, x=x, y=y: q.tensor_tensor_scan(T.SC[:, o], T.EM[:, seg[x]:seg[y]], T.EQ[:, o], 1.0e16, A.max, A.min),
+                  r=["EM"] + ["EQ%d" % (CB * b + c) for c in range(x, y)], w=sk[-1:], c=cv(seg[y] - seg[x], .5))
+        V(lambda q: q.tensor_tensor(T.dE[:], T.SC[:, 0:NB * SEG].indirect(T.E16[:, 0:1]), T.DJ[:], A.subtract), r=sk + ["E16", "DJ"], w=["dE"], c=cgat(16))
         V(lambda q: q.tensor_tensor(T.dF[:], T.dE[:], T.CF[:], A.min), r=["dE", "CF"], w=["dF"])
         V(lambda q: q.tensor_scalar(T.SL[:, 16 * t:16 * t + 16], T.dF[:], -1.0 / SQ, None, A.mult), r=["dF"], w=["SL%d" % t])
 
@@ -813,117 +1040,110 @@ def rank_program(g, core, T, topo):
             add("n", "n", ("arr" + key, len(common) * len(others)), ["sent" + key], ["got" + key], cfix(0.0))
 
     def update(t):
-        F = T["F%d" % (t + 1)]
-        wk = "win%d" % (t + 1)
-        L = lambda a, b: T.LL[:, 64 * t + 16 * a:64 * t + 16 * b]
+        F = T.F3 if t in SEP else T["F%d" % (t + 1)]
+        wk = "win3" if t in SEP else "win%d" % (t + 1)
+        N, nk = (T.p0, "win4") if t == 2 else (T["F%d" % (t + 1)], "win%d" % (t + 1))
+        nr = ["dump%d" % (t + t // 2)] + ["cq%d_%d" % (t, x) for x in range(NF)] if t in SEP else []
+        L = lambda i: T.LL[:, 64 * t + 16 * i:64 * t + 16 * i + 16]
         lk = "gotSL%d" % t
         cols = lambda i: slice(256 * i, 256 * i + 256)
-        for i in range(2 if UF[t][2] == "p" else 3):
-            move("s", T.sv[:, cols(i)], T.LV[:, 768 * t + 256 * i:768 * t + 256 * i + 256], ["gotSV%d" % t, "INC"], ["sv%d" % i], cv(256), scale=col(INC))
-        fr = [wk, "dump%d" % t, lk] + ["cp%d_%d" % (t, i) for i in range(NF)]
-        for i in range(2):
-            if UF[t][i] == "g":
-                move("s", T.g1[:, cols(i)], F[:].indirect(L(i, i + 1)), fr, ["g1_%d" % i], cgat(256))
-                V(lambda q, i=i: q.tensor_tensor(F[:].indirect(L(i, i + 1)), T.g1[:, cols(i)], T.sv[:, cols(i)], A.add), r=["g1_%d" % i, "sv%d" % i, lk], w=[wk], c=csca(256))
+
+        def scatter(f, i, r, w, row=False):
+            for b in range(NB):
+                o, x = 64 * t + 16 * i + CB * b, slice(256 * i + WB * b, 256 * i + WB * b + WB)
+                V(lambda q, o=o, x=x: f(q, T.LL[:, o:o + CB], x), r=r + [lk], w=[w], c=csca(WB), row=NOWAIT and (row or b > 0))
+        for i in range(3):
+            if UF[t][i] != "p":
+                move("s", T.sv[:, cols(i)], T.LV[:, 768 * t + 256 * i:768 * t + 256 * i + 256], ["gotSV%d" % t, "INC"], ["sv%d" % i], cv(256), scale=col(INC))
+        fr = [wk, "dump%d" % (2 if t in SEP else t), lk] + ["cp%d_%d" % (3 if t in SEP else t, i) for i in range(NF)]
+        zt = T.ZX[:, 0:256]
+        for i in range(3):
+            if UF[t][i] == "p":
+                move("s", T.g1[:, cols(i)], F[:].indirect(L(i)), fr, ["g1_%d" % i], cgat(256))
+                PE([lambda q: q.matmul(zt, T.IDI[:], T.LV[:, 768 * t + 512:768 * t + 768], True, False),
+                    lambda q: q.matmul(zt, T.IDN[:, 0:128], T.g1[:, cols(2)], False, True)], ["IDI", "IDN", "gotSV%d" % t, "g1_2"], ["zX"], cmm(256, 5), ["bX"])
+            elif UF[t][i] == "g":
+                move("s", T.g1[:, cols(i)], F[:].indirect(L(i)), fr, ["g1_%d" % i], cgat(256))
+                scatter(lambda q, o, x: q.tensor_tensor(F[:].indirect(o), T.g1[:, x], T.sv[:, x], A.add), i, ["g1_%d" % i, "sv%d" % i], wk)
             else:
-                V(lambda q, i=i: q.tensor_tensor(T.g1[:, cols(i)], F[:].indirect(L(i, i + 1)), T.sv[:, cols(i)], A.add), r=fr + ["sv%d" % i], w=["g1_%d" % i], c=cgat(256))
-                V(lambda q, i=i: q.tensor_copy(F[:].indirect(L(i, i + 1)), T.g1[:, cols(i)]), r=["g1_%d" % i, lk], w=[wk], c=csca(256))
-        zt = T["Z%d" % HC][:, 0:256]
-        if UF[t][2] == "p":
-            move("s", T.t1[:], F[:].indirect(L(2, 3)), fr, ["g1_2"], cgat(256))
-            PE([lambda q: q.matmul(zt, T.IDI[:], T.LV[:, 768 * t + 512:768 * t + 768], True, False),
-                lambda q: q.matmul(zt, T.IDN[:, 0:128], T.t1[:], False, True)], ["IDI", "IDN", "gotSV%d" % t, "g1_2"], ["t1"], cmm(256, 5), ["bZ%d" % HC])
-            S(lambda q: q.activation(T.r1[:, cols(2)], zt, AF.Relu, bias=col(TOP), scale=-1.0), r=["t1", "TOP"], w=["r12"], c=cv(256), bk=["bZ%d" % HC])
-        else:
-            V(lambda q: q.tensor_tensor(T.t1[:], F[:].indirect(L(2, 3)), T.sv[:, 512:768], A.add), r=fr + ["sv2"], w=["t1", "g1_2"], c=cgat(256))
+                V(lambda q, i=i: q.tensor_tensor(T.g1[:, cols(i)], F[:].indirect(L(i)), T.sv[:, cols(i)], A.add), r=fr + ["sv%d" % i], w=["g1_%d" % i], c=cgat(256))
+                if i < 2:
+                    scatter(lambda q, o, x: q.tensor_copy(F[:].indirect(o), T.g1[:, x]), i, ["g1_%d" % i], wk)
 
         for i in range(3):
-            src, r, c = (T.t1[:], ["t1"], cv(256)) if i == 2 else (F[:].indirect(L(i, i + 1)), [wk, lk], cgat(256)) \
-                if UF[t][i] == "g" else (T.g1[:, cols(i)], ["g1_%d" % i], cv(256))
+            src, r, c = (F[:].indirect(L(i)), [wk, lk], cgat(256)) if UF[t][i] == "g" else (T.g1[:, cols(i)], ["g1_%d" % i], cv(256))
+            bk = []
+            if UF[t][i] == "p":
+                src, r, bk = zt, ["zX"], ["bX"]
             if FLS[t][i] == "v":
-                V(lambda q, i=i, src=src: q.tensor_scalar(T.i1[:, cols(i)], src, -0.4921875, 255.0, A.add, A.min), r=r, w=["i1%d" % i], c=c)
+                V(lambda q, i=i, src=src: q.tensor_scalar(T.i1[:, cols(i)], src, -0.4921875, 255.0, A.add, A.min), r=r, w=["i1%d" % i], c=c, bk=bk)
             else:
-                if UF[t][i] != "p":
-                    S(lambda q, i=i, src=src: q.activation(T.r1[:, cols(i)], src, AF.Relu, bias=col(TOP), scale=-1.0), r=r + ["TOP"], w=["r1%d" % i], c=c)
+                S(lambda q, i=i, src=src: q.activation(T.r1[:, cols(i)], src, AF.Relu, bias=col(TOP), scale=-1.0), r=r + ["TOP"], w=["r1%d" % i], c=c, bk=bk)
                 S(lambda q, i=i: q.activation(T.r2[:, cols(i)], T.r1[:, cols(i)], AF.Copy, bias=MAGIC + 255, scale=-1.0), r=["r1%d" % i], w=["i1%d" % i], c=cv(256))
-                if t == 2 and LAST:
+                if t == 2:
                     S(lambda q, i=i: q.activation(T.r2[:, cols(i)], T.r2[:, cols(i)], AF.Copy, bias=-MAGIC), w=["i1%d" % i], c=cv(256))
         for i in range(3):
-            if t == 2 and LAST:
-                V(lambda q, i=i: q.tensor_copy(T.p0[:].indirect(L(i, i + 1)), (T.i1 if FLS[t][i] == "v" else T.r2)[:, cols(i)]),
-                  r=["i1%d" % i, lk, "dump3"] + ["cp3_%d" % x for x in range(NF)], w=["win4"], c=csca(256))
-            elif FLS[t][i] == "v":
-                V(lambda q, i=i: q.tensor_copy(F[:].indirect(L(i, i + 1)), T.i1[:, cols(i)]), r=["i1%d" % i, lk], w=[wk], c=csca(256))
+            src = T.i1 if FLS[t][i] == "v" else T.r2
+            if t == 2 or FLS[t][i] == "v":
+                scatter(lambda q, o, x, src=src: q.tensor_copy(N[:].indirect(o), src[:, x]), i, ["i1%d" % i] + nr, nk, i > 0)
             else:
-                V(lambda q, i=i: q.tensor_scalar(F[:].indirect(L(i, i + 1)), T.r2[:, cols(i)], 1.0, -MAGIC, A.mult, A.add), r=["i1%d" % i, lk], w=[wk], c=csca(256))
+                scatter(lambda q, o, x: q.tensor_scalar(N[:].indirect(o), T.r2[:, x], 1.0, -MAGIC, A.mult, A.add), i, ["i1%d" % i] + nr, nk, i > 0)
 
-    hot[0] = HOT[0]
     conv(1)
     parents(1)
-    first(2)
     conv(2)
-    first(3)
-    hot[0] = 0.0
-    package(0, 2)
-    package(0, 3)
+    for e in (2, 3):
+        package(0, e)
+        first(e) if FIRST else clist(0, e)
     for t in range(3):
-        for i in range(NF):
-            w = 4096 // NF
-            G(lambda q, t=t, i=i, w=w: q.affine_select(T["F%d" % (t + 1)][:, w * i:w * i + w], win(t)[:, w * i:w * i + w], [[0, w]], A.is_equal, 0.0, 0, 0),
-              r=wkey(t), w=["cp%d_%d" % (t, i)], c=(0, 2 * w, 0, 0, 0, 0.17))
-        for i in range(NF if t == 2 and LAST else 0):
-            add("g", "c", [lambda q, i=i, w=w: q.affine_select(T.p0[:, w * i:w * i + w], T.F2[:, w * i:w * i + w], [[0, w]], A.is_equal, 0.0, 0, 0)],
-                wkey(2), ["cp3_%d" % i] + (wkey(0) if i == 0 else []), (0, 2 * w, 0, 0, 0, 0.17))
-            if i:
-                ops[-1]["order"].append(len(ops) - 2)
+        w = 4096 // NF
+        new = T.p0 if t == 2 else T["F%d" % (t + 1)]
+        for dst, key, old in ((T.F3, "cp3", ["win3"]), (new, "cq%d" % t, wkey(0) if t == 2 else [])) if t in SEP else ((new, "cp%d" % t, []),):
+            for i in range(NF):
+                G(lambda q, t=t, i=i, dst=dst: q.affine_select(dst[:, w * i:w * i + w], win(t)[:, w * i:w * i + w], [[0, w]], A.is_equal, 0.0, 0, 0),
+                  r=wkey(t), w=["%s_%d" % (key, i)] + (old if i == 0 else []), c=cgp(w, 0.17))
+                if i and old:
+                    ops[-1]["order"].append(len(ops) - 2)
+        tag[0] = "parents%d" % t
         if t < 2:
             parents(2)
             conv(3)
         keys(t)
-        if t == 2 and FREE:
-            keys_free()
         for e in (1, 2, 3):
-            for i in range(NP):
-                hot[0] = 0.0 if i else HOT[t]
-                gy(t, e, i)
-            for h in HA:
-                hot[0] = HOT[t] if h == HC else 0.0
+            for a, b in YP[t]:
+                tag[0] = "y%d%d_%d" % (t, e, a // 96)
+                gy(t, e, a, b)
+            for h, (a, b) in enumerate(CH[t]):
+                tag[0] = "x%d%d_%d" % (t, e, h)
                 diff(t, e, h)
-                for i in range(NP):
-                    if chunk(PCS[i][0]) == h:
-                        gx(t, e, i)
+                for x, y in split(a, b, XW[t]):
+                    gx(t, e, x, y)
                 tops(t, e, h)
+        tag[0] = "claims%d" % t
         dedupe(t)
         send(t)
+        tag[0] = "prices%d" % t
         update(t)
-        hot[0] = 0.0
-        if t == 2 and LAST:
+        if t == 2:
             dma("y", [(T.yp[:], T.p0[:, 0:4096])], ["win4"], ["yp"], 128, 8192)
-        elif t == 2:
-            dma("g", [(T.yp[:], T.F3[:, 0:4096])], ["win3"], ["yp"], 128, 8192)
-        if t < 2:
-            clist(t + 1, 1)
-            for i in range(1, NP):
-                gm(t, i)
-            if QC:
-                tclaim(t)
-            for hs in TG:
-                tnew(t, [h for h in hs if h != HC or not QC])
-            outh(t, list(HS))
+            for a, b in OH:
+                outh(t, a, b)
         else:
-            for h in HS:
-                outh(t, [h])
-        hot[0] = HOT[t + 1] if t < 2 else 0.0
+            clist(t + 1, 1)
+            for a, b in MP:
+                tag[0] = "max%d_%d" % (t, a)
+                gm(t, a, b)
+            for a, b in TG[t]:
+                tag[0] = "next%d_%d" % (t, a)
+                tnew(t, a, b)
+            outh(t, 0, 256)
+        tag[0] = "bind%d" % t
         bind(t)
-        if t == 2 and FREE:
-            bind_free()
-        if t < 2:
-            package(t + 1, 2)
-            package(t + 1, 3)
-            clist(t + 1, 2)
-            clist(t + 1, 3)
-        hot[0] = 0.0
         outv(t)
+        if t < 2:
+            for e in (2, 3):
+                package(t + 1, e)
+                clist(t + 1, e)
 
     order = plan(ops)
     total, snap, tok = {}, {}, {}

@@ -11,34 +11,49 @@ YP = [[(256, 272), (0, 64), (64, 128), (128, 192), (192, 256)]] * 2 + \
      [[(256, 272), (0, 48), (48, 96), (96, 144), (144, 192), (192, 256)]]
 MP = [(0, 64), (64, 128), (128, 192), (192, 256)]
 TG = [[(0, 96), (96, 192), (192, 272)]] * 2
-SR = [(2, 3, 48), (2, 3, 96)]
+SR = []
+LAST = True
+NY = 1
+PS = 4
+KSUM = True
+LATE = False
+UPK = (2.0, 2.0, 4.0)
+XC = (0, 1, 2)
+GV = "oms"
+OS = 2
+OV = 4
+RBP = 1
+PKI = 1
+VM = 1
+XS3 = 1
+XONE = False
 NB = 2
 SP = (0, 3, 8)
 SCAN = True
-A16 = False
+A16 = 3
 NOWAIT = False
 YT = (0, 1)
 TAIL = True
 PKS = ()
 SEP = (2,)
 UCOPY = True
-FIRST = True
-OH = [(0, 96), (96, 256)]
+FIRST = (2, 3)
+OH = [(0, 96), (96, 192), (192, 256)]
 BIG = 32768.0
 SQ = 8192.0
 XB = 1.2
 UF = ("ggt", "ggt", "ttt")
-FLS = ("sss", "sss", "ssv")
+FLS = ("svv", "svv", "svv")
 PCALL = 0.010
 REACH = 0.35
-LOADS = ["win0a", "pkA", "wtI", "VT", "win0", "pkC", "pkJ", "TI", "pkI", "incI"]
+LOADS = ["win0a", "VT", "pkA", "wtI", "win0", "pkC", "TIa", "pkJ", "TI", "pkI", "incI"]
 LA = 96
 L0 = [(0, LA, ["pkA"]), (LA, 256, ["pkJ"]), (256, LW, ["pkC"])]
 LEAN = 10.0
 SLOPES = [3.0, 8.0, 20.0, 50.0]
 SEED = 4
-DUE = (9.0, 9.5, 100.0, 0.2)
-PA = 2048
+DUE = (9.0, 9.2, 97.0, 0.2)
+PA = 1024
 NF = 8
 MAGIC = 1.5 * 2 ** 23
 SW = 576
@@ -47,10 +62,11 @@ SCRATCH = {
     "p0": ("sbuf", [128, 4352], "bfloat16"),
     "F1": ("sbuf", [128, 4352], "float32"),
     "F2": ("sbuf", [128, 4352], "float32"),
-    "F3": ("sbuf", [128, 4352], "float32"),
-    "pkI": ("sbuf", [128, 768], "int32"),
-    "pkJ": ("sbuf", [128, LW], "int32"),
+    "PI": ("sbuf", [128, 1280], "int32"),
     "PK": ("sbuf", [128, 1792], "float32"),
+    "SELT": ("sbuf", [128, 2048], "bfloat16"),
+    "SEL1": ("sbuf", [128, 2048], "bfloat16"),
+    "big": ("sbuf", [128, 256], "bfloat16"),
     "VT": ("sbuf", [128, 1024], "int32"),
     "small": ("sbuf", [128, 8], "int32"),
     "slI": ("sbuf", [128, 4], "int32"),
@@ -107,21 +123,22 @@ SCRATCH = {
     "CF": ("sbuf", [128, 16], "float32"),
     "IDW": ("sbuf", [128, 4096], "float32"),
     "RB": ("sbuf", [128, 256], "float32"),
-    "EI": ("sbuf", [128, 2176], "bfloat16"),
-    "EQ": ("sbuf", [128, 2176], "bfloat16"),
-    "EM": ("sbuf", [128, 2176], "bfloat16"),
-    "SC": ("sbuf", [128, 2176], "bfloat16"),
+    "EI": ("sbuf", [128, 576], "bfloat16"),
+    "EQ": ("sbuf", [128, 1152], "bfloat16"),
+    "EM": ("sbuf", [128, 576], "bfloat16"),
+    "SC": ("sbuf", [128, 1152], "bfloat16"),
     "E16": ("sbuf", [128, 2], "uint16"),
     "DJ": ("sbuf", [128, 16], "float32"),
     "DJt": ("sbuf", [128, 16], "float32"),
     "dE": ("sbuf", [128, 16], "float32"),
     "dF": ("sbuf", [128, 16], "float32"),
-    "SV": ("sbuf", [128, 768], "bfloat16"),
+    "SV": ("sbuf", [128, 3 * 768], "bfloat16"),
     "SL": ("sbuf", [128, 48], "uint16"),
-    "LV": ("sbuf", [128, 3 * 768], "bfloat16"),
+    "LV": ("sbuf", [128, 3 * 1536], "bfloat16"),
     "LL": ("sbuf", [128, 3 * 64], "uint16"),
-    "sv": ("sbuf", [128, 768], "float32"),
-    "g1": ("sbuf", [128, 768], "float32"),
+    "LR": ("sbuf", [128, 3 * 64], "uint16"),
+    "O": ("sbuf", [128, 4352], "bfloat16"),
+    "pg": ("sbuf", [128, 768], "bfloat16"),
     "i1": ("sbuf", [128, 768], "int32"),
     "r1": ("sbuf", [128, 768], "float32"),
     "r2": ("sbuf", [128, 768], "float32"),
@@ -135,11 +152,11 @@ SCRATCH = {
     "ZR": ("psum", [128, 512], "float32"),
 }
 NDMA = 70
-SEMAPHORES = ["cv", "cs", "cp", "cg", "lsem"] + ["arrS%s%d" % (x, t) for x in "VL" for t in range(3)] + ["d%d" % i for i in range(NDMA)]
+SEMAPHORES = ["cv", "cs", "cp", "cg", "lsem"] + ["%s%d" % (x, t) for x in ("arrSV", "arrSL", "arrR", "arrX", "arrZ", "lr") for t in range(3)] + ["d%d" % i for i in range(NDMA)]
 
 MODELS = [
     (0.02, 0.83e-3, 1.25e-3, 3.0e-3, 0.83e-3, 0.14, 2.0, 3.0, 0.035, 0.06e-3),
-    (0.03, 0.87e-3, 1.02e-3, 1.9e-3, 0.87e-3, 0.16, 2.0, 3.0, 0.03, 0.05e-3),
+    (0.015, 0.84e-3, 0.88e-3, 1.6e-3, 0.84e-3, 0.13, 2.0, 3.0, 0.035, 0.055e-3),
     (0.03, 1.10e-3, 1.35e-3, 5.2e-3, 0.90e-3, 0.15, 2.2, 3.5, 0.04, 0.08e-3),
     (0.02, 1.00e-3, 1.95e-3, 2.2e-3, 0.92e-3, 0.22, 2.4, 2.5, 0.05, 0.04e-3),
     (0.03, 1.20e-3, 2.10e-3, 5.0e-3, 1.10e-3, 0.20, 2.2, 4.0, 0.04, 0.07e-3),
@@ -147,7 +164,7 @@ MODELS = [
 TRIES, STARTS, TURN, FLIP = 15, 1, True, 9.0
 STEPS = ((1000, 1),)
 BACK, FAR, WIDE, TOP, KEEP, JIT = 1500, 8, 40, 4, 20, 0.002
-ROUNDS, SPAN, SHORT, SHAKE, HEAT, HOME = 900, 60, 120, (8.0, 0.3, 1.0), 0.006, 0.3
+ROUNDS, SPAN, SHORT, SHAKE, HEAT, HOME = 1400, 100, 150, (12.0, 0.2, 1.0), 0.01, 0.3
 
 
 def cv(n, per=1.0):
@@ -675,7 +692,7 @@ def rank_program(g, core, T, topo):
         add(e, "d", pairs, r, w, cfix((0.6 if e == "g" else 0.06) * len(pairs)), up, rows=rows / 16, nbytes=rows * rb / 16)
         ops[-1]["order"] += before
 
-    PF, RF, GF, CQ, BQ, RQ, INC, W2, W3, SLF, HR, HX, HD, C14, C15, TOP, R0 = 0, 1, 2, 3, 4, 5, 6, 7, 8, 9, 12, 13, 14, 15, 16, 17, 18
+    PF, RF, GF, CQ, BQ, RQ, INC, W2, W3, SLF, HR, HX, HD, C14, C15, TOP, R0, VB, VC = 0, 1, 2, 3, 4, 5, 6, 7, 8, 9, 12, 13, 14, 15, 16, 17, 18, 20, 21
     sm = T.sm
     col = lambda c: sm[:, c:c + 1]
     TT = lambda t: T["TT%d" % (t % 2)]
@@ -700,16 +717,17 @@ def rank_program(g, core, T, topo):
 
     add("v", "c", [lambda q: q.memset(T.VT[:], 0)], [], ["VT"], cv(1024), up=1650)
     clear = len(ops) - 1
+    pkJ = lambda a, b: T.PI[:, 768 + a:768 + b]
     loads = {
         "win0a": ([(T.p0[:, 0:PA], T.price[:, 0:PA])], ["win0a"], 128, 2 * PA),
-        "VT": ([(T.VT[0:128:16, :], T.prev[:])] + [(T.VT[1:128:16, :], T.packs[0:128:16, :])] * FIRST, ["VT"], 64 + 64 * FIRST, 512),
-        "pkA": ([(T.pkJ[:, 0:LA], T.packs[:, 768:768 + LA]), (T.slI[:, 0:3], T.slack[:]), (T.TI[:, 0:LA], T.lots[:, 0:LA])],
-                ["pkA", "slI"] + kb("TI", 0, LA), 384, 8 * LA // 3 + 4),
-        "pkJ": ([(T.pkJ[:, LA:256], T.packs[:, 768 + LA:1024])], ["pkJ"], 128, 1024 - 4 * LA),
-        "pkC": ([(T.pkJ[:, 256:LW], T.packs[0:128:16, 768:1024]), (T.TI[:, 256:LW], T.lots[0:128:16, :])], ["pkC"] + kb("TI", 256, LW), 256, 64),
+        "VT": ([(T.VT[0:128:16, :], T.prev[:])] + [(T.VT[1:128:16, :], T.packs[0:128:16, :])], ["VT"], 128, 512),
+        "pkA": ([(pkJ(0, LA), T.packs[:, 768:768 + LA]), (T.slI[:, 0:3], T.slack[:])], ["pkA", "slI"], 256, 2 * LA + 6),
+        "TIa": ([(T.TI[:, 0:LA], T.lots[:, 0:LA])], ["TIa"] + kb("TI", 0, LA), 128, 4 * LA),
+        "pkJ": ([(pkJ(LA, 256), T.packs[:, 768 + LA:1024])], ["pkJ"], 128, 1024 - 4 * LA),
+        "pkC": ([(pkJ(256, LW), T.packs[0:128:16, 768:1024]), (T.TI[:, 256:LW], T.lots[0:128:16, :])], ["pkC"] + kb("TI", 256, LW), 256, 64),
         "win0": ([(T.p0[:, PA:4096], T.price[:, PA:4096])], ["win0"], 128, 8192 - 2 * PA),
         "TI": ([(T.TI[:, LA:256], T.lots[:, LA:256])], ["TI"] + kb("TI", LA, 256), 128, 1024 - 4 * LA),
-        "pkI": ([(T.pkI[:], T.packs[:, 0:768])], ["pkI"], 128, 3072),
+        "pkI": ([(T.PI[:, 0:768], T.packs[:, 0:768])], ["pkI"], 128, 3072),
         "wtI": ([(T.small[:, 4:5], T.wt[:])], ["wtI"], 128, 4),
         "incI": ([(T.small[:, 0:1], T.inc[:])], ["incI"], 128, 4),
     }
@@ -726,17 +744,31 @@ def rank_program(g, core, T, topo):
     G(lambda q: q.iota(T.i16[:, 0:16], [[16, 16]], 0, 0, **fl), w=["i16"], up=100)
     G(lambda q: q.iota(T.i16[:, 16:32], [[0, NB], [16, CB]], 0, 0, **fl), w=["j16"], up=100)
     G(lambda q: q.iota(T.IXG[:], [[1, 8], [0, 16]], 0, 0, **fl), w=["IXG"], c=cgp(128), up=100)
-    G(lambda q: q.iota(sm[:, HR:HX + 1], [[-9 * 512, 2]], 17 * 256, 0, **fl), w=["HR", "HX"], up=100)
+    G(lambda q: q.iota(sm[:, HR:HX + 1], [[8 * 512, 2]], -17 * 256, 0, **fl), w=["HR", "HX"], up=100)
     G(lambda q: q.iota(col(HD), [[0, 1]], 512 * WB - 768, 0, **fl), w=["HD"], up=100)
     G(lambda q: q.iota(T.KS[:], [[0, 72]], 0, 0, **fl), w=["KS%d" % d for d in range(4)], c=cgp(72), up=100)
-    G(lambda q: q.iota(T.KO[:], [[-4096, 2], [0, 18]], 0, 0, **fl), w=["KO"])
-    G(lambda q: q.iota(T.ones[:], [[0, 1024]], 1, 0, **fl), w=["ones"], c=cgp(1024))
-    G(lambda q: q.affine_select(T.MK[:], T.ones[:], [[0, 64], [1, 16]], A.not_equal, 0.0, 0, 0), r=["ones"], w=["MK"], c=cgp(1024, 0.17))
-    G(lambda q: q.iota(T.cB[:, 0:256], [[0, 256]], 0, 0, **fl), w=["cB"], c=cgp(256), up=60)
-    for x in range(2):
-        G(lambda q, x=x: q.iota(T.IDW[:, 2048 * x:2048 * x + 2048], [[1, 2048]], 2048 * x, 0, **fl), w=["IDW%d" % x], c=cgp(2048))
-    IDW = ["IDW0", "IDW1"]
-    for t in range(3):
+    G(lambda q: q.iota(T.KO[:], [[4096, 2], [0, 18]], 0, 0, **fl), w=["KO"])
+    if "o" in GV:
+        V(lambda q: q.memset(T.ones[:], 1.0), w=["ones"], c=cv(512))
+    else:
+        G(lambda q: q.iota(T.ones[:], [[0, 1024]], 1, 0, **fl), w=["ones"], c=cgp(1024))
+    if "m" in GV:
+        V(lambda q: q.memset(T.MK[:], 1.0), w=["MK"], c=cv(512))
+        V(lambda q: q.memset(T.MK[:, 0:1024:16], 0.0), w=["MK"])
+    else:
+        G(lambda q: q.affine_select(T.MK[:], T.ones[:], [[0, 64], [1, 16]], A.not_equal, 0.0, 0, 0), r=["ones"], w=["MK"], c=cgp(1024, 0.17))
+    G(lambda q: q.iota(T.cB[:], [[0, 384]], 0, 0, **fl), w=["cB"], c=cgp(384), up=60)
+    NI = 3 if RBP else 8
+    for x in range(NI):
+        G(lambda q, x=x: q.iota(T.IDW[:, 512 * x:512 * x + 512], [[1, 512]], 512 * x, 0, **fl), w=["IDW%d" % x], c=cgp(512))
+    IDW = ["IDW%d" % x for x in range(NI)]
+    idw = T.IDW[:, 0:512 * NI]
+    for t in (1, 2):
+        V(lambda q, t=t: q.memset(T.big[:, WB * t - WB:WB * t], 2.0 ** (16 * t)), w=["big%d" % t])
+    for x in range(2 * RBP):
+        G(lambda q, x=x: q.affine_select(T.SELT[:, 1024 * x:1024 * x + 1024], T.ones[:], [[-1, 8], [-16, 8], [0, 16]], A.is_equal, 0.0, -8 * x, 1),
+          r=["ones"], w=["SELT%d" % x], c=cgp(1024, 0.17))
+    for t in range(2):
         G(lambda q, t=t: q.iota(T["F%d" % (t + 1)][:, 4096:4352], [[0, 256]], 0, 0, **fl), w=["dump%d" % t], c=cgp(256))
     G(lambda q: q.iota(T.p0[:, 4096:4352], [[0, 256]], 0, 0, **fl), w=["dump3"], c=cgp(256))
     for c in range(CB):
@@ -746,8 +778,11 @@ def rank_program(g, core, T, topo):
     ops[-1]["order"].append(clear)
     V(lambda q: q.memset(T.one16[:], 1.0), w=["one16"])
     for e in (1, 2, 3):
-        G(lambda q, e=e: q.iota(T.SG[:, SW * e - SW:SW * e], [[0, SW]], 0, 0, **fl), w=kb("SG%d" % e, 0, LW), c=cgp(SW), up=50)
-    for ap, x in ((T.cB[0:1, 0:128], -15.5 * BIG), (T.cB[0:1, 128:256], 33.0), (T.cB[32:33, 128:256], 192.0 * 2048), (T.cB[0:1, 256:384], 16 * BIG)):
+        if "s" in GV:
+            V(lambda q, e=e: q.memset(T.SG[:, SW * e - SW:SW * e], 0.0), w=kb("SG%d" % e, 0, LW), c=cv(SW, .5))
+        else:
+            G(lambda q, e=e: q.iota(T.SG[:, SW * e - SW:SW * e], [[0, SW]], 0, 0, **fl), w=kb("SG%d" % e, 0, LW), c=cgp(SW), up=50)
+    for ap, x in ((T.cB[0:1, 0:128], -0.5 * BIG), (T.cB[0:1, 128:256], 33.0), (T.cB[32:33, 128:256], 192.0 * 2048), (T.cB[32:33, 256:384], 2048.0)):
         V(lambda q, ap=ap, x=x: q.memset(ap, x), w=["cB"])
     V(lambda q: q.tensor_copy(col(PF), T.pI[:, 0:1]), r=["pI"], w=["PF"])
     for x, (y, op) in enumerate(((15, A.bitwise_and), (4, A.logical_shift_right), (CB - 1, A.bitwise_and))):
@@ -763,13 +798,20 @@ def rank_program(g, core, T, topo):
     SELK = ["SELK"] + ["SELK%d" % gg for gg in range(8)]
     V(lambda q: q.tensor_copy(sm[:, SLF:SLF + 3], T.slI[:, 0:3]), r=["slI"], w=["SLF"])
     for a, b, k in L0:
-        V(lambda q, a=a, b=b: q.tensor_copy(T.AL[:, a:b], T.pkJ[:, a:b]), r=k, w=ak(0, 1, a, b), c=cv(b - a))
+        V(lambda q, a=a, b=b: q.tensor_copy(T.AL[:, a:b], pkJ(a, b)), r=k, w=ak(0, 1, a, b), c=cv(b - a))
         V(lambda q, a=a, b=b: q.tensor_copy(T.TT0[:, a:b], T.TI[:, a:b]), r=kb("TI", a, b), w=tk(0, a, b), c=cv(b - a))
         V(lambda q, a=a, b=b: q.tensor_scalar(TH(0, a, b), T.TT0[:, a:b], -2048.0, None, A.add), r=tk(0, a, b), w=fk(0, a, b), c=cv(b - a, .5))
         V(lambda q, a=a, b=b: q.tensor_scalar(TH(1, a, b), T.AL[:, a:b], -2048.0, None, A.add), r=ak(0, 1, a, b), w=fk(1, a, b), c=cv(b - a, .5))
-    V(lambda q: q.tensor_copy(PKn(0, 0, 256), T.pkJ[:, 0:256]), r=["pkA", "pkJ"], w=pk(0, 0, 256), c=cv(256))
-    V(lambda q: q.tensor_copy(T.PK[:, 0:768], T.pkI[:]), r=["pkI"], w=kb("PK", 0, 768), c=cv(768))
+    if not PKI:
+        V(lambda q: q.tensor_copy(PKn(0, 0, 256), pkJ(0, 256)), r=["pkA", "pkJ"], w=pk(0, 0, 256), c=cv(256))
+        V(lambda q: q.tensor_copy(T.PK[:, 0:768], T.PI[:, 0:768]), r=["pkI"], w=kb("PK", 0, 768), c=cv(768))
     V(lambda q: q.tensor_scalar(sm[:, R0:R0 + 2], T.row8[:, 0:2], col(RF), None, A.is_equal), r=["row8", "RF"], w=["R0"])
+    if VM:
+        V(lambda q: q.tensor_scalar(col(VB), col(R0 + 1), -2048.0, None, A.mult), r=["R0"], w=["VB"])
+        V(lambda q: q.tensor_scalar(col(VC), col(R0 + 1), 2.0 ** -13, col(R0), A.mult, A.add), r=["R0"], w=["VC"])
+        for i in range(2):
+            S(lambda q, i=i: q.activation(T.SEL1[:, 1024 * i:1024 * i + 1024], T.SELK[:, 1024 * i:1024 * i + 1024], AF.Copy, scale=col(R0 + 1)),
+              r=SELK + ["R0"], w=["SEL1%d" % i], c=cv(1024))
     V(lambda q: q.tensor_scalar(T.VH[:], T.VT[:, 768:1024], col(R0), None, A.mult), r=["VT", "R0"], w=["VH"], c=cv(256))
     V(lambda q: q.memset(col(TOP), 255.4921875), w=["TOP"])
     V(lambda q: q.tensor_scalar(T.IDN[:, 0:128], T.IX[:], col(PF), None, A.is_equal), r=["IX", "PF"], w=["IDN"], c=cv(128))
@@ -782,12 +824,13 @@ def rank_program(g, core, T, topo):
     move("s", col(C14), col(CQ), ["RF"], ["c14"], cv(1), -8.0, WB - 8.0)
     move("s", col(C15), col(BQ), ["RF"], ["c15"], cv(1), float(SEG), WB - 1.0)
     V(lambda q: q.tensor_scalar(T.E16[:, 0:1], col(C14), col(CQ), col(C15), A.mult, A.add), r=["c14", "c15", "RF"], w=["E16"])
-    move("s", T.DJt[:], T.L1c[:, 0:16], ["L1c"], ["DJt"], cv(1), SQ, 4096.0 * SQ)
+    move("s", T.DJt[:], T.L1c[:, 0:16], ["L1c"], ["DJt"], cv(1), SQ, 2048.0 * SQ + SQ * SQ)
     add("s", "c", [lambda q: q.activation(T.dF[:], T.L1c[:, 16:32], AF.Sigmoid, bias=col(HD), scale=-512.0)], ["L1c", "HD"], ["dF"],
         (1, 64, 0, 0, 0, 1.3), up=90)
-    V(lambda q: q.tensor_tensor(T.DJ[:], T.dF[:], T.DJt[:], A.mult), r=["dF", "DJt"], w=["DJ"])
+    V(lambda q: q.tensor_tensor(T.dE[:], T.dF[:], T.DJt[:], A.mult), r=["dF", "DJt"], w=["dE"])
+    move("s", T.DJ[:], T.dE[:], ["dE"], ["DJ"], cv(1), bias=-SQ * SQ)
     V(lambda q: q.tensor_scalar(col(INC), T.small[:, 0:1], 1.0 / 64, None, A.mult), r=["incI"], w=["INC"])
-    if any("p" in x for x in UF):
+    if True:
         move("s", T.IDI[:], T.IDN[:, 0:128], ["IDN", "INC"], ["IDI"], cv(128), scale=col(INC))
     V(lambda q: q.tensor_scalar(col(W2), T.small[:, 4:5], 2.0, None, A.mult), r=["wtI"], w=["W2"])
     V(lambda q: q.tensor_scalar(col(W3), T.small[:, 4:5], 2.0 / BIG, None, A.mult), r=["wtI"], w=["W3"])
@@ -806,15 +849,27 @@ def rank_program(g, core, T, topo):
         PE([lambda q, k=k: q.matmul(z, T.SELK[:, 128 * k:128 * k + 128], T.VH[:, k:256:16], k == 0, k == 15)
             for k in range(16)], ["VH"] + SELK, ["zc"], cmm(16, 16), ["bC"])
         if d < 3:
-            V(lambda q: q.tensor_scalar(LU(d), z, 1.0 / BIG, None, A.mult), r=["zc"], w=["LU%d" % d], bk=["bC"])
-        move("s", KS[:, 18 * d:18 * d + 16], z, ["zc"], ["KS%d" % d], cv(1), 1.0 / BIG, 4096.0 * (1 - d), ["bC"])
+            V(lambda q: q.tensor_scalar(LU(d), z, 1.0 / BIG, 0.25, A.mult, A.add), r=["zc"], w=["LU%d" % d], bk=["bC"])
+        move("s", KS[:, 18 * d:18 * d + 16], z, ["zc"], ["KS%d" % d], cv(1), 1.0 / BIG, 4096.0 * (d - 1), ["bC"])
 
     def parents(d):
+        if VM:
+            return V(lambda q: q.tensor_scalar(T.VH[:], T.VT[:].indirect(LU(d)), col(VB), col(VC), A.add, A.mult),
+                     r=["VT", "VB", "VC", "LU%d" % d], w=["VH"], c=cgat(256))
         V(lambda q: q.tensor_scalar(T.VH[:], T.VT[:].indirect(LU(d)), col(R0), None, A.mult), r=["VT", "R0", "LU%d" % d], w=["VH"], c=cgat(256))
 
     def first(e):
         z = T.ZX[:, 0:16]
         lots, lk = aless(0, e, 256, LW)
+        if VM:
+            PE([lambda q, k=k: q.matmul(z, T.SEL1[:, 128 * k:128 * k + 128], T.VH[:, 16 * k:16 * k + 16], k == 0, k == 15)
+                for k in range(16)], ["VH", "SEL10", "SEL11"], ["zX"], cmm(16, 16), ["bX"])
+            V(lambda q: q.tensor_scalar(alist(0, e, 256, LW), z, 8192.0 / BIG, 2048.0, A.mult, A.add), r=["zX"], w=ak(0, e, 256, LW), bk=["bX"])
+            if A16:
+                V(lambda q: q.tensor_scalar(lots, z, 8192.0 / BIG, None, A.mult), r=["zX"], w=lk, bk=["bX"])
+            else:
+                move("s", lots, z, ["zX"], lk, cv(1), scale=8192.0 / BIG, bk=["bX"])
+            return
         V(lambda q: q.tensor_scalar(T.VG[:], T.VT[:].indirect(LU(e - 1)), -2048.0, col(R0 + 1), A.add, A.mult),
           r=["VT", "R0", "LU%d" % (e - 1)], w=["VG"], c=cgat(256))
         PE([lambda q, k=k: q.matmul(z, T.SELK[:, 128 * k:128 * k + 128], T.VG[:, 16 * k:16 * k + 16], k == 0, k == 15)
@@ -824,13 +879,21 @@ def rank_program(g, core, T, topo):
 
     def keys(t):
         c = 18 if t == 2 else 36
-        move("s", KS[:, 0:16], T.L1c[:, 0:16], ["L1c"], ["KS0"], cv(1), bias=4096.0 + 768 + 256 * t)
-        move("s", KM[:, 3, 0:c], KS[:, 36:36 + c], ["KS%d" % d for d in range(2, 2 + c // 18)], ["KM3"], cv(1), bias=3 * 4096.0)
+        move("s", KS[:, 0:16], T.L1c[:, 0:16], ["L1c"], ["KS0"], cv(1), bias=-4096.0 + 768 + 256 * t)
+        move("s", KM[:, 3, 0:c], KS[:, 36:36 + c], ["KS%d" % d for d in range(2, 2 + c // 18)], ["KM3"], cv(1), bias=-3 * 4096.0)
 
     def package(t, e):
         src, r = T.PK[:, 0:1024 + 256 * t].indirect(LU(e - 1)), kb("PK", 0, 1024 + 256 * t) + ["LU%d" % (e - 1)]
+        if PKI:
+            own = (t, e) == (2, 2)
+            src, r = T.PI[:, 0:1024 + 256 * own].indirect(LU(e - 1)), ["pkI", "pkA", "pkJ", "LU%d" % (e - 1)] + kb("PI", 0, 256 * own)
         lots, lk = aless(t, e, 0, 256)
-        if A16:
+        if A16 == 3:
+            wide, wk = T.AE[:, LW * (e - 2):LW * (e - 2) + 256], ["AF%d" % e]
+            move("s", wide, src, r, wk, cgat(256), bias=-2048.0)
+            V(lambda q: q.tensor_scalar(alist(t, e, 0, 256), wide, 2048.0, None, A.add), r=wk, w=ak(t, e, 0, 256), c=cv(256))
+            G(lambda q: q.affine_select(lots, wide, [[0, 256]], A.is_equal, 0.0, 0, 0), r=wk, w=lk, c=cgp(256, 0.17))
+        elif A16:
             if A16 == 2:
                 move("s", T.AE[:, 0:256], src, r, ["AF"], cgat(256))
                 V(lambda q: q.tensor_copy(alist(t, e, 0, 256), T.AE[:, 0:256]), r=["AF"], w=ak(t, e, 0, 256), c=cv(256))
@@ -842,7 +905,7 @@ def rank_program(g, core, T, topo):
             V(lambda q: q.tensor_scalar(alist(t, e, 0, 256), lots, 2048.0, None, A.add), r=lk, w=ak(t, e, 0, 256), c=cv(256))
 
     def clist(t, e):
-        dma("y", [(alist(t, e, 256, LW), alist(t, e, 0, 256)[t:128:16, :])], ak(t, e, 0, 256), ak(t, e, 256, LW), 128, 32)
+        dma("y", [(alist(t, e, 256, LW), alist(t, e, 0, 256)[t:128:16, :])], ak(t, e, 0, 256) + ["freeR%d" % (t - 1)] * (e == 1), ak(t, e, 256, LW), 128, 32)
         if e == 1:
             dma("y", [(PKn(t, 256, LW), PKn(t, 0, 256)[t:128:16, :])], pk(t, 0, 256), pk(t, 256, LW), 128, 64)
             V(lambda q: q.tensor_scalar(TH(t - 1, 256, LW), alist(t, e, 256, LW), -2048.0, None, A.add), r=ak(t, e, 256, LW), w=fk(t - 1, 256, LW))
@@ -854,6 +917,9 @@ def rank_program(g, core, T, topo):
         o = 16 * LW * (e - 1)
         move("s", T.Y[:, o + 16 * a:o + 16 * b], win(t).indirect(alist(t, e, a, b)), wkey(t) + ak(t, e, a, b) + ["SLF"],
              kb("Y%d" % e, a, b), cgat(16 * (b - a)), bias=col(SLF + t))
+        if LATE and t == 2 and e > 1 and a < 256:
+            ops[-1]["order"] += sorted({lastw[k] for k in kb("Y%d" % (e - 1), 0, 256)})
+            ops[-1]["both"], ops[-1]["body"] = None, ops[-1]["both"]["s"]
 
     def diff(t, e, h):
         a, b = CH[t][h]
@@ -862,11 +928,13 @@ def rank_program(g, core, T, topo):
         narrow = e == 1 or A16
         ID = T.IDH if narrow else T.IDN
         z = T["Z%d" % h]
-        d = z[:, 192:192 + 2 * m:2] if SCAN else z[:, 192:192 + m]
-        PE([lambda q: q.matmul(d, ID[:, 128:256], lots, True, False),
-            lambda q: q.matmul(d, T.IDH[:, 0:128], TH(t, a, b), False, True)] +
-           [lambda q: q.matmul(z[:, 193:192 + 2 * m:2], ID[:, 0:128], lots, True, True)] * SCAN,
-           ["IDN", "IDM", "IDH"] + lk + fk(t, a, b), ["zD%d" % h], cmm(m, 1 + (1 + SCAN) * (1 if narrow else 4)), ["bZ%d" % h])
+        d = z[:, 192:192 + 2 * m:2]
+        last = LAST and (t, e) == (2, 3) and b <= 256
+        PE([lambda q: q.matmul(d, ID[:, 0:128], lots, True, False),
+            lambda q: q.matmul(d, T.IDH[:, 128:256], TH(t, a, b), False, True),
+            lambda q: q.matmul(z[:, 193:192 + 2 * m:2], T.IDH[:, 0:128], TH(t, a, b), True, not last)] +
+           [lambda q: q.matmul(z[:, 193:192 + 2 * m:2], T.cB[32:33, 256:384], T.ones[32:33, 0:m], False, True)] * last,
+           ["IDN", "IDM", "IDH"] + ["cB", "ones"] * last + lk + fk(t, a, b), ["zD%d" % h], cmm(m, 2 + last + (1 if narrow else 4)), ["bZ%d" % h])
 
     def gx(t, e, a, b):
         o = 16 * LW * (e - 1)
@@ -879,6 +947,8 @@ def rank_program(g, core, T, topo):
                 ops[-1]["due"] = DUE[0] + DUE[1] * (3 * t + e - 1 + a / 256)
             return
         S(lambda q: q.activation(T.XS[:, 0:c1 - c0], lst, AF.Copy), r=r, w=["XS"], c=cgat(c1 - c0))
+        if LATE:
+            ops[-1]["order"] += sorted({lastw[k] for k in kb("Y%d" % e, 0, 256)})
         for x, y in split(a, b, 32):
             z = T.ZX[:, 0:16 * (y - x)]
             PE([lambda q, x=x, y=y, z=z: q.matmul(z, T.IDB[:, 128:256], T.XS[:, 16 * x - c0:16 * y - c0], True, False),
@@ -892,20 +962,20 @@ def rank_program(g, core, T, topo):
         m, l = b - a, min(b, 256)
         Z, dk, bk = T["Z%d" % h], ["zD%d" % h], ["bZ%d" % h]
         z = Z[:, 0:m]
-        PE([lambda q, k=k: q.matmul(z, T.SELK[:, 128 * k:128 * k + 128], T.C[:, 16 * a + k:16 * b:16], k == 0, k == 15) for k in range(16)],
-           kb("C", a, b) + SELK, ["zC%d" % h], cmm(m, 16), bk)
+        ps = PS if a < 256 else 1
+        for x in range(0, 16, 16 // ps):
+            add("p", "c", [lambda q, k=k: q.matmul(z, T.SELK[:, 128 * k:128 * k + 128], T.C[:, 16 * a + k:16 * b:16], k == 0, k == 15) for k in range(x, x + 16 // ps)],
+                kb("C", a, b) + SELK, ["zC%d" % h], cmm(m, 16 // ps), bk=bk, row=x > 0)
         o = SW * (e - 1)
         mask, mk = T.SG[:, o + 2 * a + 1:o + 2 * b:2], kb("SG%d" % e, a, b)
-        VS("s", lambda q: q.tensor_scalar(mask, z, 8.5 * BIG, None, A.is_lt),
-           lambda q: q.activation(mask, z, AF.Sigmoid, bias=col(HR), scale=-512.0 / BIG), ["zC%d" % h, "HR"], mk, cv(m), bk)
-        if SCAN:
-            V(lambda q: q.tensor_tensor_scan(T["TH%d" % (t % 2)][:, 2 * a:2 * b], T.SG[:, o + 2 * a:o + 2 * b], Z[:, 192:192 + 2 * m], 0.0, A.mult, A.add),
-              r=dk + mk, w=fk(t, a, b), c=cv(2 * m), bk=bk)
-        else:
-            d = Z[:, 192:192 + m]
-            lots, lk = aless(t, e, a, b)
-            V(lambda q: q.tensor_tensor(d, d, mask, A.mult), r=mk, w=dk, c=cv(m), bk=bk)
-            V(lambda q: q.tensor_tensor(TH(t, a, b), d, lots, A.add), r=dk + lk, w=fk(t, a, b), c=cv(m), bk=bk)
+        VS("s", lambda q: q.tensor_scalar(mask, z, 8.5 * BIG, None, A.is_gt),
+           lambda q: q.activation(mask, z, AF.Sigmoid, bias=col(HR), scale=512.0 / BIG), ["zC%d" % h, "HR"], mk, cv(m), bk)
+        if LAST and (t, e) == (2, 3) and b <= 256:
+            V(lambda q: q.tensor_tensor(T.qF[:, a:b], Z[:, 192:192 + 2 * m:2], mask, A.mult), r=dk + mk, w=kb("qF", a, b), c=cv(m), bk=bk)
+            V(lambda q: q.tensor_tensor(PKn(t + 1, a, b), Z[:, 193:192 + 2 * m:2], T.qF[:, a:b], A.add), r=dk + kb("qF", a, b), w=pk(t + 1, a, b), c=cv(m), bk=bk)
+            return
+        V(lambda q: q.tensor_tensor_scan(T["TH%d" % (t % 2)][:, 2 * a:2 * b], T.SG[:, o + 2 * a:o + 2 * b], Z[:, 192:192 + 2 * m], 0.0, A.mult, A.add),
+          r=dk + mk, w=fk(t, a, b), c=cv(2 * m), bk=bk)
         x = max(a, 256) if (t, e) == (2, 3) else a
         if x < b:
             V(lambda q: q.tensor_scalar(TT(t)[:, x:b], TH(t, x, b), 2048.0, None, A.add), r=fk(t, x, b), w=tk(t, x, b), c=cv(b - x, .5))
@@ -915,8 +985,10 @@ def rank_program(g, core, T, topo):
             move("s", PKn(t + 1, a, l), y, ["zP%d" % h], pk(t + 1, a, l), cv(l - a), bias=2048.0, bk=bk)
         elif e == 3 and a < l:
             V(lambda q: q.tensor_scalar(PKn(t + 1, a, l), TH(t, a, l), 2048.0, None, A.add), r=fk(t, a, l), w=pk(t + 1, a, l), c=cv(l - a))
+        if PKI and (t, e) == (0, 3) and a < l:
+            V(lambda q: q.tensor_copy(pkJ(256 + a, 256 + l), TT(t)[:, a:l]), r=tk(t, a, l), w=kb("PI", a, l) + ["pkC"] * (a == 0), c=cv(l - a))
         if e == 3 and b == LW:
-            V(lambda q: q.tensor_scalar(T.CF[:], TH(t, 256, LW), 2048.0, -SQ, A.add, A.mult), r=fk(t, 256, LW), w=["CF"])
+            V(lambda q: q.tensor_scalar(T.CF[:], TH(t, 256, LW), -SQ, None, A.mult), r=fk(t, 256, LW), w=["CF"])
 
     def gm(t, a, b):
         x, y = 16 * a, 16 * b
@@ -936,10 +1008,21 @@ def rank_program(g, core, T, topo):
                                                first and k == 0, first and k == 15) for k in range(16)]
             return fs
         pc = cmm(m, 1) if b < LW else cmm(64, 16 + m // 64)
-        PE(sums(T.ZM, True), sk, ["zU"], pc, ["bM"])
+        if b == LW and KSUM:
+            zu, zk, bu = T.Z0[:, 256:256 + m], "zK", "bZ0"
+            PE([lambda q: q.matmul(zu, T.cB[0:1, 256:384], T.ones[0:1, 0:m], True, False)], ["cB", "ones"], [zk], cmm(m), [bu])
+            for x, y in MP:
+                fs = [lambda q, k=k: q.matmul(zu[:, l - a:m], T.SELW[:, 128 * k:128 * k + 128], T.SM[:, 256 * k + 15:256 * k + 256:16], False, k == 15)
+                      for k in range(x // 16, y // 16)]
+                if y == 256:
+                    fs = [lambda q: q.matmul(zu[:, 0:l - a], T.WT[:], T.SM[:, 16 * a + 15:16 * l:16], False, False)] + fs
+                add("p", "c", fs, kb("SM", min(x, a) if y == 256 else x, y) + ["WT", "SELW0", "SELW1"], [zk], cmm(64, len(fs)), bk=[bu], row=True)
+        else:
+            zu, zk, bu = T.ZM[:, a:b], "zU", "bM"
+            PE(sums(T.ZM, True), sk, ["zU"], pc, ["bM"])
         if b == LW and UCOPY:
-            move("s", T.kf[:, a:b], T.ZM[:, a:b], ["zU"], kb("kf", a, b), cv(m), 1.0 / 2048, 191.5 + 1.0 / 2048, ["bM"])
-            move("s", T.uF[:, a:b], T.ZM[:, a:b], ["zU"], ["uF"], cv(m), bias=192.0 * 2048 + 33, bk=["bM"])
+            move("s", T.kf[:, a:b], zu, [zk], kb("kf", a, b), cv(m), 1.0 / 2048, 191.5 + 1.0 / 2048, [bu])
+            move("s", T.uF[:, a:b], zu, [zk], ["uF"], cv(m), bias=192.0 * 2048 + 33, bk=[bu])
             PE([lambda q: q.matmul(T.ZR[:, a:b], T.IDB[:, 0:128], T.kf[:, a:b], True, False),
                 lambda q: q.matmul(T.ZR[:, a:b], T.IDN[:, 0:128], T.uF[:, a:b], False, True)], ["IDB", "IDN", "uF"] + kb("kf", a, b), ["zR"], cmm(m, 5), ["bR"])
         else:
@@ -959,16 +1042,15 @@ def rank_program(g, core, T, topo):
         a = CH[t][-1][0] if t == 2 and TAIL else 288
         x = 36 + a // 16
         PE([lambda q: q.matmul(zb, T.cB[0:1, 0:128], T.ones[0:1, 0:54], True, False)] +
-           [lambda q: q.matmul(zb[:, x:54], T.cB[0:1, 256:384], T.ones[0:1, x:54], False, False)] * (x < 54) +
            [lambda q, k=k: q.matmul(zb[:, 0:x], T.SELK[:, 128 * k:128 * k + 128], T.SG[:, 2 * k + 1:2 * SW + 2 * a:32], False, k == 15) for k in range(16)],
            kb("SG1", 0, LW) + kb("SG2", 0, LW) + kb("SG3", 0, min(a, LW)) + SELK + ["cB", "ones"], ["zB"], cmm(54, 17), ["bC"])
         c = 18 if t == 2 else 36
         ds = range(c // 18)
         for d in ds:
-            V(lambda q, d=d: q.tensor_tensor(KM[:, 0:3, 18 * d:18 * d + 18], zb, KS[:, 18 * d:18 * d + 54], A.max),
+            V(lambda q, d=d: q.tensor_tensor(KM[:, 0:3, 18 * d:18 * d + 18], zb, KS[:, 18 * d:18 * d + 54], A.min),
               r=["zB"] + ["KS%d" % e for e in range(d, d + 3)], w=["KM_%d" % d], bk=["bC"])
-        V(lambda q: q.tensor_tensor(T.k1[:, :, 0:c], KM[:, 0:2, 0:c], KM[:, 2:4, 0:c], A.min), r=["KM3"] + ["KM_%d" % d for d in ds], w=["k1"], c=cv(4 * c))
-        V(lambda q: q.tensor_tensor(T.kI[:, 0:c], T.k1[:, 0, 0:c], T.k1[:, 1, 0:c], A.min), r=["k1"], w=["kI"], c=cv(2 * c))
+        V(lambda q: q.tensor_tensor(T.k1[:, :, 0:c], KM[:, 0:2, 0:c], KM[:, 2:4, 0:c], A.max), r=["KM3"] + ["KM_%d" % d for d in ds], w=["k1"], c=cv(4 * c))
+        V(lambda q: q.tensor_tensor(T.kI[:, 0:c], T.k1[:, 0, 0:c], T.k1[:, 1, 0:c], A.max), r=["k1"], w=["kI"], c=cv(2 * c))
         V(lambda q: q.tensor_scalar(T.kJ[:, 0:c], T.kI[:, 0:c], 4095, None, A.bitwise_and), r=["kI"], w=["kJ"])
         if t < 2 or t not in YT or TAIL:
             V(lambda q: q.tensor_copy(T.LU[:, 18:18 + c], T.kJ[:, 0:c]), r=["kJ"], w=["LU%d" % (d + 1) for d in ds])
@@ -983,18 +1065,18 @@ def rank_program(g, core, T, topo):
             dma("y", [(T.yv[gg:gg + 1, x], T.YW[gg // 2 * 32:gg // 2 * 32 + a // 16, 32 * t + gg % 2 * 16:32 * t + gg % 2 * 16 + 16]) for gg in range(8)],
                 ["YV%d" % t], ["yv%d" % t], a // 2, 64)
         else:
-            move("s", T.YV[:, x], T.IDW[:].indirect(T.LU[:, 18:18 + a // 16]), IDW + ["LU1"], ["YV%d" % t], cgat(a))
+            move("s", T.YV[:, x], idw.indirect(T.LU[:, 18:18 + a // 16]), IDW + ["LU1"], ["YV%d" % t], cgat(a))
             dma("y", [(T.yv[:, x], T.YV[0:128:16, x])], ["YV%d" % t], ["yv%d" % t], 16, 2 * a)
         if a < 256:
             m, z = 256 - a, T.ZR[:, 0:256 - a]
             for d in (1, 2):
-                move("s", T.KF[:, 128 * d:128 * d + m], T.IDW[:].indirect(T.LU[:, 18 * d + a // 16:18 * d + 16]), IDW + ["LU%d" % d], ["KF%d" % d],
-                     cgat(m), scale=3.0 - 2 * d)
+                move("s", T.KF[:, 128 * d:128 * d + m], idw.indirect(T.LU[:, 18 * d + a // 16:18 * d + 16]), IDW + ["LU%d" % d], ["KF%d" % d],
+                     cgat(m), scale=2.0 * d - 3)
             PE([lambda q: q.matmul(z, T.cB[0:1, 0:128], T.ones[0:1, 0:m], True, False),
                 lambda q: q.matmul(z, T.BE[:], T.SG[:, 2 * SW + 2 * a + 1:2 * SW + 512:2], False, True)],
                kb("SG3", a, 256) + ["BE", "cB", "ones"], ["zR"], cmm(m, 2), ["bR"])
-            V(lambda q: q.tensor_tensor(T.KF[:, 0:m], z, T.KF[:, 256:256 + m], A.max), r=["zR", "KF2"], w=["KF0"], c=cv(m), bk=["bR"])
-            V(lambda q: q.tensor_tensor(T.KF[:, 256:256 + m], T.KF[:, 0:m], T.KF[:, 128:128 + m], A.min), r=["KF0", "KF1"], w=["KF2"], c=cv(2 * m))
+            V(lambda q: q.tensor_tensor(T.KF[:, 0:m], z, T.KF[:, 256:256 + m], A.min), r=["zR", "KF2"], w=["KF0"], c=cv(m), bk=["bR"])
+            V(lambda q: q.tensor_tensor(T.KF[:, 256:256 + m], T.KF[:, 0:m], T.KF[:, 128:128 + m], A.max), r=["KF0", "KF1"], w=["KF2"], c=cv(2 * m))
             S(lambda q: q.activation(T.YV[:, 512 + a:768], T.KF[:, 256:256 + m], AF.Abs), r=["KF2"], w=["YVf"], c=cv(m))
             dma("y", [(T.yv[:, 512 + a:768], T.YV[0:128:16, 512 + a:768])], ["YVf"], ["yvf"], 8, 4 * m)
 
@@ -1003,9 +1085,18 @@ def rank_program(g, core, T, topo):
 
     def dedupe(t):
         cl, ck = TT(t)[:, 256:LW], tk(t, 256, LW)
-        move("s", T.RB[:], T.IDW[:].indirect(cl), IDW + ck, ["RB"], cgat(256), scale=-SQ)
-        move("s", T.SV[:, 256 * t:256 * t + 256], win(t).indirect(cl), wkey(t) + ck, ["SV%d" % t], cgat(256))
-        for c in range(16):
+        if RBP:
+            PE([lambda q, r=r: q.matmul(T.ZM[:, r:256:16], T.SELT[:, 128 * r:128 * r + 128], TH(t, 256, LW), True, True) for r in range(16)],
+               ["SELT0", "SELT1"] + fk(t, 256, LW), ["zU"], cmm(16, 16), ["bM"])
+        else:
+            move("s", T.RB[:], T.IDW[:].indirect(cl), IDW + ck, ["RB"], cgat(256), scale=-SQ, bias=2048 * SQ)
+        move("s", T.SV[:, 768 * t:768 * t + 256], win(t).indirect(cl), wkey(t) + ck, ["SV%d" % t], cgat(256))
+        for c in range(16 * RBP):
+            o = SEG * (c // CB)
+            eq, rb = T.EQ[:, o + seg[c % CB]:o + seg[c % CB + 1]], T.ZM[:, 16 * c:WB * (c // CB + 1)]
+            S(lambda q, c=c, eq=eq, rb=rb: q.activation(eq, rb, AF.Square, bias=T.CF[:, c:c + 1], scale=SQ),
+              ["zU", "CF"], ["EQ%d" % c], cv(WB - 16 * (c % CB)), ["bM"])
+        for c in range(0 if RBP else 16):
             o = SEG * (c // CB)
             eq, rb = T.EQ[:, o + seg[c % CB]:o + seg[c % CB + 1]], T.RB[:, 16 * c:WB * (c // CB + 1)]
             VS("s", lambda q, c=c, eq=eq, rb=rb: q.tensor_scalar(eq, rb, T.CF[:, c:c + 1], SQ * SQ, A.not_equal, A.mult),
@@ -1020,7 +1111,7 @@ def rank_program(g, core, T, topo):
                   r=["EM"] + ["EQ%d" % (CB * b + c) for c in range(x, y)], w=sk[-1:], c=cv(seg[y] - seg[x], .5))
         V(lambda q: q.tensor_tensor(T.dE[:], T.SC[:, 0:NB * SEG].indirect(T.E16[:, 0:1]), T.DJ[:], A.subtract), r=sk + ["E16", "DJ"], w=["dE"], c=cgat(16))
         V(lambda q: q.tensor_tensor(T.dF[:], T.dE[:], T.CF[:], A.min), r=["dE", "CF"], w=["dF"])
-        V(lambda q: q.tensor_scalar(T.SL[:, 16 * t:16 * t + 16], T.dF[:], -1.0 / SQ, None, A.mult), r=["dF"], w=["SL%d" % t])
+        V(lambda q: q.tensor_scalar(T.SL[:, 16 * t:16 * t + 16], T.dF[:], -1.0 / SQ, 2048.0, A.mult, A.add), r=["dF"], w=["SL%d" % t])
 
     others = [d for d in range(n) if d != rank]
     common = [e for e in topo.engines(core, T.cores[others[0]]) if all(e in topo.engines(core, T.cores[d]) for d in others)]
@@ -1039,11 +1130,77 @@ def rank_program(g, core, T, topo):
             add("g", "r", tr, [key], ["sent" + key], cfix(3.0 if t == 0 and w == 256 else 0.8), rows=48, nbytes=48 * 2 * w * XB)
             add("n", "n", ("arr" + key, len(common) * len(others)), ["sent" + key], ["got" + key], cfix(0.0))
 
-    def update(t):
-        F = T.F3 if t in SEP else T["F%d" % (t + 1)]
-        wk = "win3" if t in SEP else "win%d" % (t + 1)
+    out = lambda t, i, k=1: T.SV[:, 768 * t + 256 * i:768 * t + 256 * (i + k)]
+    land = lambda t, i, k=1: T.LV[:, 1536 * t + 256 * i:1536 * t + 256 * (i + k)]
+
+    def post(key, moves, r, rb, lsem="lsem", first=False):
+        share = len(common) // len(moves)
+        trs, rows, got = [], 0, 0
+        for k, (src, to) in enumerate(moves):
+            ids = [DstId(rid=x[0], pnc=x[1]) for x in (topo.addr(T.cores[(rank + s) % n]) for s, _ in to)]
+            trs.append(RemoteDMATransfer(dst_ids=ids, dma_engine_mask=sum(1 << e for e in common[share * k:share * k + share]),
+                                         remote_sem=T.sem["arr" + key], srcs=[src], dsts=[x for _, x in to], alu_op=0))
+            rows, got = max(rows, 128 * len(to) // share), got + share * len(to)
+        add("g", "r", (trs, lsem, share * len(moves)), r, ["sent" + key], cfix(3.0 if first else 0.8), rows=rows, nbytes=rows * rb * XB)
+        add("n", "n", ("arr" + key, got), ["sent" + key], ["got" + key], cfix(0.0))
+
+    def offers(t):
+        slot = lambda buf, to: [(s, buf[:, 64 * t + 16 * (n - 1 - s):64 * t + 16 * (n - s)]) for s in to]
+        post("R%d" % t, [(TT(t)[:, 256:LW], slot(T.LR, (n - 1, n - 2)))], tk(t, 256, LW), 32, "lr%d" % t, t == 0)
+        add("n", "n", ("lr%d" % t, len(common)), ["sentR%d" % t], ["freeR%d" % t], cfix(0.0))
+        post("SV%d" % t, [(out(t, 0), [(n - 1, land(t, 0)), (1, land(t, 5))] + [(n - 2, land(t, 3))] * XS3)], ["SV%d" % t], 512)
+        post("SL%d" % t, [(T.SL[:, 16 * t:16 * t + 16], slot(T.LL, range(1, n)))], ["SL%d" % t], 32)
+        for b in range(NB):
+            to, x = T.O[:].indirect(T.SL[:, 16 * t + CB * b:16 * t + CB * b + CB]), out(t, 0)[:, WB * b:WB * b + WB]
+            V((lambda q, to=to, x=x: q.tensor_tensor(to, x, T.big[:, WB * t - WB:WB * t], A.mult)) if t else (lambda q, to=to, x=x: q.tensor_copy(to, x)),
+              r=["SV%d" % t, "SL%d" % t] + (["big%d" % t] if t else ["Oz%d" % i for i in range(NF)]), w=["O"], c=csca(WB))
+        for i in range(2):
+            move("s", out(t, 1 + i), T.O[:].indirect(T.LR[:, 64 * t + 16 * i:64 * t + 16 * i + 16]), ["O", "gotR%d" % t], ["SX%d%d" % (t, i)],
+                 cgat(256), scale=2.0 ** (-16 * t))
+        near, far = (out(t, 1, 2), [(n - 1, land(t, 1, 2))]), (out(t, 0, 2), [(n - 2, land(t, 3, 2))])
+        if XS3:
+            post("X%d" % t, [near], ["SX%d0" % t, "SX%d1" % t], 1024)
+            post("Z%d" % t, [(out(t, 1), [(n - 2, land(t, 4))])], ["SX%d0" % t], 512)
+        elif XONE:
+            post("X%d" % t, [near, far], ["SV%d" % t, "SX%d0" % t, "SX%d1" % t], 1024)
+        else:
+            post("X%d" % t, [far], ["SV%d" % t, "SX%d0" % t], 1024)
+            post("Z%d" % t, [near], ["SX%d0" % t, "SX%d1" % t], 1024)
+
+    def settle(t):
         N, nk = (T.p0, "win4") if t == 2 else (T["F%d" % (t + 1)], "win%d" % (t + 1))
-        nr = ["dump%d" % (t + t // 2)] + ["cq%d_%d" % (t, x) for x in range(NF)] if t in SEP else []
+        nr = ["dump%d" % (t + t // 2), "gotSL%d" % t] + ["cp%d_%d" % (t, x) for x in range(NF)]
+        for i in range(3):
+            x = slice(256 * i, 256 * i + 256)
+            z, zk = T.ZX[:, 256 * (i % 2):256 * (i % 2) + 256], ["zX%d" % (i % 2)]
+            if i < 2:
+                move("s", T.pg[:, x], win(t).indirect(T.LR[:, 64 * t + 16 * i:64 * t + 16 * i + 16]), wkey(t) + ["gotR%d" % t], ["pg%d" % i], cgat(256))
+            else:
+                move("s", T.pg[:, x], (T["F%d" % t] if t else T.p0)[:].indirect(T.LL[:, 64 * t + 16 * i:64 * t + 16 * i + 16]),
+                     wkey(t) + ["gotSL%d" % t, "dump%d" % (t - 1 if t else 3)], ["pg%d" % i], cgat(256))
+            parts = [(T.IDH[:, 0:128], T.pg[:, x])] + [(T.IDI[:], land(t, k)) for k in ((0,), (1, 3), (5, 2, 4))[i]]
+            PE([lambda q, k=k, z=z, p=p, last=len(parts) - 1: q.matmul(z, p[0], p[1], k == 0, k == last) for k, p in enumerate(parts)],
+               ["IDI", "IDH", "pg%d" % i, "gotSV%d" % t] + ["gotX%d" % t] * (i > 0) + ["gotZ%d" % t] * (i > XS3 and not XONE), zk, cmm(256, len(parts)), ["bX"])
+            if FLS[t][i] == "v":
+                V(lambda q, x=x, z=z: q.tensor_scalar(T.i1[:, x], z, -0.4921875, 255.0, A.add, A.min), r=zk, w=["i1%d" % i], c=cv(256), bk=["bX"])
+            else:
+                S(lambda q, x=x, z=z: q.activation(T.r1[:, x], z, AF.Relu, bias=col(TOP), scale=-1.0), r=zk + ["TOP"], w=["r1%d" % i], c=cv(256), bk=["bX"])
+                S(lambda q, x=x: q.activation(T.r2[:, x], T.r1[:, x], AF.Copy, bias=MAGIC + 255, scale=-1.0), r=["r1%d" % i], w=["i1%d" % i], c=cv(256))
+                if t == 2:
+                    S(lambda q, x=x: q.activation(T.r2[:, x], T.r2[:, x], AF.Copy, bias=-MAGIC), w=["i1%d" % i], c=cv(256))
+            for b in range(NB):
+                o, y = T.LL[:, 64 * t + 16 * i + CB * b:64 * t + 16 * i + CB * b + CB], slice(256 * i + WB * b, 256 * i + WB * b + WB)
+                if t == 2 or FLS[t][i] == "v":
+                    f = lambda q, o=o, y=y, src=T.i1 if FLS[t][i] == "v" else T.r2: q.tensor_copy(N[:].indirect(o), src[:, y])
+                else:
+                    f = lambda q, o=o, y=y: q.tensor_scalar(N[:].indirect(o), T.r2[:, y], 1.0, -MAGIC, A.mult, A.add)
+                V(f, r=["i1%d" % i] + nr, w=[nk], c=csca(WB))
+
+    def update(t):
+        F = T.F1 if t == 2 else T["F%d" % (t + 1)]
+        wk = "win1" if t == 2 else "win%d" % (t + 1)
+        N, nk = (T.p0, "win4") if t == 2 else (T["F%d" % (t + 1)], "win%d" % (t + 1))
+        nr = ["dump3"] + ["cp%d_%d" % (t, x) for x in range(NF)] if t == 2 else []
         L = lambda i: T.LL[:, 64 * t + 16 * i:64 * t + 16 * i + 16]
         lk = "gotSL%d" % t
         cols = lambda i: slice(256 * i, 256 * i + 256)
@@ -1055,7 +1212,7 @@ def rank_program(g, core, T, topo):
         for i in range(3):
             if UF[t][i] != "p":
                 move("s", T.sv[:, cols(i)], T.LV[:, 768 * t + 256 * i:768 * t + 256 * i + 256], ["gotSV%d" % t, "INC"], ["sv%d" % i], cv(256), scale=col(INC))
-        fr = [wk, "dump%d" % (2 if t in SEP else t), lk] + ["cp%d_%d" % (3 if t in SEP else t, i) for i in range(NF)]
+        fr = [wk, "dump%d" % (t % 2), lk] + ["cp%d_%d" % (t + t // 2, i) for i in range(NF)]
         zt = T.ZX[:, 0:256]
         for i in range(3):
             if UF[t][i] == "p":
@@ -1093,20 +1250,30 @@ def rank_program(g, core, T, topo):
     parents(1)
     conv(2)
     for e in (2, 3):
+        if VM and e == 3:
+            parents(2)
         package(0, e)
-        first(e) if FIRST else clist(0, e)
+        first(e) if e in FIRST else clist(0, e)
     for t in range(3):
         w = 4096 // NF
         new = T.p0 if t == 2 else T["F%d" % (t + 1)]
-        for dst, key, old in ((T.F3, "cp3", ["win3"]), (new, "cq%d" % t, wkey(0) if t == 2 else [])) if t in SEP else ((new, "cp%d" % t, []),):
+        for dst, key, old in [(T.F1, 3, wkey(1))] * (t == 2 and t not in XC) + [(new, t, wkey(0) if t == 2 else [])]:
             for i in range(NF):
                 G(lambda q, t=t, i=i, dst=dst: q.affine_select(dst[:, w * i:w * i + w], win(t)[:, w * i:w * i + w], [[0, w]], A.is_equal, 0.0, 0, 0),
-                  r=wkey(t), w=["%s_%d" % (key, i)] + (old if i == 0 else []), c=cgp(w, 0.17))
+                  r=wkey(t), w=["cp%d_%d" % (key, i)] + (old if i == 0 else []), c=cgp(w, 0.17))
                 if i and old:
                     ops[-1]["order"].append(len(ops) - 2)
+        for i in range(NF if t == 0 and XC else 0):
+            if i < OV:
+                V(lambda q, i=i: q.memset(T.O[:, (w + 32) * i:(w + 32) * (i + 1)], 0.0), w=["Oz%d" % i], c=cv(w + 32, .5))
+            elif i < OV + OS:
+                S(lambda q, i=i: q.activation(T.O[:, (w + 32) * i:(w + 32) * (i + 1)], T.ones[:, 0:w + 32], AF.Copy, scale=0.0), r=["ones"], w=["Oz%d" % i], c=cv(w + 32))
+            else:
+                G(lambda q, i=i: q.iota(T.O[:, (w + 32) * i:(w + 32) * (i + 1)], [[0, w + 32]], 0, 0, **fl), w=["Oz%d" % i], c=cgp(w + 32))
         tag[0] = "parents%d" % t
         if t < 2:
-            parents(2)
+            if t or not VM:
+                parents(2)
             conv(3)
         keys(t)
         for e in (1, 2, 3):
@@ -1121,11 +1288,12 @@ def rank_program(g, core, T, topo):
                 tops(t, e, h)
         tag[0] = "claims%d" % t
         dedupe(t)
-        send(t)
+        offers(t)
         tag[0] = "prices%d" % t
-        update(t)
+        settle(t) if t in XC else update(t)
         if t == 2:
-            dma("y", [(T.yp[:], T.p0[:, 0:4096])], ["win4"], ["yp"], 128, 8192)
+            for i in range(0, 128, 128 // NY):
+                dma("y", [(T.yp[i:i + 128 // NY, :], T.p0[i:i + 128 // NY, 0:4096])], ["win4"], ["yp%d" % i], 128 // NY, 8192)
             for a, b in OH:
                 outh(t, a, b)
         else:
@@ -1145,6 +1313,10 @@ def rank_program(g, core, T, topo):
                 package(t + 1, e)
                 clist(t + 1, e)
 
+    for o in ops:
+        for t in range(3):
+            if o["tag"] in ("x%d1_0" % t, "x%d2_0" % t, "x%d3_0" % t, "claims%d" % t, "prices%d" % t) or o["tag"][0:2] == "y%d" % t and o["name"].endswith("_32"):
+                o["up"] += UPK[t]
     order = plan(ops)
     total, snap, tok = {}, {}, {}
     seen = {e: {} for e in Q}
@@ -1195,8 +1367,8 @@ def rank_program(g, core, T, topo):
             tok[i] = (s, total[s])
             snap[tok[i]] = dict(seen[e])
         else:
-            g.remote_dma_fused([body], local_sem=T.sem.lsem)
-            total["lsem"] = total.get("lsem", 0) + len(common)
+            g.remote_dma_fused(body[0], local_sem=T.sem[body[1]])
+            total[body[1]] = total.get(body[1], 0) + body[2]
     for s in sorted(total):
         if seen["g"].get(s, 0) < total[s]:
             g.wait_ge(T.sem[s], total[s])

import numpy as np
from concourse.bass import DstId, RemoteDMATransfer
from concourse.mybir import dt, AluOpType, AxisListType, ActivationFunctionType

A = AluOpType
AF = ActivationFunctionType
LW = 272
CH = [[(256, 272), (0, 96), (96, 192), (192, 256)]] * 3
XW = (64, 64, 48)
YP = [[(256, 272), (0, 64), (64, 128), (128, 192), (192, 256)]] * 2 + \
     [[(256, 272), (0, 48), (48, 96), (96, 144), (144, 192), (192, 256)]]
MP = [(0, 64), (64, 128), (128, 192), (192, 256)]
TG = [[(0, 96), (96, 192), (192, 272)]] * 2
SR = []
LAST = True
NY = 1
PS = 4
KSUM = True
LATE = False
UPK = (2.0, 2.0, 4.0)
XC = (0, 1, 2)
GV = "oms"
OS = 2
OV = 4
RBP = 1
PKI = 1
VM = 1
XS3 = 1
XONE = False
NB = 2
SP = (0, 3, 8)
SCAN = True
A16 = 3
NOWAIT = False
YT = (0, 1)
TAIL = True
PKS = ()
SEP = (2,)
UCOPY = True
FIRST = (2, 3)
OH = [(0, 96), (96, 192), (192, 256)]
BIG = 32768.0
SQ = 8192.0
XB = 1.2
UF = ("ggt", "ggt", "ttt")
FLS = ("svv", "svv", "svv")
PCALL = 0.010
REACH = 0.35
LOADS = ["win0a", "VT", "pkA", "wtI", "win0", "pkC", "TIa", "pkJ", "TI", "pkI", "incI"]
LA = 96
L0 = [(0, LA, ["pkA"]), (LA, 256, ["pkJ"]), (256, LW, ["pkC"])]
LEAN = 10.0
SLOPES = [3.0, 8.0, 20.0, 50.0]
SEED = 4
DUE = (9.0, 9.2, 97.0, 0.2)
PA = 1024
NF = 8
MAGIC = 1.5 * 2 ** 23
SW = 576

SCRATCH = {
    "p0": ("sbuf", [128, 4352], "bfloat16"),
    "F1": ("sbuf", [128, 4352], "float32"),
    "F2": ("sbuf", [128, 4352], "float32"),
    "PI": ("sbuf", [128, 1280], "int32"),
    "PK": ("sbuf", [128, 1792], "float32"),
    "SELT": ("sbuf", [128, 2048], "bfloat16"),
    "SEL1": ("sbuf", [128, 2048], "bfloat16"),
    "big": ("sbuf", [128, 256], "bfloat16"),
    "VT": ("sbuf", [128, 1024], "int32"),
    "small": ("sbuf", [128, 8], "int32"),
    "slI": ("sbuf", [128, 4], "int32"),
    "sm": ("sbuf", [128, 32], "float32"),
    "pI": ("sbuf", [128, 8], "int32"),
    "row8": ("sbuf", [128, 8], "float32"),
    "B8": ("sbuf", [128, 8], "float32"),
    "one16": ("sbuf", [128, 16], "float32"),
    "SELK": ("sbuf", [128, 2048], "bfloat16"),
    "SELW": ("sbuf", [128, 2048], "bfloat16"),
    "ones": ("sbuf", [128, 1024], "bfloat16"),
    "cB": ("sbuf", [128, 384], "bfloat16"),
    "IX": ("sbuf", [128, 128], "float32"),
    "IDN": ("sbuf", [128, 256], "float32"),
    "IDH": ("sbuf", [128, 256], "bfloat16"),
    "IDB": ("sbuf", [128, 256], "bfloat16"),
    "IXG": ("sbuf", [128, 128], "float32"),
    "IDI": ("sbuf", [128, 128], "bfloat16"),
    "WT": ("sbuf", [128, 128], "bfloat16"),
    "TT0": ("sbuf", [128, LW], "uint16"),
    "TT1": ("sbuf", [128, LW], "uint16"),
    "TH0": ("sbuf", [128, 2 * LW], "float16"),
    "TH1": ("sbuf", [128, 2 * LW], "float16"),
    "TI": ("sbuf", [128, LW], "int32"),
    "AL": ("sbuf", [128, 3 * LW], "uint16"),
    "AE": ("sbuf", [128, 2 * LW], "float32"),
    "AH": ("sbuf", [128, 2 * LW], "float16"),
    "Y": ("sbuf", [128, 48 * LW], "bfloat16"),
    "C": ("sbuf", [128, 16 * LW], "bfloat16"),
    "XS": ("sbuf", [128, 1536], "bfloat16"),
    "XM": ("sbuf", [128, 4096], "bfloat16"),
    "SM": ("sbuf", [128, 4096], "bfloat16"),
    "MK": ("sbuf", [128, 1024], "bfloat16"),
    "SG": ("sbuf", [128, 3 * SW], "bfloat16"),
    "kf": ("sbuf", [128, LW], "bfloat16"),
    "uF": ("sbuf", [128, LW], "float32"),
    "qF": ("sbuf", [128, LW], "float32"),
    "qI": ("sbuf", [128, LW], "int32"),
    "KS": ("sbuf", [128, 72], "float32"),
    "KO": ("sbuf", [128, 36], "float32"),
    "KM": ("sbuf", [128, 4, 36], "float32"),
    "k1": ("sbuf", [128, 2, 36], "float32"),
    "kI": ("sbuf", [128, 36], "int32"),
    "kJ": ("sbuf", [128, 36], "int32"),
    "LU": ("sbuf", [128, 54], "uint16"),
    "i16": ("sbuf", [128, 32], "float32"),
    "L1c": ("sbuf", [128, 32], "float32"),
    "VH": ("sbuf", [128, 256], "float16"),
    "VG": ("sbuf", [128, 256], "float16"),
    "YV": ("sbuf", [128, 768], "float32"),
    "YW": ("sbuf", [128, 96], "float32"),
    "KF": ("sbuf", [128, 384], "float32"),
    "BE": ("sbuf", [128, 128], "bfloat16"),
    "CF": ("sbuf", [128, 16], "float32"),
    "IDW": ("sbuf", [128, 4096], "float32"),
    "RB": ("sbuf", [128, 256], "float32"),
    "EI": ("sbuf", [128, 576], "bfloat16"),
    "EQ": ("sbuf", [128, 1152], "bfloat16"),
    "EM": ("sbuf", [128, 576], "bfloat16"),
    "SC": ("sbuf", [128, 1152], "bfloat16"),
    "E16": ("sbuf", [128, 2], "uint16"),
    "DJ": ("sbuf", [128, 16], "float32"),
    "DJt": ("sbuf", [128, 16], "float32"),
    "dE": ("sbuf", [128, 16], "float32"),
    "dF": ("sbuf", [128, 16], "float32"),
    "SV": ("sbuf", [128, 3 * 768], "bfloat16"),
    "SL": ("sbuf", [128, 48], "uint16"),
    "LV": ("sbuf", [128, 3 * 1536], "bfloat16"),
    "LL": ("sbuf", [128, 3 * 64], "uint16"),
    "LR": ("sbuf", [128, 3 * 64], "uint16"),
    "O": ("sbuf", [128, 4352], "bfloat16"),
    "pg": ("sbuf", [128, 768], "bfloat16"),
    "i1": ("sbuf", [128, 768], "int32"),
    "r1": ("sbuf", [128, 768], "float32"),
    "r2": ("sbuf", [128, 768], "float32"),
    "Z0": ("psum", [128, 512], "float32"),
    "Z1": ("psum", [128, 512], "float32"),
    "Z2": ("psum", [128, 512], "float32"),
    "Z3": ("psum", [128, 512], "float32"),
    "ZC": ("psum", [128, 512], "float32"),
    "ZX": ("psum", [128, 512], "float32"),
    "ZM": ("psum", [128, 512], "float32"),
    "ZR": ("psum", [128, 512], "float32"),
}
NDMA = 70
SEMAPHORES = ["cv", "cs", "cp", "cg", "lsem"] + ["%s%d" % (x, t) for x in ("arrSV", "arrSL", "arrR", "arrX", "arrZ", "lr") for t in range(3)] + ["d%d" % i for i in range(NDMA)]

MODELS = [
    (0.02, 0.83e-3, 1.25e-3, 3.0e-3, 0.83e-3, 0.14, 2.0, 3.0, 0.035, 0.06e-3),
    (0.015, 0.84e-3, 0.88e-3, 1.6e-3, 0.84e-3, 0.13, 2.0, 3.0, 0.035, 0.055e-3),
    (0.03, 1.10e-3, 1.35e-3, 5.2e-3, 0.90e-3, 0.15, 2.2, 3.5, 0.04, 0.08e-3),
    (0.02, 1.00e-3, 1.95e-3, 2.2e-3, 0.92e-3, 0.22, 2.4, 2.5, 0.05, 0.04e-3),
    (0.03, 1.20e-3, 2.10e-3, 5.0e-3, 1.10e-3, 0.20, 2.2, 4.0, 0.04, 0.07e-3),
]
TRIES, STARTS, TURN, FLIP = 15, 1, True, 9.0
STEPS = ((1000, 1),)
BACK, FAR, WIDE, TOP, KEEP, JIT = 1500, 8, 40, 4, 20, 0.002
ROUNDS, SPAN, SHORT, SHAKE, HEAT, HOME = 1400, 100, 150, (12.0, 0.2, 1.0), 0.01, 0.3


def cv(n, per=1.0):
    return (1.0, max(64, n * per), 0, 0, 0, 0)


def cgat(n):
    return (0.0, 65, n, 0, 0, 0)


def csca(n):
    return (0.0, 60, 0, n, 0, 0)


def cmm(n, k=1):
    return (0, 0, 0, 0, k * max(64, n), PCALL * k)


def cfix(x):
    return (0, 0, 0, 0, 0, x)


def cgp(n, fix=0.13):
    return (0, 2 * n, 0, 0, 0, fix)


def price_ops(ops, md):
    cost, dur, lat = [], [], []
    for o in ops:
        c = o["cost"]
        cost.append(c[0] * md[0] * (1.3 if o["e"] == "s" else 1.0) + c[1] * md[1] + c[2] * md[2] + c[3] * md[3] + c[4] * md[4] + c[5])
        dur.append(o["rows"] * md[8] + o["bytes"] * md[9])
        lat.append({"d": md[6], "n": md[7]}.get(o["kind"], 0.0))
    return cost, dur, lat


def run_order(ops, order, pr, wake, why=None, old=None, at=0):
    cost, dur, lat = pr
    free, last = dict.fromkeys("vspgyn", 0.0), dict.fromkeys("vspgyn", -1)
    dfree, dlast = 0.0, -1
    seen, gone = (old[1][:], old[2][:]) if old else ([0.0] * len(ops), [0.0] * len(ops))
    if old:
        todo = set("vspgyd")
        for k in range(at - 1, -1, -1):
            i = order[k]
            e = ops[i]["e"]
            if e in todo:
                free[e] = gone[i]
                todo.discard(e)
            if dur[i] and "d" in todo:
                dfree = seen[i] - lat[i] - wake
                todo.discard("d")
            if not todo:
                break
        wait = PLAN["wait"]
        for i in order[at:]:
            e, full = wait[i]
            s = free[e]
            for p in full:
                if seen[p] > s:
                    s = seen[p]
            s += cost[i]
            if e != "n":
                free[e] = gone[i] = s
                if dur[i]:
                    s = dfree = (dfree if dfree > s else s) + dur[i]
            seen[i] = s + lat[i] + wake
        return max(seen), seen, gone
    for i in order:
        e, full = ops[i]["wait"]
        s, w = free[e], -1
        for p in full:
            if seen[p] > s:
                s, w = seen[p], p
        f = s + cost[i]
        if why is not None:
            why[i] = (w, False, last[e]) if w >= 0 else (last[e], True, last[e])
            last[e] = i
        if e != "n":
            free[e] = gone[i] = f
        if dur[i]:
            if dfree > f:
                f = dfree
                if why is not None:
                    why[i] = (dlast, True, dlast)
            f = dfree = f + dur[i]
            dlast = i
        seen[i] = f + lat[i] + wake
    return max(seen), seen, gone


def moved(ops, order, i, j, link, ahead):
    a, b = order.index(j), order.index(i)
    if a > b:
        return None
    span = order[a:b + 1] if ahead else order[a:b + 1][::-1]
    take, held = {span[-1]}, set()
    for x in span[::-1]:
        e = ops[x]["e"]
        if x in take or e in held:
            take.add(x)
            take.update(p for p, f in link[x])
            if e != ops[span[-1]]["e"] and e != "n":
                held.add(e)
    if span[0] in take:
        return None
    span = [x for x in span if x in take] + [x for x in span if x not in take]
    return order[:a] + (span if ahead else span[::-1]) + order[b + 1:]


def schedule(ops, pred, succ, prio, pr, wake, slope, back=False):
    cost, dur, lat = pr
    m = len(ops)
    left = [len(p) for p in pred]
    ready = [0.0] * m
    free, pend = {}, {}
    for i, o in enumerate(ops):
        free[o["e"]] = 0.0
        pend.setdefault(o["e"], [])
        if not left[i]:
            ready[i] = dur[i] + lat[i] if back else 0.0
            pend[o["e"]].append(i)
    names = sorted(pend)
    order, dfree, fin = [], 0.0, [0.0] * m
    for _ in range(m):
        t0, e = 1e30, None
        for x in names:
            if pend[x]:
                t = max(free[x], min(ready[i] for i in pend[x]))
                if t < t0:
                    t0, e = t, x
        i = max(pend[e], key=lambda i: (prio[i] - slope * max(0.0, ready[i] - t0), -i))
        fill = [k for k in pend[e] if k != i and max(t0, ready[k]) + cost[k] <= ready[i]]
        if fill:
            i = max(fill, key=lambda i: (prio[i], -i))
        s = max(t0, ready[i])
        order.append(i)
        pend[e].remove(i)
        f = fin[i] = s + cost[i]
        free[e] = f if e != "n" else 0.0
        done = f
        if dur[i] and not back:
            done = dfree = max(f, dfree) + dur[i]
        for j, full in succ[i]:
            delay = (dur[j] + lat[j] if back else lat[i]) + wake
            ready[j] = max(ready[j], done + delay if full else f)
            left[j] -= 1
            if not left[j]:
                pend[ops[j]["e"]].append(j)
    return order, fin


def refine(ops, order, eng, pred, succ, priced, ref, rng, steps, lo=0, hi=10 ** 6):
    m, nm = len(ops), len(MODELS)
    fp = [o["wait"][1] for o in ops]
    fs = [[j for j, f in succ[i] if f] for i in range(m)]
    ap = [[p for p, f in pred[i]] for i in range(m)]
    aq = [[j for j, f in succ[i]] for i in range(m)]
    eng = eng[:]
    late = [[x + md[5] for x in pr[2]] for pr, md in zip(priced, MODELS)]
    st = [[[0.0] * (m + 1) for _ in range(6)] for _ in MODELS]
    prev, nxt, dprev, dnxt = ([m] * (m + 1) for _ in range(4))
    isd = [x > 0 for x in priced[0][1]]

    before, behind, past = {}, {}, [0.0] * nm

    def times(order, a, b):
        last = dict(before)
        for i in order:
            e = eng[i]
            if e != "n":
                p = prev[i] = last.get(e, m)
                nxt[p] = last[e] = i
            if isd[i]:
                p = dprev[i] = last.get("d", m)
                dnxt[p] = last["d"] = i
        for e, i in last.items():
            (dnxt if e == "d" else nxt)[i] = behind.get(e, m)
        ahead, back = order[a:], order[b::-1]
        cur = []
        for k in range(nm):
            cost, dur, lt = priced[k][0], priced[k][1], late[k]
            end, seen, dend, q, after, qd = st[k]
            for i in ahead:
                s = end[prev[i]]
                for p in fp[i]:
                    if seen[p] > s:
                        s = seen[p]
                s = end[i] = s + cost[i]
                if isd[i]:
                    d = dend[dprev[i]]
                    s = dend[i] = (d if d > s else s) + dur[i]
                seen[i] = s + lt[i]
            for i in back:
                s = 0.0
                for j in fs[i]:
                    if q[j] > s:
                        s = q[j]
                s += lt[i]
                if isd[i]:
                    d = qd[dnxt[i]]
                    s = qd[i] = (d if d > s else s) + dur[i]
                after[i] = s
                d = q[nxt[i]]
                q[i] = (d if d > s else s) + cost[i]
            cur.append(max(past[k], max([end[i] - cost[i] + q[i] for i in order]), max([dend[i] - dur[i] + qd[i] for i in dmas], default=0.0)))
        return cur

    def guess(k, seq, a, b, old):
        cost, lt = priced[k][0], late[k]
        end, seen, dend, q, after, qd = st[k]
        t, new, heads = end[a], {}, []
        for w in seq:
            for p in fp[w]:
                x = new.get(p) or seen[p]
                if x > t:
                    t = x
            heads.append(t)
            t += cost[w]
            if not isd[w]:
                new[w] = t + lt[w]
        t, new, best = q[b], {}, 0.0
        for w in seq[::-1]:
            x = after[w]
            for j in fs[w]:
                if j in new and new[j] + lt[w] > x:
                    x = new[j] + lt[w]
            t = new[w] = (x if x > t else t) + cost[w]
            x = heads.pop() + t
            if x > best:
                best = x
        if best < cur[k] and max(end[w] - cost[w] + q[w] for w in old) < cur[k] - 1e-6:
            return cur[k]
        return best

    def sort(order):
        cost, end, seen = priced[0][0], st[0][0], st[0][1]
        place = {x: n for n, x in enumerate(order)}
        return sorted(order, key=lambda x: (end[x] - cost[x] + 1e-9 * place[x]))
    dmas = []
    times(order, 0, m - 1)
    head, order, tail = order[:lo], order[lo:hi], order[hi:]
    inside = set(order)
    for part, ends in ((head, before), (tail[::-1], behind)):
        for i in part:
            ends[eng[i]] = i
            if isd[i]:
                ends["d"] = i
        ends.pop("n", 0)
    later = set(tail)
    past[:] = [max([x[1][i] + x[3][j] for i in head for j in fs[i] if j in later], default=0.0) for x in st]
    dmas = [i for i in order if isd[i]]
    top = len(order) - 1
    best, tabu, since = (1e30, order, eng[:]), {}, 0
    for it in range(steps + 1):
        if it % 100 == 0:
            if since > BACK:
                order, since = best[1], 0
                eng[:] = best[2]
                times(order, 0, top)
            order = sort(order)
            for i in range(m):
                ops[i]["e"] = eng[i]
            cur = times(order, 0, top)
        sc = sum(a / b for a, b in zip(cur, ref))
        since += 1
        if sc < best[0] - 1e-9:
            best, since = (sc, order, eng[:]), 0
        k = it % nm
        cost, dur = priced[k][0:2]
        end, seen, dend, q, after, qd = st[k]
        x = cur[k] - 1e-7
        i = next((i for i in order[::-1] if end[i] - cost[i] + q[i] > x or isd[i] and dend[i] - dur[i] + qd[i] > x), m)
        if i == m:
            continue
        rows, row, cand = [], [i], []
        while True:
            if isd[i] and dend[dprev[i]] > end[i]:
                j = dprev[i]
                while dend[dprev[j]] > end[j]:
                    j = dprev[j]
                if j not in inside:
                    break
                cand.append(("d", i, dprev[i]))
                i = j
                rows.append(row)
                row = [i]
                continue
            s, j = end[prev[i]], prev[i]
            for p in fp[i]:
                if seen[p] > s:
                    s, j = seen[p], p
            if j not in inside:
                break
            if j != prev[i] or s > end[j]:
                rows.append(row)
                row = []
            row.append(j)
            i = j
        rows.append(row)
        for row in rows:
            n = len(row)
            for x in range(min(n - 1, FAR)):
                cand += [("a", row[n - 2 - x], row[-1]), ("b", row[0], row[x + 1]), ("b", row[n - 2 - x], row[-1]), ("a", row[0], row[x + 1])][0:4 if x else 2]
            if n > 1:
                cand += [("f", w, w) for w in row if ops[w]["both"] and priced[0][0][w] < FLIP]
        pick = []
        for c in (cand if len(cand) <= WIDE else [cand[x] for x in rng.choice(len(cand), WIDE, replace=False)]):
            kind, v, u = c
            if kind == "d":
                pick.append((cur[k], c, None))
                continue
            if kind == "f":
                e = "s" if eng[v] == "v" else "v"
                x = order.index(v) - 1
                while x >= 0 and eng[order[x]] != e:
                    x -= 1
                a = order[x] if x >= 0 else before.get(e, m)
                arg = ([v], a, nxt[a] if a < m else next(w for w in order if eng[w] == e), [v])
            else:
                old, w = [u], u
                while w != v:
                    w = nxt[w]
                    old.append(w)
                if kind == "a":
                    if any(p in old or end[p] - cost[p] >= end[u] for p in ap[v]):
                        continue
                    arg = ([v] + old[:-1], prev[u], nxt[v], old)
                else:
                    if any(j in old or end[j] <= end[v] - cost[v] for j in aq[u]):
                        continue
                    arg = (old[1:] + [u], prev[u], nxt[v], old)
            pick.append((guess(k, *arg), c, arg))
        pick.sort(key=lambda x: x[0])
        good = []
        for one, c, arg in pick[0:TOP]:
            s2 = sum((one if x == k else guess(x, *arg) if arg else cur[x]) / ref[x] for x in range(nm)) + JIT * rng.random()
            kind, v, u = c
            if kind == "f":
                made = [(v, v)]
                s2 += LEAN * priced[0][0][v] / ref[0] * (1 if eng[v] == "s" else -1)
            else:
                made = [(v, u)] if kind == "d" else [(v, w) for w in arg[3][:-1]] if kind == "a" else [(w, u) for w in arg[3][1:]]
            if s2 < best[0] or not any(tabu.get(x, -1) >= it for x in made):
                good.append((s2, c, made))
        good.sort(key=lambda x: x[0])
        for s2, (kind, v, u), made in good:
            new = order if kind == "f" else moved(ops, order, v, u, succ if kind == "b" else pred, kind != "b")
            if new is None:
                continue
            if kind == "f":
                eng[v] = ops[v]["e"] = "s" if eng[v] == "v" else "v"
                a, b = 0, top
            else:
                a, b = order.index(u), order.index(v)
            order = new
            for x, y in made:
                tabu[y, x] = it + KEEP + int(rng.integers(KEEP))
            cur = times(order, a, b)
            break
    return best[0], head + best[1] + tail, best[2]


def shaken(ops, order, lo, hi, pred, rng):
    part = order[lo:hi]
    shift = {x: rng.normal(0.0, SHAKE[0]) * (rng.random() < SHAKE[1]) for x in sorted({ops[i]["tag"] for i in part})}
    key = {}
    for n, i in enumerate(part):
        key[i] = n + shift[ops[i]["tag"]] + rng.normal(0.0, SHAKE[2])
    for i in sorted(part):
        for p, f in pred[i]:
            if p in key and key[p] >= key[i]:
                key[i] = key[p] + 1e-3
    return order[:lo] + sorted(part, key=key.get) + order[hi:]


PLAN = {}


def plan(ops):
    if "order" in PLAN:
        return PLAN["order"]
    m = len(ops)
    above = []
    for o in ops:
        far = near = 0
        for p in o["full"]:
            far |= above[p]
            near |= 1 << p
        above.append(far | near)
        o["wait"] = (o["e"], [p for p in o["full"] if not far >> p & 1])
    pred = [[(p, True) for p in o["wait"][1]] + [(p, False) for p in o["order"]] for o in ops]
    succ = [[] for _ in ops]
    for i in range(m):
        for p, f in pred[i]:
            succ[p].append((i, f))
    priced = [price_ops(ops, md) for md in MODELS]
    cost, dur, lat = priced[0]
    wake = MODELS[0][5]
    up = np.array([o["up"] for o in ops])
    base = [0.0] * m
    for i in range(m - 1, -1, -1):
        b = 0.0
        for j, f in succ[i]:
            b = max(b, base[j] + (dur[i] + lat[i] + wake if f else 0.0))
        base[i] = b + cost[i] + (0.0 if succ[i] else dur[i] + lat[i])
    if DUE:
        for i in range(m - 1, -1, -1):
            b = -DUE[2]
            for j, f in succ[i]:
                b = max(b, base[j] + (dur[i] + lat[i] + wake + DUE[3] if f else 0.0))
            base[i] = max(b + cost[i] + (0.0 if succ[i] else dur[i] + lat[i]), -ops[i].get("due", 1e9))
    rng = np.random.default_rng(SEED)
    ref, best, field, first = None, None, [], [o["e"] for o in ops]
    for k in range(TRIES * STARTS):
        slope = float(rng.choice(SLOPES))
        if best is None:
            prio = np.array(base) + rng.normal(0.0, 0.5, m) * (k > 0)
        elif k % TRIES % 10 == 1 and TURN:
            prio = np.array(schedule(ops, succ, pred, list(best[4]), priced[0], wake, slope, True)[1])
        else:
            prio = best[2] + rng.normal(0.0, (8.0, 2.0, 0.5)[k % 3], m) * (rng.random(m) < (0.1, 0.03, 0.01, 0.005)[k % 4])
            slope = best[3] if k % 5 else slope
        order, fin = schedule(ops, pred, succ, [float(x) for x in prio + up], priced[0], wake, slope)
        ts = [run_order(ops, order, pr, md[5])[0] for pr, md in zip(priced, MODELS)]
        if ref is None:
            ref = ts
        sc = sum(a / b for a, b in zip(ts, ref))
        if best is None or sc <= best[0]:
            best = (sc, order, prio, slope, fin, ts)
        if k % TRIES == TRIES - 1:
            field.append(best[0:2] + (first,))
            best = None
    for steps, keep in STEPS:
        field = sorted((refine(ops, x[1], x[2], pred, succ, priced, ref, rng, steps) for x in field), key=lambda x: x[0])[0:keep]
    for k in range(ROUNDS):
        lo = int(rng.integers(-SPAN // 2, m - SPAN // 2))
        lo, hi = max(lo, 0), min(lo + SPAN, m)
        eng = field[0][2][:]
        for i in field[0][1][lo:hi]:
            if ops[i]["both"] and rng.random() < HOME:
                eng[i] = first[i]
        new = refine(ops, shaken(ops, field[0][1], lo, hi, pred, rng), eng, pred, succ, priced, ref, rng, SHORT, lo, hi)
        new = refine(ops, new[1], new[2], pred, succ, priced, ref, rng, 0)
        if new[0] <= field[0][0] + HEAT * (1 - k / ROUNDS):
            field[0] = new
    order = field[0][1]
    for o, e in zip(ops, field[0][2]):
        o["e"] = e
        o["wait"] = (e, o["wait"][1])
    PLAN["queues"] = field[0][2]
    PLAN["order"] = order
    PLAN["ops"] = ops
    return order


def kb(name, a, b):
    return ["%s_%d" % (name, i) for i in range(a // 8, (b + 7) // 8)]


def split(a, b, w):
    n = -(-(b - a) // w)
    cut = [a + 8 * ((b - a) // 8 * i // n) for i in range(n + 1)]
    return list(zip(cut, cut[1:]))


def rank_program(g, core, T, topo):
    rank = T.rank_of(core)
    if rank is None:
        return
    n = len(T.cores)
    Q = {"v": g.vector, "s": g.scalar, "p": g.tensor, "g": g, "y": g.sync}
    CSEM = {"v": "cv", "s": "cs", "p": "cp", "g": "cg"}
    ops = []
    lastw, readers, lastb = {}, {}, {}
    tag = ["set-up"]

    def add(e, kind, body, r, w, cost, up=0.0, bk=(), rows=0, nbytes=0, both=None, row=False):
        i = len(ops)
        full, order = set(), set()
        for k in r:
            if k in lastw:
                full.add(lastw[k])
        for k in w:
            if k in lastw:
                (order if row else full).add(lastw[k])
            full.update(readers.get(k, []))
        for k in bk:
            if k in lastb:
                (order if ops[lastb[k]]["e"] == e and not both and not ops[lastb[k]]["both"] else full).add(lastb[k])
            lastb[k] = i
        full.discard(i)
        ops.append({"tag": tag[0], "e": e, "kind": kind, "body": body, "full": sorted(full), "order": sorted(order - full),
                    "cost": cost, "up": up, "name": (list(w) + [""])[0], "rows": rows, "bytes": nbytes, "both": both})
        for k in r:
            readers.setdefault(k, []).append(i)
        for k in w:
            lastw[k] = i
            readers[k] = []

    def V(f, r=(), w=(), c=cv(1), bk=(), row=False):
        add("v", "c", [f], r, w, c, bk=bk, row=row)

    def S(f, r=(), w=(), c=cv(1), bk=()):
        add("s", "c", [f], r, w, c, bk=bk)

    def VS(e, fv, fs, r, w, c, bk=()):
        add(e, "c", None, r, w, c, bk=bk, both={"v": [fv], "s": [fs]})

    def move(e, out, in_, r, w, c, scale=None, bias=None, bk=()):
        sc, op = ([scale, bias], [A.mult, A.add]) if scale is not None and bias is not None else \
            ([scale, None], [A.mult]) if scale is not None else ([bias or 0.0, None], [A.add])
        kw = {k: x for k, x in (("scale", scale), ("bias", bias)) if x is not None}
        func = AF.Copy if bias is None or isinstance(bias, float) else AF.Identity
        VS(e, lambda q: q.tensor_scalar(out, in_, *sc, *op), lambda q: q.activation(out, in_, func, **kw), r, w, c, bk)

    def PE(fs, r, w, c, bk):
        add("p", "c", fs, r, w, c, bk=bk)

    def G(f, r=(), w=(), c=cfix(0.2), up=0.0):
        add("g", "c", [f], r, w, c, up)

    def dma(e, pairs, r, w, rows, rb, up=0.0, issued=()):
        before = [lastw[k] for k in issued]
        add(e, "d", pairs, r, w, cfix((0.6 if e == "g" else 0.06) * len(pairs)), up, rows=rows / 16, nbytes=rows * rb / 16)
        ops[-1]["order"] += before

    PF, RF, GF, CQ, BQ, RQ, INC, W2, W3, SLF, HR, HX, HD, C14, C15, TOP, R0, VB, VC = 0, 1, 2, 3, 4, 5, 6, 7, 8, 9, 12, 13, 14, 15, 16, 17, 18, 20, 21
    sm = T.sm
    col = lambda c: sm[:, c:c + 1]
    TT = lambda t: T["TT%d" % (t % 2)]
    tk = lambda t, a, b: kb("TT%d" % (t % 2), a, b)
    TH = lambda t, a, b: T["TH%d" % (t % 2)][:, 2 * a + 1:2 * b:2]
    fk = lambda t, a, b: kb("TH%d" % (t % 2), a, b)
    win = lambda t: T.p0[:, 0:4096] if t == 0 else T["F%d" % t][:, 0:4096]
    wkey = lambda t: ["win%d" % t] + ([] if t else ["win0a"])
    PKn = lambda t, a, b: T.PK[:, 768 + 256 * t + a:768 + 256 * t + b]
    pk = lambda t, a, b: kb("PK", 768 + 256 * t + a, 768 + 256 * t + b)

    def alist(t, e, a, b):
        return TT(t - 1)[:, a:b] if e == 1 and t > 0 else T.AL[:, LW * (e - 1) + a:LW * (e - 1) + b]

    def ak(t, e, a, b):
        return tk(t - 1, a, b) if e == 1 and t > 0 else kb("AL%d" % e, a, b)

    def aless(t, e, a, b):
        if e == 1:
            return TH(t - 1, a, b), fk(t - 1, a, b)
        return (T.AH if A16 else T.AE)[:, LW * (e - 2) + a:LW * (e - 2) + b], kb("AE%d" % e, a, b)

    add("v", "c", [lambda q: q.memset(T.VT[:], 0)], [], ["VT"], cv(1024), up=1650)
    clear = len(ops) - 1
    pkJ = lambda a, b: T.PI[:, 768 + a:768 + b]
    loads = {
        "win0a": ([(T.p0[:, 0:PA], T.price[:, 0:PA])], ["win0a"], 128, 2 * PA),
        "VT": ([(T.VT[0:128:16, :], T.prev[:])] + [(T.VT[1:128:16, :], T.packs[0:128:16, :])], ["VT"], 128, 512),
        "pkA": ([(pkJ(0, LA), T.packs[:, 768:768 + LA]), (T.slI[:, 0:3], T.slack[:])], ["pkA", "slI"], 256, 2 * LA + 6),
        "TIa": ([(T.TI[:, 0:LA], T.lots[:, 0:LA])], ["TIa"] + kb("TI", 0, LA), 128, 4 * LA),
        "pkJ": ([(pkJ(LA, 256), T.packs[:, 768 + LA:1024])], ["pkJ"], 128, 1024 - 4 * LA),
        "pkC": ([(pkJ(256, LW), T.packs[0:128:16, 768:1024]), (T.TI[:, 256:LW], T.lots[0:128:16, :])], ["pkC"] + kb("TI", 256, LW), 256, 64),
        "win0": ([(T.p0[:, PA:4096], T.price[:, PA:4096])], ["win0"], 128, 8192 - 2 * PA),
        "TI": ([(T.TI[:, LA:256], T.lots[:, LA:256])], ["TI"] + kb("TI", LA, 256), 128, 1024 - 4 * LA),
        "pkI": ([(T.PI[:, 0:768], T.packs[:, 0:768])], ["pkI"], 128, 3072),
        "wtI": ([(T.small[:, 4:5], T.wt[:])], ["wtI"], 128, 4),
        "incI": ([(T.small[:, 0:1], T.inc[:])], ["incI"], 128, 4),
    }
    for x, y in zip([None] + LOADS, LOADS):
        dma("y", loads[y][0], [], *loads[y][1:], up=1500, issued=[x] if x else [])

    fl = dict(allow_small_or_imprecise_dtypes=True)
    WB, CB = 256 // NB, 16 // NB
    seg = [WB * c - 8 * c * (c - 1) for c in range(CB + 1)]
    SEG = seg[CB]
    G(lambda q: q.iota(T.pI[:, 0:1], [[1, 1]], 0, 1), w=["pI"], up=100)
    G(lambda q: q.iota(T.row8[:], [[1, 8]], 0, 0, **fl), w=["row8"], up=100)
    G(lambda q: q.iota(T.IX[:], [[1, 128]], 0, 0, **fl), w=["IX"], c=cgp(128), up=100)
    G(lambda q: q.iota(T.i16[:, 0:16], [[16, 16]], 0, 0, **fl), w=["i16"], up=100)
    G(lambda q: q.iota(T.i16[:, 16:32], [[0, NB], [16, CB]], 0, 0, **fl), w=["j16"], up=100)
    G(lambda q: q.iota(T.IXG[:], [[1, 8], [0, 16]], 0, 0, **fl), w=["IXG"], c=cgp(128), up=100)
    G(lambda q: q.iota(sm[:, HR:HX + 1], [[8 * 512, 2]], -17 * 256, 0, **fl), w=["HR", "HX"], up=100)
    G(lambda q: q.iota(col(HD), [[0, 1]], 512 * WB - 768, 0, **fl), w=["HD"], up=100)
    G(lambda q: q.iota(T.KS[:], [[0, 72]], 0, 0, **fl), w=["KS%d" % d for d in range(4)], c=cgp(72), up=100)
    G(lambda q: q.iota(T.KO[:], [[4096, 2], [0, 18]], 0, 0, **fl), w=["KO"])
    if "o" in GV:
        V(lambda q: q.memset(T.ones[:], 1.0), w=["ones"], c=cv(512))
    else:
        G(lambda q: q.iota(T.ones[:], [[0, 1024]], 1, 0, **fl), w=["ones"], c=cgp(1024))
    if "m" in GV:
        V(lambda q: q.memset(T.MK[:], 1.0), w=["MK"], c=cv(512))
        V(lambda q: q.memset(T.MK[:, 0:1024:16], 0.0), w=["MK"])
    else:
        G(lambda q: q.affine_select(T.MK[:], T.ones[:], [[0, 64], [1, 16]], A.not_equal, 0.0, 0, 0), r=["ones"], w=["MK"], c=cgp(1024, 0.17))
    G(lambda q: q.iota(T.cB[:], [[0, 384]], 0, 0, **fl), w=["cB"], c=cgp(384), up=60)
    NI = 3 if RBP else 8
    for x in range(NI):
        G(lambda q, x=x: q.iota(T.IDW[:, 512 * x:512 * x + 512], [[1, 512]], 512 * x, 0, **fl), w=["IDW%d" % x], c=cgp(512))
    IDW = ["IDW%d" % x for x in range(NI)]
    idw = T.IDW[:, 0:512 * NI]
    for t in (1, 2):
        V(lambda q, t=t: q.memset(T.big[:, WB * t - WB:WB * t], 2.0 ** (16 * t)), w=["big%d" % t])
    for x in range(2 * RBP):
        G(lambda q, x=x: q.affine_select(T.SELT[:, 1024 * x:1024 * x + 1024], T.ones[:], [[-1, 8], [-16, 8], [0, 16]], A.is_equal, 0.0, -8 * x, 1),
          r=["ones"], w=["SELT%d" % x], c=cgp(1024, 0.17))
    for t in range(2):
        G(lambda q, t=t: q.iota(T["F%d" % (t + 1)][:, 4096:4352], [[0, 256]], 0, 0, **fl), w=["dump%d" % t], c=cgp(256))
    G(lambda q: q.iota(T.p0[:, 4096:4352], [[0, 256]], 0, 0, **fl), w=["dump3"], c=cgp(256))
    for c in range(CB):
        G(lambda q, c=c: q.iota(T.EI[:, seg[c]:seg[c + 1]], [[1, WB - 16 * c]], 0, 0, **fl), w=["EI%d" % c], c=cgp(WB - 16 * c), up=60)

    add("v", "c", [lambda q: q.memset(T.SELK[:], 0.0)], [], ["SELK"], cv(1024))
    ops[-1]["order"].append(clear)
    V(lambda q: q.memset(T.one16[:], 1.0), w=["one16"])
    for e in (1, 2, 3):
        if "s" in GV:
            V(lambda q, e=e: q.memset(T.SG[:, SW * e - SW:SW * e], 0.0), w=kb("SG%d" % e, 0, LW), c=cv(SW, .5))
        else:
            G(lambda q, e=e: q.iota(T.SG[:, SW * e - SW:SW * e], [[0, SW]], 0, 0, **fl), w=kb("SG%d" % e, 0, LW), c=cgp(SW), up=50)
    for ap, x in ((T.cB[0:1, 0:128], -0.5 * BIG), (T.cB[0:1, 128:256], 33.0), (T.cB[32:33, 128:256], 192.0 * 2048), (T.cB[32:33, 256:384], 2048.0)):
        V(lambda q, ap=ap, x=x: q.memset(ap, x), w=["cB"])
    V(lambda q: q.tensor_copy(col(PF), T.pI[:, 0:1]), r=["pI"], w=["PF"])
    for x, (y, op) in enumerate(((15, A.bitwise_and), (4, A.logical_shift_right), (CB - 1, A.bitwise_and))):
        V(lambda q, x=x, y=y, op=op: q.tensor_scalar(T.pI[:, 1 + x:2 + x], T.pI[:, 0:1], y, None, op), r=["pI"], w=["pI%d" % (1 + x)])
    V(lambda q: q.tensor_scalar(T.pI[:, 4:5], T.pI[:, 0:1], CB.bit_length() - 1, NB - 1, A.logical_shift_right, A.bitwise_and), r=["pI"], w=["pI4"])
    V(lambda q: q.tensor_copy(sm[:, RF:BQ + 1], T.pI[:, 1:5]), r=["pI1", "pI2", "pI3", "pI4"], w=["RF"])
    V(lambda q: q.tensor_scalar(T.B8[:], T.row8[:], col(GF), None, A.is_equal), r=["row8", "RF"], w=["B8"])
    move("s", T.L1c[:], T.i16[:], ["i16", "j16", "RF"], ["L1c"], cv(1), bias=col(RF))
    for gg in range(8):
        V(lambda q, gg=gg: q.tensor_scalar(T.SELK[:, 16 * gg:16 * gg + 129 * 15 + 1:129], T.one16[:],
                                           T.B8[:, gg:gg + 1], BIG, A.mult, A.mult),
          r=["one16", "B8", "SELK"], w=["SELK%d" % gg])
    SELK = ["SELK"] + ["SELK%d" % gg for gg in range(8)]
    V(lambda q: q.tensor_copy(sm[:, SLF:SLF + 3], T.slI[:, 0:3]), r=["slI"], w=["SLF"])
    for a, b, k in L0:
        V(lambda q, a=a, b=b: q.tensor_copy(T.AL[:, a:b], pkJ(a, b)), r=k, w=ak(0, 1, a, b), c=cv(b - a))
        V(lambda q, a=a, b=b: q.tensor_copy(T.TT0[:, a:b], T.TI[:, a:b]), r=kb("TI", a, b), w=tk(0, a, b), c=cv(b - a))
        V(lambda q, a=a, b=b: q.tensor_scalar(TH(0, a, b), T.TT0[:, a:b], -2048.0, None, A.add), r=tk(0, a, b), w=fk(0, a, b), c=cv(b - a, .5))
        V(lambda q, a=a, b=b: q.tensor_scalar(TH(1, a, b), T.AL[:, a:b], -2048.0, None, A.add), r=ak(0, 1, a, b), w=fk(1, a, b), c=cv(b - a, .5))
    if not PKI:
        V(lambda q: q.tensor_copy(PKn(0, 0, 256), pkJ(0, 256)), r=["pkA", "pkJ"], w=pk(0, 0, 256), c=cv(256))
        V(lambda q: q.tensor_copy(T.PK[:, 0:768], T.PI[:, 0:768]), r=["pkI"], w=kb("PK", 0, 768), c=cv(768))
    V(lambda q: q.tensor_scalar(sm[:, R0:R0 + 2], T.row8[:, 0:2], col(RF), None, A.is_equal), r=["row8", "RF"], w=["R0"])
    if VM:
        V(lambda q: q.tensor_scalar(col(VB), col(R0 + 1), -2048.0, None, A.mult), r=["R0"], w=["VB"])
        V(lambda q: q.tensor_scalar(col(VC), col(R0 + 1), 2.0 ** -13, col(R0), A.mult, A.add), r=["R0"], w=["VC"])
        for i in range(2):
            S(lambda q, i=i: q.activation(T.SEL1[:, 1024 * i:1024 * i + 1024], T.SELK[:, 1024 * i:1024 * i + 1024], AF.Copy, scale=col(R0 + 1)),
              r=SELK + ["R0"], w=["SEL1%d" % i], c=cv(1024))
    V(lambda q: q.tensor_scalar(T.VH[:], T.VT[:, 768:1024], col(R0), None, A.mult), r=["VT", "R0"], w=["VH"], c=cv(256))
    V(lambda q: q.memset(col(TOP), 255.4921875), w=["TOP"])
    V(lambda q: q.tensor_scalar(T.IDN[:, 0:128], T.IX[:], col(PF), None, A.is_equal), r=["IX", "PF"], w=["IDN"], c=cv(128))
    S(lambda q: q.activation(T.IDN[:, 128:256], T.IDN[:, 0:128], AF.Copy, scale=-1.0), r=["IDN"], w=["IDM"], c=cv(128))
    S(lambda q: q.activation(T.IDH[:], T.IDN[:], AF.Copy), r=["IDN", "IDM"], w=["IDH"], c=cv(256))
    S(lambda q: q.activation(T.IDB[:], T.IDN[:], AF.Copy, scale=-2048.0), r=["IDN", "IDM"], w=["IDB"], c=cv(256))
    move("s", col(RQ), col(RF), ["RF"], ["RQ"], cv(1), bias=1.0)
    V(lambda q: q.tensor_scalar(T.EM[:, 0:SEG], T.EI[:, 0:SEG], col(RQ), 1.0e16, A.is_equal, A.mult),
      r=["RQ"] + ["EI%d" % c for c in range(CB)], w=["EM"], c=cv(SEG, .5))
    move("s", col(C14), col(CQ), ["RF"], ["c14"], cv(1), -8.0, WB - 8.0)
    move("s", col(C15), col(BQ), ["RF"], ["c15"], cv(1), float(SEG), WB - 1.0)
    V(lambda q: q.tensor_scalar(T.E16[:, 0:1], col(C14), col(CQ), col(C15), A.mult, A.add), r=["c14", "c15", "RF"], w=["E16"])
    move("s", T.DJt[:], T.L1c[:, 0:16], ["L1c"], ["DJt"], cv(1), SQ, 2048.0 * SQ + SQ * SQ)
    add("s", "c", [lambda q: q.activation(T.dF[:], T.L1c[:, 16:32], AF.Sigmoid, bias=col(HD), scale=-512.0)], ["L1c", "HD"], ["dF"],
        (1, 64, 0, 0, 0, 1.3), up=90)
    V(lambda q: q.tensor_tensor(T.dE[:], T.dF[:], T.DJt[:], A.mult), r=["dF", "DJt"], w=["dE"])
    move("s", T.DJ[:], T.dE[:], ["dE"], ["DJ"], cv(1), bias=-SQ * SQ)
    V(lambda q: q.tensor_scalar(col(INC), T.small[:, 0:1], 1.0 / 64, None, A.mult), r=["incI"], w=["INC"])
    if True:
        move("s", T.IDI[:], T.IDN[:, 0:128], ["IDN", "INC"], ["IDI"], cv(128), scale=col(INC))
    V(lambda q: q.tensor_scalar(col(W2), T.small[:, 4:5], 2.0, None, A.mult), r=["wtI"], w=["W2"])
    V(lambda q: q.tensor_scalar(col(W3), T.small[:, 4:5], 2.0 / BIG, None, A.mult), r=["wtI"], w=["W3"])
    V(lambda q: q.tensor_scalar(T.WT[:], T.IXG[:], col(GF), col(W2), A.is_equal, A.mult), r=["IXG", "RF", "W2"], w=["WT"], c=cv(128))
    if TAIL:
        V(lambda q: q.tensor_scalar(T.BE[:], T.IXG[:], col(GF), BIG, A.is_equal, A.mult), r=["IXG", "RF"], w=["BE"], c=cv(128))
    for i in range(2):
        S(lambda q, i=i: q.activation(T.SELW[:, 1024 * i:1024 * i + 1024], T.SELK[:, 1024 * i:1024 * i + 1024], AF.Copy, scale=col(W3)),
          r=SELK + ["W3"], w=["SELW%d" % i], c=cv(1024))

    KS, KM = T.KS, T.KM
    LU = lambda d: T.LU[:, 18 * d:18 * d + 16]

    def conv(d):
        z = T.ZC[:, 0:16]
        PE([lambda q, k=k: q.matmul(z, T.SELK[:, 128 * k:128 * k + 128], T.VH[:, k:256:16], k == 0, k == 15)
            for k in range(16)], ["VH"] + SELK, ["zc"], cmm(16, 16), ["bC"])
        if d < 3:
            V(lambda q: q.tensor_scalar(LU(d), z, 1.0 / BIG, 0.25, A.mult, A.add), r=["zc"], w=["LU%d" % d], bk=["bC"])
        move("s", KS[:, 18 * d:18 * d + 16], z, ["zc"], ["KS%d" % d], cv(1), 1.0 / BIG, 4096.0 * (d - 1), ["bC"])

    def parents(d):
        if VM:
            return V(lambda q: q.tensor_scalar(T.VH[:], T.VT[:].indirect(LU(d)), col(VB), col(VC), A.add, A.mult),
                     r=["VT", "VB", "VC", "LU%d" % d], w=["VH"], c=cgat(256))
        V(lambda q: q.tensor_scalar(T.VH[:], T.VT[:].indirect(LU(d)), col(R0), None, A.mult), r=["VT", "R0", "LU%d" % d], w=["VH"], c=cgat(256))

    def first(e):
        z = T.ZX[:, 0:16]
        lots, lk = aless(0, e, 256, LW)
        if VM:
            PE([lambda q, k=k: q.matmul(z, T.SEL1[:, 128 * k:128 * k + 128], T.VH[:, 16 * k:16 * k + 16], k == 0, k == 15)
                for k in range(16)], ["VH", "SEL10", "SEL11"], ["zX"], cmm(16, 16), ["bX"])
            V(lambda q: q.tensor_scalar(alist(0, e, 256, LW), z, 8192.0 / BIG, 2048.0, A.mult, A.add), r=["zX"], w=ak(0, e, 256, LW), bk=["bX"])
            if A16:
                V(lambda q: q.tensor_scalar(lots, z, 8192.0 / BIG, None, A.mult), r=["zX"], w=lk, bk=["bX"])
            else:
                move("s", lots, z, ["zX"], lk, cv(1), scale=8192.0 / BIG, bk=["bX"])
            return
        V(lambda q: q.tensor_scalar(T.VG[:], T.VT[:].indirect(LU(e - 1)), -2048.0, col(R0 + 1), A.add, A.mult),
          r=["VT", "R0", "LU%d" % (e - 1)], w=["VG"], c=cgat(256))
        PE([lambda q, k=k: q.matmul(z, T.SELK[:, 128 * k:128 * k + 128], T.VG[:, 16 * k:16 * k + 16], k == 0, k == 15)
            for k in range(16)], ["VG"] + SELK, ["zX"], cmm(16, 16), ["bX"])
        V(lambda q: q.tensor_scalar(alist(0, e, 256, LW), z, 1.0 / BIG, 2048.0, A.mult, A.add), r=["zX"], w=ak(0, e, 256, LW), bk=["bX"])
        move("s", lots, z, ["zX"], lk, cv(1), scale=1.0 / BIG, bk=["bX"])

    def keys(t):
        c = 18 if t == 2 else 36
        move("s", KS[:, 0:16], T.L1c[:, 0:16], ["L1c"], ["KS0"], cv(1), bias=-4096.0 + 768 + 256 * t)
        move("s", KM[:, 3, 0:c], KS[:, 36:36 + c], ["KS%d" % d for d in range(2, 2 + c // 18)], ["KM3"], cv(1), bias=-3 * 4096.0)

    def package(t, e):
        src, r = T.PK[:, 0:1024 + 256 * t].indirect(LU(e - 1)), kb("PK", 0, 1024 + 256 * t) + ["LU%d" % (e - 1)]
        if PKI:
            own = (t, e) == (2, 2)
            src, r = T.PI[:, 0:1024 + 256 * own].indirect(LU(e - 1)), ["pkI", "pkA", "pkJ", "LU%d" % (e - 1)] + kb("PI", 0, 256 * own)
        lots, lk = aless(t, e, 0, 256)
        if A16 == 3:
            wide, wk = T.AE[:, LW * (e - 2):LW * (e - 2) + 256], ["AF%d" % e]
            move("s", wide, src, r, wk, cgat(256), bias=-2048.0)
            V(lambda q: q.tensor_scalar(alist(t, e, 0, 256), wide, 2048.0, None, A.add), r=wk, w=ak(t, e, 0, 256), c=cv(256))
            G(lambda q: q.affine_select(lots, wide, [[0, 256]], A.is_equal, 0.0, 0, 0), r=wk, w=lk, c=cgp(256, 0.17))
        elif A16:
            if A16 == 2:
                move("s", T.AE[:, 0:256], src, r, ["AF"], cgat(256))
                V(lambda q: q.tensor_copy(alist(t, e, 0, 256), T.AE[:, 0:256]), r=["AF"], w=ak(t, e, 0, 256), c=cv(256))
            else:
                V(lambda q: q.tensor_copy(alist(t, e, 0, 256), src), r=r, w=ak(t, e, 0, 256), c=cgat(256))
            V(lambda q: q.tensor_scalar(lots, alist(t, e, 0, 256), -2048.0, None, A.add), r=ak(t, e, 0, 256), w=lk, c=cv(256, .5))
        else:
            move("s", lots, src, r, lk, cgat(256), bias=-2048.0)
            V(lambda q: q.tensor_scalar(alist(t, e, 0, 256), lots, 2048.0, None, A.add), r=lk, w=ak(t, e, 0, 256), c=cv(256))

    def clist(t, e):
        dma("y", [(alist(t, e, 256, LW), alist(t, e, 0, 256)[t:128:16, :])], ak(t, e, 0, 256) + ["freeR%d" % (t - 1)] * (e == 1), ak(t, e, 256, LW), 128, 32)
        if e == 1:
            dma("y", [(PKn(t, 256, LW), PKn(t, 0, 256)[t:128:16, :])], pk(t, 0, 256), pk(t, 256, LW), 128, 64)
            V(lambda q: q.tensor_scalar(TH(t - 1, 256, LW), alist(t, e, 256, LW), -2048.0, None, A.add), r=ak(t, e, 256, LW), w=fk(t - 1, 256, LW))
        else:
            (a, ka), (b, kc) = aless(t, e, 0, 256), aless(t, e, 256, LW)
            dma("y", [(b, a[t:128:16, :])], ka, kc, 128, 32 if A16 else 64)

    def gy(t, e, a, b):
        o = 16 * LW * (e - 1)
        move("s", T.Y[:, o + 16 * a:o + 16 * b], win(t).indirect(alist(t, e, a, b)), wkey(t) + ak(t, e, a, b) + ["SLF"],
             kb("Y%d" % e, a, b), cgat(16 * (b - a)), bias=col(SLF + t))
        if LATE and t == 2 and e > 1 and a < 256:
            ops[-1]["order"] += sorted({lastw[k] for k in kb("Y%d" % (e - 1), 0, 256)})
            ops[-1]["both"], ops[-1]["body"] = None, ops[-1]["both"]["s"]

    def diff(t, e, h):
        a, b = CH[t][h]
        m = b - a
        lots, lk = aless(t, e, a, b)
        narrow = e == 1 or A16
        ID = T.IDH if narrow else T.IDN
        z = T["Z%d" % h]
        d = z[:, 192:192 + 2 * m:2]
        last = LAST and (t, e) == (2, 3) and b <= 256
        PE([lambda q: q.matmul(d, ID[:, 0:128], lots, True, False),
            lambda q: q.matmul(d, T.IDH[:, 128:256], TH(t, a, b), False, True),
            lambda q: q.matmul(z[:, 193:192 + 2 * m:2], T.IDH[:, 0:128], TH(t, a, b), True, not last)] +
           [lambda q: q.matmul(z[:, 193:192 + 2 * m:2], T.cB[32:33, 256:384], T.ones[32:33, 0:m], False, True)] * last,
           ["IDN", "IDM", "IDH"] + ["cB", "ones"] * last + lk + fk(t, a, b), ["zD%d" % h], cmm(m, 2 + last + (1 if narrow else 4)), ["bZ%d" % h])

    def gx(t, e, a, b):
        o = 16 * LW * (e - 1)
        c0, c1 = 16 * a, 16 * b
        lst = win(t).indirect(TT(t)[:, a:b])
        r = wkey(t) + tk(t, a, b)
        if (t, e, a) not in SR:
            V(lambda q: q.tensor_tensor(T.C[:, c0:c1], lst, T.Y[:, o + c0:o + c1], A.is_gt), r=r + kb("Y%d" % e, a, b), w=kb("C", a, b), c=cgat(c1 - c0))
            if DUE and a < 256:
                ops[-1]["due"] = DUE[0] + DUE[1] * (3 * t + e - 1 + a / 256)
            return
        S(lambda q: q.activation(T.XS[:, 0:c1 - c0], lst, AF.Copy), r=r, w=["XS"], c=cgat(c1 - c0))
        if LATE:
            ops[-1]["order"] += sorted({lastw[k] for k in kb("Y%d" % e, 0, 256)})
        for x, y in split(a, b, 32):
            z = T.ZX[:, 0:16 * (y - x)]
            PE([lambda q, x=x, y=y, z=z: q.matmul(z, T.IDB[:, 128:256], T.XS[:, 16 * x - c0:16 * y - c0], True, False),
                lambda q, x=x, y=y, z=z: q.matmul(z, T.IDB[:, 0:128], T.Y[:, o + 16 * x:o + 16 * y], False, True)],
               ["XS", "IDB"] + kb("Y%d" % e, x, y), ["zX"], cmm(16 * (y - x), 2), ["bX"])
            S(lambda q, x=x, y=y, z=z: q.activation(T.C[:, 16 * x:16 * y], z, AF.Sigmoid, bias=col(HX), scale=0.25),
              r=["zX", "HX"], w=kb("C", x, y), c=cv(16 * (y - x)), bk=["bX"])

    def tops(t, e, h):
        a, b = CH[t][h]
        m, l = b - a, min(b, 256)
        Z, dk, bk = T["Z%d" % h], ["zD%d" % h], ["bZ%d" % h]
        z = Z[:, 0:m]
        ps = PS if a < 256 else 1
        for x in range(0, 16, 16 // ps):
            add("p", "c", [lambda q, k=k: q.matmul(z, T.SELK[:, 128 * k:128 * k + 128], T.C[:, 16 * a + k:16 * b:16], k == 0, k == 15) for k in range(x, x + 16 // ps)],
                kb("C", a, b) + SELK, ["zC%d" % h], cmm(m, 16 // ps), bk=bk, row=x > 0)
        o = SW * (e - 1)
        mask, mk = T.SG[:, o + 2 * a + 1:o + 2 * b:2], kb("SG%d" % e, a, b)
        VS("s", lambda q: q.tensor_scalar(mask, z, 8.5 * BIG, None, A.is_gt),
           lambda q: q.activation(mask, z, AF.Sigmoid, bias=col(HR), scale=512.0 / BIG), ["zC%d" % h, "HR"], mk, cv(m), bk)
        if LAST and (t, e) == (2, 3) and b <= 256:
            V(lambda q: q.tensor_tensor(T.qF[:, a:b], Z[:, 192:192 + 2 * m:2], mask, A.mult), r=dk + mk, w=kb("qF", a, b), c=cv(m), bk=bk)
            V(lambda q: q.tensor_tensor(PKn(t + 1, a, b), Z[:, 193:192 + 2 * m:2], T.qF[:, a:b], A.add), r=dk + kb("qF", a, b), w=pk(t + 1, a, b), c=cv(m), bk=bk)
            return
        V(lambda q: q.tensor_tensor_scan(T["TH%d" % (t % 2)][:, 2 * a:2 * b], T.SG[:, o + 2 * a:o + 2 * b], Z[:, 192:192 + 2 * m], 0.0, A.mult, A.add),
          r=dk + mk, w=fk(t, a, b), c=cv(2 * m), bk=bk)
        x = max(a, 256) if (t, e) == (2, 3) else a
        if x < b:
            V(lambda q: q.tensor_scalar(TT(t)[:, x:b], TH(t, x, b), 2048.0, None, A.add), r=fk(t, x, b), w=tk(t, x, b), c=cv(b - x, .5))
        if e == 3 and a < l and t in PKS:
            y = Z[:, 384:384 + l - a]
            PE([lambda q: q.matmul(y, T.IDH[:, 0:128], TH(t, a, l), True, True)], ["IDH"] + fk(t, a, l), ["zP%d" % h], cmm(l - a), bk)
            move("s", PKn(t + 1, a, l), y, ["zP%d" % h], pk(t + 1, a, l), cv(l - a), bias=2048.0, bk=bk)
        elif e == 3 and a < l:
            V(lambda q: q.tensor_scalar(PKn(t + 1, a, l), TH(t, a, l), 2048.0, None, A.add), r=fk(t, a, l), w=pk(t + 1, a, l), c=cv(l - a))
        if PKI and (t, e) == (0, 3) and a < l:
            V(lambda q: q.tensor_copy(pkJ(256 + a, 256 + l), TT(t)[:, a:l]), r=tk(t, a, l), w=kb("PI", a, l) + ["pkC"] * (a == 0), c=cv(l - a))
        if e == 3 and b == LW:
            V(lambda q: q.tensor_scalar(T.CF[:], TH(t, 256, LW), -SQ, None, A.mult), r=fk(t, 256, LW), w=["CF"])

    def gm(t, a, b):
        x, y = 16 * a, 16 * b
        move("s", T.XM[:, x:y], win(t).indirect(TT(t)[:, a:b]), wkey(t) + tk(t, a, b), kb("XM", a, b), cgat(y - x))
        V(lambda q: q.tensor_tensor_scan(T.SM[:, x:y], T.MK[:, 0:y - x], T.XM[:, x:y], 0.0, A.mult, A.max),
          r=["MK"] + kb("XM", a, b), w=kb("SM", a, b), c=cv((y - x) // 2))

    def tnew(t, a, b):
        l = min(b, 256)
        m = b - a
        sk = (kb("SM", 0, 256) if b == LW else kb("SM", a, b)) + ["WT", "SELW0", "SELW1"]

        def sums(z, first):
            fs = [lambda q: q.matmul(z[:, a:l], T.WT[:], T.SM[:, 16 * a + 15:16 * l:16], first, first)] if l > a else []
            if b == LW:
                fs += [lambda q, k=k: q.matmul(z[:, 256:LW], T.SELW[:, 128 * k:128 * k + 128], T.SM[:, 256 * k + 15:256 * k + 256:16],
                                               first and k == 0, first and k == 15) for k in range(16)]
            return fs
        pc = cmm(m, 1) if b < LW else cmm(64, 16 + m // 64)
        if b == LW and KSUM:
            zu, zk, bu = T.Z0[:, 256:256 + m], "zK", "bZ0"
            PE([lambda q: q.matmul(zu, T.cB[0:1, 256:384], T.ones[0:1, 0:m], True, False)], ["cB", "ones"], [zk], cmm(m), [bu])
            for x, y in MP:
                fs = [lambda q, k=k: q.matmul(zu[:, l - a:m], T.SELW[:, 128 * k:128 * k + 128], T.SM[:, 256 * k + 15:256 * k + 256:16], False, k == 15)
                      for k in range(x // 16, y // 16)]
                if y == 256:
                    fs = [lambda q: q.matmul(zu[:, 0:l - a], T.WT[:], T.SM[:, 16 * a + 15:16 * l:16], False, False)] + fs
                add("p", "c", fs, kb("SM", min(x, a) if y == 256 else x, y) + ["WT", "SELW0", "SELW1"], [zk], cmm(64, len(fs)), bk=[bu], row=True)
        else:
            zu, zk, bu = T.ZM[:, a:b], "zU", "bM"
            PE(sums(T.ZM, True), sk, ["zU"], pc, ["bM"])
        if b == LW and UCOPY:
            move("s", T.kf[:, a:b], zu, [zk], kb("kf", a, b), cv(m), 1.0 / 2048, 191.5 + 1.0 / 2048, [bu])
            move("s", T.uF[:, a:b], zu, [zk], ["uF"], cv(m), bias=192.0 * 2048 + 33, bk=[bu])
            PE([lambda q: q.matmul(T.ZR[:, a:b], T.IDB[:, 0:128], T.kf[:, a:b], True, False),
                lambda q: q.matmul(T.ZR[:, a:b], T.IDN[:, 0:128], T.uF[:, a:b], False, True)], ["IDB", "IDN", "uF"] + kb("kf", a, b), ["zR"], cmm(m, 5), ["bR"])
        else:
            PE([lambda q: q.matmul(T.ZR[:, a:b], T.cB[0:33, 128:256], T.ones[0:33, 0:m], True, False)] + sums(T.ZR, False),
               sk + ["cB", "ones"], ["zR"], pc, ["bR"])
            move("s", T.kf[:, a:b], T.ZM[:, a:b], ["zU"], kb("kf", a, b), cv(m), 1.0 / 2048, 191.5 + 1.0 / 2048, ["bM"])
            PE([lambda q: q.matmul(T.ZR[:, a:b], T.IDB[:, 0:128], T.kf[:, a:b], False, True)], ["IDB"] + kb("kf", a, b), ["zR"], cmm(m), ["bR"])
        V(lambda q: q.tensor_tensor(T.qF[:, a:b], T.ZR[:, a:b], PKn(t + 1, a, b), A.mult), r=["zR"] + pk(t + 1, a, b), w=kb("qF", a, b), c=cv(m), bk=["bR"])
        V(lambda q: q.tensor_scalar(T.qI[:, a:b], T.qF[:, a:b], 2464.0 * (t + 1), None, A.add), r=kb("qF", a, b), w=kb("qI", a, b), c=cv(m))
        V(lambda q: q.tensor_scalar(T.TI[:, a:b], T.qI[:, a:b], 5, 4095, A.logical_shift_right, A.bitwise_and),
          r=kb("qI", a, b), w=kb("TI", a, b), c=cv(m))
        V(lambda q: q.tensor_copy(TT(t + 1)[:, a:b], T.TI[:, a:b]), r=kb("TI", a, b), w=tk(t + 1, a, b), c=cv(m))
        V(lambda q: q.tensor_scalar(TH(t + 1, a, b), TT(t + 1)[:, a:b], -2048.0, None, A.add), r=tk(t + 1, a, b), w=fk(t + 1, a, b), c=cv(m, .5))

    def bind(t):
        zb = T.ZC[:, 64:118]
        a = CH[t][-1][0] if t == 2 and TAIL else 288
        x = 36 + a // 16
        PE([lambda q: q.matmul(zb, T.cB[0:1, 0:128], T.ones[0:1, 0:54], True, False)] +
           [lambda q, k=k: q.matmul(zb[:, 0:x], T.SELK[:, 128 * k:128 * k + 128], T.SG[:, 2 * k + 1:2 * SW + 2 * a:32], False, k == 15) for k in range(16)],
           kb("SG1", 0, LW) + kb("SG2", 0, LW) + kb("SG3", 0, min(a, LW)) + SELK + ["cB", "ones"], ["zB"], cmm(54, 17), ["bC"])
        c = 18 if t == 2 else 36
        ds = range(c // 18)
        for d in ds:
            V(lambda q, d=d: q.tensor_tensor(KM[:, 0:3, 18 * d:18 * d + 18], zb, KS[:, 18 * d:18 * d + 54], A.min),
              r=["zB"] + ["KS%d" % e for e in range(d, d + 3)], w=["KM_%d" % d], bk=["bC"])
        V(lambda q: q.tensor_tensor(T.k1[:, :, 0:c], KM[:, 0:2, 0:c], KM[:, 2:4, 0:c], A.max), r=["KM3"] + ["KM_%d" % d for d in ds], w=["k1"], c=cv(4 * c))
        V(lambda q: q.tensor_tensor(T.kI[:, 0:c], T.k1[:, 0, 0:c], T.k1[:, 1, 0:c], A.max), r=["k1"], w=["kI"], c=cv(2 * c))
        V(lambda q: q.tensor_scalar(T.kJ[:, 0:c], T.kI[:, 0:c], 4095, None, A.bitwise_and), r=["kI"], w=["kJ"])
        if t < 2 or t not in YT or TAIL:
            V(lambda q: q.tensor_copy(T.LU[:, 18:18 + c], T.kJ[:, 0:c]), r=["kJ"], w=["LU%d" % (d + 1) for d in ds])
        if t < 2 or t in YT:
            V(lambda q: q.tensor_tensor(KS[:, 18:18 + c], T.kJ[:, 0:c], T.KO[:, 0:c], A.add), r=["kJ", "KO"], w=["KS%d" % (d + 1) for d in ds], c=cv(2 * c))

    def outv(t):
        a = CH[t][-1][0] if t == 2 and TAIL else 256
        x = slice(256 * t, 256 * t + a)
        if t in YT:
            V(lambda q: q.transpose(T.YW[:, 32 * t:32 * t + 32], KS[:, 18:50]), r=["KS1", "KS2"], w=["YV%d" % t])
            dma("y", [(T.yv[gg:gg + 1, x], T.YW[gg // 2 * 32:gg // 2 * 32 + a // 16, 32 * t + gg % 2 * 16:32 * t + gg % 2 * 16 + 16]) for gg in range(8)],
                ["YV%d" % t], ["yv%d" % t], a // 2, 64)
        else:
            move("s", T.YV[:, x], idw.indirect(T.LU[:, 18:18 + a // 16]), IDW + ["LU1"], ["YV%d" % t], cgat(a))
            dma("y", [(T.yv[:, x], T.YV[0:128:16, x])], ["YV%d" % t], ["yv%d" % t], 16, 2 * a)
        if a < 256:
            m, z = 256 - a, T.ZR[:, 0:256 - a]
            for d in (1, 2):
                move("s", T.KF[:, 128 * d:128 * d + m], idw.indirect(T.LU[:, 18 * d + a // 16:18 * d + 16]), IDW + ["LU%d" % d], ["KF%d" % d],
                     cgat(m), scale=2.0 * d - 3)
            PE([lambda q: q.matmul(z, T.cB[0:1, 0:128], T.ones[0:1, 0:m], True, False),
                lambda q: q.matmul(z, T.BE[:], T.SG[:, 2 * SW + 2 * a + 1:2 * SW + 512:2], False, True)],
               kb("SG3", a, 256) + ["BE", "cB", "ones"], ["zR"], cmm(m, 2), ["bR"])
            V(lambda q: q.tensor_tensor(T.KF[:, 0:m], z, T.KF[:, 256:256 + m], A.min), r=["zR", "KF2"], w=["KF0"], c=cv(m), bk=["bR"])
            V(lambda q: q.tensor_tensor(T.KF[:, 256:256 + m], T.KF[:, 0:m], T.KF[:, 128:128 + m], A.max), r=["KF0", "KF1"], w=["KF2"], c=cv(2 * m))
            S(lambda q: q.activation(T.YV[:, 512 + a:768], T.KF[:, 256:256 + m], AF.Abs), r=["KF2"], w=["YVf"], c=cv(m))
            dma("y", [(T.yv[:, 512 + a:768], T.YV[0:128:16, 512 + a:768])], ["YVf"], ["yvf"], 8, 4 * m)

    def outh(t, a, b):
        dma("y", [(T.yh[:, 256 * t + a:256 * t + b], PKn(t + 1, a, b))], pk(t + 1, a, b), ["yh%d_%d" % (t, a)], 128, 4 * (b - a))

    def dedupe(t):
        cl, ck = TT(t)[:, 256:LW], tk(t, 256, LW)
        if RBP:
            PE([lambda q, r=r: q.matmul(T.ZM[:, r:256:16], T.SELT[:, 128 * r:128 * r + 128], TH(t, 256, LW), True, True) for r in range(16)],
               ["SELT0", "SELT1"] + fk(t, 256, LW), ["zU"], cmm(16, 16), ["bM"])
        else:
            move("s", T.RB[:], T.IDW[:].indirect(cl), IDW + ck, ["RB"], cgat(256), scale=-SQ, bias=2048 * SQ)
        move("s", T.SV[:, 768 * t:768 * t + 256], win(t).indirect(cl), wkey(t) + ck, ["SV%d" % t], cgat(256))
        for c in range(16 * RBP):
            o = SEG * (c // CB)
            eq, rb = T.EQ[:, o + seg[c % CB]:o + seg[c % CB + 1]], T.ZM[:, 16 * c:WB * (c // CB + 1)]
            S(lambda q, c=c, eq=eq, rb=rb: q.activation(eq, rb, AF.Square, bias=T.CF[:, c:c + 1], scale=SQ),
              ["zU", "CF"], ["EQ%d" % c], cv(WB - 16 * (c % CB)), ["bM"])
        for c in range(0 if RBP else 16):
            o = SEG * (c // CB)
            eq, rb = T.EQ[:, o + seg[c % CB]:o + seg[c % CB + 1]], T.RB[:, 16 * c:WB * (c // CB + 1)]
            VS("s", lambda q, c=c, eq=eq, rb=rb: q.tensor_scalar(eq, rb, T.CF[:, c:c + 1], SQ * SQ, A.not_equal, A.mult),
               lambda q, c=c, eq=eq, rb=rb: q.activation(eq, rb, AF.Square, bias=T.CF[:, c:c + 1], scale=-1.0),
               ["RB", "CF"], ["EQ%d" % c], cv(WB - 16 * (c % CB)))
        sk = []
        for b in range(NB):
            for x, y in zip(SP, SP[1:]):
                o = slice(SEG * b + seg[x], SEG * b + seg[y])
                sk.append("SC%d" % (CB * b + x))
                V(lambda q, o=o, x=x, y=y: q.tensor_tensor_scan(T.SC[:, o], T.EM[:, seg[x]:seg[y]], T.EQ[:, o], 1.0e16, A.max, A.min),
                  r=["EM"] + ["EQ%d" % (CB * b + c) for c in range(x, y)], w=sk[-1:], c=cv(seg[y] - seg[x], .5))
        V(lambda q: q.tensor_tensor(T.dE[:], T.SC[:, 0:NB * SEG].indirect(T.E16[:, 0:1]), T.DJ[:], A.subtract), r=sk + ["E16", "DJ"], w=["dE"], c=cgat(16))
        V(lambda q: q.tensor_tensor(T.dF[:], T.dE[:], T.CF[:], A.min), r=["dE", "CF"], w=["dF"])
        V(lambda q: q.tensor_scalar(T.SL[:, 16 * t:16 * t + 16], T.dF[:], -1.0 / SQ, 2048.0, A.mult, A.add), r=["dF"], w=["SL%d" % t])

    others = [d for d in range(n) if d != rank]
    common = [e for e in topo.engines(core, T.cores[others[0]]) if all(e in topo.engines(core, T.cores[d]) for d in others)]
    mask = sum(1 << e for e in common)

    def send(t):
        for key, buf, land, w, st in (("SV%d" % t, T.SV, T.LV, 256, 768), ("SL%d" % t, T.SL, T.LL, 16, 64)):
            ids, dsts = [], []
            for d in others:
                rid, pid = topo.addr(T.cores[d])[0:2]
                slot = (rank - d - 1) % n
                ids.append(DstId(rid=rid, pnc=pid))
                dsts.append(land[:, st * t + w * slot:st * t + w * slot + w])
            tr = RemoteDMATransfer(dst_ids=ids, dma_engine_mask=mask, remote_sem=T.sem["arr" + key],
                                   srcs=[buf[:, w * t:w * t + w]], dsts=dsts, alu_op=0)
            add("g", "r", tr, [key], ["sent" + key], cfix(3.0 if t == 0 and w == 256 else 0.8), rows=48, nbytes=48 * 2 * w * XB)
            add("n", "n", ("arr" + key, len(common) * len(others)), ["sent" + key], ["got" + key], cfix(0.0))

    out = lambda t, i, k=1: T.SV[:, 768 * t + 256 * i:768 * t + 256 * (i + k)]
    land = lambda t, i, k=1: T.LV[:, 1536 * t + 256 * i:1536 * t + 256 * (i + k)]

    def post(key, moves, r, rb, lsem="lsem", first=False):
        share = len(common) // len(moves)
        trs, rows, got = [], 0, 0
        for k, (src, to) in enumerate(moves):
            ids = [DstId(rid=x[0], pnc=x[1]) for x in (topo.addr(T.cores[(rank + s) % n]) for s, _ in to)]
            trs.append(RemoteDMATransfer(dst_ids=ids, dma_engine_mask=sum(1 << e for e in common[share * k:share * k + share]),
                                         remote_sem=T.sem["arr" + key], srcs=[src], dsts=[x for _, x in to], alu_op=0))
            rows, got = max(rows, 128 * len(to) // share), got + share * len(to)
        add("g", "r", (trs, lsem, share * len(moves)), r, ["sent" + key], cfix(3.0 if first else 0.8), rows=rows, nbytes=rows * rb * XB)
        add("n", "n", ("arr" + key, got), ["sent" + key], ["got" + key], cfix(0.0))

    def offers(t):
        slot = lambda buf, to: [(s, buf[:, 64 * t + 16 * (n - 1 - s):64 * t + 16 * (n - s)]) for s in to]
        post("R%d" % t, [(TT(t)[:, 256:LW], slot(T.LR, (n - 1, n - 2)))], tk(t, 256, LW), 32, "lr%d" % t, t == 0)
        add("n", "n", ("lr%d" % t, len(common)), ["sentR%d" % t], ["freeR%d" % t], cfix(0.0))
        post("SV%d" % t, [(out(t, 0), [(n - 1, land(t, 0)), (1, land(t, 5))] + [(n - 2, land(t, 3))] * XS3)], ["SV%d" % t], 512)
        post("SL%d" % t, [(T.SL[:, 16 * t:16 * t + 16], slot(T.LL, range(1, n)))], ["SL%d" % t], 32)
        for b in range(NB):
            to, x = T.O[:].indirect(T.SL[:, 16 * t + CB * b:16 * t + CB * b + CB]), out(t, 0)[:, WB * b:WB * b + WB]
            V((lambda q, to=to, x=x: q.tensor_tensor(to, x, T.big[:, WB * t - WB:WB * t], A.mult)) if t else (lambda q, to=to, x=x: q.tensor_copy(to, x)),
              r=["SV%d" % t, "SL%d" % t] + (["big%d" % t] if t else ["Oz%d" % i for i in range(NF)]), w=["O"], c=csca(WB))
        for i in range(2):
            move("s", out(t, 1 + i), T.O[:].indirect(T.LR[:, 64 * t + 16 * i:64 * t + 16 * i + 16]), ["O", "gotR%d" % t], ["SX%d%d" % (t, i)],
                 cgat(256), scale=2.0 ** (-16 * t))
        near, far = (out(t, 1, 2), [(n - 1, land(t, 1, 2))]), (out(t, 0, 2), [(n - 2, land(t, 3, 2))])
        if XS3:
            post("X%d" % t, [near], ["SX%d0" % t, "SX%d1" % t], 1024)
            post("Z%d" % t, [(out(t, 1), [(n - 2, land(t, 4))])], ["SX%d0" % t], 512)
        elif XONE:
            post("X%d" % t, [near, far], ["SV%d" % t, "SX%d0" % t, "SX%d1" % t], 1024)
        else:
            post("X%d" % t, [far], ["SV%d" % t, "SX%d0" % t], 1024)
            post("Z%d" % t, [near], ["SX%d0" % t, "SX%d1" % t], 1024)

    def settle(t):
        N, nk = (T.p0, "win4") if t == 2 else (T["F%d" % (t + 1)], "win%d" % (t + 1))
        nr = ["dump%d" % (t + t // 2), "gotSL%d" % t] + ["cp%d_%d" % (t, x) for x in range(NF)]
        for i in range(3):
            x = slice(256 * i, 256 * i + 256)
            z, zk = T.ZX[:, 256 * (i % 2):256 * (i % 2) + 256], ["zX%d" % (i % 2)]
            if i < 2:
                move("s", T.pg[:, x], win(t).indirect(T.LR[:, 64 * t + 16 * i:64 * t + 16 * i + 16]), wkey(t) + ["gotR%d" % t], ["pg%d" % i], cgat(256))
            else:
                move("s", T.pg[:, x], (T["F%d" % t] if t else T.p0)[:].indirect(T.LL[:, 64 * t + 16 * i:64 * t + 16 * i + 16]),
                     wkey(t) + ["gotSL%d" % t, "dump%d" % (t - 1 if t else 3)], ["pg%d" % i], cgat(256))
            parts = [(T.IDH[:, 0:128], T.pg[:, x])] + [(T.IDI[:], land(t, k)) for k in ((0,), (1, 3), (5, 2, 4))[i]]
            PE([lambda q, k=k, z=z, p=p, last=len(parts) - 1: q.matmul(z, p[0], p[1], k == 0, k == last) for k, p in enumerate(parts)],
               ["IDI", "IDH", "pg%d" % i, "gotSV%d" % t] + ["gotX%d" % t] * (i > 0) + ["gotZ%d" % t] * (i > XS3 and not XONE), zk, cmm(256, len(parts)), ["bX"])
            if FLS[t][i] == "v":
                V(lambda q, x=x, z=z: q.tensor_scalar(T.i1[:, x], z, -0.4921875, 255.0, A.add, A.min), r=zk, w=["i1%d" % i], c=cv(256), bk=["bX"])
            else:
                S(lambda q, x=x, z=z: q.activation(T.r1[:, x], z, AF.Relu, bias=col(TOP), scale=-1.0), r=zk + ["TOP"], w=["r1%d" % i], c=cv(256), bk=["bX"])
                S(lambda q, x=x: q.activation(T.r2[:, x], T.r1[:, x], AF.Copy, bias=MAGIC + 255, scale=-1.0), r=["r1%d" % i], w=["i1%d" % i], c=cv(256))
                if t == 2:
                    S(lambda q, x=x: q.activation(T.r2[:, x], T.r2[:, x], AF.Copy, bias=-MAGIC), w=["i1%d" % i], c=cv(256))
            for b in range(NB):
                o, y = T.LL[:, 64 * t + 16 * i + CB * b:64 * t + 16 * i + CB * b + CB], slice(256 * i + WB * b, 256 * i + WB * b + WB)
                if t == 2 or FLS[t][i] == "v":
                    f = lambda q, o=o, y=y, src=T.i1 if FLS[t][i] == "v" else T.r2: q.tensor_copy(N[:].indirect(o), src[:, y])
                else:
                    f = lambda q, o=o, y=y: q.tensor_scalar(N[:].indirect(o), T.r2[:, y], 1.0, -MAGIC, A.mult, A.add)
                V(f, r=["i1%d" % i] + nr, w=[nk], c=csca(WB))

    def update(t):
        F = T.F1 if t == 2 else T["F%d" % (t + 1)]
        wk = "win1" if t == 2 else "win%d" % (t + 1)
        N, nk = (T.p0, "win4") if t == 2 else (T["F%d" % (t + 1)], "win%d" % (t + 1))
        nr = ["dump3"] + ["cp%d_%d" % (t, x) for x in range(NF)] if t == 2 else []
        L = lambda i: T.LL[:, 64 * t + 16 * i:64 * t + 16 * i + 16]
        lk = "gotSL%d" % t
        cols = lambda i: slice(256 * i, 256 * i + 256)

        def scatter(f, i, r, w, row=False):
            for b in range(NB):
                o, x = 64 * t + 16 * i + CB * b, slice(256 * i + WB * b, 256 * i + WB * b + WB)
                V(lambda q, o=o, x=x: f(q, T.LL[:, o:o + CB], x), r=r + [lk], w=[w], c=csca(WB), row=NOWAIT and (row or b > 0))
        for i in range(3):
            if UF[t][i] != "p":
                move("s", T.sv[:, cols(i)], T.LV[:, 768 * t + 256 * i:768 * t + 256 * i + 256], ["gotSV%d" % t, "INC"], ["sv%d" % i], cv(256), scale=col(INC))
        fr = [wk, "dump%d" % (t % 2), lk] + ["cp%d_%d" % (t + t // 2, i) for i in range(NF)]
        zt = T.ZX[:, 0:256]
        for i in range(3):
            if UF[t][i] == "p":
                move("s", T.g1[:, cols(i)], F[:].indirect(L(i)), fr, ["g1_%d" % i], cgat(256))
                PE([lambda q: q.matmul(zt, T.IDI[:], T.LV[:, 768 * t + 512:768 * t + 768], True, False),
                    lambda q: q.matmul(zt, T.IDN[:, 0:128], T.g1[:, cols(2)], False, True)], ["IDI", "IDN", "gotSV%d" % t, "g1_2"], ["zX"], cmm(256, 5), ["bX"])
            elif UF[t][i] == "g":
                move("s", T.g1[:, cols(i)], F[:].indirect(L(i)), fr, ["g1_%d" % i], cgat(256))
                scatter(lambda q, o, x: q.tensor_tensor(F[:].indirect(o), T.g1[:, x], T.sv[:, x], A.add), i, ["g1_%d" % i, "sv%d" % i], wk)
            else:
                V(lambda q, i=i: q.tensor_tensor(T.g1[:, cols(i)], F[:].indirect(L(i)), T.sv[:, cols(i)], A.add), r=fr + ["sv%d" % i], w=["g1_%d" % i], c=cgat(256))
                if i < 2:
                    scatter(lambda q, o, x: q.tensor_copy(F[:].indirect(o), T.g1[:, x]), i, ["g1_%d" % i], wk)

        for i in range(3):
            src, r, c = (F[:].indirect(L(i)), [wk, lk], cgat(256)) if UF[t][i] == "g" else (T.g1[:, cols(i)], ["g1_%d" % i], cv(256))
            bk = []
            if UF[t][i] == "p":
                src, r, bk = zt, ["zX"], ["bX"]
            if FLS[t][i] == "v":
                V(lambda q, i=i, src=src: q.tensor_scalar(T.i1[:, cols(i)], src, -0.4921875, 255.0, A.add, A.min), r=r, w=["i1%d" % i], c=c, bk=bk)
            else:
                S(lambda q, i=i, src=src: q.activation(T.r1[:, cols(i)], src, AF.Relu, bias=col(TOP), scale=-1.0), r=r + ["TOP"], w=["r1%d" % i], c=c, bk=bk)
                S(lambda q, i=i: q.activation(T.r2[:, cols(i)], T.r1[:, cols(i)], AF.Copy, bias=MAGIC + 255, scale=-1.0), r=["r1%d" % i], w=["i1%d" % i], c=cv(256))
                if t == 2:
                    S(lambda q, i=i: q.activation(T.r2[:, cols(i)], T.r2[:, cols(i)], AF.Copy, bias=-MAGIC), w=["i1%d" % i], c=cv(256))
        for i in range(3):
            src = T.i1 if FLS[t][i] == "v" else T.r2
            if t == 2 or FLS[t][i] == "v":
                scatter(lambda q, o, x, src=src: q.tensor_copy(N[:].indirect(o), src[:, x]), i, ["i1%d" % i] + nr, nk, i > 0)
            else:
                scatter(lambda q, o, x: q.tensor_scalar(N[:].indirect(o), T.r2[:, x], 1.0, -MAGIC, A.mult, A.add), i, ["i1%d" % i] + nr, nk, i > 0)

    conv(1)
    parents(1)
    conv(2)
    for e in (2, 3):
        if VM and e == 3:
            parents(2)
        package(0, e)
        first(e) if e in FIRST else clist(0, e)
    for t in range(3):
        w = 4096 // NF
        new = T.p0 if t == 2 else T["F%d" % (t + 1)]
        for dst, key, old in [(T.F1, 3, wkey(1))] * (t == 2 and t not in XC) + [(new, t, wkey(0) if t == 2 else [])]:
            for i in range(NF):
                G(lambda q, t=t, i=i, dst=dst: q.affine_select(dst[:, w * i:w * i + w], win(t)[:, w * i:w * i + w], [[0, w]], A.is_equal, 0.0, 0, 0),
                  r=wkey(t), w=["cp%d_%d" % (key, i)] + (old if i == 0 else []), c=cgp(w, 0.17))
                if i and old:
                    ops[-1]["order"].append(len(ops) - 2)
        for i in range(NF if t == 0 and XC else 0):
            if i < OV:
                V(lambda q, i=i: q.memset(T.O[:, (w + 32) * i:(w + 32) * (i + 1)], 0.0), w=["Oz%d" % i], c=cv(w + 32, .5))
            elif i < OV + OS:
                S(lambda q, i=i: q.activation(T.O[:, (w + 32) * i:(w + 32) * (i + 1)], T.ones[:, 0:w + 32], AF.Copy, scale=0.0), r=["ones"], w=["Oz%d" % i], c=cv(w + 32))
            else:
                G(lambda q, i=i: q.iota(T.O[:, (w + 32) * i:(w + 32) * (i + 1)], [[0, w + 32]], 0, 0, **fl), w=["Oz%d" % i], c=cgp(w + 32))
        tag[0] = "parents%d" % t
        if t < 2:
            if t or not VM:
                parents(2)
            conv(3)
        keys(t)
        for e in (1, 2, 3):
            for a, b in YP[t]:
                tag[0] = "y%d%d_%d" % (t, e, a // 96)
                gy(t, e, a, b)
            for h, (a, b) in enumerate(CH[t]):
                tag[0] = "x%d%d_%d" % (t, e, h)
                diff(t, e, h)
                for x, y in split(a, b, XW[t]):
                    gx(t, e, x, y)
                tops(t, e, h)
        tag[0] = "claims%d" % t
        dedupe(t)
        offers(t)
        tag[0] = "prices%d" % t
        settle(t) if t in XC else update(t)
        if t == 2:
            for i in range(0, 128, 128 // NY):
                dma("y", [(T.yp[i:i + 128 // NY, :], T.p0[i:i + 128 // NY, 0:4096])], ["win4"], ["yp%d" % i], 128 // NY, 8192)
            for a, b in OH:
                outh(t, a, b)
        else:
            clist(t + 1, 1)
            for a, b in MP:
                tag[0] = "max%d_%d" % (t, a)
                gm(t, a, b)
            for a, b in TG[t]:
                tag[0] = "next%d_%d" % (t, a)
                tnew(t, a, b)
            outh(t, 0, 256)
        tag[0] = "bind%d" % t
        bind(t)
        outv(t)
        if t < 2:
            for e in (2, 3):
                package(t + 1, e)
                clist(t + 1, e)

    for o in ops:
        for t in range(3):
            if o["tag"] in ("x%d1_0" % t, "x%d2_0" % t, "x%d3_0" % t, "claims%d" % t, "prices%d" % t) or o["tag"][0:2] == "y%d" % t and o["name"].endswith("_32"):
                o["up"] += UPK[t]
    order = plan(ops)
    total, snap, tok = {}, {}, {}
    seen = {e: {} for e in Q}
    nd = [0]

    def merge(d, s, v):
        if d.get(s, 0) < v:
            d[s] = v

    def sync(e, toks):
        best = {}
        for s, v in toks:
            if seen[e].get(s, 0) < v:
                merge(best, s, v)
        for s in sorted(best):
            if any(o != s and best[o] and snap.get((o, best[o]), {}).get(s, 0) >= best[s] for o in best):
                best[s] = 0
        for s in sorted(best):
            v = best[s]
            if v:
                Q[e].wait_ge(T.sem[s], v)
                merge(seen[e], s, v)
                for o, w in snap.get((s, v), {}).items():
                    merge(seen[e], o, w)

    for i in order:
        o = ops[i]
        e, kind = PLAN["queues"][i], o["kind"]
        body = o["both"][e] if o["both"] else o["body"]
        if kind == "n":
            total[body[0]] = body[1]
            tok[i] = body
            continue
        sync(e, [tok[p] for p in o["full"] if p in tok])
        if kind == "c":
            s = CSEM[e]
            for f in body:
                f(Q[e]).then_inc(T.sem[s], 1)
                total[s] = total.get(s, 0) + 1
                snap[(s, total[s])] = dict(seen[e])
            tok[i] = (s, total[s])
        elif kind == "d":
            s = "d%d" % nd[0]
            nd[0] += 1
            for out, in_ in body:
                Q[e].dma_start(out, in_).then_inc(T.sem[s], 16)
            total[s] = 16 * len(body)
            tok[i] = (s, total[s])
            snap[tok[i]] = dict(seen[e])
        else:
            g.remote_dma_fused(body[0], local_sem=T.sem[body[1]])
            total[body[1]] = total.get(body[1], 0) + body[2]
    for s in sorted(total):
        if seen["g"].get(s, 0) < total[s]:
            g.wait_ge(T.sem[s], total[s])
